import numpy as np, ml_dtypes
CORES = [23,119,17,113]
N = 4
BF = ml_dtypes.bfloat16
W, A, S, CAP, RO = 4096, 1024, 4, 128, 5
P, BL = A // S, W // CAP
WT = 2 * np.arange(16) + 1
def counts(rng, fat):
    return np.where(fat, rng.integers(9, 17, fat.shape), rng.integers(0, 9, fat.shape))
def cols(rng, n, top):
    on = np.argsort(rng.random((N, 8, 16, W)), axis=2) < n[:, :, None, :]
    return np.where(on, 1 + (top * rng.random((N, 8, 16, W))).astype(np.int64), 0)
def lines(rng, fat, share):
    o = np.argsort(np.where(fat, 0.0, 1.0) + 0.5 * rng.random((N, 8, W)), axis=-1); nf = np.add.reduce(fat.astype(np.int64), axis=-1)[:, :, None, None]
    v = rng.random((N, 8, 16, A))
    k = np.where(rng.random((N, 8, 16, A)) < share, (v * nf).astype(np.int64), nf + (v * (W - nf)).astype(np.int64))
    return np.take_along_axis(o, k.reshape(N, 8, 16 * A), 2).reshape(N, 8, 16, A)
def hop(e, u):
    return (((e * u) >> 5) + e) & (W - 1)
def first(X):
    u = np.add.reduce(X * WT.reshape(1, 1, 16, 1), axis=2) & (W - 1); h = hop(np.arange(W).reshape(1, 1, W), u)
    y = np.take_along_axis(X, h[:, :, None, :], 3)
    return np.add.reduce(np.sign(y - X), axis=2), np.add.reduce((X > 0).astype(np.int64), axis=2)
def top16(s):
    v = np.full(16, 255); d = (65280 - s) & (W - 1)
    for w in range(15, -1, -1):
        c = min(254, d // (2 * w + 1)); v[w] -= c; d -= c * (2 * w + 1)
    return v
def pack(X, E, M):
    return {"xt": X.reshape(N, 128, W).astype(np.float32).astype(BF), "led": E.reshape(N, 128, A).astype(np.int32), "mk": M.reshape(N, 128, A).astype(np.float32).astype(BF)}
def setup_inputs(rng):
    fat = rng.random((N, 8, W)) < rng.choice(np.array([0.3, 0.5, 0.7]), (N, 8, 1))
    X = cols(rng, counts(rng, fat), 255)
    share = rng.choice(np.array([0.01, 0.05, 0.15, 0.6]), (N, 8, 1, A)) * rng.choice(np.array([0.2, 1.0, 1.5]), (N, 8, 1, 1))
    return pack(X, lines(rng, fat, share), rng.integers(0, 2, (N, 8, 16, A)))
def setup_inputs_spread(rng):
    fat = rng.random((N, 8, W)) < rng.choice(np.array([0.2, 0.5, 0.8]), (N, 8, 1))
    top = np.minimum(np.exp2(8 * rng.random((N, 8, 1, W))).astype(np.int64), 255)
    X = cols(rng, counts(rng, fat), top)
    E = lines(rng, fat, rng.choice(np.array([0.01, 0.05, 0.2, 0.7]), (N, 8, 1, A)))
    low = (W * rng.random((N, 8, 16, A)) ** 4).astype(np.int64); E = np.where(rng.random((N, 8, 1, A)) < 0.25, low, E)
    return pack(X, E, (rng.random((N, 8, 16, A)) < rng.random((N, 8, 1, A))).astype(np.int64))
def setup_inputs_ends(rng):
    kind = rng.integers(0, 3, (N, 8, 1, W))
    X = np.where(kind == 0, 0, np.where(kind == 1, 255, 255 * rng.integers(0, 2, (N, 8, 16, W))))
    X[..., 1] = 1; X[..., hop(1, 256)] = 255
    X[..., 2] = 255; X[..., hop(2, 65280 & (W - 1))] = 0
    X[..., W - 2] = 254; X[..., hop(W - 2, 65024 & (W - 1))] = 255
    X[..., W - 1] = top16(W - 1); X[..., hop(W - 1, W - 1)] = 0
    sh = (N, 8, 16, A)
    other = np.where(rng.random(sh) < 0.5, rng.choice(np.array([1, 2, W - 2]), sh), rng.integers(0, W, sh))
    E = np.where(rng.random(sh) < 0.7, (W - 1) * rng.integers(0, 2, sh), other)
    M = (rng.random(sh) < rng.choice(np.array([0.0, 0.5, 1.0]), (N, 8, 1, A))).astype(np.int64)
    i = np.arange(P) * S; q = N - 1
    for r in (0, q):
        for g in range(8):
            k = 2 * rng.integers(0, 8, P); E[r, g, k, i] = W - 1; M[r, g, k, i] = 1
    E[1, 0, :, 0::S] = 0; M[1, 0, :, 0::S] = 0
    E[q, 0, :, 0] = 0; M[q, 0, :, 0] = 0
    a, b, c, d = int(i[CAP - 1]), int(i[P - 1]), int(i[P - 2]), int(i[3])
    E[q, 7, :, a] = W - 1; M[q, 7, :, a] = 1
    E[q, 7, :, b] = 0; M[q, 7, :, b] = 0; E[q, 7, 14:, b] = W - 1; M[q, 7, 14:, b] = 1
    E[q, 7, :, c] = 0; M[q, 7, :, c] = 0; E[q, 7, 14, c] = W - 2; M[q, 7, 14, c] = 1; E[q, 7, 15, c] = 1
    E[:, 7, 0::2, d] = 2; M[:, 7, 0::2, d] = 1; E[:, 7, 1::2, d] = W - 1; M[:, 7, 1::2, d] = 0
    return pack(X, E, M)
def setup_inputs_corners(rng):
    fat = rng.random((N, 8, W)) < 0.5; X = cols(rng, counts(rng, fat), 255)
    E = lines(rng, fat, 0.1); M = rng.integers(0, 2, (N, 8, 16, A)); g, n = first(X)
    room = (0, 1, CAP - 1, CAP, CAP + 1, P, CAP, P - 1); even = np.arange(16)[:, None] % 2 == 0
    for q in range(N):
        for b in range(8):
            gg = g[q, b]; hot = np.flatnonzero((n[q, b] >= 9) & (gg != 0)); thin = np.flatnonzero(n[q, b] <= 8)
            c = int(rng.choice(np.array(room)))
            if q == 0: c = room[b]
            if q == N - 1: c = room[(b + 4) % 8]
            o = np.concatenate([np.array([P - 1]), rng.permutation(P - 1)]); yes = o[:c]; z = np.zeros((1, P), bool); z[0, o[c:]] = True
            e = np.where(rng.random((16, P)) < 0.2, (W - 1) * rng.integers(0, 2, (16, P)), rng.integers(0, W, (16, P)))
            m = (rng.random((16, P)) < rng.choice(np.array([0.0, 0.5, 1.0]), (1, P))).astype(np.int64)
            ge = gg[e]; m = np.where(even & z & (ge != 0), (ge > 0).astype(np.int64), m)
            e = np.where(~even & z, rng.choice(thin, (16, P)), e)
            k = 2 * rng.integers(0, 8, c); hh = rng.choice(hot, c); e[k, yes] = hh; m[k, yes] = (gg[hh] < 0).astype(np.int64)
            E[q, b, :, 0::S] = e; M[q, b, :, 0::S] = m
    return pack(X, E, M)
def setup_inputs_ties(rng):
    fat = rng.random((N, 8, W)) < 0.5
    n = np.where(fat, np.where(rng.random((N, 8, W)) < 0.8, 9, 16), 8); X = cols(rng, n, rng.choice(np.array([1, 2, 3]), (N, 8, 1, W)))
    E = lines(rng, fat, rng.choice(np.array([0.02, 0.2, 0.5]), (N, 8, 1, A)))
    E = np.take_along_axis(E, rng.integers(0, 3, (N, 8, 16, A)), 2)
    return pack(X, E, (rng.random((N, 8, 16, A)) < rng.choice(np.array([0.1, 0.5, 0.9]), (N, 8, 1, A))).astype(np.int64))
def setup_inputs_deep(rng):
    fat = rng.random((N, 8, W)) < 0.5; X = cols(rng, counts(rng, fat), 255)
    X[..., 0] = 0
    X[..., 3] = 253; X[..., hop(3, 64768 & (W - 1))] = 255
    X[..., 5] = 252; X[..., hop(5, 64512 & (W - 1))] = 255
    X[..., 7] = 255; X[..., hop(7, 65280 & (W - 1))] = 255; X[..., hop(7, 62976 & (W - 1))] = 255
    X[..., 11] = W >> 8
    X[..., W - 3] = top16(W - 21); X[..., hop(W - 3, W - 21)] = 0; X[..., hop(W - 3, W - 21) + 1] = 255
    X[..., 1001] = 255; X[..., 0, 1001] = 254; X[..., hop(1001, 65279 & (W - 1))] = 0
    X[..., 13] = 0; X[..., 7:, 13] = 255; X[..., hop(13, 52785 & (W - 1))] = 0
    X[..., 17] = 0; X[..., :9, 17] = 255; X[..., hop(17, 20655 & (W - 1))] = 0
    E = lines(rng, fat, 0.1); M = rng.integers(0, 2, (N, 8, 16, A)); s, n = first(X)
    h = hop(np.arange(W).reshape(1, 1, W), np.add.reduce(X * WT.reshape(1, 1, 16, 1), axis=2) & (W - 1))
    kind = np.argsort(rng.random((N, 8, P)), axis=-1) % 7
    for q in range(N):
        for b in range(8):
            if b in (1, 6):
                far = np.arange(W) >= (W >> 2); nn = n[q, b]; hh = h[q, b]
                thin = np.flatnonzero((nn <= 8) & far); hot = np.flatnonzero((nn >= 9) & (s[q, b] < 0) & (nn[hh] <= 8) & far[hh])
                E[q, b] = rng.choice(thin, (16, A))
                c = int(rng.integers(CAP >> 3, (CAP >> 2) + 1)); i = S * rng.permutation(P)[:c]; k = 2 * rng.integers(0, 8, c)
                E[q, b, k, i] = rng.choice(hot, c); M[q, b, k, i] = 1
                continue
            for v in range(1, 7):
                i = S * np.flatnonzero(kind[q, b] == v); k = 2 * rng.integers(0, 8, len(i))
                E[q, b, :, i] = 0; M[q, b, :, i] = 0
                if v == 1:
                    for w, e, m in ((0, 3, 1), (2, 3, 1), (4, 3, 1), (6, 5, 1), (7, 7, 1), (8, 7, 0), (9, 7, 1), (10, 7, 0), (11, 7, 1), (12, 7, 0), (13, 7, 0), (14, 7, 0)):
                        E[q, b, w, i] = e; M[q, b, w, i] = m
                elif v == 2:
                    E[q, b, k, i] = W - 3; M[q, b, k, i] = 1
                elif v == 3:
                    E[q, b, k, i] = 11; M[q, b, k, i] = 1; E[q, b, k + 1, i] = 7
                else:
                    E[q, b, k, i] = (1001, 13, 17)[v - 4]; M[q, b, k, i] = 1
    return pack(X, E, M)
def check_inputs(d):
    bad = []
    for k, lo, hi in (("xt", 0, 255), ("led", 0, W - 1), ("mk", 0, 1)):
        v = np.asarray(d[k]).astype(np.float64)
        if np.min(v) < lo or np.max(v) > hi or np.any(v != np.floor(v)): bad.append("range of " + k)
    return bad
def look(X, ix):
    return np.take_along_axis(X, ix.reshape(N, 8, 1, 16 * P), 3).reshape(N, 8, 16, 16, P)
def reference(xt, led, mk):
    X = xt.astype(np.float32).astype(np.int64).reshape(N, 8, 16, W)
    E = led.astype(np.int64).reshape(N, 8, 16, A); M = mk.astype(np.float32).astype(np.int64).reshape(N, 8, 16, A)
    kappa = np.zeros((N, 1, 1, 1), np.int64); ks = np.arange(16).reshape(1, 1, 16, 1)
    for t in range(RO):
        c = t % S; e = E[:, :, :, c::S].copy(); m = M[:, :, :, c::S].copy()
        x = look(X, e); q = x.copy(); b = np.zeros((N, 8, 16, P), np.int64)
        for k in range(16):
            mm = m[:, :, k][:, :, None, :]
            if k % 2 == 0: b = b + mm * x[:, :, :, k]
            else:
                q[:, :, :, k] = np.minimum(b, x[:, :, :, k]); b = b - mm * q[:, :, :, k]
        u = np.add.reduce(WT.reshape(1, 1, 16, 1, 1) * q, axis=2) & (W - 1)
        h = (((e * u) >> 5) + e + kappa) & (W - 1)
        g = np.add.reduce(np.sign(look(X, h) - q), axis=2); over = np.add.reduce((q > 0).astype(np.int64), axis=2)
        con = (over >= 9) & (((m == 1) & (g < 0)) | ((m == 0) & (g > 0)))
        best = np.argmax(np.where(con, np.abs(g), 0), axis=2)
        flip = np.any(con, axis=2)
        win = flip[:, :, None, :] & (ks == best[:, :, None, :])
        E[:, :, :, c::S] = np.where(win, h, e); M[:, :, :, c::S] = np.where(win, 1 - m, m)
        f = flip.astype(np.int64); kappa = (np.add.reduce(f.reshape(N, 8 * P), axis=1) & 31).reshape(N, 1, 1, 1)
        place = np.add.accumulate(f, axis=2) - 1; go = flip & (place < CAP)
        qb = np.take_along_axis(q, best[:, :, None, None, :], 3)[:, :, :, 0]; ub = np.take_along_axis(u, best[:, :, None, :], 2)[:, :, 0]
        new = X.copy()
        for r in range(N):
            d = (r + 1 + t % (N - 1)) % N
            for v in range(8):
                i = np.flatnonzero(go[r, v]); col = BL * place[r, v, i] + (ub[r, v, i] & (BL - 1))
                new[d, v][:, col] = (X[d, v][:, col] + qb[r, v][:, i]) >> 1
        X = new
    return {"yx": X.reshape(N, 128, W).astype(np.float32).astype(BF), "yl": E.reshape(N, 128, A).astype(np.float32), "ym": M.reshape(N, 128, A).astype(np.float32).astype(BF)}

@@ -1,0 +1,552 @@
+from concourse.bass import DstId, RemoteDMATransfer
+from concourse.mybir import dt, AluOpType, AxisListType, ActivationFunctionType
+
+OP = AluOpType
+AF = ActivationFunctionType
+RO = 5
+XC = 16
+XW = XC + 512 * 32
+LOOK_S = ((0, 0), (0, 1))
+EVEN_V = (0, 1)
+
+SCRATCH = {"xw": ("sbuf", [128, XW], "bfloat16"), "alt": ("sbuf", [128, 2048], "bfloat16")}
+for _n, _w, _d in (
+        ("ei0", 1024, "int32"), ("ef", 1024, "float32"), ("mm", 1024, "bfloat16"), ("sgn", 1024, "bfloat16"), ("ylb", 1024, "float32"),
+        ("d0", 4096, "bfloat16"), ("bb", 4096, "bfloat16"), ("qq", 4096, "bfloat16"), ("dq", 4096, "bfloat16"), ("sg", 4096, "bfloat16"),
+        ("ov", 4096, "bfloat16"), ("yb", 4096, "bfloat16"),
+        ("dl16", 256, "uint16"), ("el16", 256, "uint16"), ("h16", 256, "uint16"), ("ei", 256, "int32"), ("ek", 256, "int32"),
+        ("ui", 256, "int32"), ("ua", 256, "int32"), ("ta", 256, "int32"), ("tb", 256, "int32"), ("tc", 256, "int32"), ("hh", 256, "int32"),
+        ("hf", 256, "float32"), ("de", 256, "float32"), ("td", 256, "float32"), ("tm", 256, "bfloat16"), ("av", 256, "float32"), ("ai", 256, "int32"),
+        ("pi", 1, "int32"), ("ci", 8, "int32"), ("cf", 32, "float32"), ("m1", 160, "float32"), ("si", 128, "float32"), ("clf", 8, "float32"),
+        ("cl", 8, "uint16"), ("icf", 16, "float32"), ("icn", 16, "bfloat16"), ("icr", 16, "bfloat16"), ("i16", 16, "int32"), ("mg", 128, "float32"),
+        ("idn", 128, "bfloat16"), ("nid", 128, "bfloat16"), ("nk", 128, "bfloat16"), ("g8", 8, "bfloat16"), ("rcp", 8, "bfloat16"),
+        ("wu", 144, "bfloat16"), ("pm", 512, "float32"), ("iv", 512, "float32"), ("nbl", 128, "bfloat16"), ("lt", 128, "bfloat16"),
+        ("idx", 128, "bfloat16"), ("t1", 128, "bfloat16"), ("am", 128, "bfloat16"), ("one", 128, "bfloat16"), ("mr", 128, "bfloat16"),
+        ("ke", 128, "bfloat16"), ("z16", 16, "bfloat16"),
+        ("ge", 256, "bfloat16"), ("gsg", 256, "bfloat16"), ("sgt", 256, "bfloat16"), ("kt0", 128, "bfloat16"), ("kt1", 128, "bfloat16"),
+        ("sc0", 128, "bfloat16"), ("sc1", 128, "bfloat16"), ("lm0", 128, "bfloat16"), ("lm1", 128, "bfloat16"), ("wn0", 128, "bfloat16"),
+        ("wn1", 128, "bfloat16"), ("nf", 16, "bfloat16"), ("nfs", 32, "bfloat16"), ("nfi", 16, "bfloat16"), ("kn", 16, "int32"), ("li", 16, "int32"),
+        ("lj", 16, "int32"), ("l16", 16, "uint16"), ("ofi", 16, "int32"), ("uwi", 16, "int32"), ("uwa", 16, "int32"), ("tgi", 16, "int32"),
+        ("kc", 1, "float32"), ("kci", 1, "int32"), ("kcj", 1, "int32"), ("kap", 1, "float32")):
+    SCRATCH[_n] = ("sbuf", [128, _w], _d)
+for _t in range(8):
+    SCRATCH["p%d" % _t] = ("psum", [128, 512], "float32")
+for _t in range(RO):
+    SCRATCH["qw%d" % _t] = ("sbuf", [128, 256], "bfloat16")
+    SCRATCH["lq%d" % _t] = ("sbuf", [128, 256], "bfloat16")
+    SCRATCH["tg%d" % _t] = ("sbuf", [128, 16], "uint16")
+    SCRATCH["lt%d" % _t] = ("sbuf", [128, 16], "uint16")
+SEMAPHORES = ["cv", "cs", "cp", "cg", "ls"] + ["aq%d" % _t for _t in range(RO)] + ["at%d" % _t for _t in range(RO)] \
+    + ["dm%d" % _t for _t in range(24)]
+
+PASSES = 12
+CYC = 0.001
+GAT = 0.00150
+SCA = 0.0030
+
+
+def rank_program(g, core, T, topo):
+    rank = T.rank_of(core)
+    if rank is None:
+        return
+    n_ranks = len(T.cores)
+    eng = {"v": g.vector, "s": g.scalar, "p": g.tensor, "g": g, "y": g.sync}
+    semname = {"v": "cv", "s": "cs", "p": "cp", "g": "cg"}
+
+    nodes = []
+    wr, rd, bank = {}, {}, {}
+    ndma = [0]
+
+    def node(q, calls, cost, R, W, B=(), kind="c", key=None, late=0.0, extra=()):
+        d = set(extra)
+        for (b, lo, hi) in R:
+            for (l, h, i) in wr.get(b, ()):
+                if l < hi and lo < h:
+                    d.add(i)
+        for (b, lo, hi) in W:
+            for (l, h, i) in wr.get(b, ()):
+                if l < hi and lo < h:
+                    d.add(i)
+            for (l, h, i) in rd.get(b, ()):
+                if l < hi and lo < h:
+                    d.add(i)
+        me = len(nodes)
+        order = set()
+        for b in B:
+            if b in bank:
+                (order if nodes[bank[b]]["q"] == q else d).add(bank[b])
+                for j in nodes[bank[b]]["chain"].get(b, ()):
+                    if nodes[j]["q"] != q:
+                        d.add(j)
+        chain = {}
+        for b in B:
+            last = {}
+            if b in bank:
+                for j in nodes[bank[b]]["chain"].get(b, ()):
+                    last[nodes[j]["q"]] = j
+                last[nodes[bank[b]]["q"]] = bank[b]
+            chain[b] = list(last.values())
+        nodes.append({"q": q, "calls": calls, "cost": cost, "deps": d, "order": order - d, "kind": kind, "key": key, "late": late, "chain": chain})
+        for b in B:
+            bank[b] = me
+        for (b, lo, hi) in W:
+            wr[b] = [e for e in wr.get(b, ()) if not (lo <= e[0] and e[1] <= hi)] + [(lo, hi, me)]
+            rd[b] = [e for e in rd.get(b, ()) if not (lo <= e[0] and e[1] <= hi)]
+        for (b, lo, hi) in R:
+            rd.setdefault(b, []).append((lo, hi, me))
+        return me
+
+    def dma(q, out, in_, R, W, by):
+        name = "dm%d" % ndma[0]
+        ndma[0] += 1
+        node(q, [lambda e: e.dma_start(out, in_)], 0.1, R, W, (), "d", name, 2.0 + by * 4e-6)
+
+    def A(b, lo=0, hi=1 << 20):
+        return (b, lo, hi)
+
+    def cy(n):
+        return max(64, n) * CYC
+
+    def mms(lst, n, R, B):
+        node("p", [lambda e, a=a: e.matmul(*a) for a in lst], len(lst) * n * CYC, R, [], B)
+
+    def ts(out, in0, s1, o1, R, W, B=(), s2=None, o2=None, n=64):
+        if o2 is None:
+            node("v", [lambda e: e.tensor_scalar(out, in0, s1, None, o1)], cy(n), R, W, B)
+        else:
+            node("v", [lambda e: e.tensor_scalar(out, in0, s1, s2, o1, o2)], cy(n), R, W, B)
+
+    def tt(out, a, b, o, R, W, B=(), n=64, cost=None):
+        node("v", [lambda e: e.tensor_tensor(out, a, b, o)], cost or cy(n), R, W, B)
+
+    def cp(out, in_, R, W, B=(), n=64, cost=None):
+        node("v", [lambda e: e.tensor_copy(out, in_)], cost or cy(n), R, W, B)
+
+    def scn(out, a, b, init, o1, o2, R, W, n):
+        node("v", [lambda e: e.tensor_tensor_scan(out, a, b, init, o1, o2)], cy(n), R, W)
+
+    def act(out, in_, f, R, W, B=(), n=64, cost=None, **kw):
+        node("s", [lambda e: e.activation(out, in_, f, **kw)], cost or cy(n), R, W, B)
+
+    def fill(ap, c, W, n=64):
+        node("v", [lambda e: e.memset(ap, c)], cy(n), [], W)
+
+    def iota(ap, pat, base, cm, W, n, fl=True):
+        if fl:
+            node("g", [lambda e: e.iota(ap, pat, base, cm, allow_small_or_imprecise_dtypes=True)], 0.13 + 2 * n * CYC, [], W)
+        else:
+            node("g", [lambda e: e.iota(ap, pat, base, cm)], 0.13 + 2 * n * CYC, [], W)
+
+    MM4 = [A("mm%d" % c) for c in range(4)]
+    dma("y", T.ei0[:], T.led[:], [], [A("ei0")], 524288)
+    dma("s", T.mm[:], T.mk[:], [], MM4, 262144)
+    dma("y", T.xw[:, XC:XC + 2048], T.xt[:, 0:2048], [], [A("xw", XC, XC + 2048)], 1048576)
+    dma("s", T.xw[:, XC + 2048:XC + 4096], T.xt[:, 2048:4096], [], [A("xw", XC + 2048, XC + 4096)], 1048576)
+    dma("y", T.xw[:, XC + 4096:XC + 8192], T.xt[:], [], [A("xw", XC + 4096, XC + 8192)], 2500000)
+    dma("s", T.xw[:, XC + 8192:XC + 12288], T.xt[:], [], [A("xw", XC + 8192, XC + 12288)], 2500000)
+
+    iota(T.pi[:], [[0, 1]], 0, 1, [A("pi")], 1, False)
+    iota(T.m1[:], [[1, 160]], 1, 0, [A("m1")], 160)
+    iota(T.clf[:], [[16, 8]], 15, 0, [A("clf")], 8)
+    iota(T.mg[:], [[16, 8], [0, 16]], 0, 0, [A("mg")], 128)
+    iota(T.si[:], [[0, 8], [1, 16]], 0, 0, [A("si")], 128)
+    iota(T.icf[:], [[16, 16]], 0, 1, [A("icf")], 16)
+    fill(T.xw[:, 0:16], 0.0, [A("xw", 0, 16)])
+    fill(T.xw[:, 1:2], 4096.0, [A("xw", 0, 16)])
+    fill(T.alt[:, 0::2], 4096.0, [A("alt", 0, 1)], 512)
+    fill(T.alt[:, 1::2], 0.0, [A("alt", 1, 2)], 512)
+
+    def ci(j):
+        return T.ci[:, j:j + 1]
+
+    def cf(j):
+        return T.cf[:, j:j + 1]
+
+    def rc(j):
+        return ("cf", j, j + 1)
+    ts(ci(0), T.pi[:], 15, OP.bitwise_and, [A("pi")], [("ci", 0, 1)])
+    ts(ci(1), T.pi[:], 3, OP.logical_shift_right, [A("pi")], [("ci", 1, 2)], (), 1, OP.bitwise_and)
+    ts(ci(2), T.pi[:], 1, OP.bitwise_and, [A("pi")], [("ci", 2, 3)])
+    ts(ci(3), T.pi[:], 1, OP.logical_shift_right, [A("pi")], [("ci", 3, 4)], (), 7, OP.bitwise_and)
+    ts(ci(4), T.pi[:], 7, OP.bitwise_and, [A("pi")], [("ci", 4, 5)])
+    cp(T.cf[:, 0:5], T.ci[:, 0:5], [("ci", 0, 5)], [("cf", 0, 5)])
+    cp(cf(5), T.pi[:], [A("pi")], [rc(5)])
+    tt(cf(6), cf(5), cf(0), OP.subtract, [rc(5), rc(0)], [rc(6)])
+    ts(cf(7), cf(2), -1.0, OP.mult, [rc(2)], [rc(7)], (), 1.0, OP.add)
+    ts(cf(8), cf(1), -1.0, OP.mult, [rc(1)], [rc(8)], (), 1.0, OP.add)
+    tt(cf(9), cf(6), cf(3), OP.add, [rc(6), rc(3)], [rc(9)])
+    ts(cf(10), cf(4), 2.0, OP.mult, [rc(4), rc(6)], [rc(10)], (), cf(6), OP.add)
+    for par in range(2):
+        for b in range(2):
+            j = 11 + 2 * par + b
+            ts(cf(j), cf(9), float(8 * b + 1), OP.add, [rc(9), rc(7), rc(2)], [rc(j)], (), cf(2 if par else 7), OP.mult)
+            j = 15 + 2 * par + b
+            ts(cf(j), cf(10), float(par + 1), OP.add, [rc(10), rc(1), rc(8)], [rc(j)], (), cf(1 if b else 8), OP.mult)
+    for j in range(4):
+        ts(T.pm[:, 128 * j:128 * j + 128], T.m1[:, 0:128], cf(11 + j), OP.is_equal, [A("m1"), rc(11 + j)], [("pm", j, j + 1)], n=128)
+        ts(T.iv[:, 128 * j:128 * j + 128], T.m1[:, 0:128], cf(15 + j), OP.is_equal, [A("m1"), rc(15 + j)], [("iv", j, j + 1)], n=128)
+    ts(cf(19), cf(0), 14.5, OP.is_lt, [rc(0)], [rc(19)])
+    ts(cf(20), cf(0), 14.5, OP.is_gt, [rc(0)], [rc(20)])
+    ts(cf(21), cf(0), 2.0, OP.mult, [rc(0)], [rc(21)], (), 1.0, OP.add)
+    ts(cf(22), cf(6), 16.0, OP.add, [rc(6)], [rc(22)])
+    ts(cf(23), cf(0), -1.0, OP.mult, [rc(0)], [rc(23)])
+    ts(cf(25), cf(6), 0.0625, OP.mult, [rc(6)], [rc(25)], (), 1.0, OP.add)
+    ts(cf(26), cf(5), 1.0, OP.add, [rc(5)], [rc(26)])
+    ts(T.wu[:], T.m1[:, 0:144], cf(22), OP.is_equal, [A("m1"), rc(22), rc(21)], [A("wu")], (), cf(21), OP.mult, n=144)
+    ts(T.idn[:], T.m1[:, 0:128], cf(26), OP.is_equal, [A("m1"), rc(26)], [A("idn")], n=128)
+    ts(T.nid[:], T.m1[:, 0:128], cf(26), OP.is_equal, [A("m1"), rc(26)], [A("nid")], (), -1.0, OP.mult, n=128)
+    ts(T.idx[:], T.m1[:, 0:128], cf(26), OP.is_equal, [A("m1"), rc(26)], [A("idx")], (), 256.0, OP.mult, n=128)
+    ts(T.nk[:], T.m1[:, 0:128], cf(26), OP.is_equal, [A("m1"), rc(26), rc(23)], [A("nk")], (), cf(23), OP.mult, n=128)
+    ts(T.g8[:], T.m1[:, 0:8], cf(25), OP.is_equal, [A("m1"), rc(25)], [A("g8")], (), 16.0, OP.mult)
+    ts(T.rcp[:], T.m1[:, 0:8], cf(25), OP.is_equal, [A("m1"), rc(25)], [A("rcp")])
+    ts(T.nbl[:], T.mg[:], cf(6), OP.is_equal, [A("mg"), rc(6)], [A("nbl")], (), -1.0, OP.mult, n=128)
+    ts(T.lt[:], T.m1[:, 0:128], cf(26), OP.is_gt, [A("m1"), rc(26)], [A("lt")], n=128)
+    tt(T.t1[:], T.nbl[:], T.lt[:], OP.mult, [A("nbl"), A("lt")], [A("t1")], n=256)
+    tt(T.am[:], T.idx[:], T.t1[:], OP.add, [A("idx"), A("t1")], [A("am")], n=256)
+    ts(T.icf[:], T.icf[:], cf(6), OP.subtract, [A("icf"), rc(6)], [A("icf")])
+    cp(T.icn[:], T.icf[:], [A("icf")], [A("icn")])
+    ts(T.icr[:], T.icf[:], -1.0, OP.mult, [A("icf")], [A("icr")], (), 255.0, OP.add)
+    ts(T.i16[:], T.icf[:], 16.0, OP.mult, [A("icf")], [A("i16")])
+    ts(T.mr[:], T.si[:], cf(0), OP.is_equal, [A("si"), rc(0)], [A("mr")], n=128)
+    cp(T.cl[:], T.clf[:], [A("clf")], [A("cl")])
+    fill(T.ke[:], 512.0, [A("ke")])
+    fill(T.ke[:, 0::16], 0.5, [A("ke")])
+    fill(T.z16[:], 0.0, [A("z16")])
+    fill(T.nfs[:], 0.0, [A("nfs")])
+    fill(T.one[:], 1.0, [A("one")])
+    for z in range(4):
+        lo = XC + 12288 + 1024 * z
+        fill(T.xw[:, lo:lo + 1024], 0.0, [A("xw", lo, lo + 1024)], 512)
+
+    def early_lists(c):
+        ts(T.ef[:, c::4], T.ei0[:, c::4], 16.0, OP.add, [A("ei0")], [A("ef%d" % c)], n=256)
+
+    def prep_x(c):
+        E, M = A("ef%d" % c), A("mm%d" % c)
+        tt(T.td[:], T.ef[:, c::4], T.mm[:, c::4], OP.mult, [E, M], [A("td")], n=512)
+        ts(T.dl16[:], T.td[:], cf(19), OP.mult, [A("td"), rc(19), rc(20)], [A("dl16")], (), cf(20), OP.add, n=256)
+        for par in range(2):
+            mms([(T.p0[:, 128 * par:128 * par + 128], T.pm[:, 256 * par + 128 * b:256 * par + 128 * b + 128], T.ef[:, c + 4 * b::8], b == 0, b == 1)
+                 for b in range(2)], 512, [A("pm"), E], [0])
+        cp(T.el16[:], T.p0[:, 0:256], [], [A("el16")], [0], n=256)
+        ts(T.ei[:], T.p0[:, 0:256], -16.0, OP.add, [], [A("ei")], [0], n=256)
+
+    def prep_s(c):
+        act(T.sgn[:, c::4], T.mm[:, c::4], AF.Copy, [A("mm%d" % c)], [A("sgn%d" % c)], n=256, scale=-2.0, bias=1.0)
+        mms([(T.p3[:, 256 + 128 * H:384 + 128 * H], T.sgn[:, 512 * H + c:512 * H + 512:4], T.idn[:], True, True) for H in range(2)],
+            128, [A("sgn%d" % c), A("idn")], [3])
+        act(T.sgt[:], T.p3[:, 256:512], AF.Copy, [], [A("sgt")], [3], n=256)
+
+    items = T.xw[:, XC:XC + 4096]
+    all_x = T.xw[:, 0:XC + 4096]
+    RX = ("xw", 0, XC + 4096)
+
+    def gather_even(H):
+        out = T.qq[:, 2048 * H:2048 * H + 2048:2]
+        src = all_x.indirect(T.el16[:, 64 * H:64 * H + 64])
+        f = cp if H in EVEN_V else (lambda o, i, R, W, cost: act(o, i, AF.Copy, R, W, cost=cost))
+        f(out, src, [RX, A("el16")], [("qe", H, H + 1)], cost=0.06 + 1024 * GAT)
+
+    def gather_d(H):
+        act(T.d0[:, 2048 * H:2048 * H + 2048], all_x.indirect(T.dl16[:, 128 * H:128 * H + 128]), AF.Copy,
+            [RX, A("dl16")], [("d0", H, H + 1)], cost=0.06 + 2048 * GAT)
+
+    def hashes(H, par, ps, col, B):
+        mms([(ps[:, col:col + 64], T.wu[:, 15 - r:143 - r], T.qq[:, 2048 * H + 2 * r + par:2048 * H + 2048:32], r == 0, r == 15) for r in range(16)],
+            64, [A("wu"), ("qo" if par else "qe", H, H + 1)], [B])
+
+    def hop(lo, hi, src, B, first):
+        s = slice(lo, hi)
+        n = hi - lo
+
+        def rg(b):
+            return (b, lo, hi)
+        cp(T.ui[:, s], src, [], [rg("ui")], [B], n=n)
+        ts(T.ua[:, s], T.ui[:, s], 4095, OP.bitwise_and, [rg("ui")], [rg("ua")], n=n)
+        tt(T.ta[:, s], T.ei[:, s], T.ua[:, s], OP.mult, [A("ei"), rg("ua")], [rg("ta")], n=2 * n)
+        ts(T.tb[:, s], T.ta[:, s], 5, OP.logical_shift_right, [rg("ta")], [rg("tb")], n=n)
+        e, en = (T.ei, "ei") if first else (T.ek, "ek")
+        tt(T.tc[:, s], T.tb[:, s], e[:, s], OP.add, [rg("tb"), A(en)], [rg("tc")], n=2 * n)
+        ts(T.hh[:, s], T.tc[:, s], 4095, OP.bitwise_and, [rg("tc")], [rg("hh")], n=n)
+        cp(T.h16[:, s], T.hh[:, s], [rg("hh")], [rg("h16")], n=n)
+
+    def scan(H):
+        s = slice(2048 * H, 2048 * H + 2048)
+        scn(T.bb[:, s], T.d0[:, s], T.alt[:], 0.0, OP.subtract, OP.min, [("d0", H, H + 1), A("alt")], [("bb", H, H + 1)], 1024)
+
+    def odd_min(H):
+        tt(T.qq[:, 2048 * H + 1:2048 * H + 2048:2], all_x.indirect(T.el16[:, 128 + 64 * H:192 + 64 * H]),
+           T.bb[:, 2048 * H:2048 * H + 2048:2], OP.min, [RX, A("el16"), ("bb", H, H + 1)], [("qo", H, H + 1)], cost=0.06 + 1024 * GAT)
+
+    def look(H, par):
+        s = slice(2048 * H + par, 2048 * H + 2048, 2)
+        lo = 128 * par + 64 * H
+        z = 2 * H + par
+        Q = ("qo" if par else "qe", H, H + 1)
+        if (H, par) in LOOK_S:
+            act(T.yb[:, 1024 * z:1024 * z + 1024], items.indirect(T.h16[:, lo:lo + 64]), AF.Copy, [RX, ("h16", lo, lo + 64)], [("yb", z, z + 1)],
+                cost=0.07 + 1024 * GAT)
+            for x in range(2):
+                ps, B = (T.p5, 5) if x else (T.p4, 4)
+                qs = slice(2048 * H + par + 1024 * x, 2048 * H + 1024 * x + 1024, 2)
+                mms([(ps[:], T.idn[:], T.yb[:, 1024 * z + 512 * x:1024 * z + 512 * x + 512], True, False),
+                     (ps[:], T.nid[:], T.qq[:, qs], False, True)], 512, [A("idn"), A("nid"), ("yb", z, z + 1), Q], [B])
+                act(T.sg[:, qs], ps[:], AF.Sign, [], [("sg", 4 * H + 2 * par + x, 4 * H + 2 * par + x + 1)], [B], n=512)
+            return
+        tt(T.dq[:, s], items.indirect(T.h16[:, lo:lo + 64]), T.qq[:, s], OP.subtract,
+           [RX, ("h16", lo, lo + 64), Q], [("dq", z, z + 1)], cost=0.06 + 1024 * GAT)
+        ts(T.sg[:, s], T.dq[:, s], 1.0, OP.min, [("dq", z, z + 1)], [("sg", 2 * z, 2 * z + 2)], (), -1.0, OP.max, n=512)
+
+    def score(H, par, c):
+        ps, B = (T.p7, 7) if H else (T.p6, 6)
+        if par == 0:
+            mms([(ps[:, 0:128], T.sgn[:, 512 * H + c:512 * H + 512:4], T.nk[:], True, False)], 128, [A("sgn%d" % c), A("nk")], [B])
+        z = 2 * H + par
+        mms([(ps[:, k:128:16], T.sg[:, 2048 * H + k:2048 * H + 2048:16], T.g8[:], False, k == 15) for k in range(par, 16, 2)],
+            64, [("sg", 2 * z, 2 * z + 2), A("g8")], [B])
+
+    def over(H):
+        act(T.ov[:, 2048 * H:2048 * H + 2048], T.qq[:, 2048 * H:2048 * H + 2048], AF.Sign,
+            [("qe", H, H + 1), ("qo", H, H + 1)], [("ov", H, H + 1)], n=2048)
+        mms([(T.p3[:, 128 * H + k:128 * H + 128:16], T.ov[:, 2048 * H + k:2048 * H + 2048:16], T.g8[:], True, True) for k in range(16)],
+            64, [("ov", H, H + 1), A("g8")], [3])
+
+    def gate(H):
+        s = slice(128 * H, 128 * H + 128)
+        ts(T.ge[:, s], T.p3[:, s], 136.0, OP.is_gt, [], [("ge", H, H + 1)], [3], n=128)
+        tt(T.gsg[:, s], T.ge[:, s], T.sgt[:, s], OP.mult, [("ge", H, H + 1), A("sgt")], [("gsg", H, H + 1)], n=256)
+
+    def keys(H):
+        ps, B = (T.p7, 7) if H else (T.p6, 6)
+        kt, sc, lm = T["kt%d" % H], T["sc%d" % H], T["lm%d" % H]
+        tt(kt[:], ps[:, 0:128], T.gsg[:, 128 * H:128 * H + 128], OP.mult, [("gsg", H, H + 1)], [A("kt%d" % H)], [B], n=128)
+        scn(sc[:], T.ke[:], kt[:], 0.5, OP.min, OP.max, [A("ke"), A("kt%d" % H)], [A("sc%d" % H)], 64)
+        tt(lm[:], sc[:].indirect(T.cl[:]), T.mr[:], OP.mult, [A("sc%d" % H), A("cl"), A("mr")], [A("lm%d" % H)], cost=0.25)
+        mms([(T.p4[:, 8 * H:8 * H + 8], lm[:], T.rcp[:], True, True)], 64, [A("lm%d" % H), A("rcp")], [4])
+
+    def send(t):
+        dst = T.cores[(rank + 1 + t % (n_ranks - 1)) % n_ranks]
+        es = topo.engines(core, dst)[:8]
+        mask = sum(1 << e for e in es)
+        rid, pid, _ = topo.addr(dst)
+        src = T.cores[(rank - 1 - t % (n_ranks - 1)) % n_ranks]
+        n_in = len(topo.engines(src, core)[:8])
+        for a, b, sm in (("qw", "lq", "aq"), ("tg", "lt", "at")):
+            sn, dn, name = "%s%d" % (a, t), "%s%d" % (b, t), "%s%d" % (sm, t)
+            i = node("g", [lambda e, sn=sn, dn=dn, name=name: e.remote_dma(T[dn][:], T[sn][:], T.sem[name], T.sem.ls, pid, rid, mask)],
+                     1.0, [A(sn)], [], (), "r", len(es))
+            node(None, [], 0.0, [], [A(dn)], (), "a", (name, n_in), 2.5 if a == "qw" else 1.5, (i,))
+
+    def update(t, c):
+        ts(T.hf[:], T.hh[:], 16.0, OP.add, [A("hh")], [A("hf")], n=256)
+        for b in range(2):
+            mms([(T.p2[:, 128 * b:128 * b + 128], T.iv[:, 256 * par + 128 * b:256 * par + 128 * b + 128], T.hf[:, 128 * par:128 * par + 128],
+                  par == 0, par == 1) for par in range(2)], 512, [A("iv"), A("hf")], [2])
+        for H in range(2):
+            kt, sc, wn = T["kt%d" % H], T["sc%d" % H], T["wn%d" % H]
+            tt(wn[:], sc[:].indirect(T.cl[:]), kt[:], OP.is_equal, [A("kt%d" % H), A("cl"), A("sc%d" % H)], [A("wn%d" % H)], cost=0.25)
+            mms([(T.p2[:, 256 + 128 * H:384 + 128 * H], wn[:], T.idn[:], True, True)], 128, [A("wn%d" % H), A("idn")], [2])
+        E, M, S = A("ef%d" % c), A("mm%d" % c), A("sgn%d" % c)
+        for b in range(2):
+            d = T.de[:, 128 * b:128 * b + 128]
+            e = T.ef[:, c + 4 * b::8]
+            rg = ("de", b, b + 1)
+            tt(d, T.p2[:, 128 * b:128 * b + 128], e, OP.subtract, [E], [rg], [2], n=128)
+            tt(d, T.p2[:, 256 + b:512:2], d, OP.mult, [rg], [rg], [2], n=128)
+            tt(e, e, d, OP.add, [E, rg], [("ef%d" % c, b, b + 1)], n=256)
+        tt(T.tm[:], T.p2[:, 256:512], T.sgn[:, c::4], OP.mult, [S], [A("tm")], [2], n=256)
+        tt(T.mm[:, c::4], T.mm[:, c::4], T.tm[:], OP.add, [M, A("tm")], [M], n=512)
+
+    def out_lines(c):
+        act(T.ylb[:, c::4], T.ef[:, c::4], AF.Copy, [A("ef%d" % c)], [A("yl%d" % c)], n=256, bias=-16.0)
+
+    early_lists(0)
+    prep_x(0)
+    prep_s(0)
+    for c in range(1, 4):
+        early_lists(c)
+    win = T.xw[:, XC:XW]
+    WX = ("xw", XC, XW)
+    for t in range(RO):
+        c = t % 4
+        first = t == 0
+        gather_even(0)
+        gather_even(1)
+        gather_d(0)
+        gather_d(1)
+        hashes(0, 0, T.p0, 0, 0)
+        hashes(1, 0, T.p1, 64, 1)
+        hop(0, 64, T.p0[:, 0:64], 0, first)
+        hop(64, 128, T.p1[:, 64:128], 1, first)
+        scan(0)
+        odd_min(0)
+        hashes(0, 1, T.p1, 0, 1)
+        scan(1)
+        odd_min(1)
+        hashes(1, 1, T.p2, 0, 2)
+        hop(128, 192, T.p1[:, 0:64], 1, first)
+        hop(192, 256, T.p2[:, 0:64], 2, first)
+        for H, par in ((0, 0), (1, 0), (0, 1), (1, 1)):
+            look(H, par)
+        over(0)
+        gate(0)
+        over(1)
+        gate(1)
+        for H in range(2):
+            score(H, 0, c)
+            score(H, 1, c)
+            keys(H)
+        kl = T.p4[:, 0:16]
+        mms([(T.p5[:, 0:16], T.idn[:], T.icn[:], True, False)], 64, [A("idn"), A("icn")], [5])
+        ts(T.kn[:], kl, -1.0, OP.mult, [], [A("kn")], [4])
+        ts(T.nf[:], kl, 0.75, OP.is_lt, [], [A("nf")], [4])
+        ts(T.li[:], T.kn[:], 15, OP.bitwise_and, [A("kn")], [A("li")])
+        tt(T.lj[:], T.li[:], T.i16[:], OP.add, [A("li"), A("i16")], [A("lj")])
+        cp(T.l16[:], T.lj[:], [A("lj")], [A("l16")])
+        qw, qn = T["qw%d" % t], "qw%d" % t
+        cp(qw[:], T.qq[:].indirect(T.l16[:]), [A("qe"), A("qo"), A("l16")], [A(qn)], cost=0.05 + 256 * GAT)
+        mms([(T.p1[:, 0:16], T.wu[:, 15 - r:143 - r], qw[:, r::16], r == 0, r == 15) for r in range(16)], 64, [A("wu"), A(qn)], [1])
+        scn(T.nfs[:, 1:17], T.nf[:], T.z16[:], 0.0, OP.add, OP.max, [A("nf"), A("z16")], [A("nfs")], 16)
+        tt(T.nfi[:], T.nf[:], T.icr[:], OP.mult, [A("nf"), A("icr")], [A("nfi")])
+        mms([(T.p5[:, 0:16], T.am[:], T.nf[:], False, False), (T.p5[:, 0:16], T.nbl[:], T.nfs[:, 0:16], False, False),
+             (T.p5[:, 0:16], T.idn[:], T.nfi[:], False, True)], 64, [A("am"), A("nf"), A("nbl"), A("nfs"), A("idn"), A("nfi")], [5])
+        ts(T.ofi[:], T.p5[:, 0:16], 32.0, OP.mult, [], [A("ofi")], [5])
+        cp(T.uwi[:], T.p1[:, 0:16], [], [A("uwi")], [1])
+        ts(T.uwa[:], T.uwi[:], 31, OP.bitwise_and, [A("uwi")], [A("uwa")])
+        tt(T.tgi[:], T.uwa[:], T.ofi[:], OP.add, [A("uwa"), A("ofi")], [A("tgi")])
+        cp(T["tg%d" % t][:], T.tgi[:], [A("tgi")], [A("tg%d" % t)])
+        send(t)
+        if t == 3:
+            update(t, c)
+        if t < RO - 1:
+            if t < 3:
+                prep_x(t + 1)
+                prep_s(t + 1)
+            else:
+                prep_x(0)
+                prep_s(0)
+            mms([(T.p5[:, 32:48], T.one[:], T.nf[:], True, True)], 64, [A("one"), A("nf")], [5])
+            node("v", [lambda e: e.tensor_reduce(T.kc[:], T.p5[:, 32:48], AxisListType.X, OP.add)], cy(16), [], [A("kc")], [5])
+            ts(T.kci[:], T.kc[:], -1.0, OP.mult, [A("kc")], [A("kci")])
+            ts(T.kcj[:], T.kci[:], 31, OP.bitwise_and, [A("kci")], [A("kcj")])
+            cp(T.kap[:], T.kcj[:], [A("kcj")], [A("kap")])
+            ts(T.ek[:], T.ei[:], T.kap[:], OP.add, [A("ei"), A("kap")], [A("ek")], n=256)
+        if t != 3:
+            update(t, c)
+        if t > 0:
+            out_lines(c)
+        lt = T["lt%d" % t]
+        L = A("lt%d" % t)
+        tt(T.av[:], win.indirect(lt[:]), T["lq%d" % t][:], OP.add, [WX, L, A("lq%d" % t)], [A("av")], cost=0.05 + 256 * GAT)
+        ts(T.ai[:], T.av[:], 0.5, OP.mult, [A("av")], [A("ai")], (), -0.25, OP.add, n=256)
+        cp(win.indirect(lt[:]), T.ai[:], [A("ai"), L], [WX], cost=0.05 + 256 * SCA)
+    dma("y", T.ym[:], T.mm[:], MM4, [], 262144)
+    dma("s", T.yl[:], T.ylb[:], [A("yl%d" % c) for c in range(4)], [], 524288)
+    dma("y", T.yx[:, 0:2048], T.xw[:, XC:XC + 2048], [WX], [], 1048576)
+    dma("s", T.yx[:, 2048:4096], T.xw[:, XC + 2048:XC + 4096], [WX], [], 1048576)
+
+    n = len(nodes)
+    before = [[] for _ in range(n)]
+    after = [[] for _ in range(n)]
+    for i, d in enumerate(nodes):
+        for j in d["deps"] | d["order"]:
+            f = nodes[j]
+            lag = f["late"] + ((0.03 if f["q"] == d["q"] else 0.1) if j in d["deps"] else 0.0)
+            before[i].append((j, lag))
+            after[j].append((i, lag))
+
+    def arrange(pre, post, prio):
+        left = [len(x) for x in pre]
+        end = [0.0] * n
+        free = {q: 0.0 for q in eng}
+        ready = {q: [] for q in eng}
+        out, todo = [], [i for i in range(n) if not pre[i]]
+        first = True
+        while True:
+            while todo:
+                i = todo.pop()
+                rel = [i] if first and not pre[i] else []
+                if not rel:
+                    for j, _ in post[i]:
+                        left[j] -= 1
+                        if left[j] == 0:
+                            rel.append(j)
+                for j in rel:
+                    r = max([end[k] + lag for k, lag in pre[j]] + [0.0])
+                    if nodes[j]["q"] is None:
+                        end[j] = r
+                        out.append(j)
+                        todo.append(j)
+                    else:
+                        ready[nodes[j]["q"]].append((r, j))
+            first = False
+            best = None
+            for q in eng:
+                if ready[q]:
+                    s0 = min(max(free[q], r) for r, _ in ready[q])
+                    if best is None or s0 < best[0]:
+                        best = (s0, q)
+            if best is None:
+                return out, end
+            s0, q = best
+            pick = max((x for x in ready[q] if max(free[q], x[0]) <= s0 + 0.06), key=lambda x: (prio[x[1]], -x[1]))
+            ready[q].remove(pick)
+            i = pick[1]
+            free[q] = end[i] = max(free[q], pick[0]) + nodes[i]["cost"]
+            out.append(i)
+            todo.append(i)
+    prio = [0.0] * n
+    for i in range(n - 1, -1, -1):
+        prio[i] = nodes[i]["cost"] + max([prio[j] + lag for j, lag in after[i]] + [0.0])
+    best = None
+    for _ in range(PASSES):
+        out, end = arrange(before, after, prio)
+        if best is None or max(end) < best[0]:
+            best = (max(end), out, end)
+        _, prio = arrange(after, before, end)
+    orders, fin = best[1], best[2]
+
+    cnt = {q: 0 for q in eng}
+    known = {q: {} for q in eng}
+    stamp, snap = {}, {}
+    nloc = 0
+    for i in orders:
+        d = nodes[i]
+        q = d["q"]
+        if q is None:
+            stamp[i] = (d["key"][0], 1, d["key"][1])
+            snap[i] = {}
+            continue
+        kq = known[q]
+        latest = {}
+        for j in d["deps"]:
+            s, k, v = stamp[j]
+            if s not in latest or latest[s][0] < k:
+                latest[s] = (k, v, j)
+        for s in sorted(latest, key=lambda s: -fin[latest[s][2]]):
+            k, v, j = latest[s]
+            if kq.get(s, 0) >= k:
+                continue
+            eng[q].wait_ge(T.sem[s], v)
+            kq[s] = k
+            for s2, k2 in snap[j].items():
+                if k2 > kq.get(s2, 0):
+                    kq[s2] = k2
+        snap[i] = dict(kq)
+        if d["kind"] == "d":
+            d["calls"][0](eng[q]).then_inc(T.sem[d["key"]], 16)
+            stamp[i] = (d["key"], 1, 16)
+        elif d["kind"] == "r":
+            d["calls"][0](eng[q])
+            nloc += d["key"]
+            stamp[i] = ("ls", nloc, nloc)
+        else:
+            for f in d["calls"]:
+                f(eng[q]).then_inc(T.sem[semname[q]], 1)
+                cnt[q] += 1
+            stamp[i] = (semname[q], cnt[q], cnt[q])
+    for q in ("v", "s", "p", "g"):
+        g.wait_ge(T.sem[semname[q]], cnt[q])
+    for j in range(ndma[0]):
+        g.wait_ge(T.sem["dm%d" % j], 16)
+    g.wait_ge(T.sem.ls, nloc)

@@ -6,28 +6,34 @@ AF = ActivationFunctionType
 RO = 5
 XC = 16
 XW = XC + 512 * 32
-LOOK_S = ((0, 0), (0, 1))
-EVEN_V = (0, 1)
+DEL = 2.0 ** -10
+BIG = 8192.0
+LOOK_S = ((0, 0), (1, 0))
+EVEN_V = (0,)
+CUT = 2816
 
 SCRATCH = {"xw": ("sbuf", [128, XW], "bfloat16"), "alt": ("sbuf", [128, 2048], "bfloat16")}
 for _n, _w, _d in (
-        ("ei0", 1024, "int32"), ("ef", 1024, "float32"), ("mm", 1024, "bfloat16"), ("sgn", 1024, "bfloat16"), ("ylb", 1024, "float32"),
+        ("ei0", 1024, "int32"), ("ef", 1024, "float16"), ("mm", 1024, "bfloat16"), ("ylb", 1024, "float32"),
         ("d0", 4096, "bfloat16"), ("bb", 4096, "bfloat16"), ("qq", 4096, "bfloat16"), ("dq", 4096, "bfloat16"), ("sg", 4096, "bfloat16"),
-        ("ov", 4096, "bfloat16"), ("yb", 4096, "bfloat16"),
-        ("dl16", 256, "uint16"), ("el16", 256, "uint16"), ("h16", 256, "uint16"), ("ei", 256, "int32"), ("ek", 256, "int32"),
+        ("yb", 4096, "bfloat16"),
+        ("dl16", 256, "uint16"), ("el16", 256, "uint16"), ("h16", 256, "uint16"),
         ("ui", 256, "int32"), ("ua", 256, "int32"), ("ta", 256, "int32"), ("tb", 256, "int32"), ("tc", 256, "int32"), ("hh", 256, "int32"),
-        ("hf", 256, "float32"), ("de", 256, "float32"), ("td", 256, "float32"), ("tm", 256, "bfloat16"), ("av", 256, "float32"), ("ai", 256, "int32"),
+        ("hf", 256, "float16"), ("eb", 256, "float32"), ("av", 256, "float16"), ("aw", 256, "float16"), ("ax", 256, "bfloat16"),
         ("pi", 1, "int32"), ("ci", 8, "int32"), ("cf", 32, "float32"), ("m1", 160, "float32"), ("si", 128, "float32"), ("clf", 8, "float32"),
-        ("cl", 8, "uint16"), ("icf", 16, "float32"), ("icn", 16, "bfloat16"), ("icr", 16, "bfloat16"), ("i16", 16, "int32"), ("mg", 128, "float32"),
-        ("idn", 128, "bfloat16"), ("nid", 128, "bfloat16"), ("nk", 128, "bfloat16"), ("g8", 8, "bfloat16"), ("rcp", 8, "bfloat16"),
-        ("wu", 144, "bfloat16"), ("pm", 512, "float32"), ("iv", 512, "float32"), ("nbl", 128, "bfloat16"), ("lt", 128, "bfloat16"),
-        ("idx", 128, "bfloat16"), ("t1", 128, "bfloat16"), ("am", 128, "bfloat16"), ("one", 128, "bfloat16"), ("mr", 128, "bfloat16"),
-        ("ke", 128, "bfloat16"), ("z16", 16, "bfloat16"),
-        ("ge", 256, "bfloat16"), ("gsg", 256, "bfloat16"), ("sgt", 256, "bfloat16"), ("kt0", 128, "bfloat16"), ("kt1", 128, "bfloat16"),
-        ("sc0", 128, "bfloat16"), ("sc1", 128, "bfloat16"), ("lm0", 128, "bfloat16"), ("lm1", 128, "bfloat16"), ("wn0", 128, "bfloat16"),
-        ("wn1", 128, "bfloat16"), ("nf", 16, "bfloat16"), ("nfs", 32, "bfloat16"), ("nfi", 16, "bfloat16"), ("kn", 16, "int32"), ("li", 16, "int32"),
-        ("lj", 16, "int32"), ("l16", 16, "uint16"), ("ofi", 16, "int32"), ("uwi", 16, "int32"), ("uwa", 16, "int32"), ("tgi", 16, "int32"),
-        ("kc", 1, "float32"), ("kci", 1, "int32"), ("kcj", 1, "int32"), ("kap", 1, "float32")):
+        ("cl", 8, "uint16"), ("icf", 16, "float32"), ("icn", 16, "bfloat16"), ("icr", 16, "bfloat16"), ("mg", 128, "float32"),
+        ("zf", 16, "float32"), ("zc", 16, "bfloat16"), ("thr", 16, "float32"),
+        ("idn", 128, "bfloat16"), ("nid", 128, "bfloat16"), ("nk", 128, "bfloat16"), ("nk2", 128, "bfloat16"), ("n2", 128, "bfloat16"),
+        ("idh", 128, "float16"), ("big", 128, "bfloat16"), ("nbig", 128, "bfloat16"), ("i32", 128, "bfloat16"),
+        ("g8", 8, "bfloat16"), ("g1", 8, "bfloat16"), ("rcp", 8, "bfloat16"),
+        ("wu", 144, "bfloat16"), ("pm", 512, "float16"), ("iv", 512, "float16"), ("nbl", 128, "bfloat16"), ("lt", 128, "bfloat16"),
+        ("t1", 128, "bfloat16"), ("am", 128, "bfloat16"), ("one", 128, "bfloat16"), ("mr", 128, "bfloat16"),
+        ("ke", 128, "bfloat16"), ("z16", 16, "bfloat16"), ("c2k", 512, "bfloat16"), ("c75", 128, "bfloat16"),
+        ("cr", 256, "int32"), ("ge", 256, "bfloat16"), ("gsg", 256, "bfloat16"), ("kt0", 128, "bfloat16"), ("kt1", 128, "bfloat16"),
+        ("sc0", 128, "bfloat16"), ("sc1", 128, "bfloat16"), ("lm0", 128, "bfloat16"), ("lm1", 128, "bfloat16"), ("nw0", 128, "bfloat16"),
+        ("nw1", 128, "bfloat16"), ("nf", 16, "bfloat16"), ("nfs", 32, "bfloat16"), ("nfi", 16, "bfloat16"), ("kn", 16, "int32"), ("li", 16, "int32"),
+        ("l16", 16, "uint16"), ("uwi", 16, "int32"), ("uwa", 16, "int32"), ("tgi", 16, "int32"),
+        ("kci", 1, "int32"), ("kcj", 1, "int32"), ("kap", 1, "float32")):
     SCRATCH[_n] = ("sbuf", [128, _w], _d)
 for _t in range(8):
     SCRATCH["p%d" % _t] = ("psum", [128, 512], "float32")
@@ -40,9 +46,9 @@ SEMAPHORES = ["cv", "cs", "cp", "cg", "ls"] + ["aq%d" % _t for _t in range(RO)] 
     + ["dm%d" % _t for _t in range(24)]
 
 PASSES = 12
-CYC = 0.001
-GAT = 0.00150
-SCA = 0.0030
+CYC = 0.00104
+GAT = 0.00162
+SCA = 0.0039
 
 
 def rank_program(g, core, T, topo):
@@ -73,22 +79,14 @@ def rank_program(g, core, T, topo):
         me = len(nodes)
         order = set()
         for b in B:
-            if b in bank:
-                (order if nodes[bank[b]]["q"] == q else d).add(bank[b])
-                for j in nodes[bank[b]]["chain"].get(b, ()):
-                    if nodes[j]["q"] != q:
-                        d.add(j)
-        chain = {}
-        for b in B:
-            last = {}
-            if b in bank:
-                for j in nodes[bank[b]]["chain"].get(b, ()):
-                    last[nodes[j]["q"]] = j
-                last[nodes[bank[b]]["q"]] = bank[b]
-            chain[b] = list(last.values())
-        nodes.append({"q": q, "calls": calls, "cost": cost, "deps": d, "order": order - d, "kind": kind, "key": key, "late": late, "chain": chain})
-        for b in B:
-            bank[b] = me
+            prev, cur = bank.get(b, ([], []))
+            if cur and nodes[cur[-1]]["q"] != q:
+                prev, cur = cur, []
+            d.update(prev)
+            if cur and q == "p":
+                order.add(cur[-1])
+            bank[b] = (prev, cur + [me])
+        nodes.append({"q": q, "calls": calls, "cost": cost, "deps": d, "order": order - d, "kind": kind, "key": key, "late": late})
         for (b, lo, hi) in W:
             wr[b] = [e for e in wr.get(b, ()) if not (lo <= e[0] and e[1] <= hi)] + [(lo, hi, me)]
             rd[b] = [e for e in rd.get(b, ()) if not (lo <= e[0] and e[1] <= hi)]
@@ -96,10 +94,10 @@ def rank_program(g, core, T, topo):
             rd.setdefault(b, []).append((lo, hi, me))
         return me
 
-    def dma(q, out, in_, R, W, by):
+    def dma(q, out, in_, R, W, by, extra=()):
         name = "dm%d" % ndma[0]
         ndma[0] += 1
-        node(q, [lambda e: e.dma_start(out, in_)], 0.1, R, W, (), "d", name, 2.0 + by * 4e-6)
+        return node(q, [lambda e: e.dma_start(out, in_)], 0.1, R, W, (), "d", name, 2.0 + by * 5e-6, extra)
 
     def A(b, lo=0, hi=1 << 20):
         return (b, lo, hi)
@@ -108,7 +106,11 @@ def rank_program(g, core, T, topo):
         return max(64, n) * CYC
 
     def mms(lst, n, R, B):
-        node("p", [lambda e, a=a: e.matmul(*a) for a in lst], len(lst) * n * CYC, R, [], B)
+        last = len(lst) - 1
+        node("p", [lambda e, a=a, j=j: e.matmul(a[0], a[1], a[2], j == 0, j == last) for j, a in enumerate(lst)], n * CYC, R, [], B)
+
+    def mmx(lst, n, R, B):
+        node("p", [lambda e, a=a: e.matmul(*a) for a in lst], n * CYC, R, [], B)
 
     def ts(out, in0, s1, o1, R, W, B=(), s2=None, o2=None, n=64):
         if o2 is None:
@@ -140,10 +142,16 @@ def rank_program(g, core, T, topo):
     MM4 = [A("mm%d" % c) for c in range(4)]
     dma("y", T.ei0[:], T.led[:], [], [A("ei0")], 524288)
     dma("s", T.mm[:], T.mk[:], [], MM4, 262144)
-    dma("y", T.xw[:, XC:XC + 2048], T.xt[:, 0:2048], [], [A("xw", XC, XC + 2048)], 1048576)
-    dma("s", T.xw[:, XC + 2048:XC + 4096], T.xt[:, 2048:4096], [], [A("xw", XC + 2048, XC + 4096)], 1048576)
-    dma("y", T.xw[:, XC + 4096:XC + 8192], T.xt[:], [], [A("xw", XC + 4096, XC + 8192)], 2500000)
-    dma("s", T.xw[:, XC + 8192:XC + 12288], T.xt[:], [], [A("xw", XC + 8192, XC + 12288)], 2500000)
+    parts = ((0, CUT // 2, "y", "v"), (CUT, 4096, "s", "s"), (CUT // 2, CUT, "y", "v"))
+    loads = [dma(q, T.xw[:, XC + lo:XC + hi], T.xt[:, lo:hi], [], [A("xw", XC + lo, XC + hi)], 1800000) for lo, hi, q, _ in parts]
+    for lo, hi, _, q in parts:
+        ap, rg = T.xw[:, XC + lo:XC + hi], A("xw", XC + lo, XC + hi)
+        if q == "v":
+            ts(ap, ap, -DEL, OP.add, [rg], [rg], n=(hi - lo) // 2)
+        else:
+            act(ap, ap, AF.Copy, [rg], [rg], n=hi - lo, bias=-DEL)
+    for z in range(1, 3):
+        dma("y", T.xw[:, XC + 4096 * z:XC + 4096 * z + 4096], T.xt[:], [], [A("xw", XC + 4096 * z, XC + 4096 * z + 4096)], 1048576 * z, loads)
 
     iota(T.pi[:], [[0, 1]], 0, 1, [A("pi")], 1, False)
     iota(T.m1[:], [[1, 160]], 1, 0, [A("m1")], 160)
@@ -151,10 +159,12 @@ def rank_program(g, core, T, topo):
     iota(T.mg[:], [[16, 8], [0, 16]], 0, 0, [A("mg")], 128)
     iota(T.si[:], [[0, 8], [1, 16]], 0, 0, [A("si")], 128)
     iota(T.icf[:], [[16, 16]], 0, 1, [A("icf")], 16)
+    iota(T.zf[:], [[256, 16]], 256, 0, [A("zf")], 16)
+    iota(T.xw[:, XC + 12288:XW], [[0, 4096]], 0, 0, [A("xw", XC + 12288, XW)], 4096)
     fill(T.xw[:, 0:16], 0.0, [A("xw", 0, 16)])
     fill(T.xw[:, 1:2], 4096.0, [A("xw", 0, 16)])
     fill(T.alt[:, 0::2], 4096.0, [A("alt", 0, 1)], 512)
-    fill(T.alt[:, 1::2], 0.0, [A("alt", 1, 2)], 512)
+    fill(T.alt[:, 1::2], DEL, [A("alt", 1, 2)], 512)
 
     def ci(j):
         return T.ci[:, j:j + 1]
@@ -186,56 +196,58 @@ def rank_program(g, core, T, topo):
         ts(T.pm[:, 128 * j:128 * j + 128], T.m1[:, 0:128], cf(11 + j), OP.is_equal, [A("m1"), rc(11 + j)], [("pm", j, j + 1)], n=128)
         ts(T.iv[:, 128 * j:128 * j + 128], T.m1[:, 0:128], cf(15 + j), OP.is_equal, [A("m1"), rc(15 + j)], [("iv", j, j + 1)], n=128)
     ts(cf(19), cf(0), 14.5, OP.is_lt, [rc(0)], [rc(19)])
-    ts(cf(20), cf(0), 14.5, OP.is_gt, [rc(0)], [rc(20)])
+    ts(cf(20), cf(19), 2048.0 + XC - BIG - 1.0, OP.mult, [rc(19)], [rc(20)], (), 1.0, OP.add)
     ts(cf(21), cf(0), 2.0, OP.mult, [rc(0)], [rc(21)], (), 1.0, OP.add)
     ts(cf(22), cf(6), 16.0, OP.add, [rc(6)], [rc(22)])
     ts(cf(23), cf(0), -1.0, OP.mult, [rc(0)], [rc(23)])
+    ts(cf(24), cf(0), 2.0, OP.mult, [rc(0)], [rc(24)])
     ts(cf(25), cf(6), 0.0625, OP.mult, [rc(6)], [rc(25)], (), 1.0, OP.add)
     ts(cf(26), cf(5), 1.0, OP.add, [rc(5)], [rc(26)])
+    ts(cf(27), cf(0), 16.0, OP.mult, [rc(0)], [rc(27)])
     ts(T.wu[:], T.m1[:, 0:144], cf(22), OP.is_equal, [A("m1"), rc(22), rc(21)], [A("wu")], (), cf(21), OP.mult, n=144)
     ts(T.idn[:], T.m1[:, 0:128], cf(26), OP.is_equal, [A("m1"), rc(26)], [A("idn")], n=128)
-    ts(T.nid[:], T.m1[:, 0:128], cf(26), OP.is_equal, [A("m1"), rc(26)], [A("nid")], (), -1.0, OP.mult, n=128)
-    ts(T.idx[:], T.m1[:, 0:128], cf(26), OP.is_equal, [A("m1"), rc(26)], [A("idx")], (), 256.0, OP.mult, n=128)
-    ts(T.nk[:], T.m1[:, 0:128], cf(26), OP.is_equal, [A("m1"), rc(26), rc(23)], [A("nk")], (), cf(23), OP.mult, n=128)
+    cp(T.idh[:], T.idn[:], [A("idn")], [A("idh")])
+    for name, f in (("nid", -1.0), ("n2", -2.0), ("big", BIG), ("nbig", -BIG), ("i32", 32.0)):
+        ts(T[name][:], T.idn[:], f, OP.mult, [A("idn")], [A(name)])
+    ts(T.nk[:], T.idn[:], cf(23), OP.mult, [A("idn"), rc(23)], [A("nk")])
+    ts(T.nk2[:], T.idn[:], cf(24), OP.mult, [A("idn"), rc(24)], [A("nk2")])
     ts(T.g8[:], T.m1[:, 0:8], cf(25), OP.is_equal, [A("m1"), rc(25)], [A("g8")], (), 16.0, OP.mult)
-    ts(T.rcp[:], T.m1[:, 0:8], cf(25), OP.is_equal, [A("m1"), rc(25)], [A("rcp")])
-    ts(T.nbl[:], T.mg[:], cf(6), OP.is_equal, [A("mg"), rc(6)], [A("nbl")], (), -1.0, OP.mult, n=128)
+    ts(T.g1[:], T.m1[:, 0:8], cf(25), OP.is_equal, [A("m1"), rc(25)], [A("g1")])
+    ts(T.rcp[:], T.m1[:, 0:8], cf(25), OP.is_equal, [A("m1"), rc(25)], [A("rcp")], (), -1.0, OP.mult)
+    ts(T.nbl[:], T.mg[:], cf(6), OP.is_equal, [A("mg"), rc(6)], [A("nbl")], (), -32.0, OP.mult, n=128)
     ts(T.lt[:], T.m1[:, 0:128], cf(26), OP.is_gt, [A("m1"), rc(26)], [A("lt")], n=128)
     tt(T.t1[:], T.nbl[:], T.lt[:], OP.mult, [A("nbl"), A("lt")], [A("t1")], n=256)
-    tt(T.am[:], T.idx[:], T.t1[:], OP.add, [A("idx"), A("t1")], [A("am")], n=256)
+    tt(T.am[:], T.big[:], T.t1[:], OP.add, [A("big"), A("t1")], [A("am")], n=256)
     ts(T.icf[:], T.icf[:], cf(6), OP.subtract, [A("icf"), rc(6)], [A("icf")])
     cp(T.icn[:], T.icf[:], [A("icf")], [A("icn")])
     ts(T.icr[:], T.icf[:], -1.0, OP.mult, [A("icf")], [A("icr")], (), 255.0, OP.add)
-    ts(T.i16[:], T.icf[:], 16.0, OP.mult, [A("icf")], [A("i16")])
+    cp(T.zc[:], T.zf[:], [A("zf")], [A("zc")])
+    ts(T.thr[:], T.zf[:], -0.8, OP.add, [A("zf")], [A("thr")])
     ts(T.mr[:], T.si[:], cf(0), OP.is_equal, [A("si"), rc(0)], [A("mr")], n=128)
     cp(T.cl[:], T.clf[:], [A("clf")], [A("cl")])
     fill(T.ke[:], 512.0, [A("ke")])
-    fill(T.ke[:, 0::16], 0.5, [A("ke")])
+    fill(T.ke[:, 0::16], 0.625, [A("ke")])
     fill(T.z16[:], 0.0, [A("z16")])
     fill(T.nfs[:], 0.0, [A("nfs")])
     fill(T.one[:], 1.0, [A("one")])
-    for z in range(4):
-        lo = XC + 12288 + 1024 * z
-        fill(T.xw[:, lo:lo + 1024], 0.0, [A("xw", lo, lo + 1024)], 512)
+    fill(T.c2k[:, 0:256], 2048.0, [A("c2k", 0, 1)], 128)
+    fill(T.c2k[:, 256:512], 0.0, [A("c2k", 1, 2)], 128)
+    fill(T.c75[:], 7.5 * DEL, [A("c75")])
 
     def early_lists(c):
-        ts(T.ef[:, c::4], T.ei0[:, c::4], 16.0, OP.add, [A("ei0")], [A("ef%d" % c)], n=256)
+        ts(T.ef[:, c::4], T.ei0[:, c::4], -2048.0, OP.add, [A("ei0")], [A("ef%d" % c)], n=256)
 
-    def prep_x(c):
+    def prep(c):
         E, M = A("ef%d" % c), A("mm%d" % c)
-        tt(T.td[:], T.ef[:, c::4], T.mm[:, c::4], OP.mult, [E, M], [A("td")], n=512)
-        ts(T.dl16[:], T.td[:], cf(19), OP.mult, [A("td"), rc(19), rc(20)], [A("dl16")], (), cf(20), OP.add, n=256)
-        for par in range(2):
-            mms([(T.p0[:, 128 * par:128 * par + 128], T.pm[:, 256 * par + 128 * b:256 * par + 128 * b + 128], T.ef[:, c + 4 * b::8], b == 0, b == 1)
-                 for b in range(2)], 512, [A("pm"), E], [0])
-        cp(T.el16[:], T.p0[:, 0:256], [], [A("el16")], [0], n=256)
-        ts(T.ei[:], T.p0[:, 0:256], -16.0, OP.add, [], [A("ei")], [0], n=256)
-
-    def prep_s(c):
-        act(T.sgn[:, c::4], T.mm[:, c::4], AF.Copy, [A("mm%d" % c)], [A("sgn%d" % c)], n=256, scale=-2.0, bias=1.0)
-        mms([(T.p3[:, 256 + 128 * H:384 + 128 * H], T.sgn[:, 512 * H + c:512 * H + 512:4], T.idn[:], True, True) for H in range(2)],
-            128, [A("sgn%d" % c), A("idn")], [3])
-        act(T.sgt[:], T.p3[:, 256:512], AF.Copy, [], [A("sgt")], [3], n=256)
+        mms([(T.p0[:, 0:256], T.idn[:], T.c2k[:, 0:256])]
+            + [(T.p0[:, 128 * par:128 * par + 128], T.pm[:, 256 * par + 128 * b:256 * par + 128 * b + 128], T.ef[:, c + 4 * b::8])
+               for par in range(2) for b in range(2)], 768, [A("pm"), E, A("idn"), A("c2k")], [0])
+        ts(T.el16[:], T.p0[:, 0:256], float(XC), OP.add, [], [A("el16")], [0], n=256)
+        mms([(T.p7[:, 256:512], T.idh[:], T.ef[:, c::4]), (T.p7[:, 256:512], T.big[:], T.mm[:, c::4])], 512, [E, M, A("idh"), A("big")], [7])
+        ts(T.dl16[:], T.p7[:, 256:512], cf(19), OP.mult, [rc(19), rc(20)], [A("dl16")], [7], cf(20), OP.add, n=256)
+        for H in range(2):
+            o = T.p3[:, 256 + 128 * H:384 + 128 * H]
+            mms([(o, T.one[:], T.idn[:]), (o, T.mm[:, 512 * H + c:512 * H + 512:4], T.n2[:])], 256, [M, A("one"), A("idn"), A("n2")], [3])
 
     items = T.xw[:, XC:XC + 4096]
     all_x = T.xw[:, 0:XC + 4096]
@@ -248,12 +260,12 @@ def rank_program(g, core, T, topo):
         f(out, src, [RX, A("el16")], [("qe", H, H + 1)], cost=0.06 + 1024 * GAT)
 
     def gather_d(H):
-        act(T.d0[:, 2048 * H:2048 * H + 2048], all_x.indirect(T.dl16[:, 128 * H:128 * H + 128]), AF.Copy,
+        act(T.d0[:, 2048 * H:2048 * H + 2048], all_x.indirect(T.dl16[:, 128 * H:128 * H + 128]), AF.Relu,
             [RX, A("dl16")], [("d0", H, H + 1)], cost=0.06 + 2048 * GAT)
 
     def hashes(H, par, ps, col, B):
-        mms([(ps[:, col:col + 64], T.wu[:, 15 - r:143 - r], T.qq[:, 2048 * H + 2 * r + par:2048 * H + 2048:32], r == 0, r == 15) for r in range(16)],
-            64, [A("wu"), ("qo" if par else "qe", H, H + 1)], [B])
+        mms([(ps[:, col:col + 64], T.wu[:, 15 - r:143 - r], T.qq[:, 2048 * H + 2 * r + par:2048 * H + 2048:32]) for r in range(16)],
+            1024, [A("wu"), ("qo" if par else "qe", H, H + 1)], [B])
 
     def hop(lo, hi, src, B, first):
         s = slice(lo, hi)
@@ -263,16 +275,16 @@ def rank_program(g, core, T, topo):
             return (b, lo, hi)
         cp(T.ui[:, s], src, [], [rg("ui")], [B], n=n)
         ts(T.ua[:, s], T.ui[:, s], 4095, OP.bitwise_and, [rg("ui")], [rg("ua")], n=n)
-        tt(T.ta[:, s], T.ei[:, s], T.ua[:, s], OP.mult, [A("ei"), rg("ua")], [rg("ta")], n=2 * n)
+        tt(T.ta[:, s], T.p0[:, s], T.ua[:, s], OP.mult, [rg("ua")], [rg("ta")], [0], n=n)
         ts(T.tb[:, s], T.ta[:, s], 5, OP.logical_shift_right, [rg("ta")], [rg("tb")], n=n)
-        e, en = (T.ei, "ei") if first else (T.ek, "ek")
-        tt(T.tc[:, s], T.tb[:, s], e[:, s], OP.add, [rg("tb"), A(en)], [rg("tc")], n=2 * n)
+        o = 0 if first else 256
+        tt(T.tc[:, s], T.p0[:, o + lo:o + hi], T.tb[:, s], OP.add, [rg("tb")], [rg("tc")], [0], n=n)
         ts(T.hh[:, s], T.tc[:, s], 4095, OP.bitwise_and, [rg("tc")], [rg("hh")], n=n)
         cp(T.h16[:, s], T.hh[:, s], [rg("hh")], [rg("h16")], n=n)
 
     def scan(H):
         s = slice(2048 * H, 2048 * H + 2048)
-        scn(T.bb[:, s], T.d0[:, s], T.alt[:], 0.0, OP.subtract, OP.min, [("d0", H, H + 1), A("alt")], [("bb", H, H + 1)], 1024)
+        scn(T.bb[:, s], T.d0[:, s], T.alt[:], DEL, OP.subtract, OP.min, [("d0", H, H + 1), A("alt")], [("bb", H, H + 1)], 1024)
 
     def odd_min(H):
         tt(T.qq[:, 2048 * H + 1:2048 * H + 2048:2], all_x.indirect(T.el16[:, 128 + 64 * H:192 + 64 * H]),
@@ -289,8 +301,8 @@ def rank_program(g, core, T, topo):
             for x in range(2):
                 ps, B = (T.p5, 5) if x else (T.p4, 4)
                 qs = slice(2048 * H + par + 1024 * x, 2048 * H + 1024 * x + 1024, 2)
-                mms([(ps[:], T.idn[:], T.yb[:, 1024 * z + 512 * x:1024 * z + 512 * x + 512], True, False),
-                     (ps[:], T.nid[:], T.qq[:, qs], False, True)], 512, [A("idn"), A("nid"), ("yb", z, z + 1), Q], [B])
+                mms([(ps[:], T.idn[:], T.yb[:, 1024 * z + 512 * x:1024 * z + 512 * x + 512]),
+                     (ps[:], T.nid[:], T.qq[:, qs])], 1024, [A("idn"), A("nid"), ("yb", z, z + 1), Q], [B])
                 act(T.sg[:, qs], ps[:], AF.Sign, [], [("sg", 4 * H + 2 * par + x, 4 * H + 2 * par + x + 1)], [B], n=512)
             return
         tt(T.dq[:, s], items.indirect(T.h16[:, lo:lo + 64]), T.qq[:, s], OP.subtract,
@@ -300,29 +312,30 @@ def rank_program(g, core, T, topo):
     def score(H, par, c):
         ps, B = (T.p7, 7) if H else (T.p6, 6)
         if par == 0:
-            mms([(ps[:, 0:128], T.sgn[:, 512 * H + c:512 * H + 512:4], T.nk[:], True, False)], 128, [A("sgn%d" % c), A("nk")], [B])
+            mmx([(ps[:, 0:128], T.one[:], T.nk[:], True, False), (ps[:, 0:128], T.mm[:, 512 * H + c:512 * H + 512:4], T.nk2[:], False, False)],
+                256, [A("mm%d" % c), A("nk"), A("nk2"), A("one")], [B])
         z = 2 * H + par
-        mms([(ps[:, k:128:16], T.sg[:, 2048 * H + k:2048 * H + 2048:16], T.g8[:], False, k == 15) for k in range(par, 16, 2)],
-            64, [("sg", 2 * z, 2 * z + 2), A("g8")], [B])
-
-    def over(H):
-        act(T.ov[:, 2048 * H:2048 * H + 2048], T.qq[:, 2048 * H:2048 * H + 2048], AF.Sign,
-            [("qe", H, H + 1), ("qo", H, H + 1)], [("ov", H, H + 1)], n=2048)
-        mms([(T.p3[:, 128 * H + k:128 * H + 128:16], T.ov[:, 2048 * H + k:2048 * H + 2048:16], T.g8[:], True, True) for k in range(16)],
-            64, [("ov", H, H + 1), A("g8")], [3])
+        mmx([(ps[:, k:128:16], T.sg[:, 2048 * H + k:2048 * H + 2048:16], T.g8[:], False, k == 15) for k in range(par, 16, 2)],
+            512, [("sg", 2 * z, 2 * z + 2), A("g8")], [B])
 
     def gate(H):
         s = slice(128 * H, 128 * H + 128)
-        ts(T.ge[:, s], T.p3[:, s], 136.0, OP.is_gt, [], [("ge", H, H + 1)], [3], n=128)
-        tt(T.gsg[:, s], T.ge[:, s], T.sgt[:, s], OP.mult, [("ge", H, H + 1), A("sgt")], [("gsg", H, H + 1)], n=256)
+        mms([(T.p3[:, s], T.idn[:], T.c75[:])]
+            + [(T.p3[:, 128 * H + k:128 * H + 128:16], T.qq[:, 2048 * H + k:2048 * H + 2048:16], T.g1[:]) for k in range(16)],
+            1152, [("qe", H, H + 1), ("qo", H, H + 1), A("g1"), A("idn"), A("c75")], [3])
+        cp(T.cr[:, s], T.p3[:, s], [], [("cr", H, H + 1)], [3], n=128)
+        tt(T.ge[:, s], T.p3[:, s], T.cr[:, s], OP.is_gt, [("cr", H, H + 1)], [("ge", H, H + 1)], [3], n=128)
+        tt(T.gsg[:, s], T.p3[:, 256 + 128 * H:384 + 128 * H], T.ge[:, s], OP.mult, [("ge", H, H + 1)], [("gsg", H, H + 1)], [3], n=128)
 
     def keys(H):
         ps, B = (T.p7, 7) if H else (T.p6, 6)
         kt, sc, lm = T["kt%d" % H], T["sc%d" % H], T["lm%d" % H]
         tt(kt[:], ps[:, 0:128], T.gsg[:, 128 * H:128 * H + 128], OP.mult, [("gsg", H, H + 1)], [A("kt%d" % H)], [B], n=128)
-        scn(sc[:], T.ke[:], kt[:], 0.5, OP.min, OP.max, [A("ke"), A("kt%d" % H)], [A("sc%d" % H)], 64)
-        tt(lm[:], sc[:].indirect(T.cl[:]), T.mr[:], OP.mult, [A("sc%d" % H), A("cl"), A("mr")], [A("lm%d" % H)], cost=0.25)
-        mms([(T.p4[:, 8 * H:8 * H + 8], lm[:], T.rcp[:], True, True)], 64, [A("lm%d" % H), A("rcp")], [4])
+        scn(sc[:], T.ke[:], kt[:], 0.625, OP.min, OP.max, [A("ke"), A("kt%d" % H)], [A("sc%d" % H)], 64)
+        tt(lm[:], sc[:].indirect(T.cl[:]), T.mr[:], OP.mult, [A("sc%d" % H), A("cl"), A("mr")], [A("lm%d" % H)], cost=0.05 + 128 * GAT)
+        if H == 0:
+            mmx([(T.p4[:, 0:16], T.idn[:], T.zc[:], True, False)], 64, [A("idn"), A("zc")], [4])
+        mmx([(T.p4[:, 8 * H:8 * H + 8], lm[:], T.rcp[:], False, H == 1)], 64, [A("lm%d" % H), A("rcp")], [4])
 
     def send(t):
         dst = T.cores[(rank + 1 + t % (n_ranks - 1)) % n_ranks]
@@ -334,35 +347,36 @@ def rank_program(g, core, T, topo):
         for a, b, sm in (("qw", "lq", "aq"), ("tg", "lt", "at")):
             sn, dn, name = "%s%d" % (a, t), "%s%d" % (b, t), "%s%d" % (sm, t)
             i = node("g", [lambda e, sn=sn, dn=dn, name=name: e.remote_dma(T[dn][:], T[sn][:], T.sem[name], T.sem.ls, pid, rid, mask)],
-                     1.0, [A(sn)], [], (), "r", len(es))
-            node(None, [], 0.0, [], [A(dn)], (), "a", (name, n_in), 2.5 if a == "qw" else 1.5, (i,))
+                     0.6, [A(sn)], [], (), "r", len(es))
+            node(None, [], 0.0, [], [A(dn)], (), "a", (name, n_in), 3.3 if a == "qw" else 2.3, (i,))
 
     def update(t, c):
-        ts(T.hf[:], T.hh[:], 16.0, OP.add, [A("hh")], [A("hf")], n=256)
-        for b in range(2):
-            mms([(T.p2[:, 128 * b:128 * b + 128], T.iv[:, 256 * par + 128 * b:256 * par + 128 * b + 128], T.hf[:, 128 * par:128 * par + 128],
-                  par == 0, par == 1) for par in range(2)], 512, [A("iv"), A("hf")], [2])
+        E, M = A("ef%d" % c), A("mm%d" % c)
+        keep = t + 4 < RO
         for H in range(2):
-            kt, sc, wn = T["kt%d" % H], T["sc%d" % H], T["wn%d" % H]
-            tt(wn[:], sc[:].indirect(T.cl[:]), kt[:], OP.is_equal, [A("kt%d" % H), A("cl"), A("sc%d" % H)], [A("wn%d" % H)], cost=0.25)
-            mms([(T.p2[:, 256 + 128 * H:384 + 128 * H], wn[:], T.idn[:], True, True)], 128, [A("wn%d" % H), A("idn")], [2])
-        E, M, S = A("ef%d" % c), A("mm%d" % c), A("sgn%d" % c)
-        for b in range(2):
-            d = T.de[:, 128 * b:128 * b + 128]
-            e = T.ef[:, c + 4 * b::8]
-            rg = ("de", b, b + 1)
-            tt(d, T.p2[:, 128 * b:128 * b + 128], e, OP.subtract, [E], [rg], [2], n=128)
-            tt(d, T.p2[:, 256 + b:512:2], d, OP.mult, [rg], [rg], [2], n=128)
-            tt(e, e, d, OP.add, [E, rg], [("ef%d" % c, b, b + 1)], n=256)
-        tt(T.tm[:], T.p2[:, 256:512], T.sgn[:, c::4], OP.mult, [S], [A("tm")], [2], n=256)
-        tt(T.mm[:, c::4], T.mm[:, c::4], T.tm[:], OP.add, [M, A("tm")], [M], n=512)
-
-    def out_lines(c):
-        act(T.ylb[:, c::4], T.ef[:, c::4], AF.Copy, [A("ef%d" % c)], [A("yl%d" % c)], n=256, bias=-16.0)
+            kt, sc, nw = T["kt%d" % H], T["sc%d" % H], T["nw%d" % H]
+            tt(nw[:], sc[:].indirect(T.cl[:]), kt[:], OP.not_equal, [A("kt%d" % H), A("cl"), A("sc%d" % H)], [A("nw%d" % H)], cost=0.05 + 128 * GAT)
+        NW = [A("nw0"), A("nw1")]
+        ts(T.hf[:], T.hh[:], -2048.0, OP.add, [A("hh")], [A("hf")], n=256)
+        mms([(T.p6[:, 0:256], T.idh[:], T.ef[:, c::4])] + [(T.p6[:, 128 * H:128 * H + 128], T["nw%d" % H][:], T.nbig[:]) for H in range(2)],
+            512, NW + [E, A("idh"), A("nbig")], [6])
+        act(T.eb[:], T.p6[:, 0:256], AF.Copy, [], [A("eb")], [6], n=256, bias=BIG + (0.0 if keep else 2048.0))
+        mms([(T.p6[:, 256:512], T.idn[:], T.mm[:, c::4])] + [(T.p6[:, 256 + 128 * H:384 + 128 * H], T["nw%d" % H][:], T.idn[:]) for H in range(2)],
+            512, NW + [M, A("idn")], [6])
+        act(T.mm[:, c::4], T.p6[:, 256:512], AF.Abs, [], [M], [6], n=256, bias=-1.0)
+        k0 = 256 if keep else 0
+        mms([(T.p2[:, 0:256], T.idn[:], T.c2k[:, k0:k0 + 256])]
+            + [(T.p2[:, b:256:2], T.iv[:, 256 * par + 128 * b:256 * par + 128 * b + 128], T.hf[:, 128 * par:128 * par + 128])
+               for b in range(2) for par in range(2)]
+            + [(T.p2[:, 128 * H:128 * H + 128], T["nw%d" % H][:], T.big[:]) for H in range(2)],
+            1024, NW + [A("iv"), A("hf"), A("c2k"), A("idn"), A("big")], [2])
+        if keep:
+            tt(T.ef[:, c::4], T.p2[:, 0:256], T.eb[:], OP.min, [A("eb")], [E], [2], n=256)
+        else:
+            tt(T.ylb[:, c::4], T.p2[:, 0:256], T.eb[:], OP.min, [A("eb")], [A("yl%d" % c)], [2], n=256)
 
     early_lists(0)
-    prep_x(0)
-    prep_s(0)
+    prep(0)
     for c in range(1, 4):
         early_lists(c)
     win = T.xw[:, XC:XW]
@@ -374,74 +388,64 @@ def rank_program(g, core, T, topo):
         gather_even(1)
         gather_d(0)
         gather_d(1)
-        hashes(0, 0, T.p0, 0, 0)
-        hashes(1, 0, T.p1, 64, 1)
-        hop(0, 64, T.p0[:, 0:64], 0, first)
-        hop(64, 128, T.p1[:, 64:128], 1, first)
+        hashes(0, 0, T.p1, 0, 1)
+        hop(0, 64, T.p1[:, 0:64], 1, first)
+        hashes(1, 0, T.p2, 0, 2)
+        hop(64, 128, T.p2[:, 0:64], 2, first)
         scan(0)
         odd_min(0)
-        hashes(0, 1, T.p1, 0, 1)
+        hashes(0, 1, T.p1, 64, 1)
         scan(1)
         odd_min(1)
-        hashes(1, 1, T.p2, 0, 2)
-        hop(128, 192, T.p1[:, 0:64], 1, first)
-        hop(192, 256, T.p2[:, 0:64], 2, first)
+        hashes(1, 1, T.p2, 64, 2)
+        hop(128, 192, T.p1[:, 64:128], 1, first)
+        hop(192, 256, T.p2[:, 64:128], 2, first)
         for H, par in ((0, 0), (1, 0), (0, 1), (1, 1)):
             look(H, par)
-        over(0)
         gate(0)
-        over(1)
         gate(1)
         for H in range(2):
             score(H, 0, c)
             score(H, 1, c)
             keys(H)
         kl = T.p4[:, 0:16]
-        mms([(T.p5[:, 0:16], T.idn[:], T.icn[:], True, False)], 64, [A("idn"), A("icn")], [5])
-        ts(T.kn[:], kl, -1.0, OP.mult, [], [A("kn")], [4])
-        ts(T.nf[:], kl, 0.75, OP.is_lt, [], [A("nf")], [4])
-        ts(T.li[:], T.kn[:], 15, OP.bitwise_and, [A("kn")], [A("li")])
-        tt(T.lj[:], T.li[:], T.i16[:], OP.add, [A("li"), A("i16")], [A("lj")])
-        cp(T.l16[:], T.lj[:], [A("lj")], [A("l16")])
+        cp(T.kn[:], kl, [], [A("kn")], [4])
+        tt(T.nf[:], kl, T.thr[:], OP.is_gt, [A("thr")], [A("nf")], [4])
+        ts(T.li[:], T.kn[:], 0x0F0F, OP.bitwise_and, [A("kn")], [A("li")])
+        ts(T.l16[:], T.li[:], cf(27), OP.add, [A("li"), rc(27)], [A("l16")])
         qw, qn = T["qw%d" % t], "qw%d" % t
         cp(qw[:], T.qq[:].indirect(T.l16[:]), [A("qe"), A("qo"), A("l16")], [A(qn)], cost=0.05 + 256 * GAT)
-        mms([(T.p1[:, 0:16], T.wu[:, 15 - r:143 - r], qw[:, r::16], r == 0, r == 15) for r in range(16)], 64, [A("wu"), A(qn)], [1])
+        mms([(T.p1[:, 0:16], T.wu[:, 15 - r:143 - r], qw[:, r::16]) for r in range(16)], 1024, [A("wu"), A(qn)], [1])
         scn(T.nfs[:, 1:17], T.nf[:], T.z16[:], 0.0, OP.add, OP.max, [A("nf"), A("z16")], [A("nfs")], 16)
         tt(T.nfi[:], T.nf[:], T.icr[:], OP.mult, [A("nf"), A("icr")], [A("nfi")])
-        mms([(T.p5[:, 0:16], T.am[:], T.nf[:], False, False), (T.p5[:, 0:16], T.nbl[:], T.nfs[:, 0:16], False, False),
-             (T.p5[:, 0:16], T.idn[:], T.nfi[:], False, True)], 64, [A("am"), A("nf"), A("nbl"), A("nfs"), A("idn"), A("nfi")], [5])
-        ts(T.ofi[:], T.p5[:, 0:16], 32.0, OP.mult, [], [A("ofi")], [5])
+        mms([(T.p5[:, 0:16], T.i32[:], T.icn[:]), (T.p5[:, 0:16], T.am[:], T.nf[:]), (T.p5[:, 0:16], T.nbl[:], T.nfs[:, 0:16]),
+             (T.p5[:, 0:16], T.i32[:], T.nfi[:])], 256, [A("am"), A("nf"), A("nbl"), A("nfs"), A("i32"), A("nfi"), A("icn")], [5])
         cp(T.uwi[:], T.p1[:, 0:16], [], [A("uwi")], [1])
         ts(T.uwa[:], T.uwi[:], 31, OP.bitwise_and, [A("uwi")], [A("uwa")])
-        tt(T.tgi[:], T.uwa[:], T.ofi[:], OP.add, [A("uwa"), A("ofi")], [A("tgi")])
+        tt(T.tgi[:], T.p5[:, 0:16], T.uwa[:], OP.add, [A("uwa")], [A("tgi")], [5])
         cp(T["tg%d" % t][:], T.tgi[:], [A("tgi")], [A("tg%d" % t)])
         send(t)
-        if t == 3:
-            update(t, c)
         if t < RO - 1:
-            if t < 3:
-                prep_x(t + 1)
-                prep_s(t + 1)
-            else:
-                prep_x(0)
-                prep_s(0)
-            mms([(T.p5[:, 32:48], T.one[:], T.nf[:], True, True)], 64, [A("one"), A("nf")], [5])
-            node("v", [lambda e: e.tensor_reduce(T.kc[:], T.p5[:, 32:48], AxisListType.X, OP.add)], cy(16), [], [A("kc")], [5])
-            ts(T.kci[:], T.kc[:], -1.0, OP.mult, [A("kc")], [A("kci")])
+            prep((t + 1) % 4)
+            mms([(T.p5[:, 32:33], T.one[:], T.nfs[:, 16:17])], 64, [A("one"), A("nfs")], [5])
+            ts(T.kci[:], T.p5[:, 32:33], -1.0, OP.mult, [], [A("kci")], [5])
             ts(T.kcj[:], T.kci[:], 31, OP.bitwise_and, [A("kci")], [A("kcj")])
             cp(T.kap[:], T.kcj[:], [A("kcj")], [A("kap")])
-            ts(T.ek[:], T.ei[:], T.kap[:], OP.add, [A("ei"), A("kap")], [A("ek")], n=256)
-        if t != 3:
-            update(t, c)
-        if t > 0:
-            out_lines(c)
+            act(T.p0[:, 256:512], T.p0[:, 0:256], AF.Identity, [A("kap")], [], [0], n=256, bias=T.kap[:])
+        update(t, c)
+        last = t == RO - 1
+        if last:
+            for z in range(2):
+                ap, rg = T.xw[:, XC + 2048 * z:XC + 2048 * z + 2048], A("xw", XC + 2048 * z, XC + 2048 * z + 2048)
+                act(ap, ap, AF.Relu, [rg], [rg], n=2048)
         lt = T["lt%d" % t]
         L = A("lt%d" % t)
         tt(T.av[:], win.indirect(lt[:]), T["lq%d" % t][:], OP.add, [WX, L, A("lq%d" % t)], [A("av")], cost=0.05 + 256 * GAT)
-        ts(T.ai[:], T.av[:], 0.5, OP.mult, [A("av")], [A("ai")], (), -0.25, OP.add, n=256)
-        cp(win.indirect(lt[:]), T.ai[:], [A("ai"), L], [WX], cost=0.05 + 256 * SCA)
+        ts(T.aw[:], T.av[:], 0.5, OP.mult, [A("av")], [A("aw")], (), 1279.75, OP.add, n=128)
+        ts(T.ax[:], T.aw[:], -1280.0 - (0.0 if last else DEL), OP.add, [A("aw")], [A("ax")], n=128)
+        cp(win.indirect(lt[:]), T.ax[:], [A("ax"), L], [WX], cost=0.05 + 256 * SCA)
     dma("y", T.ym[:], T.mm[:], MM4, [], 262144)
-    dma("s", T.yl[:], T.ylb[:], [A("yl%d" % c) for c in range(4)], [], 524288)
+    dma("y", T.yl[:], T.ylb[:], [A("yl%d" % c) for c in range(4)], [], 524288)
     dma("y", T.yx[:, 0:2048], T.xw[:, XC:XC + 2048], [WX], [], 1048576)
     dma("s", T.yx[:, 2048:4096], T.xw[:, XC + 2048:XC + 4096], [WX], [], 1048576)
 
@@ -451,7 +455,7 @@ def rank_program(g, core, T, topo):
     for i, d in enumerate(nodes):
         for j in d["deps"] | d["order"]:
             f = nodes[j]
-            lag = f["late"] + ((0.03 if f["q"] == d["q"] else 0.1) if j in d["deps"] else 0.0)
+            lag = f["late"] + ((0.05 if f["q"] == d["q"] else 0.1) if j in d["deps"] else 0.0)
             before[i].append((j, lag))
             after[j].append((i, lag))
 

@@ -1,54 +1,139 @@
+import math
 from concourse.bass import DstId, RemoteDMATransfer
 from concourse.mybir import dt, AluOpType, AxisListType, ActivationFunctionType
 
 OP = AluOpType
 AF = ActivationFunctionType
 RO = 5
+ST = 2 * RO
 XC = 16
-XW = XC + 512 * 32
+XD = 8192
+XW = XC + XD + 256
 DEL = 2.0 ** -10
 BIG = 8192.0
-LOOK_S = ((0, 0), (1, 0))
-EVEN_V = (0,)
+YS = ((2, 1), (2, 1))
+EVEN_V = (1, 1)
+D_V = (0, 0)
 CUT = 2816
 
-SCRATCH = {"xw": ("sbuf", [128, XW], "bfloat16"), "alt": ("sbuf", [128, 2048], "bfloat16")}
+SCRATCH = {"xw0": ("sbuf", [128, XW], "bfloat16"), "xw1": ("sbuf", [128, XW], "bfloat16"), "alt": ("sbuf", [128, 1024], "bfloat16")}
 for _n, _w, _d in (
         ("ei0", 1024, "int32"), ("ef", 1024, "float16"), ("mm", 1024, "bfloat16"), ("ylb", 1024, "float32"),
-        ("d0", 4096, "bfloat16"), ("bb", 4096, "bfloat16"), ("qq", 4096, "bfloat16"), ("dq", 4096, "bfloat16"), ("sg", 4096, "bfloat16"),
-        ("yb", 4096, "bfloat16"),
+        ("d0", 4096, "bfloat16"), ("bb", 4096, "bfloat16"), ("qq0", 2048, "bfloat16"), ("qq1", 2048, "bfloat16"), ("dq", 4096, "bfloat16"),
+        ("sg", 4096, "bfloat16"), ("yb", 4096, "bfloat16"),
         ("dl16", 256, "uint16"), ("el16", 256, "uint16"), ("h16", 256, "uint16"),
-        ("ui", 256, "int32"), ("ua", 256, "int32"), ("ta", 256, "int32"), ("tb", 256, "int32"), ("tc", 256, "int32"), ("hh", 256, "int32"),
-        ("hf", 256, "float16"), ("eb", 256, "float32"), ("av", 256, "float16"), ("aw", 256, "float16"), ("ax", 256, "bfloat16"),
-        ("pi", 1, "int32"), ("ci", 8, "int32"), ("cf", 32, "float32"), ("m1", 160, "float32"), ("si", 128, "float32"), ("clf", 8, "float32"),
-        ("cl", 8, "uint16"), ("icf", 16, "float32"), ("icn", 16, "bfloat16"), ("icr", 16, "bfloat16"), ("mg", 128, "float32"),
-        ("zf", 16, "float32"), ("zc", 16, "bfloat16"), ("thr", 16, "float32"),
+        ("ui", 128, "int32"), ("ua", 128, "int32"), ("ta", 128, "int32"), ("tb", 128, "int32"), ("tc", 128, "int32"), ("hh", 128, "int32"),
+        ("hf", 256, "float16"), ("eb", 128, "float32"), ("av", 256, "float16"), ("aw", 256, "float16"), ("ax", 256, "bfloat16"),
+        ("qw", 128, "bfloat16"), ("qd", 256 * ST, "bfloat16"), ("lq", 256 * ST, "bfloat16"), ("tg", 16 * ST, "uint16"), ("lt", 16 * ST, "uint16"),
+        ("pi", 1, "int32"), ("ci", 8, "int32"), ("cf", 32, "float32"), ("m1", 160, "float32"), ("m64", 128, "float32"), ("si", 128, "float32"),
+        ("clf", 8, "float32"), ("cl", 8, "uint16"), ("icf", 16, "float32"), ("icn", 16, "bfloat16"), ("dum", 16, "int32"), ("mg", 128, "float32"),
+        ("zf", 8, "float32"), ("zc", 8, "bfloat16"), ("thr", 8, "float32"),
         ("idn", 128, "bfloat16"), ("nid", 128, "bfloat16"), ("nk", 128, "bfloat16"), ("nk2", 128, "bfloat16"), ("n2", 128, "bfloat16"),
-        ("idh", 128, "float16"), ("big", 128, "bfloat16"), ("nbig", 128, "bfloat16"), ("i32", 128, "bfloat16"),
-        ("g8", 8, "bfloat16"), ("g1", 8, "bfloat16"), ("rcp", 8, "bfloat16"),
-        ("wu", 144, "bfloat16"), ("pm", 512, "float16"), ("iv", 512, "float16"), ("nbl", 128, "bfloat16"), ("lt", 128, "bfloat16"),
-        ("t1", 128, "bfloat16"), ("am", 128, "bfloat16"), ("one", 128, "bfloat16"), ("mr", 128, "bfloat16"),
-        ("ke", 128, "bfloat16"), ("z16", 16, "bfloat16"), ("c2k", 512, "bfloat16"), ("c75", 128, "bfloat16"),
-        ("cr", 256, "int32"), ("ge", 256, "bfloat16"), ("gsg", 256, "bfloat16"), ("kt0", 128, "bfloat16"), ("kt1", 128, "bfloat16"),
-        ("sc0", 128, "bfloat16"), ("sc1", 128, "bfloat16"), ("lm0", 128, "bfloat16"), ("lm1", 128, "bfloat16"), ("nw0", 128, "bfloat16"),
-        ("nw1", 128, "bfloat16"), ("nf", 16, "bfloat16"), ("nfs", 32, "bfloat16"), ("nfi", 16, "bfloat16"), ("kn", 16, "int32"), ("li", 16, "int32"),
-        ("l16", 16, "uint16"), ("uwi", 16, "int32"), ("uwa", 16, "int32"), ("tgi", 16, "int32"),
+        ("idh", 128, "float16"), ("big", 128, "bfloat16"), ("nbig", 128, "bfloat16"), ("i32", 128, "bfloat16"), ("dup", 128, "bfloat16"),
+        ("dup2", 256, "bfloat16"), ("nbl2", 256, "bfloat16"), ("am2", 256, "bfloat16"),
+        ("g8", 8, "bfloat16"), ("gw", 16, "bfloat16"), ("rcp", 8, "bfloat16"),
+        ("wu", 144, "bfloat16"), ("pm", 512, "float16"), ("nbl", 128, "bfloat16"), ("low", 128, "bfloat16"),
+        ("t1", 128, "bfloat16"), ("t2", 128, "bfloat16"), ("am", 128, "bfloat16"), ("one", 128, "bfloat16"), ("mr", 128, "bfloat16"),
+        ("ke", 128, "bfloat16"), ("z16", 16, "bfloat16"), ("c2k", 256, "bfloat16"), ("c75", 256, "bfloat16"),
+        ("cr", 128, "int32"), ("ge", 128, "bfloat16"), ("gsg", 128, "bfloat16"), ("kt", 128, "bfloat16"), ("sc", 128, "bfloat16"),
+        ("lm", 128, "bfloat16"), ("nw", 128, "bfloat16"), ("nf", 16, "bfloat16"), ("nfs", 64, "bfloat16"), ("kn", 8, "int32"), ("li", 8, "int32"),
+        ("l16", 8, "uint16"), ("uwi", 8, "int32"), ("uwa", 8, "int32"), ("uwb", 8, "bfloat16"), ("tgm", 16, "int32"),
         ("kci", 1, "int32"), ("kcj", 1, "int32"), ("kap", 1, "float32")):
     SCRATCH[_n] = ("sbuf", [128, _w], _d)
+SCRATCH["hz"] = ("sbuf", [128, 34, 8], "float16")
 for _t in range(8):
     SCRATCH["p%d" % _t] = ("psum", [128, 512], "float32")
-for _t in range(RO):
-    SCRATCH["qw%d" % _t] = ("sbuf", [128, 256], "bfloat16")
-    SCRATCH["lq%d" % _t] = ("sbuf", [128, 256], "bfloat16")
-    SCRATCH["tg%d" % _t] = ("sbuf", [128, 16], "uint16")
-    SCRATCH["lt%d" % _t] = ("sbuf", [128, 16], "uint16")
-SEMAPHORES = ["cv", "cs", "cp", "cg", "ls"] + ["aq%d" % _t for _t in range(RO)] + ["at%d" % _t for _t in range(RO)] \
-    + ["dm%d" % _t for _t in range(24)]
+SEMAPHORES = ["cv", "cs", "cp", "cg", "ls"] + ["aq%d" % _t for _t in range(ST)] + ["at%d" % _t for _t in range(ST)] \
+    + ["dm%d" % _t for _t in range(40)]
 
-PASSES = 12
+ORDER = {}
+SEED = 1
+MOVES = 38000
+HEAT = 0.2
+PER = 11.2
+START = {"pre": -30.0, "soon": -1.0, "e0": 0.0, "e1": 0.9, "d0": 0.1, "d1": 2.0, "g0": 1.8, "g1": 4.0, "hop0": 2.5, "hop1": 7.0, "hf": 9.0, "gate": 8.0, "y00": 5.3, "y01": 6.2,
+         "s00": 7.1, "s01": 7.6, "y10": 8.2, "y11": 8.9, "s10": 9.8, "s11": 10.3, "v0": 5.0, "v1": 9.5, "score": 8.0, "keys": 12.0, "nw": 16.0,
+         "tail1": 13.0, "tail2": 16.0, "kappa": 14.0, "update": 17.0, "prep": 17.5, "arrive": 19.0}
+LQ, LT = 2.6, 1.6
+PASSES = 60
 CYC = 0.00104
+PCY = 0.0008
 GAT = 0.00162
 SCA = 0.0039
+
+
+def arrange(nodes, before):
+    n = len(nodes)
+    cost = [d["cost"] for d in nodes]
+    late = [d["late"] for d in nodes]
+    qs = [d["q"] for d in nodes]
+    deps = [set(j for j, _ in b) for b in before]
+    cnt, kind, base, off = {}, [], [], {}
+    for i, d in enumerate(nodes):
+        s, name = d["tag"]
+        cnt[(s, name, d["q"])] = c = cnt.get((s, name, d["q"]), 0) + 1
+        if name in ("pre", "soon"):
+            kind.append(i)
+            base.append(0.0)
+            off[i] = START[name] + 0.1 * c - (100.0 - 0.1 * i if d["kind"] == "d" else 0.0)
+        else:
+            kind.append((s % 2, name, d["q"], c))
+            base.append((s // 2) * 2 * PER)
+            off[kind[i]] = (s % 2) * PER + START[name] + 0.1 * c
+    free_kinds = [k for k in off if not (isinstance(k, int) and nodes[k]["kind"] == "d")]
+
+    def times(off):
+        at = [0.0] * n
+        for i in range(n):
+            x = base[i] + off[kind[i]]
+            for j in deps[i]:
+                if at[j] >= x:
+                    x = at[j] + 1e-6
+            at[i] = x
+        out = sorted(range(n), key=lambda i: at[i])
+        end, why, last = [0.0] * n, [-1] * n, {}
+        for i in out:
+            s, w = 0.0, -1
+            for j, lag in before[i]:
+                if end[j] + lag > s:
+                    s, w = end[j] + lag, j
+            q = qs[i]
+            if q is not None:
+                j = last.get(q, -1)
+                if j >= 0 and end[j] >= s:
+                    s, w = end[j], j
+                last[q] = i
+            end[i] = s + cost[i]
+            why[i] = w
+        top = max(range(n), key=lambda i: end[i] + late[i])
+        return end[top] + late[top], out, end, why, top, at
+    seed = [SEED]
+
+    def rnd():
+        seed[0] = (seed[0] * 1103515245 + 12345) % 2147483648
+        return seed[0] / 2147483648
+    cur = best = times(off)
+    for it in range(MOVES):
+        _, _, _, why, i, at = cur
+        pairs = []
+        while i >= 0:
+            j = why[i]
+            if j >= 0 and j not in deps[i] and nodes[i]["kind"] != "d" and nodes[j]["kind"] != "d":
+                pairs.append((j, i))
+            i = j
+        new = dict(off)
+        if pairs and rnd() < 0.8:
+            j, i = pairs[int(rnd() * len(pairs))]
+            k, sign = (i, -1.0) if rnd() < 0.5 else (j, 1.0)
+            new[kind[k]] = at[k] - base[k] + sign * (at[i] - at[j] + (1e-4, 1e-4, 0.3, 1.0)[int(rnd() * 4)] * rnd())
+        else:
+            new[free_kinds[int(rnd() * len(free_kinds))]] += 2.4 * (rnd() - 0.5)
+        r = times(new)
+        if r[0] - cur[0] < -math.log(1e-9 + rnd()) * (HEAT * (1.0 - it / MOVES) + 0.005):
+            cur, off = r, new
+            if r[0] < best[0]:
+                best = r
+    return best[:3]
 
 
 def rank_program(g, core, T, topo):
@@ -62,6 +147,10 @@ def rank_program(g, core, T, topo):
     nodes = []
     wr, rd, bank = {}, {}, {}
     ndma = [0]
+    tag = [(-1, "pre")]
+
+    def stage(s, name):
+        tag[0] = (s, name)
 
     def node(q, calls, cost, R, W, B=(), kind="c", key=None, late=0.0, extra=()):
         d = set(extra)
@@ -86,7 +175,7 @@ def rank_program(g, core, T, topo):
             if cur and q == "p":
                 order.add(cur[-1])
             bank[b] = (prev, cur + [me])
-        nodes.append({"q": q, "calls": calls, "cost": cost, "deps": d, "order": order - d, "kind": kind, "key": key, "late": late})
+        nodes.append({"q": q, "calls": calls, "cost": cost, "deps": d, "order": order - d, "kind": kind, "key": key, "late": late, "tag": tag[0]})
         for (b, lo, hi) in W:
             wr[b] = [e for e in wr.get(b, ()) if not (lo <= e[0] and e[1] <= hi)] + [(lo, hi, me)]
             rd[b] = [e for e in rd.get(b, ()) if not (lo <= e[0] and e[1] <= hi)]
@@ -94,10 +183,10 @@ def rank_program(g, core, T, topo):
             rd.setdefault(b, []).append((lo, hi, me))
         return me
 
-    def dma(q, out, in_, R, W, by, extra=()):
+    def dma(q, out, in_, R, W, late, extra=(), **kw):
         name = "dm%d" % ndma[0]
         ndma[0] += 1
-        return node(q, [lambda e: e.dma_start(out, in_)], 0.1, R, W, (), "d", name, 2.0 + by * 5e-6, extra)
+        return node(q, [lambda e: e.dma_start(out, in_, **kw)], 0.6 if q == "g" else 0.1, R, W, (), "d", name, late, extra)
 
     def A(b, lo=0, hi=1 << 20):
         return (b, lo, hi)
@@ -107,16 +196,16 @@ def rank_program(g, core, T, topo):
 
     def mms(lst, n, R, B):
         last = len(lst) - 1
-        node("p", [lambda e, a=a, j=j: e.matmul(a[0], a[1], a[2], j == 0, j == last) for j, a in enumerate(lst)], n * CYC, R, [], B)
+        node("p", [lambda e, a=a, j=j: e.matmul(a[0], a[1], a[2], j == 0, j == last) for j, a in enumerate(lst)], n * PCY, R, [], B)
 
     def mmx(lst, n, R, B):
-        node("p", [lambda e, a=a: e.matmul(*a) for a in lst], n * CYC, R, [], B)
+        node("p", [lambda e, a=a: e.matmul(*a) for a in lst], n * PCY, R, [], B)
 
-    def ts(out, in0, s1, o1, R, W, B=(), s2=None, o2=None, n=64):
+    def ts(out, in0, s1, o1, R, W, B=(), s2=None, o2=None, n=64, cost=None):
         if o2 is None:
-            node("v", [lambda e: e.tensor_scalar(out, in0, s1, None, o1)], cy(n), R, W, B)
+            node("v", [lambda e: e.tensor_scalar(out, in0, s1, None, o1)], cost or cy(n), R, W, B)
         else:
-            node("v", [lambda e: e.tensor_scalar(out, in0, s1, s2, o1, o2)], cy(n), R, W, B)
+            node("v", [lambda e: e.tensor_scalar(out, in0, s1, s2, o1, o2)], cost or cy(n), R, W, B)
 
     def tt(out, a, b, o, R, W, B=(), n=64, cost=None):
         node("v", [lambda e: e.tensor_tensor(out, a, b, o)], cost or cy(n), R, W, B)
@@ -139,32 +228,48 @@ def rank_program(g, core, T, topo):
         else:
             node("g", [lambda e: e.iota(ap, pat, base, cm)], 0.13 + 2 * n * CYC, [], W)
 
-    MM4 = [A("mm%d" % c) for c in range(4)]
-    dma("y", T.ei0[:], T.led[:], [], [A("ei0")], 524288)
-    dma("s", T.mm[:], T.mk[:], [], MM4, 262144)
-    parts = ((0, CUT // 2, "y", "v"), (CUT, 4096, "s", "s"), (CUT // 2, CUT, "y", "v"))
-    loads = [dma(q, T.xw[:, XC + lo:XC + hi], T.xt[:, lo:hi], [], [A("xw", XC + lo, XC + hi)], 1800000) for lo, hi, q, _ in parts]
-    for lo, hi, _, q in parts:
-        ap, rg = T.xw[:, XC + lo:XC + hi], A("xw", XC + lo, XC + hi)
-        if q == "v":
-            ts(ap, ap, -DEL, OP.add, [rg], [rg], n=(hi - lo) // 2)
-        else:
-            act(ap, ap, AF.Copy, [rg], [rg], n=hi - lo, bias=-DEL)
-    for z in range(1, 3):
-        dma("y", T.xw[:, XC + 4096 * z:XC + 4096 * z + 4096], T.xt[:], [], [A("xw", XC + 4096 * z, XC + 4096 * z + 4096)], 1048576 * z, loads)
+    xw = (T.xw0, T.xw1)
+
+    def MM(ph, c=None):
+        return [A("mm%d%d" % (ph, k)) for k in range(4) if c in (None, k)]
+
+    def lists_in(ph, late):
+        out = []
+        for b in range(2):
+            q = "ys"[b]
+            out.append(dma(q, T.ei0[64 * b:64 * b + 64, 512 * ph:512 * ph + 512], T.led[64 * ph:64 * ph + 64, 512 * b:512 * b + 512], [],
+                           [A("ei0%d" % ph, b, b + 1)], late))
+            out.append(dma(q, T.mm[64 * b:64 * b + 64, 512 * ph:512 * ph + 512], T.mk[64 * ph:64 * ph + 64, 512 * b:512 * b + 512], [],
+                           [A(n, b, b + 1) for n, _, _ in MM(ph)], late))
+        return out
+    lists_in(0, 2.6)
+    parts = ((0, CUT // 2, "v", 3.8), (CUT, 4096, "s", 4.8), (CUT // 2, CUT, "v", 5.9))
+    loads = []
+    for z, (lo, hi, q, late) in enumerate(parts):
+        for b in range(2):
+            loads.append(dma("ys"[b], T.xw0[64 * b:64 * b + 64, XC + lo:XC + hi], T.xt[0:64, lo:hi], [], [A("in0", 2 * z + b, 2 * z + b + 1)], late))
+    fill(T.alt[:, 0::2], 4096.0, [A("alt", 0, 1)], 256)
+    fill(T.alt[:, 1::2], DEL, [A("alt", 1, 2)], 256)
+    for z in range(4):
+        act(T.xw1[:, XC + 1024 * z:XC + 1024 * z + 1024], T.alt[:], AF.Copy, [A("alt")], [A("in1", z, z + 1)], n=1024, scale=0.0, bias=-DEL)
+    later = lists_in(1, 7.0)
+    for b in range(2):
+        later.append(dma("g", T.xw1[64 * b:64 * b + 64, XC:XC + 4096], T.xt[64:128, :], [A("in1")], [A("xw1", XC + 2048 * b, XC + 2048 * b + 2048)],
+                         4.5 + 3.5 * b, loads, accum_op=OP.add, max_dma_last_dim=4096))
+    for ph in range(2):
+        dma("y", xw[ph][:, XC + 4096:XC + XD], T.xt[:], [], [A("xw%d" % ph, XC + 4096, XC + XD)], 5.0 + 3.5 * ph, later)
+        fill(xw[ph][:, XC + XD:XW], 0.0, [A("xw%d" % ph, XC + XD, XW)], 128)
+        fill(xw[ph][:, 0:16], 0.0, [A("xw%d" % ph, 0, 16)])
+        fill(xw[ph][:, 1:2], 4096.0, [A("xw%d" % ph, 0, 16)])
 
     iota(T.pi[:], [[0, 1]], 0, 1, [A("pi")], 1, False)
     iota(T.m1[:], [[1, 160]], 1, 0, [A("m1")], 160)
+    iota(T.m64[:], [[0, 2], [1, 64]], 0, 0, [A("m64")], 128)
     iota(T.clf[:], [[16, 8]], 15, 0, [A("clf")], 8)
-    iota(T.mg[:], [[16, 8], [0, 16]], 0, 0, [A("mg")], 128)
+    iota(T.mg[:], [[0, 2], [16, 4], [0, 16]], 0, 0, [A("mg")], 128)
     iota(T.si[:], [[0, 8], [1, 16]], 0, 0, [A("si")], 128)
     iota(T.icf[:], [[16, 16]], 0, 1, [A("icf")], 16)
-    iota(T.zf[:], [[256, 16]], 256, 0, [A("zf")], 16)
-    iota(T.xw[:, XC + 12288:XW], [[0, 4096]], 0, 0, [A("xw", XC + 12288, XW)], 4096)
-    fill(T.xw[:, 0:16], 0.0, [A("xw", 0, 16)])
-    fill(T.xw[:, 1:2], 4096.0, [A("xw", 0, 16)])
-    fill(T.alt[:, 0::2], 4096.0, [A("alt", 0, 1)], 512)
-    fill(T.alt[:, 1::2], DEL, [A("alt", 1, 2)], 512)
+    iota(T.zf[:], [[256, 8]], 256, 0, [A("zf")], 8)
 
     def ci(j):
         return T.ci[:, j:j + 1]
@@ -175,52 +280,66 @@ def rank_program(g, core, T, topo):
     def rc(j):
         return ("cf", j, j + 1)
     ts(ci(0), T.pi[:], 15, OP.bitwise_and, [A("pi")], [("ci", 0, 1)])
-    ts(ci(1), T.pi[:], 3, OP.logical_shift_right, [A("pi")], [("ci", 1, 2)], (), 1, OP.bitwise_and)
-    ts(ci(2), T.pi[:], 1, OP.bitwise_and, [A("pi")], [("ci", 2, 3)])
-    ts(ci(3), T.pi[:], 1, OP.logical_shift_right, [A("pi")], [("ci", 3, 4)], (), 7, OP.bitwise_and)
-    ts(ci(4), T.pi[:], 7, OP.bitwise_and, [A("pi")], [("ci", 4, 5)])
+    ts(ci(1), T.pi[:], 1, OP.bitwise_and, [A("pi")], [("ci", 1, 2)])
+    ts(ci(2), T.pi[:], 1, OP.logical_shift_right, [A("pi")], [("ci", 2, 3)], (), 7, OP.bitwise_and)
+    ts(ci(3), T.pi[:], 63, OP.bitwise_and, [A("pi")], [("ci", 3, 4)])
+    ts(ci(4), T.pi[:], 48, OP.bitwise_and, [A("pi")], [("ci", 4, 5)])
     cp(T.cf[:, 0:5], T.ci[:, 0:5], [("ci", 0, 5)], [("cf", 0, 5)])
     cp(cf(5), T.pi[:], [A("pi")], [rc(5)])
     tt(cf(6), cf(5), cf(0), OP.subtract, [rc(5), rc(0)], [rc(6)])
-    ts(cf(7), cf(2), -1.0, OP.mult, [rc(2)], [rc(7)], (), 1.0, OP.add)
-    ts(cf(8), cf(1), -1.0, OP.mult, [rc(1)], [rc(8)], (), 1.0, OP.add)
-    tt(cf(9), cf(6), cf(3), OP.add, [rc(6), rc(3)], [rc(9)])
-    ts(cf(10), cf(4), 2.0, OP.mult, [rc(4), rc(6)], [rc(10)], (), cf(6), OP.add)
+    ts(cf(7), cf(1), -1.0, OP.mult, [rc(1)], [rc(7)], (), 1.0, OP.add)
+    tt(cf(9), cf(6), cf(2), OP.add, [rc(6), rc(2)], [rc(9)])
     for par in range(2):
         for b in range(2):
-            j = 11 + 2 * par + b
-            ts(cf(j), cf(9), float(8 * b + 1), OP.add, [rc(9), rc(7), rc(2)], [rc(j)], (), cf(2 if par else 7), OP.mult)
-            j = 15 + 2 * par + b
-            ts(cf(j), cf(10), float(par + 1), OP.add, [rc(10), rc(1), rc(8)], [rc(j)], (), cf(1 if b else 8), OP.mult)
-    for j in range(4):
-        ts(T.pm[:, 128 * j:128 * j + 128], T.m1[:, 0:128], cf(11 + j), OP.is_equal, [A("m1"), rc(11 + j)], [("pm", j, j + 1)], n=128)
-        ts(T.iv[:, 128 * j:128 * j + 128], T.m1[:, 0:128], cf(15 + j), OP.is_equal, [A("m1"), rc(15 + j)], [("iv", j, j + 1)], n=128)
+            j = 2 * par + b
+            ts(cf(11 + j), cf(9), float(8 * b + 1), OP.add, [rc(9), rc(7), rc(1)], [rc(11 + j)], (), cf(1 if par else 7), OP.mult)
+            ts(T.pm[:, 128 * j:128 * j + 128], T.m1[:, 0:128], cf(11 + j), OP.is_equal, [A("m1"), rc(11 + j)], [("pm", j, j + 1)], n=128)
     ts(cf(19), cf(0), 14.5, OP.is_lt, [rc(0)], [rc(19)])
     ts(cf(20), cf(19), 2048.0 + XC - BIG - 1.0, OP.mult, [rc(19)], [rc(20)], (), 1.0, OP.add)
+    ts(cf(26), cf(5), 1.0, OP.add, [rc(5)], [rc(26)])
+    ts(T.idn[:], T.m1[:, 0:128], cf(26), OP.is_equal, [A("m1"), rc(26)], [A("idn")], n=128)
+    cp(T.idh[:], T.idn[:], [A("idn")], [A("idh")])
+    ts(T.big[:], T.idn[:], BIG, OP.mult, [A("idn")], [A("big")])
+    fill(T.c2k[:, 0:128], 2048.0, [A("c2k", 0, 1)])
+    for z, (lo, hi, q, late) in enumerate(parts):
+        ap, rg = T.xw0[:, XC + lo:XC + hi], A("xw0", XC + lo, XC + hi)
+        if q == "v":
+            ts(ap, ap, -DEL, OP.add, [A("in0", 2 * z, 2 * z + 2)], [rg], n=(hi - lo) // 2)
+        else:
+            act(ap, ap, AF.Copy, [A("in0", 2 * z, 2 * z + 2)], [rg], n=hi - lo, bias=-DEL)
+    stage(-1, "soon")
+    fill(T.one[:], 1.0, [A("one")])
+    fill(T.hz[:], 0.0, [A("hz")], 136)
+    fill(T.c75[:, 0:128], 7.5 * DEL, [A("c75", 0, 1)])
+    fill(T.c75[:, 128:256], 0.0, [A("c75", 1, 2)])
     ts(cf(21), cf(0), 2.0, OP.mult, [rc(0)], [rc(21)], (), 1.0, OP.add)
     ts(cf(22), cf(6), 16.0, OP.add, [rc(6)], [rc(22)])
     ts(cf(23), cf(0), -1.0, OP.mult, [rc(0)], [rc(23)])
     ts(cf(24), cf(0), 2.0, OP.mult, [rc(0)], [rc(24)])
     ts(cf(25), cf(6), 0.0625, OP.mult, [rc(6)], [rc(25)], (), 1.0, OP.add)
-    ts(cf(26), cf(5), 1.0, OP.add, [rc(5)], [rc(26)])
     ts(cf(27), cf(0), 16.0, OP.mult, [rc(0)], [rc(27)])
     ts(T.wu[:], T.m1[:, 0:144], cf(22), OP.is_equal, [A("m1"), rc(22), rc(21)], [A("wu")], (), cf(21), OP.mult, n=144)
-    ts(T.idn[:], T.m1[:, 0:128], cf(26), OP.is_equal, [A("m1"), rc(26)], [A("idn")], n=128)
-    cp(T.idh[:], T.idn[:], [A("idn")], [A("idh")])
-    for name, f in (("nid", -1.0), ("n2", -2.0), ("big", BIG), ("nbig", -BIG), ("i32", 32.0)):
+    for name, f in (("n2", -2.0), ("nid", -1.0), ("nbig", -BIG), ("i32", 32.0)):
         ts(T[name][:], T.idn[:], f, OP.mult, [A("idn")], [A(name)])
     ts(T.nk[:], T.idn[:], cf(23), OP.mult, [A("idn"), rc(23)], [A("nk")])
     ts(T.nk2[:], T.idn[:], cf(24), OP.mult, [A("idn"), rc(24)], [A("nk2")])
     ts(T.g8[:], T.m1[:, 0:8], cf(25), OP.is_equal, [A("m1"), rc(25)], [A("g8")], (), 16.0, OP.mult)
-    ts(T.g1[:], T.m1[:, 0:8], cf(25), OP.is_equal, [A("m1"), rc(25)], [A("g1")])
+    ts(T.gw[:, 0:8], T.m1[:, 0:8], cf(25), OP.is_equal, [A("m1"), rc(25)], [A("gw", 0, 1)])
+    ts(T.gw[:, 8:16], T.m1[:, 0:8], cf(25), OP.is_equal, [A("m1"), rc(25), rc(21)], [A("gw", 1, 2)], (), cf(21), OP.mult)
     ts(T.rcp[:], T.m1[:, 0:8], cf(25), OP.is_equal, [A("m1"), rc(25)], [A("rcp")], (), -1.0, OP.mult)
-    ts(T.nbl[:], T.mg[:], cf(6), OP.is_equal, [A("mg"), rc(6)], [A("nbl")], (), -32.0, OP.mult, n=128)
-    ts(T.lt[:], T.m1[:, 0:128], cf(26), OP.is_gt, [A("m1"), rc(26)], [A("lt")], n=128)
-    tt(T.t1[:], T.nbl[:], T.lt[:], OP.mult, [A("nbl"), A("lt")], [A("t1")], n=256)
-    tt(T.am[:], T.big[:], T.t1[:], OP.add, [A("big"), A("t1")], [A("am")], n=256)
-    ts(T.icf[:], T.icf[:], cf(6), OP.subtract, [A("icf"), rc(6)], [A("icf")])
-    cp(T.icn[:], T.icf[:], [A("icf")], [A("icn")])
-    ts(T.icr[:], T.icf[:], -1.0, OP.mult, [A("icf")], [A("icr")], (), 255.0, OP.add)
+    ts(T.dup[:], T.m64[:], cf(3), OP.is_equal, [A("m64"), rc(3)], [A("dup")], n=128)
+    ts(T.nbl[:], T.mg[:], cf(4), OP.is_equal, [A("mg"), rc(4)], [A("nbl")], (), -32.0, OP.mult, n=128)
+    ts(T.low[:], T.m64[:], cf(3), OP.is_gt, [A("m64"), rc(3)], [A("low")], n=128)
+    tt(T.t1[:], T.nbl[:], T.low[:], OP.mult, [A("nbl"), A("low")], [A("t1")], n=256)
+    ts(T.t2[:], T.dup[:], 2.0 * BIG, OP.mult, [A("dup")], [A("t2")])
+    tt(T.am[:], T.t2[:], T.t1[:], OP.add, [A("t2"), A("t1")], [A("am")], n=256)
+    ts(cf(28), cf(5), 63.5, OP.is_lt, [rc(5)], [rc(28)])
+    ts(cf(29), cf(5), 63.5, OP.is_gt, [rc(5)], [rc(29)])
+    for name in ("dup", "nbl", "am"):
+        for b in range(2):
+            ts(T[name + "2"][:, 128 * b:128 * b + 128], T[name][:], cf(28 + b), OP.mult, [A(name), rc(28 + b)], [A(name + "2", b, b + 1)])
+    ts(T.icn[:], T.icf[:], cf(6), OP.subtract, [A("icf"), rc(6)], [A("icn")])
+    ts(T.dum[:], T.icf[:], cf(6), OP.subtract, [A("icf"), rc(6)], [A("dum")], (), float(XD), OP.add)
     cp(T.zc[:], T.zf[:], [A("zf")], [A("zc")])
     ts(T.thr[:], T.zf[:], -0.8, OP.add, [A("zf")], [A("thr")])
     ts(T.mr[:], T.si[:], cf(0), OP.is_equal, [A("si"), rc(0)], [A("mr")], n=128)
@@ -228,226 +347,265 @@ def rank_program(g, core, T, topo):
     fill(T.ke[:], 512.0, [A("ke")])
     fill(T.ke[:, 0::16], 0.625, [A("ke")])
     fill(T.z16[:], 0.0, [A("z16")])
+    fill(T.nf[:], 0.0, [A("nf")])
     fill(T.nfs[:], 0.0, [A("nfs")])
-    fill(T.one[:], 1.0, [A("one")])
-    fill(T.c2k[:, 0:256], 2048.0, [A("c2k", 0, 1)], 128)
-    fill(T.c2k[:, 256:512], 0.0, [A("c2k", 1, 2)], 128)
-    fill(T.c75[:], 7.5 * DEL, [A("c75")])
+    fill(T.c2k[:, 128:256], 0.0, [A("c2k", 1, 2)])
 
-    def early_lists(c):
-        ts(T.ef[:, c::4], T.ei0[:, c::4], -2048.0, OP.add, [A("ei0")], [A("ef%d" % c)], n=256)
+    def cls(ph, c, first=0, step=4):
+        return slice(512 * ph + c + first, 512 * ph + 512, step)
 
-    def prep(c):
-        E, M = A("ef%d" % c), A("mm%d" % c)
-        mms([(T.p0[:, 0:256], T.idn[:], T.c2k[:, 0:256])]
-            + [(T.p0[:, 128 * par:128 * par + 128], T.pm[:, 256 * par + 128 * b:256 * par + 128 * b + 128], T.ef[:, c + 4 * b::8])
-               for par in range(2) for b in range(2)], 768, [A("pm"), E, A("idn"), A("c2k")], [0])
-        ts(T.el16[:], T.p0[:, 0:256], float(XC), OP.add, [], [A("el16")], [0], n=256)
-        mms([(T.p7[:, 256:512], T.idh[:], T.ef[:, c::4]), (T.p7[:, 256:512], T.big[:], T.mm[:, c::4])], 512, [E, M, A("idh"), A("big")], [7])
-        ts(T.dl16[:], T.p7[:, 256:512], cf(19), OP.mult, [rc(19), rc(20)], [A("dl16")], [7], cf(20), OP.add, n=256)
-        for H in range(2):
-            o = T.p3[:, 256 + 128 * H:384 + 128 * H]
-            mms([(o, T.one[:], T.idn[:]), (o, T.mm[:, 512 * H + c:512 * H + 512:4], T.n2[:])], 256, [M, A("one"), A("idn"), A("n2")], [3])
+    def EF(ph, c):
+        return A("ef%d%d" % (ph, c))
 
-    items = T.xw[:, XC:XC + 4096]
-    all_x = T.xw[:, 0:XC + 4096]
-    RX = ("xw", 0, XC + 4096)
+    def early(ph, c):
+        ts(T.ef[:, cls(ph, c)], T.ei0[:, cls(ph, c)], -2048.0, OP.add, [A("ei0%d" % ph)], [EF(ph, c)], n=128)
 
-    def gather_even(H):
-        out = T.qq[:, 2048 * H:2048 * H + 2048:2]
-        src = all_x.indirect(T.el16[:, 64 * H:64 * H + 64])
-        f = cp if H in EVEN_V else (lambda o, i, R, W, cost: act(o, i, AF.Copy, R, W, cost=cost))
-        f(out, src, [RX, A("el16")], [("qe", H, H + 1)], cost=0.06 + 1024 * GAT)
+    def prep(s):
+        ph, c = s % 2, (s // 2) % 4
+        E, M = EF(ph, c), MM(ph, c)
+        o = slice(128 * ph, 128 * ph + 128)
+        mms([(T.p7[:, 128:256], T.idn[:], T.c2k[:, 0:128])]
+            + [(T.p7[:, 128 + 64 * par:192 + 64 * par], T.pm[:, 256 * par + 128 * b:256 * par + 128 * b + 128], T.ef[:, cls(ph, c, 4 * b, 8)])
+               for par in range(2) for b in range(2)], 384, [A("pm"), E, A("idn"), A("c2k", 0, 1)], [7])
+        mms([(T.p7[:, 256:384], T.idh[:], T.ef[:, cls(ph, c)]), (T.p7[:, 256:384], T.big[:], T.mm[:, cls(ph, c)])], 256,
+            [E, A("idh"), A("big")] + M, [7])
+        ts(T.dl16[:, o], T.p7[:, 256:384], cf(19), OP.mult, [rc(19), rc(20)], [A("dl16", ph, ph + 1)], [7], cf(20), OP.add, n=128)
+        ts(T.el16[:, o], T.p7[:, 128:256], float(XC), OP.add, [], [A("el16", ph, ph + 1)], [7], n=128)
+        pe = T["p%d" % ph]
+        mms([(pe[:, 0:128], T.idn[:], T.c2k[:, 0:128]), (pe[:, 0:128], T.ef[:, cls(ph, c)], T.idh[:])], 256, [E, A("idn"), A("idh"), A("c2k", 0, 1)], [ph])
+        mms([(pe[:, 256:384], T.one[:], T.idn[:]), (pe[:, 256:384], T.mm[:, cls(ph, c)], T.n2[:])], 256, M + [A("one"), A("idn"), A("n2")], [ph])
 
-    def gather_d(H):
-        act(T.d0[:, 2048 * H:2048 * H + 2048], all_x.indirect(T.dl16[:, 128 * H:128 * H + 128]), AF.Relu,
-            [RX, A("dl16")], [("d0", H, H + 1)], cost=0.06 + 2048 * GAT)
+    def head(s):
+        ph = s % 2
+        all_x, RX = xw[ph][:, 0:XC + 4096], A("xw%d" % ph, 0, XC + 4096)
+        qq, EL = T["qq%d" % ph], A("el16", ph, ph + 1)
+        for h in range(2):
+            z = 2 * ph + h
+            o = slice(1024 * z, 1024 * z + 1024)
+            stage(s, "d%d" % h)
+            src = all_x.indirect(T.dl16[:, 64 * z:64 * z + 64])
+            if h < D_V[ph]:
+                ts(T.d0[:, o], src, 0.0, OP.max, [RX, A("dl16", ph, ph + 1)], [("d0", z, z + 1)], cost=0.05 + 1024 * GAT)
+            else:
+                act(T.d0[:, o], src, AF.Relu, [RX, A("dl16", ph, ph + 1)], [("d0", z, z + 1)], cost=0.065 + 1024 * GAT)
+            stage(s, "g%d" % h)
+            scn(T.bb[:, o], T.d0[:, o], T.alt[:], DEL, OP.subtract, OP.min, [("d0", z, z + 1), A("alt")], [("bb", z, z + 1)], 512)
+            tt(qq[:, 1024 * h + 1:1024 * h + 1024:2], all_x.indirect(T.el16[:, 128 * ph + 64 + 32 * h:128 * ph + 96 + 32 * h]),
+               T.bb[:, 1024 * z:1024 * z + 1024:2], OP.min, [RX, EL, ("bb", z, z + 1)], [("qo", z, z + 1)], cost=0.05 + 512 * GAT)
+            stage(s, "e%d" % h)
+            out = qq[:, 1024 * h:1024 * h + 1024:2]
+            src = all_x.indirect(T.el16[:, 128 * ph + 32 * h:128 * ph + 32 * h + 32])
+            if h < EVEN_V[ph]:
+                cp(out, src, [RX, EL], [("qe", z, z + 1)], cost=0.05 + 512 * GAT)
+            else:
+                act(out, src, AF.Copy, [RX, EL], [("qe", z, z + 1)], cost=0.065 + 512 * GAT)
 
-    def hashes(H, par, ps, col, B):
-        mms([(ps[:, col:col + 64], T.wu[:, 15 - r:143 - r], T.qq[:, 2048 * H + 2 * r + par:2048 * H + 2048:32]) for r in range(16)],
-            1024, [A("wu"), ("qo" if par else "qe", H, H + 1)], [B])
-
-    def hop(lo, hi, src, B, first):
-        s = slice(lo, hi)
-        n = hi - lo
+    def hop(s, par):
+        ph = s % 2
+        pe, pu, qq = T["p%d" % ph], T["p%d" % (2 + ph)], T["qq%d" % ph]
+        stage(s, "hop%d" % par)
+        mms([(pu[:, par:256:2], T.idn[:], T.c75[:, 64:192])] + [(pu[:, k:256:16], qq[:, k::16], T.gw[:]) for k in range(par, 16, 2)],
+            640, [("qo" if par else "qe", 2 * ph, 2 * ph + 2), A("gw"), A("idn"), A("c75")], [2 + ph])
+        o = slice(64 * par, 64 * par + 64)
 
         def rg(b):
-            return (b, lo, hi)
-        cp(T.ui[:, s], src, [], [rg("ui")], [B], n=n)
-        ts(T.ua[:, s], T.ui[:, s], 4095, OP.bitwise_and, [rg("ui")], [rg("ua")], n=n)
-        tt(T.ta[:, s], T.p0[:, s], T.ua[:, s], OP.mult, [rg("ua")], [rg("ta")], [0], n=n)
-        ts(T.tb[:, s], T.ta[:, s], 5, OP.logical_shift_right, [rg("ta")], [rg("tb")], n=n)
-        o = 0 if first else 256
-        tt(T.tc[:, s], T.p0[:, o + lo:o + hi], T.tb[:, s], OP.add, [rg("tb")], [rg("tc")], [0], n=n)
-        ts(T.hh[:, s], T.tc[:, s], 4095, OP.bitwise_and, [rg("tc")], [rg("hh")], n=n)
-        cp(T.h16[:, s], T.hh[:, s], [rg("hh")], [rg("h16")], n=n)
+            return A(b, par, par + 1)
+        cp(T.ui[:, o], pu[:, 128 + par:256:2], [], [rg("ui")], [2 + ph])
+        ts(T.ua[:, o], T.ui[:, o], 4095, OP.bitwise_and, [rg("ui")], [rg("ua")])
+        tt(T.ta[:, o], pe[:, par:128:2], T.ua[:, o], OP.mult, [rg("ua")], [rg("ta")], [ph])
+        ts(T.tb[:, o], T.ta[:, o], 5, OP.logical_shift_right, [rg("ta")], [rg("tb")])
+        k0 = 0 if s < 2 else 128
+        tt(T.tc[:, o], pe[:, k0 + par:k0 + 128:2], T.tb[:, o], OP.add, [rg("tb")], [rg("tc")], [ph])
+        ts(T.hh[:, o], T.tc[:, o], 4095, OP.bitwise_and, [rg("tc")], [rg("hh")])
+        z0 = 17 * par
+        ts(T.hz[:, z0 + 1:z0 + 17:2, :], T.hh[:, o], -2048.0, OP.add, [rg("hh")], [rg("hz")])
+        pl = pu[:, 256 + 64 * par:320 + 64 * par]
+        mms([(pl, T.hz[:, z0 + 1 - b:z0 + 17 - b, :], T.idh[:, b::2]) for b in range(2)], 128, [rg("hz"), A("idh")], [2 + ph])
+        z = 2 * ph + par
+        ts(T.h16[:, 64 * z:64 * z + 64], pl, 2048.0, OP.add, [], [A("h16", z, z + 1)], [2 + ph])
+        stage(s, "hf")
+        ts(T.hf[:, 128 * ph + par:128 * ph + 128:2], T.hh[:, o], -2048.0, OP.add, [rg("hh")], [A("hf", z, z + 1)])
 
-    def scan(H):
-        s = slice(2048 * H, 2048 * H + 2048)
-        scn(T.bb[:, s], T.d0[:, s], T.alt[:], DEL, OP.subtract, OP.min, [("d0", H, H + 1), A("alt")], [("bb", H, H + 1)], 1024)
+    def look(s, par):
+        ph = s % 2
+        qq, Q = T["qq%d" % ph], ("qo" if par else "qe", 2 * ph, 2 * ph + 2)
+        items, RX = xw[ph][:, XC:XC + 4096], A("xw%d" % ph, 0, XC + 4096)
+        z = 2 * ph + par
+        H16 = A("h16", z, z + 1)
+        ns = YS[ph][par]
+        for x in range(ns):
+            y = 2 * z + x
+            cols = slice(512 * y, 512 * y + 512)
+            stage(s, "y%d%d" % (par, x))
+            act(T.yb[:, cols], items.indirect(T.h16[:, 32 * y:32 * y + 32]), AF.Copy, [RX, H16], [("yb", y, y + 1)], cost=0.065 + 512 * GAT)
+            ps, B = (T.p5, 5) if x % 2 else (T.p4, 4)
+            mmx([(ps[:], T.nid[:], qq[:, 1024 * x + par:1024 * x + 1024:2], True, False)], 512, [A("nid"), Q], [B])
+            mmx([(ps[:], T.idn[:], T.yb[:, cols], False, True)], 512, [A("idn"), ("yb", y, y + 1)], [B])
+            stage(s, "s%d%d" % (par, x))
+            act(T.sg[:, 2048 * ph + 1024 * x + par:2048 * ph + 1024 * x + 1024:2], ps[:], AF.Sign, [], [("sg", y, y + 1)], [B], n=512)
+        if ns < 2:
+            lo, hi = 2 * z + ns, 2 * z + 2
+            cols = slice(2048 * ph + 1024 * ns + par, 2048 * ph + 2048, 2)
+            stage(s, "v%d" % par)
+            tt(T.dq[:, cols], items.indirect(T.h16[:, 32 * lo:32 * hi]), qq[:, 1024 * ns + par:2048:2], OP.subtract,
+               [RX, H16, Q], [("dq", lo, hi)], cost=0.05 + 512 * (2 - ns) * GAT)
+            ts(T.sg[:, cols], T.dq[:, cols], 1.0, OP.min, [("dq", lo, hi)], [("sg", lo, hi)], (), -1.0, OP.max, n=256 * (2 - ns))
 
-    def odd_min(H):
-        tt(T.qq[:, 2048 * H + 1:2048 * H + 2048:2], all_x.indirect(T.el16[:, 128 + 64 * H:192 + 64 * H]),
-           T.bb[:, 2048 * H:2048 * H + 2048:2], OP.min, [RX, A("el16"), ("bb", H, H + 1)], [("qo", H, H + 1)], cost=0.06 + 1024 * GAT)
+    def mid(s):
+        ph, c = s % 2, (s // 2) % 4
+        pe, pu = T["p%d" % ph], T["p%d" % (2 + ph)]
+        hop(s, 0)
+        hop(s, 1)
+        stage(s, "gate")
+        cp(T.cr[:], pu[:, 0:128], [], [A("cr")], [2 + ph], n=128)
+        tt(T.ge[:], pu[:, 0:128], T.cr[:], OP.is_gt, [A("cr")], [A("ge")], [2 + ph], n=128)
+        tt(T.gsg[:], pe[:, 256:384], T.ge[:], OP.mult, [A("ge")], [A("gsg")], [ph], n=128)
+        look(s, 0)
+        look(s, 1)
+        stage(s, "score")
+        mmx([(T.p6[:, 0:128], T.one[:], T.nk[:], True, False), (T.p6[:, 0:128], T.mm[:, cls(ph, c)], T.nk2[:], False, False)],
+            256, MM(ph, c) + [A("nk"), A("nk2"), A("one")], [6])
+        for par in range(2):
+            mmx([(T.p6[:, k:128:16], T.sg[:, 2048 * ph + k:2048 * ph + 2048:16], T.g8[:], False, k == 15) for k in range(par, 16, 2)],
+                512, [("sg", 4 * ph + 2 * par, 4 * ph + 2 * par + 2), A("g8")], [6])
+        stage(s, "keys")
+        tt(T.kt[:], T.p6[:, 0:128], T.gsg[:], OP.mult, [A("gsg")], [A("kt")], [6], n=128)
+        scn(T.sc[:], T.ke[:], T.kt[:], 0.625, OP.min, OP.max, [A("ke"), A("kt")], [A("sc")], 64)
+        tt(T.lm[:], T.sc[:].indirect(T.cl[:]), T.mr[:], OP.mult, [A("sc"), A("cl"), A("mr")], [A("lm")], cost=0.05 + 128 * GAT)
+        stage(s, "nw")
+        tt(T.nw[:], T.sc[:].indirect(T.cl[:]), T.kt[:], OP.not_equal, [A("kt"), A("cl"), A("sc")], [A("nw")], cost=0.05 + 128 * GAT)
 
-    def look(H, par):
-        s = slice(2048 * H + par, 2048 * H + 2048, 2)
-        lo = 128 * par + 64 * H
-        z = 2 * H + par
-        Q = ("qo" if par else "qe", H, H + 1)
-        if (H, par) in LOOK_S:
-            act(T.yb[:, 1024 * z:1024 * z + 1024], items.indirect(T.h16[:, lo:lo + 64]), AF.Copy, [RX, ("h16", lo, lo + 64)], [("yb", z, z + 1)],
-                cost=0.07 + 1024 * GAT)
-            for x in range(2):
-                ps, B = (T.p5, 5) if x else (T.p4, 4)
-                qs = slice(2048 * H + par + 1024 * x, 2048 * H + 1024 * x + 1024, 2)
-                mms([(ps[:], T.idn[:], T.yb[:, 1024 * z + 512 * x:1024 * z + 512 * x + 512]),
-                     (ps[:], T.nid[:], T.qq[:, qs])], 1024, [A("idn"), A("nid"), ("yb", z, z + 1), Q], [B])
-                act(T.sg[:, qs], ps[:], AF.Sign, [], [("sg", 4 * H + 2 * par + x, 4 * H + 2 * par + x + 1)], [B], n=512)
-            return
-        tt(T.dq[:, s], items.indirect(T.h16[:, lo:lo + 64]), T.qq[:, s], OP.subtract,
-           [RX, ("h16", lo, lo + 64), Q], [("dq", z, z + 1)], cost=0.06 + 1024 * GAT)
-        ts(T.sg[:, s], T.dq[:, s], 1.0, OP.min, [("dq", z, z + 1)], [("sg", 2 * z, 2 * z + 2)], (), -1.0, OP.max, n=512)
-
-    def score(H, par, c):
-        ps, B = (T.p7, 7) if H else (T.p6, 6)
-        if par == 0:
-            mmx([(ps[:, 0:128], T.one[:], T.nk[:], True, False), (ps[:, 0:128], T.mm[:, 512 * H + c:512 * H + 512:4], T.nk2[:], False, False)],
-                256, [A("mm%d" % c), A("nk"), A("nk2"), A("one")], [B])
-        z = 2 * H + par
-        mmx([(ps[:, k:128:16], T.sg[:, 2048 * H + k:2048 * H + 2048:16], T.g8[:], False, k == 15) for k in range(par, 16, 2)],
-            512, [("sg", 2 * z, 2 * z + 2), A("g8")], [B])
-
-    def gate(H):
-        s = slice(128 * H, 128 * H + 128)
-        mms([(T.p3[:, s], T.idn[:], T.c75[:])]
-            + [(T.p3[:, 128 * H + k:128 * H + 128:16], T.qq[:, 2048 * H + k:2048 * H + 2048:16], T.g1[:]) for k in range(16)],
-            1152, [("qe", H, H + 1), ("qo", H, H + 1), A("g1"), A("idn"), A("c75")], [3])
-        cp(T.cr[:, s], T.p3[:, s], [], [("cr", H, H + 1)], [3], n=128)
-        tt(T.ge[:, s], T.p3[:, s], T.cr[:, s], OP.is_gt, [("cr", H, H + 1)], [("ge", H, H + 1)], [3], n=128)
-        tt(T.gsg[:, s], T.p3[:, 256 + 128 * H:384 + 128 * H], T.ge[:, s], OP.mult, [("ge", H, H + 1)], [("gsg", H, H + 1)], [3], n=128)
-
-    def keys(H):
-        ps, B = (T.p7, 7) if H else (T.p6, 6)
-        kt, sc, lm = T["kt%d" % H], T["sc%d" % H], T["lm%d" % H]
-        tt(kt[:], ps[:, 0:128], T.gsg[:, 128 * H:128 * H + 128], OP.mult, [("gsg", H, H + 1)], [A("kt%d" % H)], [B], n=128)
-        scn(sc[:], T.ke[:], kt[:], 0.625, OP.min, OP.max, [A("ke"), A("kt%d" % H)], [A("sc%d" % H)], 64)
-        tt(lm[:], sc[:].indirect(T.cl[:]), T.mr[:], OP.mult, [A("sc%d" % H), A("cl"), A("mr")], [A("lm%d" % H)], cost=0.05 + 128 * GAT)
-        if H == 0:
-            mmx([(T.p4[:, 0:16], T.idn[:], T.zc[:], True, False)], 64, [A("idn"), A("zc")], [4])
-        mmx([(T.p4[:, 8 * H:8 * H + 8], lm[:], T.rcp[:], False, H == 1)], 64, [A("lm%d" % H), A("rcp")], [4])
-
-    def send(t):
+    def send(s):
+        t = s // 2
         dst = T.cores[(rank + 1 + t % (n_ranks - 1)) % n_ranks]
         es = topo.engines(core, dst)[:8]
         mask = sum(1 << e for e in es)
         rid, pid, _ = topo.addr(dst)
         src = T.cores[(rank - 1 - t % (n_ranks - 1)) % n_ranks]
         n_in = len(topo.engines(src, core)[:8])
-        for a, b, sm in (("qw", "lq", "aq"), ("tg", "lt", "at")):
-            sn, dn, name = "%s%d" % (a, t), "%s%d" % (b, t), "%s%d" % (sm, t)
-            i = node("g", [lambda e, sn=sn, dn=dn, name=name: e.remote_dma(T[dn][:], T[sn][:], T.sem[name], T.sem.ls, pid, rid, mask)],
-                     0.6, [A(sn)], [], (), "r", len(es))
-            node(None, [], 0.0, [], [A(dn)], (), "a", (name, n_in), 3.3 if a == "qw" else 2.3, (i,))
+        for a, b, sm, w in (("qd", "lq", "aq", 256), ("tg", "lt", "at", 16)):
+            name, o = "%s%d" % (sm, s), slice(w * s, w * s + w)
+            i = node("g", [lambda e, a=a, b=b, o=o, name=name: e.remote_dma(T[b][:, o], T[a][:, o], T.sem[name], T.sem.ls, pid, rid, mask)],
+                     0.6, [A(a, s, s + 1)], [], (), "r", len(es))
+            node(None, [], 0.0, [], [A(b, s, s + 1)], (), "a", (name, n_in), LQ if a == "qd" else LT, (i,))
 
-    def update(t, c):
-        E, M = A("ef%d" % c), A("mm%d" % c)
-        keep = t + 4 < RO
-        for H in range(2):
-            kt, sc, nw = T["kt%d" % H], T["sc%d" % H], T["nw%d" % H]
-            tt(nw[:], sc[:].indirect(T.cl[:]), kt[:], OP.not_equal, [A("kt%d" % H), A("cl"), A("sc%d" % H)], [A("nw%d" % H)], cost=0.05 + 128 * GAT)
-        NW = [A("nw0"), A("nw1")]
-        ts(T.hf[:], T.hh[:], -2048.0, OP.add, [A("hh")], [A("hf")], n=256)
-        mms([(T.p6[:, 0:256], T.idh[:], T.ef[:, c::4])] + [(T.p6[:, 128 * H:128 * H + 128], T["nw%d" % H][:], T.nbig[:]) for H in range(2)],
-            512, NW + [E, A("idh"), A("nbig")], [6])
-        act(T.eb[:], T.p6[:, 0:256], AF.Copy, [], [A("eb")], [6], n=256, bias=BIG + (0.0 if keep else 2048.0))
-        mms([(T.p6[:, 256:512], T.idn[:], T.mm[:, c::4])] + [(T.p6[:, 256 + 128 * H:384 + 128 * H], T["nw%d" % H][:], T.idn[:]) for H in range(2)],
-            512, NW + [M, A("idn")], [6])
-        act(T.mm[:, c::4], T.p6[:, 256:512], AF.Abs, [], [M], [6], n=256, bias=-1.0)
-        k0 = 256 if keep else 0
-        mms([(T.p2[:, 0:256], T.idn[:], T.c2k[:, k0:k0 + 256])]
-            + [(T.p2[:, b:256:2], T.iv[:, 256 * par + 128 * b:256 * par + 128 * b + 128], T.hf[:, 128 * par:128 * par + 128])
-               for b in range(2) for par in range(2)]
-            + [(T.p2[:, 128 * H:128 * H + 128], T["nw%d" % H][:], T.big[:]) for H in range(2)],
-            1024, NW + [A("iv"), A("hf"), A("c2k"), A("idn"), A("big")], [2])
-        if keep:
-            tt(T.ef[:, c::4], T.p2[:, 0:256], T.eb[:], OP.min, [A("eb")], [E], [2], n=256)
-        else:
-            tt(T.ylb[:, c::4], T.p2[:, 0:256], T.eb[:], OP.min, [A("eb")], [A("yl%d" % c)], [2], n=256)
-
-    early_lists(0)
-    prep(0)
-    for c in range(1, 4):
-        early_lists(c)
-    win = T.xw[:, XC:XW]
-    WX = ("xw", XC, XW)
-    for t in range(RO):
-        c = t % 4
-        first = t == 0
-        gather_even(0)
-        gather_even(1)
-        gather_d(0)
-        gather_d(1)
-        hashes(0, 0, T.p1, 0, 1)
-        hop(0, 64, T.p1[:, 0:64], 1, first)
-        hashes(1, 0, T.p2, 0, 2)
-        hop(64, 128, T.p2[:, 0:64], 2, first)
-        scan(0)
-        odd_min(0)
-        hashes(0, 1, T.p1, 64, 1)
-        scan(1)
-        odd_min(1)
-        hashes(1, 1, T.p2, 64, 2)
-        hop(128, 192, T.p1[:, 64:128], 1, first)
-        hop(192, 256, T.p2[:, 64:128], 2, first)
-        for H, par in ((0, 0), (1, 0), (0, 1), (1, 1)):
-            look(H, par)
-        gate(0)
-        gate(1)
-        for H in range(2):
-            score(H, 0, c)
-            score(H, 1, c)
-            keys(H)
-        kl = T.p4[:, 0:16]
-        cp(T.kn[:], kl, [], [A("kn")], [4])
-        tt(T.nf[:], kl, T.thr[:], OP.is_gt, [A("thr")], [A("nf")], [4])
+    def tail(s):
+        ph = s % 2
+        qq = T["qq%d" % ph]
+        stage(s, "tail1")
+        kl = T.p7[:, 0:8]
+        mms([(kl, T.idn[:], T.zc[:]), (kl, T.lm[:], T.rcp[:])], 128, [A("idn"), A("zc"), A("lm"), A("rcp")], [7])
+        cp(T.kn[:], kl, [], [A("kn")], [7])
+        tt(T.nf[:, 0:8], kl, T.thr[:], OP.is_gt, [A("thr")], [A("nf")], [7])
         ts(T.li[:], T.kn[:], 0x0F0F, OP.bitwise_and, [A("kn")], [A("li")])
         ts(T.l16[:], T.li[:], cf(27), OP.add, [A("li"), rc(27)], [A("l16")])
-        qw, qn = T["qw%d" % t], "qw%d" % t
-        cp(qw[:], T.qq[:].indirect(T.l16[:]), [A("qe"), A("qo"), A("l16")], [A(qn)], cost=0.05 + 256 * GAT)
-        mms([(T.p1[:, 0:16], T.wu[:, 15 - r:143 - r], qw[:, r::16]) for r in range(16)], 1024, [A("wu"), A(qn)], [1])
-        scn(T.nfs[:, 1:17], T.nf[:], T.z16[:], 0.0, OP.add, OP.max, [A("nf"), A("z16")], [A("nfs")], 16)
-        tt(T.nfi[:], T.nf[:], T.icr[:], OP.mult, [A("nf"), A("icr")], [A("nfi")])
-        mms([(T.p5[:, 0:16], T.i32[:], T.icn[:]), (T.p5[:, 0:16], T.am[:], T.nf[:]), (T.p5[:, 0:16], T.nbl[:], T.nfs[:, 0:16]),
-             (T.p5[:, 0:16], T.i32[:], T.nfi[:])], 256, [A("am"), A("nf"), A("nbl"), A("nfs"), A("i32"), A("nfi"), A("icn")], [5])
-        cp(T.uwi[:], T.p1[:, 0:16], [], [A("uwi")], [1])
+        cp(T.qw[:], qq[:].indirect(T.l16[:]), [("qe", 2 * ph, 2 * ph + 2), ("qo", 2 * ph, 2 * ph + 2), A("l16")], [A("qw")], cost=0.05 + 128 * GAT)
+        for b in range(2):
+            mms([(T.p4[:, 128 * b:128 * b + 128], T.dup2[:, 128 * b:128 * b + 128], T.qw[:])], 128, [A("dup2"), A("qw")], [4])
+        QD = A("qd", s, s + 1)
+        act(T.qd[:, 256 * s:256 * s + 256], T.p4[:, 0:256], AF.Copy, [], [QD], [4], n=256)
+        n0, NS = 32 * ph, A("nfs", ph, ph + 1)
+        scn(T.nfs[:, n0 + 1:n0 + 17], T.nf[:], T.z16[:], 0.0, OP.add, OP.max, [A("nf"), A("z16")], [NS], 16)
+        lst = [(T.p7[:, 16:32], T.i32[:], T.icn[:]), (T.p7[:, 24:32], T.nbl2[:, 0:128], T.nfs[:, n0 + 8:n0 + 16])]
+        for b in range(2):
+            r = slice(128 * b, 128 * b + 128)
+            lst += [(T.p7[:, 16 + 8 * b:24 + 8 * b], T.am2[:, r], T.nf[:, 0:8]), (T.p7[:, 16 + 8 * b:24 + 8 * b], T.nbl2[:, r], T.nfs[:, n0:n0 + 8])]
+        for r0 in range(0, 16, 4):
+            mmx([(T.p7[:, 32:40], T.wu[:, 15 - r:143 - r], T.qw[:, r::16], r == 0, r == 15) for r in range(r0, r0 + 4)], 256, [A("wu"), A("qw")], [7])
+        stage(s, "tail2")
+        cp(T.uwi[:], T.p7[:, 32:40], [], [A("uwi")], [7])
         ts(T.uwa[:], T.uwi[:], 31, OP.bitwise_and, [A("uwi")], [A("uwa")])
-        tt(T.tgi[:], T.p5[:, 0:16], T.uwa[:], OP.add, [A("uwa")], [A("tgi")], [5])
-        cp(T["tg%d" % t][:], T.tgi[:], [A("tgi")], [A("tg%d" % t)])
-        send(t)
-        if t < RO - 1:
-            prep((t + 1) % 4)
-            mms([(T.p5[:, 32:33], T.one[:], T.nfs[:, 16:17])], 64, [A("one"), A("nfs")], [5])
-            ts(T.kci[:], T.p5[:, 32:33], -1.0, OP.mult, [], [A("kci")], [5])
-            ts(T.kcj[:], T.kci[:], 31, OP.bitwise_and, [A("kci")], [A("kcj")])
-            cp(T.kap[:], T.kcj[:], [A("kcj")], [A("kap")])
-            act(T.p0[:, 256:512], T.p0[:, 0:256], AF.Identity, [A("kap")], [], [0], n=256, bias=T.kap[:])
-        update(t, c)
-        last = t == RO - 1
-        if last:
+        cp(T.uwb[:], T.uwa[:], [A("uwa")], [A("uwb")])
+        mmx([a + (j == 0, False) for j, a in enumerate(lst)], 384, [A("am2"), A("nf"), A("nbl2"), NS, A("i32"), A("icn")], [7])
+        mmx([(T.p7[:, 16 + 8 * b:24 + 8 * b], T.dup2[:, 128 * b:128 * b + 128], T.uwb[:], False, b == 1) for b in range(2)], 128,
+            [A("dup2"), A("uwb")], [7])
+        tt(T.tgm[:], T.p7[:, 16:32], T.dum[:], OP.min, [A("dum")], [A("tgm")], [7])
+        cp(T.tg[:, 16 * s:16 * s + 16], T.tgm[:], [A("tgm")], [A("tg", s, s + 1)])
+        send(s)
+
+    def kappa():
+        mms([(T.p6[:, 384:385], T.one[:], T.nfs[:, 32 * ph + 8:32 * ph + 9]) for ph in range(2)], 128, [A("one"), A("nfs")], [6])
+        ts(T.kci[:], T.p6[:, 384:385], -1.0, OP.mult, [], [A("kci")], [6])
+        ts(T.kcj[:], T.kci[:], 31, OP.bitwise_and, [A("kci")], [A("kcj")])
+        cp(T.kap[:], T.kcj[:], [A("kcj")], [A("kap")])
+
+    def plus_kappa(ph):
+        pe = T["p%d" % ph]
+        act(pe[:, 128:256], pe[:, 0:128], AF.Identity, [A("kap")], [], [ph], n=128, bias=T.kap[:])
+
+    def update(s):
+        ph, t = s % 2, s // 2
+        c = t % 4
+        E, M = EF(ph, c), MM(ph, c)
+        stage(s, "update")
+        keep = t + 4 < RO
+        pu = T["p%d" % (2 + ph)]
+        mms([(T.p6[:, 128:256], T.idh[:], T.ef[:, cls(ph, c)]), (T.p6[:, 128:256], T.nw[:], T.nbig[:])], 256, [A("nw"), E, A("idh"), A("nbig")], [6])
+        mms([(T.p6[:, 256:384], T.idn[:], T.mm[:, cls(ph, c)]), (T.p6[:, 256:384], T.nw[:], T.idn[:])], 256, M + [A("nw"), A("idn")], [6])
+        act(T.eb[:], T.p6[:, 128:256], AF.Copy, [], [A("eb")], [6], n=128, bias=BIG + (0.0 if keep else 2048.0))
+        act(T.mm[:, cls(ph, c)], T.p6[:, 256:384], AF.Abs, [], M, [6], n=128, bias=-1.0)
+        k0 = 128 if keep else 0
+        mms([(pu[:, 384:512], T.idn[:], T.c2k[:, k0:k0 + 128]), (pu[:, 384:512], T.hf[:, 128 * ph:128 * ph + 128], T.idh[:]),
+             (pu[:, 384:512], T.nw[:], T.big[:])], 384, [A("nw"), A("hf", 2 * ph, 2 * ph + 2), A("c2k"), A("idn"), A("idh"), A("big")], [2 + ph])
+        if keep:
+            tt(T.ef[:, cls(ph, c)], pu[:, 384:512], T.eb[:], OP.min, [A("eb")], [E], [2 + ph], n=128)
+        else:
+            tt(T.ylb[:, cls(ph, c)], pu[:, 384:512], T.eb[:], OP.min, [A("eb")], [A("yl%d%d" % (ph, c))], [2 + ph], n=128)
+
+    def arrive(s):
+        ph = s % 2
+        stage(s, "arrive")
+        win, WX = xw[ph][:, XC:XW], A("xw%d" % ph, XC, XW)
+        plain = s == ST - 1
+        if plain:
             for z in range(2):
-                ap, rg = T.xw[:, XC + 2048 * z:XC + 2048 * z + 2048], A("xw", XC + 2048 * z, XC + 2048 * z + 2048)
+                ap, rg = xw[ph][:, XC + 2048 * z:XC + 2048 * z + 2048], A("xw%d" % ph, XC + 2048 * z, XC + 2048 * z + 2048)
                 act(ap, ap, AF.Relu, [rg], [rg], n=2048)
-        lt = T["lt%d" % t]
-        L = A("lt%d" % t)
-        tt(T.av[:], win.indirect(lt[:]), T["lq%d" % t][:], OP.add, [WX, L, A("lq%d" % t)], [A("av")], cost=0.05 + 256 * GAT)
+        lt, L = T.lt[:, 16 * s:16 * s + 16], A("lt", s, s + 1)
+        tt(T.av[:], win.indirect(lt), T.lq[:, 256 * s:256 * s + 256], OP.add, [WX, L, A("lq", s, s + 1)], [A("av")], cost=0.05 + 256 * GAT)
         ts(T.aw[:], T.av[:], 0.5, OP.mult, [A("av")], [A("aw")], (), 1279.75, OP.add, n=128)
-        ts(T.ax[:], T.aw[:], -1280.0 - (0.0 if last else DEL), OP.add, [A("aw")], [A("ax")], n=128)
-        cp(win.indirect(lt[:]), T.ax[:], [A("ax"), L], [WX], cost=0.05 + 256 * SCA)
-    dma("y", T.ym[:], T.mm[:], MM4, [], 262144)
-    dma("y", T.yl[:], T.ylb[:], [A("yl%d" % c) for c in range(4)], [], 524288)
-    dma("y", T.yx[:, 0:2048], T.xw[:, XC:XC + 2048], [WX], [], 1048576)
-    dma("s", T.yx[:, 2048:4096], T.xw[:, XC + 2048:XC + 4096], [WX], [], 1048576)
+        ts(T.ax[:], T.aw[:], -1280.0 - (0.0 if plain else DEL), OP.add, [A("aw")], [A("ax")], n=128)
+        cp(win.indirect(lt), T.ax[:], [A("ax"), L], [WX], cost=0.05 + 256 * SCA)
+        if s >= ST - 2:
+            for b in range(2):
+                ap, rg = xw[ph][:, XC + 2048 * b:XC + 2048 * b + 2048], A("xw%d" % ph, XC + 2048 * b, XC + 2048 * b + 2048)
+                if not plain:
+                    ts(ap, ap, 0.0, OP.max, [rg], [rg], n=1024)
+                dma("ys"[b] if plain else "y", T.yx[64 * ph:64 * ph + 64, 2048 * b:2048 * b + 2048],
+                    xw[ph][64 * b:64 * b + 64, XC + 2048 * b:XC + 2048 * b + 2048], [rg], [], 3.5)
+
+    def lists_out(ph):
+        for b in range(2):
+            dma("y", T.ym[64 * ph:64 * ph + 64, 512 * b:512 * b + 512], T.mm[64 * b:64 * b + 64, 512 * ph:512 * ph + 512], MM(ph), [], 2.5)
+            dma("y", T.yl[64 * ph:64 * ph + 64, 512 * b:512 * b + 512], T.ylb[64 * b:64 * b + 64, 512 * ph:512 * ph + 512],
+                [A("yl%d%d" % (ph, c)) for c in range(4)], [], 2.5)
+
+    for ph in range(2):
+        stage(ph - 2, "prep")
+        early(ph, 0)
+        prep(ph)
+    for s in range(ST):
+        if s >= 2:
+            arrive(s - 2)
+        head(s)
+        mid(s)
+        tail(s)
+        if s % 2 and s + 2 < ST:
+            stage(s, "kappa")
+            kappa()
+            plus_kappa(0)
+        update(s)
+        stage(s, "prep")
+        if s + 2 < ST:
+            if s // 2 < 3:
+                early(s % 2, s // 2 + 1)
+            prep(s + 2)
+            if s % 2:
+                plus_kappa(1)
+        else:
+            lists_out(s % 2)
+    arrive(ST - 2)
+    arrive(ST - 1)
 
     n = len(nodes)
     before = [[] for _ in range(n)]
@@ -459,56 +617,10 @@ def rank_program(g, core, T, topo):
             before[i].append((j, lag))
             after[j].append((i, lag))
 
-    def arrange(pre, post, prio):
-        left = [len(x) for x in pre]
-        end = [0.0] * n
-        free = {q: 0.0 for q in eng}
-        ready = {q: [] for q in eng}
-        out, todo = [], [i for i in range(n) if not pre[i]]
-        first = True
-        while True:
-            while todo:
-                i = todo.pop()
-                rel = [i] if first and not pre[i] else []
-                if not rel:
-                    for j, _ in post[i]:
-                        left[j] -= 1
-                        if left[j] == 0:
-                            rel.append(j)
-                for j in rel:
-                    r = max([end[k] + lag for k, lag in pre[j]] + [0.0])
-                    if nodes[j]["q"] is None:
-                        end[j] = r
-                        out.append(j)
-                        todo.append(j)
-                    else:
-                        ready[nodes[j]["q"]].append((r, j))
-            first = False
-            best = None
-            for q in eng:
-                if ready[q]:
-                    s0 = min(max(free[q], r) for r, _ in ready[q])
-                    if best is None or s0 < best[0]:
-                        best = (s0, q)
-            if best is None:
-                return out, end
-            s0, q = best
-            pick = max((x for x in ready[q] if max(free[q], x[0]) <= s0 + 0.06), key=lambda x: (prio[x[1]], -x[1]))
-            ready[q].remove(pick)
-            i = pick[1]
-            free[q] = end[i] = max(free[q], pick[0]) + nodes[i]["cost"]
-            out.append(i)
-            todo.append(i)
-    prio = [0.0] * n
-    for i in range(n - 1, -1, -1):
-        prio[i] = nodes[i]["cost"] + max([prio[j] + lag for j, lag in after[i]] + [0.0])
-    best = None
-    for _ in range(PASSES):
-        out, end = arrange(before, after, prio)
-        if best is None or max(end) < best[0]:
-            best = (max(end), out, end)
-        _, prio = arrange(after, before, end)
-    orders, fin = best[1], best[2]
+    if "order" not in ORDER:
+        ORDER["order"] = arrange(nodes, before)
+        ORDER["x"] = (nodes, before, after, None)
+    orders, fin = ORDER["order"][1], ORDER["order"][2]
 
     cnt = {q: 0 for q in eng}
     known = {q: {} for q in eng}

@@ -6,131 +6,227 @@ OP = AluOpType
 AF = ActivationFunctionType
 RO = 5
 ST = 2 * RO
-XC = 16
-XD = 8192
+XC = 32
+XR = XC + 4096
+XD = 2 * XR - XC
 XW = XC + XD + 256
+QC = 0
 DEL = 2.0 ** -10
 BIG = 8192.0
-YS = ((2, 1), (2, 1))
-EVEN_V = (1, 1)
-D_V = (0, 0)
-CUT = 2816
+UK = True
+KD = "float32" if UK else "bfloat16"
+LOW = 32.625 if UK else 0.625
+YS = (1024, 384)
+DCUT = (0, 1024, 2048)
+EV = 256
+EARLY = (2, 3)
+LATE = ()
+ONV = "p"
+PARTS = ((("v", 1024),) * 4, ())
+LOADS = ((("y", "e", 0), ("s", "e", 1), ("y", "m", 0), ("s", "m", 1), ("y", "x", 0), ("s", "x", 1)),
+         (("y", "e", 0), ("y", "e", 1), ("y", "m", 0), ("y", "m", 1), ("g", "a", 0), ("g", "a", 1)))
+GATE = 1
+STORES = ("yyyyy", "yyyyy")
+DIS = {"y": 0.5, "s": 0.5, "g": 1.8}
+DROW = 0.2
+RELU = ("VVSS", "SSSS")
 
 SCRATCH = {"xw0": ("sbuf", [128, XW], "bfloat16"), "xw1": ("sbuf", [128, XW], "bfloat16"), "alt": ("sbuf", [128, 1024], "bfloat16")}
 for _n, _w, _d in (
-        ("ei0", 1024, "int32"), ("ef", 1024, "float16"), ("mm", 1024, "bfloat16"), ("ylb", 1024, "float32"),
-        ("d0", 4096, "bfloat16"), ("bb", 4096, "bfloat16"), ("qq0", 2048, "bfloat16"), ("qq1", 2048, "bfloat16"), ("dq", 4096, "bfloat16"),
+        ("ei0", 1024, "int32"), ("ef", 1024, "float16"), ("mm", 1024, "bfloat16"), ("sm", 1024, "bfloat16"), ("ylb", 1024, "float32"),
+        ("d0", 4096, "bfloat16"), ("bb", 4096, "bfloat16"), ("qq0", QC + 2048, "bfloat16"), ("qq1", QC + 2048, "bfloat16"), ("dq", 4096, "bfloat16"),
         ("sg", 4096, "bfloat16"), ("yb", 4096, "bfloat16"),
-        ("dl16", 256, "uint16"), ("el16", 256, "uint16"), ("h16", 256, "uint16"),
-        ("ui", 128, "int32"), ("ua", 128, "int32"), ("ta", 128, "int32"), ("tb", 128, "int32"), ("tc", 128, "int32"), ("hh", 128, "int32"),
-        ("hf", 256, "float16"), ("eb", 128, "float32"), ("av", 256, "float16"), ("aw", 256, "float16"), ("ax", 256, "bfloat16"),
-        ("qw", 128, "bfloat16"), ("qd", 256 * ST, "bfloat16"), ("lq", 256 * ST, "bfloat16"), ("tg", 16 * ST, "uint16"), ("lt", 16 * ST, "uint16"),
-        ("pi", 1, "int32"), ("ci", 8, "int32"), ("cf", 32, "float32"), ("m1", 160, "float32"), ("m64", 128, "float32"), ("si", 128, "float32"),
+        ("el16", 256 * ST, "uint16"), ("h16", 256, "uint16"),
+        ("ui", 256, "int32"), ("ua", 256, "int32"), ("ta", 256, "int32"), ("tb", 256, "int32"), ("tc", 256, "int32"), ("hh", 128 * ST, "int32"),
+        ("hf", 128 * ST, "float16"), ("eb", 256, "float32"), ("av", 256, "float16"), ("aw", 256, "float16"), ("ax", 256, "bfloat16"),
+        ("qw", 256, "bfloat16"), ("qd", 128 * ST, "bfloat16"), ("lq", 128 * ST, "bfloat16"), ("tg", 16 * ST, "uint16"), ("lt", 16 * ST, "uint16"),
+        ("pi", 1, "int32"), ("ci", 8, "int32"), ("cf", 32, "float32"), ("m1", 144, "float32"), ("m64", 128, "float32"), ("si", 128, "float32"),
         ("clf", 8, "float32"), ("cl", 8, "uint16"), ("icf", 16, "float32"), ("icn", 16, "bfloat16"), ("dum", 16, "int32"), ("mg", 128, "float32"),
-        ("zf", 8, "float32"), ("zc", 8, "bfloat16"), ("thr", 8, "float32"),
-        ("idn", 128, "bfloat16"), ("nid", 128, "bfloat16"), ("nk", 128, "bfloat16"), ("nk2", 128, "bfloat16"), ("n2", 128, "bfloat16"),
-        ("idh", 128, "float16"), ("big", 128, "bfloat16"), ("nbig", 128, "bfloat16"), ("i32", 128, "bfloat16"), ("dup", 128, "bfloat16"),
-        ("dup2", 256, "bfloat16"), ("nbl2", 256, "bfloat16"), ("am2", 256, "bfloat16"),
-        ("g8", 8, "bfloat16"), ("gw", 16, "bfloat16"), ("rcp", 8, "bfloat16"),
-        ("wu", 144, "bfloat16"), ("pm", 512, "float16"), ("nbl", 128, "bfloat16"), ("low", 128, "bfloat16"),
-        ("t1", 128, "bfloat16"), ("t2", 128, "bfloat16"), ("am", 128, "bfloat16"), ("one", 128, "bfloat16"), ("mr", 128, "bfloat16"),
-        ("ke", 128, "bfloat16"), ("z16", 16, "bfloat16"), ("c2k", 256, "bfloat16"), ("c75", 256, "bfloat16"),
-        ("cr", 128, "int32"), ("ge", 128, "bfloat16"), ("gsg", 128, "bfloat16"), ("kt", 128, "bfloat16"), ("sc", 128, "bfloat16"),
-        ("lm", 128, "bfloat16"), ("nw", 128, "bfloat16"), ("nf", 16, "bfloat16"), ("nfs", 64, "bfloat16"), ("kn", 8, "int32"), ("li", 8, "int32"),
-        ("l16", 8, "uint16"), ("uwi", 8, "int32"), ("uwa", 8, "int32"), ("uwb", 8, "bfloat16"), ("tgm", 16, "int32"),
-        ("kci", 1, "int32"), ("kcj", 1, "int32"), ("kap", 1, "float32")):
+        ("zc", 8, "bfloat16"), ("thr", 8, "float32"), ("i32", 128, "bfloat16"),
+        ("dup2", 256, "bfloat16"), ("nbl2", 256, "bfloat16"), ("am2", 256, "bfloat16"), ("rcp", 8, KD), ("wu", 144, "bfloat16"), ("uwi", 8, "int32"), ("kb", 128, "bfloat16"), ("nbl", 128, "bfloat16"),
+        ("low", 128, "bfloat16"), ("am", 128, "bfloat16"), ("mr", 128, "bfloat16"), ("z16", 16, "bfloat16"),
+        ("idn", 128, "bfloat16"), ("nid", 128, "bfloat16"), ("nk", 128, "bfloat16"),
+        ("idh", 128, "float16"), ("big", 128, "bfloat16"), ("nbig", 128, "bfloat16"), ("dup", 128, "bfloat16"),
+        ("g8", 8, "bfloat16"), ("gw", 24, "bfloat16"), ("cm", 128, "bfloat16"), ("cd", 128, "bfloat16"), ("id15", 128, "float16"), ("big15", 128, "bfloat16"), ("pm", 512, "float16"),
+        ("t1", 128, "bfloat16"), ("t2", 128, "bfloat16"), ("one", 128, "bfloat16"),
+        ("ke", 128, KD), ("c2k", 128, "bfloat16"),
+        ("ge", 256, "bfloat16"), ("gsg", 256, "bfloat16"), ("kt", 128 * ST, KD), ("sc", 128 * ST, KD),
+        ("nw", 128 * ST, "bfloat16"), ("nf", 16, "bfloat16"), ("kn", 8, "int32"), ("li", 8, "int32"), ("lm", 128, KD), ("nfs", 64, "bfloat16"),
+        ("ub", 256, "int32"), ("us", 256, "bfloat16"), ("l16", 8, "uint16"), ("uwa", 8, "int32"), ("uwb", 8, "bfloat16"), ("tgm", 16, "int32"),
+        ("kcj", 1, "bfloat16"), ("kap", 1, "float32")):
     SCRATCH[_n] = ("sbuf", [128, _w], _d)
-SCRATCH["hz"] = ("sbuf", [128, 34, 8], "float16")
+SCRATCH["hz"] = ("sbuf", [128, 68, 8], "float16")
 for _t in range(8):
     SCRATCH["p%d" % _t] = ("psum", [128, 512], "float32")
 SEMAPHORES = ["cv", "cs", "cp", "cg", "ls"] + ["aq%d" % _t for _t in range(ST)] + ["at%d" % _t for _t in range(ST)] \
-    + ["dm%d" % _t for _t in range(40)]
+    + ["dm%d" % _t for _t in range(48)]
 
 ORDER = {}
 SEED = 1
-MOVES = 38000
+TRIES = 2600
+SWAPS = 3000
+HEAT2 = 0.15
+SHIFT = 3.5
 HEAT = 0.2
-PER = 11.2
-START = {"pre": -30.0, "soon": -1.0, "e0": 0.0, "e1": 0.9, "d0": 0.1, "d1": 2.0, "g0": 1.8, "g1": 4.0, "hop0": 2.5, "hop1": 7.0, "hf": 9.0, "gate": 8.0, "y00": 5.3, "y01": 6.2,
-         "s00": 7.1, "s01": 7.6, "y10": 8.2, "y11": 8.9, "s10": 9.8, "s11": 10.3, "v0": 5.0, "v1": 9.5, "score": 8.0, "keys": 12.0, "nw": 16.0,
-         "tail1": 13.0, "tail2": 16.0, "kappa": 14.0, "update": 17.0, "prep": 17.5, "arrive": 19.0}
-LQ, LT = 2.6, 1.6
-PASSES = 60
-CYC = 0.00104
-PCY = 0.0008
-GAT = 0.00162
-SCA = 0.0039
+PER = 12.0
+START = {"pre": -30.0, "fill": -29.0, "soon": -1.0, "next": 3.0, "e0": 0.0, "e1": 0.9, "d0": 0.1, "d1": 1.5, "d2": 2.5, "d3": 3.0, "g0": 1.8, "g1": 3.0, "g2": 3.7,
+         "g3": 4.2, "hop0": 2.5, "hop1": 5.5, "hf": 9.0, "gate0": 4.0, "gate1": 7.5, "gsg": 8.0, "y00": 5.3, "y01": 6.2, "s00": 7.1, "s01": 7.6, "y10": 8.2, "y11": 8.9, "s10": 9.3, "s11": 9.8, "v0": 5.0, "v1": 9.0, "score": 8.0,
+         "keys": 11.0, "nw": 15.0, "tail1": 11.5, "tail2": 14.0, "kappa": 12.5, "update": 16.0, "late": 17.0, "prep": 16.5, "arrive": 18.0}
+FIRST = ()
+MACHINES = ((0.9, 0.75, 0.7, 0.8, 1.0, 0.0, 0.9), (1.2, 1.45, 1.9, 1.0, 1.0, 0.0, 1.2))
+LAND = (2.0, 1.5)
+WAKE = (0.15, 0.04)
+MORE = {"p": 0.05, "s": 0.06}
+CALL = 0.85
+FIX = 0.03
+C0 = 26
+CYC = 0.00097
+PCY = 0.0004
+PFX = 0.015
+SX = 0.09
+OUTL = (10, 5, 6)
+GAT = 0.0016
+SCA = 0.003
+DLAT = 1.5
+DBW = 0.33e6
 
 
 def arrange(nodes, before):
     n = len(nodes)
+    qs = [d["q"] for d in nodes]
     cost = [d["cost"] for d in nodes]
     late = [d["late"] for d in nodes]
-    qs = [d["q"] for d in nodes]
-    deps = [set(j for j, _ in b) for b in before]
-    cnt, kind, base, off = {}, [], [], {}
+    pre = [list(b) for b in before]
+    last, cnt, kinds, key = {}, {}, {}, []
     for i, d in enumerate(nodes):
         s, name = d["tag"]
         cnt[(s, name, d["q"])] = c = cnt.get((s, name, d["q"]), 0) + 1
-        if name in ("pre", "soon"):
-            kind.append(i)
-            base.append(0.0)
-            off[i] = START[name] + 0.1 * c - (100.0 - 0.1 * i if d["kind"] == "d" else 0.0)
+        if d["kind"] == "d" and s < 0:
+            if d["q"] in last:
+                pre[i].append((last[d["q"]], 0.0))
+            last[d["q"]] = i
+        if name in ("pre", "fill", "soon", "next"):
+            key.append(START[name] + 0.1 * c)
         else:
-            kind.append((s % 2, name, d["q"], c))
-            base.append((s // 2) * 2 * PER)
-            off[kind[i]] = (s % 2) * PER + START[name] + 0.1 * c
-    free_kinds = [k for k in off if not (isinstance(k, int) and nodes[k]["kind"] == "d")]
+            key.append(s * PER + START[name] + 0.1 * c)
+        if name not in ("pre", "soon"):
+            kinds.setdefault((name, d["q"], c), []).append(i)
+            kinds.setdefault(name, []).append(i)
+    for a, b in FIRST:
+        for i, j in zip(kinds[a], kinds[b]):
+            pre[j].append((i, 0.0))
+    alike = [(i,) for i in range(n)]
+    for k, v in kinds.items():
+        if k not in START and k[0] != "next":
+            for i in v:
+                alike[i] = [j for j in v if (nodes[j]["tag"][0] - nodes[i]["tag"][0]) % 2 == 0]
+    kinds = list(kinds.values())
+    suc = [[] for _ in range(n)]
+    for i in range(n):
+        for j, lag in pre[i]:
+            suc[j].append((i, lag))
 
-    def times(off):
-        at = [0.0] * n
-        for i in range(n):
-            x = base[i] + off[kind[i]]
-            for j in deps[i]:
+    def feasible(at, edges, run):
+        for i in run:
+            x = at[i]
+            for j, _ in edges[i]:
                 if at[j] >= x:
-                    x = at[j] + 1e-6
+                    x = at[j] + 1e-7
             at[i] = x
-        out = sorted(range(n), key=lambda i: at[i])
-        end, why, last = [0.0] * n, [-1] * n, {}
-        for i in out:
-            s, w = 0.0, -1
-            for j, lag in before[i]:
-                if end[j] + lag > s:
-                    s, w = end[j] + lag, j
-            q = qs[i]
-            if q is not None:
-                j = last.get(q, -1)
-                if j >= 0 and end[j] >= s:
-                    s, w = end[j], j
-                last[q] = i
-            end[i] = s + cost[i]
-            why[i] = w
-        top = max(range(n), key=lambda i: end[i] + late[i])
-        return end[top] + late[top], out, end, why, top, at
+        return sorted(range(n), key=lambda i: at[i])
+
+    def place(order, edges, head):
+        end = [0.0] * n
+        busy = {q: ([], []) for q in qs}
+        for i in order:
+            r = head[i]
+            for j, lag in edges[i]:
+                e = end[j] + lag
+                if e > r:
+                    r = e
+            c = cost[i]
+            if qs[i] is not None:
+                a, b = busy[qs[i]]
+                k = m = len(a)
+                while k and b[k - 1] > r:
+                    k -= 1
+                while k < m and r + c > a[k] + 1e-9:
+                    r = b[k]
+                    k += 1
+                a.insert(k, r)
+                b.insert(k, r + c)
+            end[i] = r + c
+        return end
     seed = [SEED]
 
     def rnd():
         seed[0] = (seed[0] * 1103515245 + 12345) % 2147483648
         return seed[0] / 2147483648
-    cur = best = times(off)
-    for it in range(MOVES):
-        _, _, _, why, i, at = cur
+    up, down, zero = range(n), range(n - 1, -1, -1), [0.0] * n
+    ends = [i for i in up if not suc[i]]
+    sets = []
+    for fc, fg, fs, fp, fw, more, whole in MACHINES:
+        f = {"p": fp, "v": fc, "s": fc, "gather": fg, "scatter": fs}
+        sets.append(([c * (f.get(d["by"], 1.0) if d["kind"] == "c" else 1.0) for c, d in zip(cost, nodes)],
+                     [[(j, late[j] + (more if nodes[j]["kind"] == "a" else 0.0) + fw * (lag - late[j]) if lag else 0.0) for j, lag in b] for b in pre], whole))
+
+    def replay(order, cost, pre):
+        end, why, last = [0.0] * n, [-1] * n, {}
+        for i in order:
+            r, w = 0.0, -1
+            for j, lag in pre[i]:
+                e = end[j] + lag
+                if e > r:
+                    r = e
+                    w = j
+            q = qs[i]
+            if q is not None:
+                j = last.get(q, -1)
+                if j >= 0 and end[j] >= r:
+                    r = end[j]
+                    w = j
+                last[q] = i
+            end[i] = r + cost[i]
+            why[i] = w
+        top = max(ends, key=lambda i: end[i] + late[i])
+        return end[top] + late[top], end, why, top
+
+    def judge(order):
+        r = [replay(order, c, p) for c, p, _ in sets]
+        return sum(x[0] / s[2] for x, s in zip(r, sets)) / len(sets), order, r[0][1], r
+    best = cur = None
+    for it in range(TRIES):
+        end = place(feasible(key, pre, up), pre, zero)
+        total = judge(feasible([e - c for e, c in zip(end, cost)], pre, up))[0]
+        if cur is None or total - cur[0] < -math.log(1e-9 + rnd()) * HEAT * (1.0 - it / TRIES):
+            cur = (total, end, place(feasible([-e for e in end], suc, down), suc, late))
+            if best is None or total < best[0]:
+                best = cur
+        key = [-x for x in cur[2]] if rnd() < 0.8 else [e - c for e, c in zip(cur[1], cost)]
+        for _ in range(1 + int(rnd() * 3)):
+            x = SHIFT * (2.0 * rnd() - 1.0)
+            for i in kinds[int(rnd() * len(kinds))]:
+                key[i] += x
+    waits = [set(j for j, _ in b) for b in pre]
+    key = [e - c for e, c in zip(best[1], cost)]
+    best = cur = judge(feasible(key, pre, up))
+    for it in range(SWAPS):
+        _, _, why, i = cur[3][int(rnd() * len(sets))]
         pairs = []
         while i >= 0:
             j = why[i]
-            if j >= 0 and j not in deps[i] and nodes[i]["kind"] != "d" and nodes[j]["kind"] != "d":
+            if j >= 0 and j not in waits[i]:
                 pairs.append((j, i))
             i = j
-        new = dict(off)
-        if pairs and rnd() < 0.8:
-            j, i = pairs[int(rnd() * len(pairs))]
-            k, sign = (i, -1.0) if rnd() < 0.5 else (j, 1.0)
-            new[kind[k]] = at[k] - base[k] + sign * (at[i] - at[j] + (1e-4, 1e-4, 0.3, 1.0)[int(rnd() * 4)] * rnd())
-        else:
-            new[free_kinds[int(rnd() * len(free_kinds))]] += 2.4 * (rnd() - 0.5)
-        r = times(new)
-        if r[0] - cur[0] < -math.log(1e-9 + rnd()) * (HEAT * (1.0 - it / MOVES) + 0.005):
-            cur, off = r, new
+        j, i = pairs[int(rnd() * len(pairs))]
+        x = key[i] - key[j] + (1e-4, 1e-4, 0.3, 1.0)[int(rnd() * 4)] * rnd()
+        k, x = (i, -x) if rnd() < 0.5 else (j, x)
+        new = list(key)
+        for z in alike[k] if rnd() < 0.8 else (k,):
+            new[z] += x
+        r = judge(feasible(new, pre, up))
+        if r[0] - cur[0] < -math.log(1e-9 + rnd()) * (HEAT2 * (1.0 - it / SWAPS) + 0.003):
+            cur, key = r, new
             if r[0] < best[0]:
                 best = r
     return best[:3]
@@ -166,6 +262,10 @@ def rank_program(g, core, T, topo):
                 if l < hi and lo < h:
                     d.add(i)
         me = len(nodes)
+        by = q
+        if isinstance(cost, tuple):
+            by, n = cost
+            cost = (0.05 if q == "v" else 0.065 + SX) + n * (GAT if by == "gather" else SCA)
         order = set()
         for b in B:
             prev, cur = bank.get(b, ([], []))
@@ -175,7 +275,7 @@ def rank_program(g, core, T, topo):
             if cur and q == "p":
                 order.add(cur[-1])
             bank[b] = (prev, cur + [me])
-        nodes.append({"q": q, "calls": calls, "cost": cost, "deps": d, "order": order - d, "kind": kind, "key": key, "late": late, "tag": tag[0]})
+        nodes.append({"q": q, "calls": calls, "cost": cost, "deps": d, "order": order - d, "kind": kind, "key": key, "late": late, "tag": tag[0], "by": by})
         for (b, lo, hi) in W:
             wr[b] = [e for e in wr.get(b, ()) if not (lo <= e[0] and e[1] <= hi)] + [(lo, hi, me)]
             rd[b] = [e for e in rd.get(b, ()) if not (lo <= e[0] and e[1] <= hi)]
@@ -186,20 +286,20 @@ def rank_program(g, core, T, topo):
     def dma(q, out, in_, R, W, late, extra=(), **kw):
         name = "dm%d" % ndma[0]
         ndma[0] += 1
-        return node(q, [lambda e: e.dma_start(out, in_, **kw)], 0.6 if q == "g" else 0.1, R, W, (), "d", name, late, extra)
+        return node(q, [lambda e: e.dma_start(out, in_, **kw)], DIS[q], R, W, (), "d", name, late, extra)
 
     def A(b, lo=0, hi=1 << 20):
         return (b, lo, hi)
 
     def cy(n):
-        return max(64, n) * CYC
+        return max(64, n + C0) * CYC + FIX
 
     def mms(lst, n, R, B):
         last = len(lst) - 1
-        node("p", [lambda e, a=a, j=j: e.matmul(a[0], a[1], a[2], j == 0, j == last) for j, a in enumerate(lst)], n * PCY, R, [], B)
+        node("p", [lambda e, a=a, j=j: e.matmul(a[0], a[1], a[2], j == 0, j == last) for j, a in enumerate(lst)], n * PCY + len(lst) * PFX, R, [], B)
 
     def mmx(lst, n, R, B):
-        node("p", [lambda e, a=a: e.matmul(*a) for a in lst], n * PCY, R, [], B)
+        node("p", [lambda e, a=a: e.matmul(*a) for a in lst], n * PCY + len(lst) * PFX, R, [], B)
 
     def ts(out, in0, s1, o1, R, W, B=(), s2=None, o2=None, n=64, cost=None):
         if o2 is None:
@@ -217,7 +317,7 @@ def rank_program(g, core, T, topo):
         node("v", [lambda e: e.tensor_tensor_scan(out, a, b, init, o1, o2)], cy(n), R, W)
 
     def act(out, in_, f, R, W, B=(), n=64, cost=None, **kw):
-        node("s", [lambda e: e.activation(out, in_, f, **kw)], cost or cy(n), R, W, B)
+        node("s", [lambda e: e.activation(out, in_, f, **kw)], cost or cy(n) + SX, R, W, B)
 
     def fill(ap, c, W, n=64):
         node("v", [lambda e: e.memset(ap, c)], cy(n), [], W)
@@ -230,46 +330,64 @@ def rank_program(g, core, T, topo):
 
     xw = (T.xw0, T.xw1)
 
-    def MM(ph, c=None):
-        return [A("mm%d%d" % (ph, k)) for k in range(4) if c in (None, k)]
-
-    def lists_in(ph, late):
-        out = []
-        for b in range(2):
-            q = "ys"[b]
-            out.append(dma(q, T.ei0[64 * b:64 * b + 64, 512 * ph:512 * ph + 512], T.led[64 * ph:64 * ph + 64, 512 * b:512 * b + 512], [],
-                           [A("ei0%d" % ph, b, b + 1)], late))
-            out.append(dma(q, T.mm[64 * b:64 * b + 64, 512 * ph:512 * ph + 512], T.mk[64 * ph:64 * ph + 64, 512 * b:512 * b + 512], [],
-                           [A(n, b, b + 1) for n, _, _ in MM(ph)], late))
-        return out
-    lists_in(0, 2.6)
-    parts = ((0, CUT // 2, "v", 3.8), (CUT, 4096, "s", 4.8), (CUT // 2, CUT, "v", 5.9))
-    loads = []
-    for z, (lo, hi, q, late) in enumerate(parts):
-        for b in range(2):
-            loads.append(dma("ys"[b], T.xw0[64 * b:64 * b + 64, XC + lo:XC + hi], T.xt[0:64, lo:hi], [], [A("in0", 2 * z + b, 2 * z + b + 1)], late))
-    fill(T.alt[:, 0::2], 4096.0, [A("alt", 0, 1)], 256)
-    fill(T.alt[:, 1::2], DEL, [A("alt", 1, 2)], 256)
-    for z in range(4):
-        act(T.xw1[:, XC + 1024 * z:XC + 1024 * z + 1024], T.alt[:], AF.Copy, [A("alt")], [A("in1", z, z + 1)], n=1024, scale=0.0, bias=-DEL)
-    later = lists_in(1, 7.0)
-    for b in range(2):
-        later.append(dma("g", T.xw1[64 * b:64 * b + 64, XC:XC + 4096], T.xt[64:128, :], [A("in1")], [A("xw1", XC + 2048 * b, XC + 2048 * b + 2048)],
-                         4.5 + 3.5 * b, loads, accum_op=OP.add, max_dma_last_dim=4096))
-    for ph in range(2):
-        dma("y", xw[ph][:, XC + 4096:XC + XD], T.xt[:], [], [A("xw%d" % ph, XC + 4096, XC + XD)], 5.0 + 3.5 * ph, later)
-        fill(xw[ph][:, XC + XD:XW], 0.0, [A("xw%d" % ph, XC + XD, XW)], 128)
-        fill(xw[ph][:, 0:16], 0.0, [A("xw%d" % ph, 0, 16)])
-        fill(xw[ph][:, 1:2], 4096.0, [A("xw%d" % ph, 0, 16)])
+    def MM(ph, c=None, name="mm"):
+        return [A("%s%d%d" % (name, ph, k)) for k in range(4) if c in (None, k)]
 
     iota(T.pi[:], [[0, 1]], 0, 1, [A("pi")], 1, False)
-    iota(T.m1[:], [[1, 160]], 1, 0, [A("m1")], 160)
+    iota(T.m1[:], [[1, 144]], 1, 0, [A("m1")], 144)
+    fill(T.alt[:, 0::2], 4096.0, [A("alt", 0, 1)], 256)
+    fill(T.alt[:, 1::2], DEL, [A("alt", 1, 2)], 256)
+    stage(-1, "fill")
+    for lo in range(XC, XR, 1024):
+        act(T.xw1[:, lo:lo + 1024], T.alt[:], AF.Copy, [A("alt")], [A("in1", lo, lo + 1024)], n=1024, scale=0.0, bias=-DEL)
+    stage(-1, "pre")
+    gate, issued, landed = (), {"y": 0.0, "s": 0.0, "g": 0.0}, 0.0
+    for ph in range(2):
+        done, when = [], []
+        for q, what, b in LOADS[ph]:
+            rows, o, i = slice(64 * b, 64 * b + 64), slice(512 * ph, 512 * ph + 512), (slice(64 * ph, 64 * ph + 64), slice(512 * b, 512 * b + 512))
+            if what == "a":
+                issued[q] += DIS[q]
+                landed = max(landed, issued[q] + DLAT) + 1048576 / DBW + DROW
+                added = dma(q, T.xw1[rows, XC:XR], T.xt[i[0], :], [A("in1")], [A("xw1", XC + 2048 * b, XC + 2048 * b + 2048)], landed - issued[q], gate,
+                            accum_op=OP.add, max_dma_last_dim=4096)
+                continue
+            out, in_, W, size = {
+                "x": (xw[ph][rows, XR + XC:XR + XC + 4096], T.xt[i[0], :], [A("xw%d" % ph, XR + XC + 2048 * b, XR + XC + 2048 * b + 2048)], 524288),
+                "e": (T.ei0[rows, o], T.led[i], [A("ei0%d" % ph, b, b + 1)], 131072),
+                "m": (T.mm[rows, o], T.mk[i], [A(n, b, b + 1) for n, _, _ in MM(ph)], 65536)}[what]
+            issued[q] += DIS[q]
+            landed = max(landed, issued[q] + DLAT) + size / DBW + DROW
+            done.append(dma(q, out, in_, [], W, landed - issued[q], gate))
+            when.append(landed)
+        gate = done[GATE:GATE + 1]
+        issued["y"] = issued["g"] = max(issued["y"], when[GATE])
+    dma("y", T.xw1[:, XR + XC:2 * XR], T.xt[:], [], [A("xw1", XR + XC, 2 * XR)], DLAT + 1048576 / DBW + DROW, (added,))
+
+    def convert(ph, first):
+        o = slice(512 * ph + first, 512 * ph + 512, 4)
+        ts(T.ef[:, o], T.ei0[:, o], -2048.0, OP.add, [A("ei0%d" % ph)], MM(ph, first, "ef"), n=128)
+        if first == 0:
+            o = slice(512 * ph, 512 * ph + 512)
+            ts(T.sm[:, o], T.mm[:, o], -2.0, OP.mult, MM(ph), MM(ph, None, "sm"), (), 1.0, OP.add, n=256)
+            lo = XC
+            for q, w in PARTS[ph]:
+                rg, R = A("xw%d" % ph, lo, lo + w), A("xw%d" % ph, XR + XC, XR + XC + 4096)
+                if q == "v":
+                    ts(xw[ph][:, lo:lo + w], xw[ph][:, XR + lo:XR + lo + w], -DEL, OP.add, [R], [rg], n=w // 2)
+                else:
+                    act(xw[ph][:, lo:lo + w], xw[ph][:, XR + lo:XR + lo + w], AF.Copy, [R], [rg], n=w, bias=-DEL)
+                lo += w
+    for ph in range(2):
+        for lo in (XR, 0):
+            iota(xw[ph][:, lo:lo + XC], [[4096, 2], [0, 16]], 0, 0, [A("xw%d" % ph, lo, lo + XC)], XC)
+
     iota(T.m64[:], [[0, 2], [1, 64]], 0, 0, [A("m64")], 128)
     iota(T.clf[:], [[16, 8]], 15, 0, [A("clf")], 8)
     iota(T.mg[:], [[0, 2], [16, 4], [0, 16]], 0, 0, [A("mg")], 128)
     iota(T.si[:], [[0, 8], [1, 16]], 0, 0, [A("si")], 128)
     iota(T.icf[:], [[16, 16]], 0, 1, [A("icf")], 16)
-    iota(T.zf[:], [[256, 8]], 256, 0, [A("zf")], 8)
+    iota(T.zc[:], [[8192 if UK else 256, 8]], 8192 if UK else 256, 0, [A("zc")], 8)
 
     def ci(j):
         return T.ci[:, j:j + 1]
@@ -295,187 +413,197 @@ def rank_program(g, core, T, topo):
             ts(cf(11 + j), cf(9), float(8 * b + 1), OP.add, [rc(9), rc(7), rc(1)], [rc(11 + j)], (), cf(1 if par else 7), OP.mult)
             ts(T.pm[:, 128 * j:128 * j + 128], T.m1[:, 0:128], cf(11 + j), OP.is_equal, [A("m1"), rc(11 + j)], [("pm", j, j + 1)], n=128)
     ts(cf(19), cf(0), 14.5, OP.is_lt, [rc(0)], [rc(19)])
-    ts(cf(20), cf(19), 2048.0 + XC - BIG - 1.0, OP.mult, [rc(19)], [rc(20)], (), 1.0, OP.add)
+    ts(cf(20), cf(19), 2048.0 + XC - 16.0 - BIG, OP.mult, [rc(19)], [rc(20)], (), 16.0 - 2048.0 - XC, OP.add)
     ts(cf(26), cf(5), 1.0, OP.add, [rc(5)], [rc(26)])
     ts(T.idn[:], T.m1[:, 0:128], cf(26), OP.is_equal, [A("m1"), rc(26)], [A("idn")], n=128)
     cp(T.idh[:], T.idn[:], [A("idn")], [A("idh")])
-    ts(T.big[:], T.idn[:], BIG, OP.mult, [A("idn")], [A("big")])
-    fill(T.c2k[:, 0:128], 2048.0, [A("c2k", 0, 1)])
-    for z, (lo, hi, q, late) in enumerate(parts):
-        ap, rg = T.xw0[:, XC + lo:XC + hi], A("xw0", XC + lo, XC + hi)
-        if q == "v":
-            ts(ap, ap, -DEL, OP.add, [A("in0", 2 * z, 2 * z + 2)], [rg], n=(hi - lo) // 2)
-        else:
-            act(ap, ap, AF.Copy, [A("in0", 2 * z, 2 * z + 2)], [rg], n=hi - lo, bias=-DEL)
+    ts(T.id15[:], T.idn[:], cf(19), OP.mult, [A("idn"), rc(19)], [A("id15")])
+    ts(T.big15[:], T.idn[:], cf(19), OP.mult, [A("idn"), rc(19)], [A("big15")], (), BIG, OP.mult)
+    ts(T.cd[:], T.idn[:], 0.0, OP.mult, [A("idn"), rc(20)], [A("cd")], (), cf(20), OP.add)
+    convert(0, 0)
     stage(-1, "soon")
-    fill(T.one[:], 1.0, [A("one")])
-    fill(T.hz[:], 0.0, [A("hz")], 136)
-    fill(T.c75[:, 0:128], 7.5 * DEL, [A("c75", 0, 1)])
-    fill(T.c75[:, 128:256], 0.0, [A("c75", 1, 2)])
+    for name, v, n in (("c2k", 2048, 128), ("one", 1, 128), ("cm", 3 << 22, 128), ("ke", 16384, 128), ("z16", 0, 16), ("nf", 0, 16), ("nfs", 0, 64)):
+        iota(T[name][:], [[0, n]], v, 0, [A(name)], n)
+    for ph in range(2):
+        iota(xw[ph][:, XC + XD:XW], [[0, 256]], 0, 0, [A("xw%d" % ph, XC + XD, XW)], 256)
+
+    def times(out, in_, W, R, **kw):
+        act(out, in_, AF.Identity, R, W, n=128, **kw)
+    fill(T.hz[:], 0.0, [A("hz")], 272)
     ts(cf(21), cf(0), 2.0, OP.mult, [rc(0)], [rc(21)], (), 1.0, OP.add)
-    ts(cf(22), cf(6), 16.0, OP.add, [rc(6)], [rc(22)])
-    ts(cf(23), cf(0), -1.0, OP.mult, [rc(0)], [rc(23)])
-    ts(cf(24), cf(0), 2.0, OP.mult, [rc(0)], [rc(24)])
+    if UK:
+        ts(cf(23), cf(0), -32.0, OP.mult, [rc(0)], [rc(23)], (), 32.0, OP.add)
+    else:
+        ts(cf(23), cf(0), -1.0, OP.mult, [rc(0)], [rc(23)])
+        ts(cf(22), cf(6), 16.0, OP.add, [rc(6)], [rc(22)])
+        ts(T.wu[:], T.m1[:], cf(22), OP.is_equal, [A("m1"), rc(22), rc(21)], [A("wu")], (), cf(21), OP.mult, n=144)
     ts(cf(25), cf(6), 0.0625, OP.mult, [rc(6)], [rc(25)], (), 1.0, OP.add)
-    ts(cf(27), cf(0), 16.0, OP.mult, [rc(0)], [rc(27)])
-    ts(T.wu[:], T.m1[:, 0:144], cf(22), OP.is_equal, [A("m1"), rc(22), rc(21)], [A("wu")], (), cf(21), OP.mult, n=144)
-    for name, f in (("n2", -2.0), ("nid", -1.0), ("nbig", -BIG), ("i32", 32.0)):
-        ts(T[name][:], T.idn[:], f, OP.mult, [A("idn")], [A(name)])
-    ts(T.nk[:], T.idn[:], cf(23), OP.mult, [A("idn"), rc(23)], [A("nk")])
-    ts(T.nk2[:], T.idn[:], cf(24), OP.mult, [A("idn"), rc(24)], [A("nk2")])
-    ts(T.g8[:], T.m1[:, 0:8], cf(25), OP.is_equal, [A("m1"), rc(25)], [A("g8")], (), 16.0, OP.mult)
-    ts(T.gw[:, 0:8], T.m1[:, 0:8], cf(25), OP.is_equal, [A("m1"), rc(25)], [A("gw", 0, 1)])
-    ts(T.gw[:, 8:16], T.m1[:, 0:8], cf(25), OP.is_equal, [A("m1"), rc(25), rc(21)], [A("gw", 1, 2)], (), cf(21), OP.mult)
+    ts(cf(27), cf(0), 16.0, OP.mult, [rc(0)], [rc(27)], (), float(QC), OP.add)
     ts(T.rcp[:], T.m1[:, 0:8], cf(25), OP.is_equal, [A("m1"), rc(25)], [A("rcp")], (), -1.0, OP.mult)
+    for name, f in (("nid", -1.0), ("big", BIG), ("nbig", -BIG), ("i32", 32.0)):
+        times(T[name][:], T.idn[:], [A(name)], [A("idn")], scale=f)
+    times(T.nk[:], T.idn[:], [A("nk")], [A("idn"), rc(23)], scale=cf(23))
+    ts(T.g8[:], T.m1[:, 0:8], cf(25), OP.is_equal, [A("m1"), rc(25)], [A("g8")], (), 512.0 if UK else 16.0, OP.mult)
+    ts(T.gw[:, 0:8], T.m1[:, 0:8], cf(25), OP.is_equal, [A("m1"), rc(25), rc(21)], [A("gw", 0, 1)], (), cf(21), OP.mult)
+    ts(T.gw[:, 8:16], T.m1[:, 0:8], cf(25), OP.is_equal, [A("m1"), rc(25)], [A("gw", 1, 2)])
+    ts(T.gw[:, 16:24], T.m1[:, 0:8], cf(25), OP.is_equal, [A("m1"), rc(25)], [A("gw", 2, 3)], (), -1.0, OP.mult)
     ts(T.dup[:], T.m64[:], cf(3), OP.is_equal, [A("m64"), rc(3)], [A("dup")], n=128)
     ts(T.nbl[:], T.mg[:], cf(4), OP.is_equal, [A("mg"), rc(4)], [A("nbl")], (), -32.0, OP.mult, n=128)
     ts(T.low[:], T.m64[:], cf(3), OP.is_gt, [A("m64"), rc(3)], [A("low")], n=128)
     tt(T.t1[:], T.nbl[:], T.low[:], OP.mult, [A("nbl"), A("low")], [A("t1")], n=256)
-    ts(T.t2[:], T.dup[:], 2.0 * BIG, OP.mult, [A("dup")], [A("t2")])
+    times(T.t2[:], T.dup[:], [A("t2")], [A("dup")], scale=2.0 * BIG)
     tt(T.am[:], T.t2[:], T.t1[:], OP.add, [A("t2"), A("t1")], [A("am")], n=256)
     ts(cf(28), cf(5), 63.5, OP.is_lt, [rc(5)], [rc(28)])
     ts(cf(29), cf(5), 63.5, OP.is_gt, [rc(5)], [rc(29)])
     for name in ("dup", "nbl", "am"):
         for b in range(2):
-            ts(T[name + "2"][:, 128 * b:128 * b + 128], T[name][:], cf(28 + b), OP.mult, [A(name), rc(28 + b)], [A(name + "2", b, b + 1)])
+            times(T[name + "2"][:, 128 * b:128 * b + 128], T[name][:], [A(name + "2", b, b + 1)], [A(name), rc(28 + b)], scale=cf(28 + b))
     ts(T.icn[:], T.icf[:], cf(6), OP.subtract, [A("icf"), rc(6)], [A("icn")])
     ts(T.dum[:], T.icf[:], cf(6), OP.subtract, [A("icf"), rc(6)], [A("dum")], (), float(XD), OP.add)
-    cp(T.zc[:], T.zf[:], [A("zf")], [A("zc")])
-    ts(T.thr[:], T.zf[:], -0.8, OP.add, [A("zf")], [A("thr")])
+    act(T.thr[:], T.zc[:], AF.Copy, [A("zc")], [A("thr")], bias=-LOW - 0.175)
     ts(T.mr[:], T.si[:], cf(0), OP.is_equal, [A("si"), rc(0)], [A("mr")], n=128)
     cp(T.cl[:], T.clf[:], [A("clf")], [A("cl")])
-    fill(T.ke[:], 512.0, [A("ke")])
-    fill(T.ke[:, 0::16], 0.625, [A("ke")])
-    fill(T.z16[:], 0.0, [A("z16")])
-    fill(T.nf[:], 0.0, [A("nf")])
-    fill(T.nfs[:], 0.0, [A("nfs")])
-    fill(T.c2k[:, 128:256], 0.0, [A("c2k", 1, 2)])
+    fill(T.ke[:, 0::16], LOW, [A("ke")])
+    stage(-1, "next")
+    convert(1, 0)
+    for c in range(1, 4):
+        convert(0, c)
+        convert(1, c)
 
     def cls(ph, c, first=0, step=4):
         return slice(512 * ph + c + first, 512 * ph + 512, step)
 
-    def EF(ph, c):
-        return A("ef%d%d" % (ph, c))
+    def banks(ph):
+        return T["p%d" % ph], T["p%d" % (2 + ph)], T["p%d" % (4 + 2 * ph)], T["p%d" % (5 + 2 * ph)]
 
-    def early(ph, c):
-        ts(T.ef[:, cls(ph, c)], T.ei0[:, cls(ph, c)], -2048.0, OP.add, [A("ei0%d" % ph)], [EF(ph, c)], n=128)
-
-    def prep(s):
+    def lists(s, B):
         ph, c = s % 2, (s // 2) % 4
-        E, M = EF(ph, c), MM(ph, c)
-        o = slice(128 * ph, 128 * ph + 128)
-        mms([(T.p7[:, 128:256], T.idn[:], T.c2k[:, 0:128])]
-            + [(T.p7[:, 128 + 64 * par:192 + 64 * par], T.pm[:, 256 * par + 128 * b:256 * par + 128 * b + 128], T.ef[:, cls(ph, c, 4 * b, 8)])
-               for par in range(2) for b in range(2)], 384, [A("pm"), E, A("idn"), A("c2k", 0, 1)], [7])
-        mms([(T.p7[:, 256:384], T.idh[:], T.ef[:, cls(ph, c)]), (T.p7[:, 256:384], T.big[:], T.mm[:, cls(ph, c)])], 256,
-            [E, A("idh"), A("big")] + M, [7])
-        ts(T.dl16[:, o], T.p7[:, 256:384], cf(19), OP.mult, [rc(19), rc(20)], [A("dl16", ph, ph + 1)], [7], cf(20), OP.add, n=128)
-        ts(T.el16[:, o], T.p7[:, 128:256], float(XC), OP.add, [], [A("el16", ph, ph + 1)], [7], n=128)
-        pe = T["p%d" % ph]
-        mms([(pe[:, 0:128], T.idn[:], T.c2k[:, 0:128]), (pe[:, 0:128], T.ef[:, cls(ph, c)], T.idh[:])], 256, [E, A("idn"), A("idh"), A("c2k", 0, 1)], [ph])
-        mms([(pe[:, 256:384], T.one[:], T.idn[:]), (pe[:, 256:384], T.mm[:, cls(ph, c)], T.n2[:])], 256, M + [A("one"), A("idn"), A("n2")], [ph])
+        E, M = MM(ph, c, "ef"), MM(ph, c)
+        pu = T["p%d" % B]
+        mms([(pu[:, 0:128], T.idn[:], T.cd[:]), (pu[:, 0:128], T.id15[:], T.ef[:, cls(ph, c)]), (pu[:, 0:128], T.big15[:], T.mm[:, cls(ph, c)])]
+            + [(pu[:, 128 + 64 * par:192 + 64 * par], T.pm[:, 256 * par + 128 * b:256 * par + 128 * b + 128], T.ef[:, cls(ph, c, 4 * b, 8)])
+               for par in range(2) for b in range(2)], 640, E + M + [A("idn"), A("cd"), A("id15"), A("big15"), A("pm")], [B])
+        ts(T.el16[:, 256 * s:256 * s + 256], pu[:, 0:256], 2048.0 + XC, OP.add, [], [A("el16", s, s + 1)], [B], n=256)
+
+    def turned(s):
+        ph, c = s % 2, (s // 2) % 4
+        E, pe = MM(ph, c, "ef"), banks(ph)[0]
+        mms([(pe[:, 0:128], T.idn[:], T.c2k[:]), (pe[:, 0:128], T.ef[:, cls(ph, c)], T.idh[:]), (pe[:, 256:384], T.sm[:, cls(ph, c)], T.idn[:])],
+            384, E + MM(ph, c, "sm") + [A("idn"), A("idh"), A("c2k")], [ph])
 
     def head(s):
         ph = s % 2
         all_x, RX = xw[ph][:, 0:XC + 4096], A("xw%d" % ph, 0, XC + 4096)
-        qq, EL = T["qq%d" % ph], A("el16", ph, ph + 1)
-        for h in range(2):
-            z = 2 * ph + h
-            o = slice(1024 * z, 1024 * z + 1024)
-            stage(s, "d%d" % h)
-            src = all_x.indirect(T.dl16[:, 64 * z:64 * z + 64])
-            if h < D_V[ph]:
-                ts(T.d0[:, o], src, 0.0, OP.max, [RX, A("dl16", ph, ph + 1)], [("d0", z, z + 1)], cost=0.05 + 1024 * GAT)
-            else:
-                act(T.d0[:, o], src, AF.Relu, [RX, A("dl16", ph, ph + 1)], [("d0", z, z + 1)], cost=0.065 + 1024 * GAT)
-            stage(s, "g%d" % h)
-            scn(T.bb[:, o], T.d0[:, o], T.alt[:], DEL, OP.subtract, OP.min, [("d0", z, z + 1), A("alt")], [("bb", z, z + 1)], 512)
-            tt(qq[:, 1024 * h + 1:1024 * h + 1024:2], all_x.indirect(T.el16[:, 128 * ph + 64 + 32 * h:128 * ph + 96 + 32 * h]),
-               T.bb[:, 1024 * z:1024 * z + 1024:2], OP.min, [RX, EL, ("bb", z, z + 1)], [("qo", z, z + 1)], cost=0.05 + 512 * GAT)
+        raw, RR = (xw[ph][:, XR:2 * XR], A("xw%d" % ph, XR, 2 * XR)) if s == 0 else (all_x, RX)
+        qq, EL = T["qq%d" % ph], A("el16", s, s + 1)
+        for h, (lo, hi) in enumerate(((0, EV), (EV, 1024))):
             stage(s, "e%d" % h)
-            out = qq[:, 1024 * h:1024 * h + 1024:2]
-            src = all_x.indirect(T.el16[:, 128 * ph + 32 * h:128 * ph + 32 * h + 32])
-            if h < EVEN_V[ph]:
-                cp(out, src, [RX, EL], [("qe", z, z + 1)], cost=0.05 + 512 * GAT)
-            else:
-                act(out, src, AF.Copy, [RX, EL], [("qe", z, z + 1)], cost=0.065 + 512 * GAT)
+            if lo < hi:
+                out = qq[:, QC + 2 * lo:QC + 2 * hi:2]
+                src = raw.indirect(T.el16[:, 256 * s + 128 + lo // 16:256 * s + 128 + hi // 16])
+                W, less = [("qe", 1024 * ph + lo, 1024 * ph + hi)], -DEL if s == 0 else 0.0
+                if h == 0:
+                    ts(out, src, less, OP.add, [RR, EL], W, cost=("gather", hi - lo))
+                else:
+                    act(out, src, AF.Copy, [RR, EL], W, cost=("gather", hi - lo), bias=less)
+        for h, (lo, hi) in enumerate(zip(DCUT[:-1], DCUT[1:])):
+            n, o = hi - lo, slice(2048 * ph + lo, 2048 * ph + hi)
+            stage(s, "d%d" % h)
+            act(T.d0[:, o], raw.indirect(T.el16[:, 256 * s + lo // 16:256 * s + hi // 16]), AF.Relu, [RR, EL], [("d0", o.start, o.stop)],
+                cost=("gather", n))
+            stage(s, "g%d" % h)
+            scn(T.bb[:, o], T.d0[:, o], T.alt[:, 0:n], DEL, OP.subtract, OP.min, [("d0", o.start, o.stop), A("alt")], [("bb", o.start, o.stop)], n // 2)
+            tt(qq[:, QC + lo + 1:QC + hi:2], all_x.indirect(T.el16[:, 256 * s + 192 + lo // 32:256 * s + 192 + hi // 32]),
+               T.bb[:, o.start:o.stop:2], OP.min, [RX, EL, ("bb", o.start, o.stop)], [("qo", o.start // 2, o.stop // 2)], cost=("gather", n // 2))
 
     def hop(s, par):
         ph = s % 2
-        pe, pu, qq = T["p%d" % ph], T["p%d" % (2 + ph)], T["qq%d" % ph]
+        pe = banks(ph)[0]
+        pu, B = (banks(ph)[1], 2 + ph) if par else (banks(ph)[3], 5 + 2 * ph)
+        qq = T["qq%d" % ph]
+        z = 2 * ph + par
         stage(s, "hop%d" % par)
-        mms([(pu[:, par:256:2], T.idn[:], T.c75[:, 64:192])] + [(pu[:, k:256:16], qq[:, k::16], T.gw[:]) for k in range(par, 16, 2)],
-            640, [("qo" if par else "qe", 2 * ph, 2 * ph + 2), A("gw"), A("idn"), A("c75")], [2 + ph])
-        o = slice(64 * par, 64 * par + 64)
+        mms([(pu[:, k:64:8], qq[:, QC + 2 * k + par::16], T.gw[:, 0:8]) for k in range(8)], 512, [("qo" if par else "qe", 1024 * ph, 1024 * ph + 1024), A("gw")], [B])
+        o, o2 = slice(64 * z, 64 * z + 64), slice(128 * ph + par, 128 * ph + 128, 2)
 
         def rg(b):
-            return A(b, par, par + 1)
-        cp(T.ui[:, o], pu[:, 128 + par:256:2], [], [rg("ui")], [2 + ph])
-        ts(T.ua[:, o], T.ui[:, o], 4095, OP.bitwise_and, [rg("ui")], [rg("ua")])
+            return A(b, z, z + 1)
+        cp(T.ui[:, o2], pu[:, 0:64], [], [rg("ui")], [B])
+        ts(T.ua[:, o], T.ui[:, o2], 4095, OP.bitwise_and, [rg("ui")], [rg("ua")])
         tt(T.ta[:, o], pe[:, par:128:2], T.ua[:, o], OP.mult, [rg("ua")], [rg("ta")], [ph])
         ts(T.tb[:, o], T.ta[:, o], 5, OP.logical_shift_right, [rg("ta")], [rg("tb")])
         k0 = 0 if s < 2 else 128
-        tt(T.tc[:, o], pe[:, k0 + par:k0 + 128:2], T.tb[:, o], OP.add, [rg("tb")], [rg("tc")], [ph])
-        ts(T.hh[:, o], T.tc[:, o], 4095, OP.bitwise_and, [rg("tc")], [rg("hh")])
-        z0 = 17 * par
-        ts(T.hz[:, z0 + 1:z0 + 17:2, :], T.hh[:, o], -2048.0, OP.add, [rg("hh")], [rg("hz")])
-        pl = pu[:, 256 + 64 * par:320 + 64 * par]
-        mms([(pl, T.hz[:, z0 + 1 - b:z0 + 17 - b, :], T.idh[:, b::2]) for b in range(2)], 128, [rg("hz"), A("idh")], [2 + ph])
-        z = 2 * ph + par
-        ts(T.h16[:, 64 * z:64 * z + 64], pl, 2048.0, OP.add, [], [A("h16", z, z + 1)], [2 + ph])
-        stage(s, "hf")
-        ts(T.hf[:, 128 * ph + par:128 * ph + 128:2], T.hh[:, o], -2048.0, OP.add, [rg("hh")], [A("hf", z, z + 1)])
+        tt(T.tc[:, o], pe[:, k0 + par:k0 + 128:2], T.tb[:, o], OP.add, [rg("tb"), A("ek", ph, ph + 1)], [rg("tc")], [ph])
+        hh, HH = T.hh[:, 128 * s + par:128 * s + 128:2], A("hh", 2 * s + par, 2 * s + par + 1)
+        ts(hh, T.tc[:, o], 4095, OP.bitwise_and, [rg("tc")], [HH])
+        z0 = 17 * z
+        ts(T.hz[:, z0 + 1:z0 + 17:2, :], hh, -2048.0, OP.add, [HH], [rg("hz")])
+        pl = pu[:, 256:320]
+        mms([(pl, T.hz[:, z0 + 1 - b:z0 + 17 - b, :], T.idh[:, b::2]) for b in range(2)], 128, [rg("hz"), A("idh")], [B])
+        ts(T.h16[:, o], pl, 2048.0, OP.add, [], [rg("h16")], [B])
 
     def look(s, par):
         ph = s % 2
-        qq, Q = T["qq%d" % ph], ("qo" if par else "qe", 2 * ph, 2 * ph + 2)
+        qq, Q = T["qq%d" % ph], ("qo" if par else "qe", 1024 * ph, 1024 * ph + 1024)
         items, RX = xw[ph][:, XC:XC + 4096], A("xw%d" % ph, 0, XC + 4096)
         z = 2 * ph + par
         H16 = A("h16", z, z + 1)
-        ns = YS[ph][par]
-        for x in range(ns):
-            y = 2 * z + x
-            cols = slice(512 * y, 512 * y + 512)
+        ns = YS[par]
+        for x, (lo, hi) in enumerate(((0, min(ns, 512)), (512, ns))):
+            if lo >= hi:
+                continue
+            n, cols = hi - lo, slice(1024 * z + lo, 1024 * z + hi)
             stage(s, "y%d%d" % (par, x))
-            act(T.yb[:, cols], items.indirect(T.h16[:, 32 * y:32 * y + 32]), AF.Copy, [RX, H16], [("yb", y, y + 1)], cost=0.065 + 512 * GAT)
-            ps, B = (T.p5, 5) if x % 2 else (T.p4, 4)
-            mmx([(ps[:], T.nid[:], qq[:, 1024 * x + par:1024 * x + 1024:2], True, False)], 512, [A("nid"), Q], [B])
-            mmx([(ps[:], T.idn[:], T.yb[:, cols], False, True)], 512, [A("idn"), ("yb", y, y + 1)], [B])
+            act(T.yb[:, cols], items.indirect(T.h16[:, 64 * z + lo // 16:64 * z + hi // 16]), AF.Copy, [RX, H16], [("yb", cols.start, cols.stop)],
+                cost=("gather", n))
+            ps, B = banks(ph)[2 + x][:, 0:n], 4 + 2 * ph + x
+            mmx([(ps, T.nid[:], qq[:, QC + 2 * lo + par:QC + 2 * hi:2], True, False)], n, [A("nid"), Q], [B])
+            mmx([(ps, T.idn[:], T.yb[:, cols], False, True)], n, [A("idn"), ("yb", cols.start, cols.stop)], [B])
             stage(s, "s%d%d" % (par, x))
-            act(T.sg[:, 2048 * ph + 1024 * x + par:2048 * ph + 1024 * x + 1024:2], ps[:], AF.Sign, [], [("sg", y, y + 1)], [B], n=512)
-        if ns < 2:
-            lo, hi = 2 * z + ns, 2 * z + 2
-            cols = slice(2048 * ph + 1024 * ns + par, 2048 * ph + 2048, 2)
+            act(T.sg[:, 2048 * ph + 2 * lo + par:2048 * ph + 2 * hi:2], ps, AF.Sign, [], [("sg", cols.start, cols.stop)], [B], n=n)
+        if ns < 1024:
+            lo, hi = 1024 * z + ns, 1024 * z + 1024
+            cols = slice(2048 * ph + 2 * ns + par, 2048 * ph + 2048, 2)
             stage(s, "v%d" % par)
-            tt(T.dq[:, cols], items.indirect(T.h16[:, 32 * lo:32 * hi]), qq[:, 1024 * ns + par:2048:2], OP.subtract,
-               [RX, H16, Q], [("dq", lo, hi)], cost=0.05 + 512 * (2 - ns) * GAT)
-            ts(T.sg[:, cols], T.dq[:, cols], 1.0, OP.min, [("dq", lo, hi)], [("sg", lo, hi)], (), -1.0, OP.max, n=256 * (2 - ns))
+            tt(T.dq[:, cols], items.indirect(T.h16[:, lo // 16:hi // 16]), qq[:, QC + 2 * ns + par:QC + 2048:2], OP.subtract,
+               [RX, H16, Q], [("dq", lo, hi)], cost=("gather", hi - lo))
+            ts(T.sg[:, cols], T.dq[:, cols], 1.0, OP.min, [("dq", lo, hi)], [("sg", lo, hi)], (), -1.0, OP.max, n=(hi - lo) // 2)
 
     def mid(s):
         ph, c = s % 2, (s // 2) % 4
-        pe, pu = T["p%d" % ph], T["p%d" % (2 + ph)]
+        pe, pu = banks(ph)[:2]
+        o = slice(128 * ph, 128 * ph + 128)
+
+        def rg(b):
+            return A(b, ph, ph + 1)
         hop(s, 0)
         hop(s, 1)
-        stage(s, "gate")
-        cp(T.cr[:], pu[:, 0:128], [], [A("cr")], [2 + ph], n=128)
-        tt(T.ge[:], pu[:, 0:128], T.cr[:], OP.is_gt, [A("cr")], [A("ge")], [2 + ph], n=128)
-        tt(T.gsg[:], pe[:, 256:384], T.ge[:], OP.mult, [A("ge")], [A("gsg")], [ph], n=128)
+        stage(s, "gate0")
+        if UK:
+            ts(T.ub[:, o], T.ui[:, o], 31, OP.bitwise_and, [A("ui", 2 * ph, 2 * ph + 2)], [rg("ub")], n=128)
+            tt(T.us[:, o], pe[:, 256:384], T.ub[:, o], OP.mult, [rg("ub")], [rg("us")], [ph], n=128)
+        stage(s, "gate1")
+        qq, Q = T["qq%d" % ph], [("qe", 1024 * ph, 1024 * ph + 1024), ("qo", 1024 * ph, 1024 * ph + 1024), A("gw")]
+        mmx([(pe[:, 384 + k:512:16], qq[:, QC + k::16], T.gw[:, 8:16], k == 0, False) for k in range(16)], 1024, Q, [ph])
+        mmx([(pe[:, 384:512], T.idn[:], T.cm[:], False, False), (pe[:, 384:512], T.nid[:], T.cm[:], False, False)], 256, [A("idn"), A("nid"), A("cm")], [ph])
+        mmx([(pe[:, 384 + k:512:16], qq[:, QC + k::16], T.gw[:, 16:24], False, k == 15) for k in range(16)], 1024, Q, [ph])
+        ts(T.ge[:, o], pe[:, 384:512], 7.5 * DEL, OP.is_lt, [], [rg("ge")], [ph], n=128)
+        stage(s, "gsg")
+        tt(T.gsg[:, o], pe[:, 256:384], T.ge[:, o], OP.mult, [rg("ge")], [rg("gsg")], [ph], n=128)
         look(s, 0)
         look(s, 1)
         stage(s, "score")
-        mmx([(T.p6[:, 0:128], T.one[:], T.nk[:], True, False), (T.p6[:, 0:128], T.mm[:, cls(ph, c)], T.nk2[:], False, False)],
-            256, MM(ph, c) + [A("nk"), A("nk2"), A("one")], [6])
+        mmx([(pu[:, 384:512], T.sm[:, cls(ph, c)], T.nk[:], True, False), (pu[:, 384:512], T.nid[:], T.us[:, o], False, False)][:1 + UK], 128 + 128 * UK,
+            MM(ph, c, "sm") + [A("nk"), A("nid"), rg("us")], [2 + ph])
         for par in range(2):
-            mmx([(T.p6[:, k:128:16], T.sg[:, 2048 * ph + k:2048 * ph + 2048:16], T.g8[:], False, k == 15) for k in range(par, 16, 2)],
-                512, [("sg", 4 * ph + 2 * par, 4 * ph + 2 * par + 2), A("g8")], [6])
+            mmx([(pu[:, 384 + k:512:16], T.sg[:, 2048 * ph + k:2048 * ph + 2048:16], T.g8[:], False, k == 15) for k in range(par, 16, 2)],
+                512, [("sg", 2048 * ph + 1024 * par, 2048 * ph + 1024 * par + 1024), A("g8")], [2 + ph])
         stage(s, "keys")
-        tt(T.kt[:], T.p6[:, 0:128], T.gsg[:], OP.mult, [A("gsg")], [A("kt")], [6], n=128)
-        scn(T.sc[:], T.ke[:], T.kt[:], 0.625, OP.min, OP.max, [A("ke"), A("kt")], [A("sc")], 64)
-        tt(T.lm[:], T.sc[:].indirect(T.cl[:]), T.mr[:], OP.mult, [A("sc"), A("cl"), A("mr")], [A("lm")], cost=0.05 + 128 * GAT)
-        stage(s, "nw")
-        tt(T.nw[:], T.sc[:].indirect(T.cl[:]), T.kt[:], OP.not_equal, [A("kt"), A("cl"), A("sc")], [A("nw")], cost=0.05 + 128 * GAT)
+        kt, KT = T.kt[:, 128 * s:128 * s + 128], A("kt", s, s + 1)
+        tt(kt, pu[:, 384:512], T.gsg[:, o], OP.mult, [rg("gsg")], [KT], [2 + ph], n=128)
+        scn(T.sc[:, 128 * s:128 * s + 128], T.ke[:], kt, LOW, OP.min, OP.max, [A("ke"), KT], [A("sc", s, s + 1)], 128 if UK else 64)
 
-    def send(s):
+    def send(s, a, b, sm, w):
         t = s // 2
         dst = T.cores[(rank + 1 + t % (n_ranks - 1)) % n_ranks]
         es = topo.engines(core, dst)[:8]
@@ -483,107 +611,140 @@ def rank_program(g, core, T, topo):
         rid, pid, _ = topo.addr(dst)
         src = T.cores[(rank - 1 - t % (n_ranks - 1)) % n_ranks]
         n_in = len(topo.engines(src, core)[:8])
-        for a, b, sm, w in (("qd", "lq", "aq", 256), ("tg", "lt", "at", 16)):
-            name, o = "%s%d" % (sm, s), slice(w * s, w * s + w)
-            i = node("g", [lambda e, a=a, b=b, o=o, name=name: e.remote_dma(T[b][:, o], T[a][:, o], T.sem[name], T.sem.ls, pid, rid, mask)],
-                     0.6, [A(a, s, s + 1)], [], (), "r", len(es))
-            node(None, [], 0.0, [], [A(b, s, s + 1)], (), "a", (name, n_in), LQ if a == "qd" else LT, (i,))
+        name, o = "%s%d" % (sm, s), slice(w * s, w * s + w)
+        i = node("g", [lambda e: e.remote_dma(T[b][:, o], T[a][:, o], T.sem[name], T.sem.ls, pid, rid, mask)],
+                 CALL, [A(a, s, s + 1)], [], (), "r", len(es))
+        node(None, [], 0.0, [], [A(b, s, s + 1)], (), "a", (name, n_in), LAND[a != "qd"], (i,))
 
     def tail(s):
         ph = s % 2
         qq = T["qq%d" % ph]
+        pe, pu, ya, yb = banks(ph)
         stage(s, "tail1")
-        kl = T.p7[:, 0:8]
-        mms([(kl, T.idn[:], T.zc[:]), (kl, T.lm[:], T.rcp[:])], 128, [A("idn"), A("zc"), A("lm"), A("rcp")], [7])
-        cp(T.kn[:], kl, [], [A("kn")], [7])
-        tt(T.nf[:, 0:8], kl, T.thr[:], OP.is_gt, [A("thr")], [A("nf")], [7])
-        ts(T.li[:], T.kn[:], 0x0F0F, OP.bitwise_and, [A("kn")], [A("li")])
+        tt(T.lm[:], T.sc[:, 128 * s:128 * s + 128].indirect(T.cl[:]), T.mr[:], OP.mult, [A("sc", s, s + 1), A("cl"), A("mr")], [A("lm")],
+           cost=("gather", 128))
+        kl = pu[:, 0:8]
+        mms([(kl, T.idn[:], T.zc[:]), (kl, T.lm[:], T.rcp[:])], 320 if UK else 128, [A("idn"), A("zc"), A("lm"), A("rcp")], [2 + ph])
+        ts(T.kn[:], kl, 32.0 * UK, OP.add, [], [A("kn")], [2 + ph])
+        tt(T.nf[:, 0:8], kl, T.thr[:], OP.is_gt, [A("thr")], [A("nf")], [2 + ph])
+        ts(T.li[:], T.kn[:], 5 * UK, OP.logical_shift_right, [A("kn")], [A("li")], (), 0x0F0F, OP.bitwise_and)
         ts(T.l16[:], T.li[:], cf(27), OP.add, [A("li"), rc(27)], [A("l16")])
-        cp(T.qw[:], qq[:].indirect(T.l16[:]), [("qe", 2 * ph, 2 * ph + 2), ("qo", 2 * ph, 2 * ph + 2), A("l16")], [A("qw")], cost=0.05 + 128 * GAT)
-        for b in range(2):
-            mms([(T.p4[:, 128 * b:128 * b + 128], T.dup2[:, 128 * b:128 * b + 128], T.qw[:])], 128, [A("dup2"), A("qw")], [4])
-        QD = A("qd", s, s + 1)
-        act(T.qd[:, 256 * s:256 * s + 256], T.p4[:, 0:256], AF.Copy, [], [QD], [4], n=256)
+        cp(T.qd[:, 128 * s:128 * s + 128], qq[:].indirect(T.l16[:]), [("qe", 1024 * ph, 1024 * ph + 1024), ("qo", 1024 * ph, 1024 * ph + 1024), A("l16")],
+           [A("qd", s, s + 1)], cost=("gather", 128))
+        send(s, "qd", "lq", "aq", 128)
         n0, NS = 32 * ph, A("nfs", ph, ph + 1)
         scn(T.nfs[:, n0 + 1:n0 + 17], T.nf[:], T.z16[:], 0.0, OP.add, OP.max, [A("nf"), A("z16")], [NS], 16)
-        lst = [(T.p7[:, 16:32], T.i32[:], T.icn[:]), (T.p7[:, 24:32], T.nbl2[:, 0:128], T.nfs[:, n0 + 8:n0 + 16])]
+        lst = [(yb[:, 16:32], T.i32[:], T.icn[:]), (yb[:, 24:32], T.nbl2[:, 0:128], T.nfs[:, n0 + 8:n0 + 16])]
         for b in range(2):
             r = slice(128 * b, 128 * b + 128)
-            lst += [(T.p7[:, 16 + 8 * b:24 + 8 * b], T.am2[:, r], T.nf[:, 0:8]), (T.p7[:, 16 + 8 * b:24 + 8 * b], T.nbl2[:, r], T.nfs[:, n0:n0 + 8])]
-        for r0 in range(0, 16, 4):
-            mmx([(T.p7[:, 32:40], T.wu[:, 15 - r:143 - r], T.qw[:, r::16], r == 0, r == 15) for r in range(r0, r0 + 4)], 256, [A("wu"), A("qw")], [7])
+            lst += [(yb[:, 16 + 8 * b:24 + 8 * b], T.am2[:, r], T.nf[:, 0:8]), (yb[:, 16 + 8 * b:24 + 8 * b], T.nbl2[:, r], T.nfs[:, n0:n0 + 8])]
+        mmx([a + (j == 0, False) for j, a in enumerate(lst)], 384, [A("am2"), A("nf"), A("nbl2"), NS, A("i32"), A("icn")], [5 + 2 * ph])
         stage(s, "tail2")
-        cp(T.uwi[:], T.p7[:, 32:40], [], [A("uwi")], [7])
-        ts(T.uwa[:], T.uwi[:], 31, OP.bitwise_and, [A("uwi")], [A("uwa")])
+        if UK:
+            ts(T.uwa[:], T.kn[:], 31, OP.bitwise_and, [A("kn")], [A("uwa")])
+        else:
+            mms([(pu[:, 32:40], T.wu[:, 15 - r:143 - r], T.qd[:, 128 * s + r:128 * s + 128:16]) for r in range(16)], 1024, [A("wu"), A("qd", s, s + 1)], [2 + ph])
+            cp(T.uwi[:], pu[:, 32:40], [], [A("uwi")], [2 + ph])
+            ts(T.uwa[:], T.uwi[:], 31, OP.bitwise_and, [A("uwi")], [A("uwa")])
         cp(T.uwb[:], T.uwa[:], [A("uwa")], [A("uwb")])
-        mmx([a + (j == 0, False) for j, a in enumerate(lst)], 384, [A("am2"), A("nf"), A("nbl2"), NS, A("i32"), A("icn")], [7])
-        mmx([(T.p7[:, 16 + 8 * b:24 + 8 * b], T.dup2[:, 128 * b:128 * b + 128], T.uwb[:], False, b == 1) for b in range(2)], 128,
-            [A("dup2"), A("uwb")], [7])
-        tt(T.tgm[:], T.p7[:, 16:32], T.dum[:], OP.min, [A("dum")], [A("tgm")], [7])
+        mmx([(yb[:, 16 + 8 * b:24 + 8 * b], T.dup2[:, 128 * b:128 * b + 128], T.uwb[:], False, b == 1) for b in range(2)], 128,
+            [A("dup2"), A("uwb")], [5 + 2 * ph])
+        tt(T.tgm[:], yb[:, 16:32], T.dum[:], OP.min, [A("dum")], [A("tgm")], [5 + 2 * ph])
         cp(T.tg[:, 16 * s:16 * s + 16], T.tgm[:], [A("tgm")], [A("tg", s, s + 1)])
-        send(s)
+        send(s, "tg", "lt", "at", 16)
 
     def kappa():
-        mms([(T.p6[:, 384:385], T.one[:], T.nfs[:, 32 * ph + 8:32 * ph + 9]) for ph in range(2)], 128, [A("one"), A("nfs")], [6])
-        ts(T.kci[:], T.p6[:, 384:385], -1.0, OP.mult, [], [A("kci")], [6])
-        ts(T.kcj[:], T.kci[:], 31, OP.bitwise_and, [A("kci")], [A("kcj")])
-        cp(T.kap[:], T.kcj[:], [A("kcj")], [A("kap")])
+        pu = banks(1)[1]
+        mms([(pu[:, 48:49], T.one[:], T.nfs[:, 32 * ph + 8:32 * ph + 9]) for ph in range(2)], 128, [A("one"), A("nfs")], [3])
+        ts(T.kcj[:], pu[:, 48:49], -1.0, OP.mult, [], [A("kcj")], [3], 8176.5, OP.add)
+        ts(T.kap[:], pu[:, 48:49], -1.0, OP.mult, [A("kcj")], [A("kap")], [3], T.kcj[:], OP.subtract)
+        if "p" in ONV:
+            ts(T.kb[:], T.one[:], T.kap[:], OP.mult, [A("one"), A("kap")], [A("kb")], (), 8192.0, OP.add)
 
-    def plus_kappa(ph):
+    def plus_kappa(s):
+        ph, c = s % 2, (s // 2) % 4
         pe = T["p%d" % ph]
-        act(pe[:, 128:256], pe[:, 0:128], AF.Identity, [A("kap")], [], [ph], n=128, bias=T.kap[:])
+        if "p" in ONV:
+            mms([(pe[:, 128:256], T.idn[:], T.c2k[:]), (pe[:, 128:256], T.ef[:, cls(ph, c)], T.idh[:]), (pe[:, 128:256], T.idn[:], T.kb[:])], 384,
+                MM(ph, c, "ef") + [A("idn"), A("idh"), A("c2k"), A("kb")], [ph])
+        elif "k" in ONV:
+            ts(pe[:, 128:256], pe[:, 0:128], T.kap[:], OP.add, [A("kap")], [A("ek", ph, ph + 1)], [ph], n=128)
+        else:
+            act(pe[:, 128:256], pe[:, 0:128], AF.Identity, [A("kap")], [], [ph], n=128, bias=T.kap[:])
 
-    def update(s):
+    def update(s, bk, at=None):
         ph, t = s % 2, s // 2
         c = t % 4
-        E, M = EF(ph, c), MM(ph, c)
-        stage(s, "update")
+        o = slice(128 * s, 128 * s + 128)
+        E, M, NW = MM(ph, c, "ef"), MM(ph, c), A("nw", s, s + 1)
+        pe, pu, ya, yb = banks(bk)
+        nw, eb, EB = T.nw[:, o], T.eb[:, 128 * ph:128 * ph + 128], A("eb", ph, ph + 1)
+        stage(at or s, "late" if at else "hf")
+        ts(T.hf[:, o], T.hh[:, o], -2048.0, OP.add, [A("hh", 2 * s, 2 * s + 2)], [A("hf", s, s + 1)], n=128)
+        stage(at or s, "late" if at else "nw")
+        tt(nw, T.sc[:, o].indirect(T.cl[:]), T.kt[:, o], OP.not_equal, [A("kt", s, s + 1), A("cl"), A("sc", s, s + 1)], [NW], cost=("gather", 128))
+        stage(at or s, "late" if at else "update")
         keep = t + 4 < RO
-        pu = T["p%d" % (2 + ph)]
-        mms([(T.p6[:, 128:256], T.idh[:], T.ef[:, cls(ph, c)]), (T.p6[:, 128:256], T.nw[:], T.nbig[:])], 256, [A("nw"), E, A("idh"), A("nbig")], [6])
-        mms([(T.p6[:, 256:384], T.idn[:], T.mm[:, cls(ph, c)]), (T.p6[:, 256:384], T.nw[:], T.idn[:])], 256, M + [A("nw"), A("idn")], [6])
-        act(T.eb[:], T.p6[:, 128:256], AF.Copy, [], [A("eb")], [6], n=128, bias=BIG + (0.0 if keep else 2048.0))
-        act(T.mm[:, cls(ph, c)], T.p6[:, 256:384], AF.Abs, [], M, [6], n=128, bias=-1.0)
-        k0 = 128 if keep else 0
-        mms([(pu[:, 384:512], T.idn[:], T.c2k[:, k0:k0 + 128]), (pu[:, 384:512], T.hf[:, 128 * ph:128 * ph + 128], T.idh[:]),
-             (pu[:, 384:512], T.nw[:], T.big[:])], 384, [A("nw"), A("hf", 2 * ph, 2 * ph + 2), A("c2k"), A("idn"), A("idh"), A("big")], [2 + ph])
+        mms([(pe[:, 0:128], T.idh[:], T.ef[:, cls(ph, c)]), (pe[:, 0:128], nw, T.nbig[:]),
+             (pe[:, 128:256], T.idn[:], T.mm[:, cls(ph, c)]), (pe[:, 128:256], nw, T.idn[:])], 512, E + M + [NW, A("idh"), A("nbig"), A("idn")], [bk])
+        act(eb, pe[:, 0:128], AF.Copy, [], [EB], [bk], n=128, bias=BIG + (0.0 if keep else 2048.0))
+        act(T.mm[:, cls(ph, c)], pe[:, 128:256], AF.Abs, [], M, [bk], n=128, bias=-1.0)
+        lst = [(yb[:, 128:256], T.hf[:, o], T.idh[:]), (yb[:, 128:256], nw, T.big[:])]
+        if not keep:
+            lst.append((yb[:, 128:256], T.idn[:], T.c2k[:]))
+        mms(lst, 128 * len(lst), [NW, A("hf", s, s + 1), A("c2k"), A("idn"), A("idh"), A("big")], [5 + 2 * bk])
         if keep:
-            tt(T.ef[:, cls(ph, c)], pu[:, 384:512], T.eb[:], OP.min, [A("eb")], [E], [2 + ph], n=128)
+            ts(T.sm[:, cls(ph, c)], T.mm[:, cls(ph, c)], -2.0, OP.mult, M, MM(ph, c, "sm"), (), 1.0, OP.add)
+            tt(T.ef[:, cls(ph, c)], yb[:, 128:256], eb, OP.min, [EB], E, [5 + 2 * bk], n=128)
         else:
-            tt(T.ylb[:, cls(ph, c)], pu[:, 384:512], T.eb[:], OP.min, [A("eb")], [A("yl%d%d" % (ph, c))], [2 + ph], n=128)
+            tt(T.ylb[:, cls(ph, c)], yb[:, 128:256], eb, OP.min, [EB], [A("yl%d%d" % (ph, c))], [5 + 2 * bk], n=128)
+
+    def back(ph, which):
+        for z, q in enumerate(RELU[ph]):
+            if q in which:
+                ap, rg = xw[ph][:, XC + 1024 * z:XC + 1024 * z + 1024], A("xw%d" % ph, XC + 1024 * z, XC + 1024 * z + 1024)
+                if q in "sS":
+                    act(ap, ap, AF.Relu, [rg], [rg], n=1024)
+                else:
+                    ts(ap, ap, 0.0, OP.max, [rg], [rg], n=512)
 
     def arrive(s):
         ph = s % 2
         stage(s, "arrive")
         win, WX = xw[ph][:, XC:XW], A("xw%d" % ph, XC, XW)
-        plain = s == ST - 1
-        if plain:
-            for z in range(2):
-                ap, rg = xw[ph][:, XC + 2048 * z:XC + 2048 * z + 2048], A("xw%d" % ph, XC + 2048 * z, XC + 2048 * z + 2048)
-                act(ap, ap, AF.Relu, [rg], [rg], n=2048)
+        last = s >= ST - 2
+        if last:
+            back(ph, "SV")
         lt, L = T.lt[:, 16 * s:16 * s + 16], A("lt", s, s + 1)
-        tt(T.av[:], win.indirect(lt), T.lq[:, 256 * s:256 * s + 256], OP.add, [WX, L, A("lq", s, s + 1)], [A("av")], cost=0.05 + 256 * GAT)
+        ya = banks(ph)[2]
+        mms([(ya[:, 128 * b:128 * b + 128], T.dup2[:, 128 * b:128 * b + 128], T.lq[:, 128 * s:128 * s + 128]) for b in range(2)], 256,
+            [A("dup2"), A("lq", s, s + 1)], [4 + 2 * ph])
+        if "q" in ONV:
+            cp(T.qw[:], ya[:, 0:256], [], [A("qw")], [4 + 2 * ph], n=256)
+        else:
+            act(T.qw[:], ya[:, 0:256], AF.Copy, [], [A("qw")], [4 + 2 * ph], n=256)
+        tt(T.av[:], win.indirect(lt), T.qw[:], OP.add, [WX, L, A("qw")], [A("av")], cost=("gather", 256))
         ts(T.aw[:], T.av[:], 0.5, OP.mult, [A("av")], [A("aw")], (), 1279.75, OP.add, n=128)
-        ts(T.ax[:], T.aw[:], -1280.0 - (0.0 if plain else DEL), OP.add, [A("aw")], [A("ax")], n=128)
-        cp(win.indirect(lt), T.ax[:], [A("ax"), L], [WX], cost=0.05 + 256 * SCA)
-        if s >= ST - 2:
-            for b in range(2):
-                ap, rg = xw[ph][:, XC + 2048 * b:XC + 2048 * b + 2048], A("xw%d" % ph, XC + 2048 * b, XC + 2048 * b + 2048)
-                if not plain:
-                    ts(ap, ap, 0.0, OP.max, [rg], [rg], n=1024)
-                dma("ys"[b] if plain else "y", T.yx[64 * ph:64 * ph + 64, 2048 * b:2048 * b + 2048],
-                    xw[ph][64 * b:64 * b + 64, XC + 2048 * b:XC + 2048 * b + 2048], [rg], [], 3.5)
+        ts(T.ax[:], T.aw[:], -1280.0 - (0.0 if last else DEL), OP.add, [A("aw")], [A("ax")], n=128)
+        cp(win.indirect(lt), T.ax[:], [A("ax"), L], [WX], cost=("scatter", 256))
+        if last:
+            back(ph, "sv")
+            dma(STORES[ph][4], T.yx[64 * ph:64 * ph + 64, :], xw[ph][0:64, XC:XR], [A("xw%d" % ph, XC, XR)], [],
+                DLAT + 524288 / DBW + DROW + (0.0 if ph else OUTL[2]))
 
     def lists_out(ph):
         for b in range(2):
-            dma("y", T.ym[64 * ph:64 * ph + 64, 512 * b:512 * b + 512], T.mm[64 * b:64 * b + 64, 512 * ph:512 * ph + 512], MM(ph), [], 2.5)
-            dma("y", T.yl[64 * ph:64 * ph + 64, 512 * b:512 * b + 512], T.ylb[64 * b:64 * b + 64, 512 * ph:512 * ph + 512],
-                [A("yl%d%d" % (ph, c)) for c in range(4)], [], 2.5)
+            dma(STORES[ph][b], T.ym[64 * ph:64 * ph + 64, 512 * b:512 * b + 512], T.mm[64 * b:64 * b + 64, 512 * ph:512 * ph + 512], MM(ph), [], OUTL[ph])
+            dma(STORES[ph][2 + b], T.yl[64 * ph:64 * ph + 64, 512 * b:512 * b + 512], T.ylb[64 * b:64 * b + 64, 512 * ph:512 * ph + 512],
+                [A("yl%d%d" % (ph, c)) for c in range(4)], [], OUTL[ph])
 
     for ph in range(2):
         stage(ph - 2, "prep")
-        early(ph, 0)
-        prep(ph)
+        lists(ph, 2 + ph)
+        turned(ph)
+    stage(-1, "next")
+    for s in EARLY:
+        lists(s, 6)
     for s in range(ST):
         if s >= 2:
             arrive(s - 2)
@@ -593,33 +754,36 @@ def rank_program(g, core, T, topo):
         if s % 2 and s + 2 < ST:
             stage(s, "kappa")
             kappa()
-            plus_kappa(0)
-        update(s)
-        stage(s, "prep")
+            plus_kappa(s + 1)
+        if s not in LATE:
+            update(s, s % 2)
         if s + 2 < ST:
-            if s // 2 < 3:
-                early(s % 2, s // 2 + 1)
-            prep(s + 2)
+            stage(s, "prep")
+            if s + 2 not in EARLY:
+                lists(s + 2, 2 + s % 2)
+            turned(s + 2)
             if s % 2:
-                plus_kappa(1)
+                plus_kappa(s + 2)
         else:
+            for z in LATE:
+                if s == ST - 2:
+                    update(z, 0, s)
+            stage(s, "prep")
             lists_out(s % 2)
     arrive(ST - 2)
     arrive(ST - 1)
 
     n = len(nodes)
     before = [[] for _ in range(n)]
-    after = [[] for _ in range(n)]
     for i, d in enumerate(nodes):
         for j in d["deps"] | d["order"]:
             f = nodes[j]
-            lag = f["late"] + ((0.05 if f["q"] == d["q"] else 0.1) if j in d["deps"] else 0.0)
+            lag = f["late"] + ((WAKE[0] if f["q"] == d["q"] else WAKE[1] + MORE.get(f["q"], 0.0)) if j in d["deps"] else 0.0)
             before[i].append((j, lag))
-            after[j].append((i, lag))
 
     if "order" not in ORDER:
         ORDER["order"] = arrange(nodes, before)
-        ORDER["x"] = (nodes, before, after, None)
+        ORDER["x"] = (nodes, before)
     orders, fin = ORDER["order"][1], ORDER["order"][2]
 
     cnt = {q: 0 for q in eng}

@@ -13,15 +13,13 @@ XW = XC + XD + 256
 QC = 0
 DEL = 2.0 ** -10
 BIG = 8192.0
-UK = True
-KD = "float32" if UK else "bfloat16"
-LOW = 32.625 if UK else 0.625
+KD = "float32"
+LOW = 32.625
 YS = (1024, 384)
 DCUT = (0, 1024, 2048)
 EV = 256
 EARLY = (2, 3)
 LATE = ()
-ONV = "p"
 PARTS = ((("v", 1024),) * 4, ())
 LOADS = ((("y", "e", 0), ("s", "e", 1), ("y", "m", 0), ("s", "m", 1), ("y", "x", 0), ("s", "x", 1)),
          (("y", "e", 0), ("y", "e", 1), ("y", "m", 0), ("y", "m", 1), ("g", "a", 0), ("g", "a", 1)))
@@ -37,22 +35,23 @@ for _n, _w, _d in (
         ("d0", 4096, "bfloat16"), ("bb", 4096, "bfloat16"), ("qq0", QC + 2048, "bfloat16"), ("qq1", QC + 2048, "bfloat16"), ("dq", 4096, "bfloat16"),
         ("sg", 4096, "bfloat16"), ("yb", 4096, "bfloat16"),
         ("el16", 256 * ST, "uint16"), ("h16", 256, "uint16"),
-        ("ui", 256, "int32"), ("ua", 256, "int32"), ("ta", 256, "int32"), ("tb", 256, "int32"), ("tc", 256, "int32"), ("hh", 128 * ST, "int32"),
-        ("hf", 128 * ST, "float16"), ("eb", 256, "float32"), ("av", 256, "float16"), ("aw", 256, "float16"), ("ax", 256, "bfloat16"),
-        ("qw", 256, "bfloat16"), ("qd", 128 * ST, "bfloat16"), ("lq", 128 * ST, "bfloat16"), ("tg", 16 * ST, "uint16"), ("lt", 16 * ST, "uint16"),
-        ("pi", 1, "int32"), ("ci", 8, "int32"), ("cf", 32, "float32"), ("m1", 144, "float32"), ("m64", 128, "float32"), ("si", 128, "float32"),
+        ("es", 512, "float32"), ("ta", 256, "int32"), ("tb", 256, "int32"), ("tc", 256, "int32"), ("hh", 128 * ST, "int32"),
+        ("hf", 128 * ST, "float16"), ("eb", 256, "float32"), ("av", 256, "float16"), ("ax", 256, "bfloat16"),
+        ("qw", 256, "float32"), ("qd", 128 * ST, "bfloat16"), ("lq", 128 * ST, "bfloat16"), ("tg", 16 * ST, "uint16"), ("lt", 16 * ST, "uint16"),
+        ("pi", 1, "int32"), ("ci", 8, "int32"), ("cf", 32, "float32"), ("m1", 128, "float32"), ("m64", 128, "float32"), ("low", 128, "bfloat16"), ("t2", 128, "bfloat16"), ("si", 128, "float32"),
         ("clf", 8, "float32"), ("cl", 8, "uint16"), ("icf", 16, "float32"), ("icn", 16, "bfloat16"), ("dum", 16, "int32"), ("mg", 128, "float32"),
         ("zc", 8, "bfloat16"), ("thr", 8, "float32"), ("i32", 128, "bfloat16"),
-        ("dup2", 256, "bfloat16"), ("nbl2", 256, "bfloat16"), ("am2", 256, "bfloat16"), ("rcp", 8, KD), ("wu", 144, "bfloat16"), ("uwi", 8, "int32"), ("kb", 128, "bfloat16"), ("nbl", 128, "bfloat16"),
-        ("low", 128, "bfloat16"), ("am", 128, "bfloat16"), ("mr", 128, "bfloat16"), ("z16", 16, "bfloat16"),
+        ("dup2", 256, "bfloat16"), ("nbl2", 256, "bfloat16"), ("am2", 256, "bfloat16"), ("rcp", 8, KD), ("kb", 64, "bfloat16"), ("nbl", 128, "bfloat16"),
+        ("am", 128, "bfloat16"), ("mr", 128, "bfloat16"), ("z16", 16, "bfloat16"),
         ("idn", 128, "bfloat16"), ("nid", 128, "bfloat16"), ("nk", 128, "bfloat16"),
         ("idh", 128, "float16"), ("big", 128, "bfloat16"), ("nbig", 128, "bfloat16"), ("dup", 128, "bfloat16"),
-        ("g8", 8, "bfloat16"), ("gw", 24, "bfloat16"), ("cm", 128, "bfloat16"), ("cd", 128, "bfloat16"), ("id15", 128, "float16"), ("big15", 128, "bfloat16"), ("pm", 512, "float16"),
-        ("t1", 128, "bfloat16"), ("t2", 128, "bfloat16"), ("one", 128, "bfloat16"),
+        ("g8", 8, "bfloat16"), ("gw", 32, "bfloat16"), ("i2040", 128, "bfloat16"), ("i75", 128, "bfloat16"), ("i155", 128, "bfloat16"),
+        ("i4k", 128, "bfloat16"), ("n4k", 128, "bfloat16"), ("n32", 128, "bfloat16"), ("cm", 128, "bfloat16"), ("cd", 128, "bfloat16"), ("id15", 128, "float16"), ("big15", 128, "bfloat16"), ("pm", 512, "float16"),
+        ("t1", 128, "bfloat16"), ("one", 128, "bfloat16"),
         ("ke", 128, KD), ("c2k", 128, "bfloat16"),
-        ("ge", 256, "bfloat16"), ("gsg", 256, "bfloat16"), ("kt", 128 * ST, KD), ("sc", 128 * ST, KD),
+        ("i19", 128, "bfloat16"), ("n19", 128, "bfloat16"), ("i128", 128, "bfloat16"), ("kt", 128 * ST, KD), ("sc", 128 * ST, KD),
         ("nw", 128 * ST, "bfloat16"), ("nf", 16, "bfloat16"), ("kn", 8, "int32"), ("li", 8, "int32"), ("lm", 128, KD), ("nfs", 64, "bfloat16"),
-        ("ub", 256, "int32"), ("us", 256, "bfloat16"), ("l16", 8, "uint16"), ("uwa", 8, "int32"), ("uwb", 8, "bfloat16"), ("tgm", 16, "int32"),
+        ("us", 256, "bfloat16"), ("l16", 8, "uint16"), ("uwa", 8, "int32"), ("uwb", 8, "bfloat16"), ("tgm", 16, "int32"),
         ("kcj", 1, "bfloat16"), ("kap", 1, "float32")):
     SCRATCH[_n] = ("sbuf", [128, _w], _d)
 SCRATCH["hz"] = ("sbuf", [128, 68, 8], "float16")
@@ -62,28 +61,29 @@ SEMAPHORES = ["cv", "cs", "cp", "cg", "ls"] + ["aq%d" % _t for _t in range(ST)] 
     + ["dm%d" % _t for _t in range(48)]
 
 ORDER = {}
-SEED = 1
-TRIES = 2600
-SWAPS = 3000
-HEAT2 = 0.15
-SHIFT = 3.5
-HEAT = 0.2
-PER = 12.0
+SEED = 4
+TRIES = 1700
+SWAPS = 9000
+HEAT2 = 0.08
+SHIFT = 2.5
+HEAT = 0.15
+PER = 10.5
 START = {"pre": -30.0, "fill": -29.0, "soon": -1.0, "next": 3.0, "e0": 0.0, "e1": 0.9, "d0": 0.1, "d1": 1.5, "d2": 2.5, "d3": 3.0, "g0": 1.8, "g1": 3.0, "g2": 3.7,
          "g3": 4.2, "hop0": 2.5, "hop1": 5.5, "hf": 9.0, "gate0": 4.0, "gate1": 7.5, "gsg": 8.0, "y00": 5.3, "y01": 6.2, "s00": 7.1, "s01": 7.6, "y10": 8.2, "y11": 8.9, "s10": 9.3, "s11": 9.8, "v0": 5.0, "v1": 9.0, "score": 8.0,
          "keys": 11.0, "nw": 15.0, "tail1": 11.5, "tail2": 14.0, "kappa": 12.5, "update": 16.0, "late": 17.0, "prep": 16.5, "arrive": 18.0}
 FIRST = ()
-MACHINES = ((0.9, 0.75, 0.7, 0.8, 1.0, 0.0, 0.9), (1.2, 1.45, 1.9, 1.0, 1.0, 0.0, 1.2))
-LAND = (2.0, 1.5)
+MACHINES = ((0.89, 0.74, 0.75, 0.9, 1.0, 0.0, 0.9), (1.2, 1.45, 1.9, 1.2, 1.0, 0.0, 1.25))
+LAND = (1.9, 1.4)
 WAKE = (0.15, 0.04)
-MORE = {"p": 0.05, "s": 0.06}
-CALL = 0.85
+MORE = {"p": 0.08, "s": 0.06}
+CALL = 0.75
 FIX = 0.03
 C0 = 26
 CYC = 0.00097
-PCY = 0.0004
-PFX = 0.015
-SX = 0.09
+PCY = 0.00038
+PFX = 0.01
+PGR = 0.07
+SX = 0.08
 OUTL = (10, 5, 6)
 GAT = 0.0016
 SCA = 0.003
@@ -296,10 +296,10 @@ def rank_program(g, core, T, topo):
 
     def mms(lst, n, R, B):
         last = len(lst) - 1
-        node("p", [lambda e, a=a, j=j: e.matmul(a[0], a[1], a[2], j == 0, j == last) for j, a in enumerate(lst)], n * PCY + len(lst) * PFX, R, [], B)
+        node("p", [lambda e, a=a, j=j: e.matmul(a[0], a[1], a[2], j == 0, j == last) for j, a in enumerate(lst)], n * PCY + len(lst) * PFX + PGR, R, [], B)
 
     def mmx(lst, n, R, B):
-        node("p", [lambda e, a=a: e.matmul(*a) for a in lst], n * PCY + len(lst) * PFX, R, [], B)
+        node("p", [lambda e, a=a: e.matmul(*a) for a in lst], n * PCY + len(lst) * PFX + PGR * lst[0][3], R, [], B)
 
     def ts(out, in0, s1, o1, R, W, B=(), s2=None, o2=None, n=64, cost=None):
         if o2 is None:
@@ -334,7 +334,8 @@ def rank_program(g, core, T, topo):
         return [A("%s%d%d" % (name, ph, k)) for k in range(4) if c in (None, k)]
 
     iota(T.pi[:], [[0, 1]], 0, 1, [A("pi")], 1, False)
-    iota(T.m1[:], [[1, 144]], 1, 0, [A("m1")], 144)
+    iota(T.cf[:, 5:6], [[0, 1]], 0, 1, [("cf", 5, 6)], 1)
+    iota(T.m1[:], [[1, 128]], 1, 0, [A("m1")], 128)
     fill(T.alt[:, 0::2], 4096.0, [A("alt", 0, 1)], 256)
     fill(T.alt[:, 1::2], DEL, [A("alt", 1, 2)], 256)
     stage(-1, "fill")
@@ -382,12 +383,14 @@ def rank_program(g, core, T, topo):
         for lo in (XR, 0):
             iota(xw[ph][:, lo:lo + XC], [[4096, 2], [0, 16]], 0, 0, [A("xw%d" % ph, lo, lo + XC)], XC)
 
+    iota(T.one[:], [[0, 128]], 1, 0, [A("one")], 128)
+    node("g", [lambda e: e.affine_select(T.idn[:], T.one[:], [[1, 128]], OP.is_equal, 0.0, 0, -1)], 0.17 + 256 * CYC, [A("one")], [A("idn")])
     iota(T.m64[:], [[0, 2], [1, 64]], 0, 0, [A("m64")], 128)
     iota(T.clf[:], [[16, 8]], 15, 0, [A("clf")], 8)
     iota(T.mg[:], [[0, 2], [16, 4], [0, 16]], 0, 0, [A("mg")], 128)
     iota(T.si[:], [[0, 8], [1, 16]], 0, 0, [A("si")], 128)
     iota(T.icf[:], [[16, 16]], 0, 1, [A("icf")], 16)
-    iota(T.zc[:], [[8192 if UK else 256, 8]], 8192 if UK else 256, 0, [A("zc")], 8)
+    iota(T.zc[:], [[8192, 8]], 8192, 0, [A("zc")], 8)
 
     def ci(j):
         return T.ci[:, j:j + 1]
@@ -400,10 +403,9 @@ def rank_program(g, core, T, topo):
     ts(ci(0), T.pi[:], 15, OP.bitwise_and, [A("pi")], [("ci", 0, 1)])
     ts(ci(1), T.pi[:], 1, OP.bitwise_and, [A("pi")], [("ci", 1, 2)])
     ts(ci(2), T.pi[:], 1, OP.logical_shift_right, [A("pi")], [("ci", 2, 3)], (), 7, OP.bitwise_and)
-    ts(ci(3), T.pi[:], 63, OP.bitwise_and, [A("pi")], [("ci", 3, 4)])
-    ts(ci(4), T.pi[:], 48, OP.bitwise_and, [A("pi")], [("ci", 4, 5)])
+    ts(ci(3), T.pi[:], 48, OP.bitwise_and, [A("pi")], [("ci", 3, 4)])
+    ts(ci(4), T.pi[:], 63, OP.bitwise_and, [A("pi")], [("ci", 4, 5)])
     cp(T.cf[:, 0:5], T.ci[:, 0:5], [("ci", 0, 5)], [("cf", 0, 5)])
-    cp(cf(5), T.pi[:], [A("pi")], [rc(5)])
     tt(cf(6), cf(5), cf(0), OP.subtract, [rc(5), rc(0)], [rc(6)])
     ts(cf(7), cf(1), -1.0, OP.mult, [rc(1)], [rc(7)], (), 1.0, OP.add)
     tt(cf(9), cf(6), cf(2), OP.add, [rc(6), rc(2)], [rc(9)])
@@ -414,15 +416,13 @@ def rank_program(g, core, T, topo):
             ts(T.pm[:, 128 * j:128 * j + 128], T.m1[:, 0:128], cf(11 + j), OP.is_equal, [A("m1"), rc(11 + j)], [("pm", j, j + 1)], n=128)
     ts(cf(19), cf(0), 14.5, OP.is_lt, [rc(0)], [rc(19)])
     ts(cf(20), cf(19), 2048.0 + XC - 16.0 - BIG, OP.mult, [rc(19)], [rc(20)], (), 16.0 - 2048.0 - XC, OP.add)
-    ts(cf(26), cf(5), 1.0, OP.add, [rc(5)], [rc(26)])
-    ts(T.idn[:], T.m1[:, 0:128], cf(26), OP.is_equal, [A("m1"), rc(26)], [A("idn")], n=128)
     cp(T.idh[:], T.idn[:], [A("idn")], [A("idh")])
     ts(T.id15[:], T.idn[:], cf(19), OP.mult, [A("idn"), rc(19)], [A("id15")])
     ts(T.big15[:], T.idn[:], cf(19), OP.mult, [A("idn"), rc(19)], [A("big15")], (), BIG, OP.mult)
     ts(T.cd[:], T.idn[:], 0.0, OP.mult, [A("idn"), rc(20)], [A("cd")], (), cf(20), OP.add)
     convert(0, 0)
     stage(-1, "soon")
-    for name, v, n in (("c2k", 2048, 128), ("one", 1, 128), ("cm", 3 << 22, 128), ("ke", 16384, 128), ("z16", 0, 16), ("nf", 0, 16), ("nfs", 0, 64)):
+    for name, v, n in (("c2k", 2048, 128), ("cm", 3 << 22, 128), ("ke", 16384, 128), ("z16", 0, 16), ("nf", 0, 16), ("nfs", 0, 64)):
         iota(T[name][:], [[0, n]], v, 0, [A(name)], n)
     for ph in range(2):
         iota(xw[ph][:, XC + XD:XW], [[0, 256]], 0, 0, [A("xw%d" % ph, XC + XD, XW)], 256)
@@ -431,25 +431,22 @@ def rank_program(g, core, T, topo):
         act(out, in_, AF.Identity, R, W, n=128, **kw)
     fill(T.hz[:], 0.0, [A("hz")], 272)
     ts(cf(21), cf(0), 2.0, OP.mult, [rc(0)], [rc(21)], (), 1.0, OP.add)
-    if UK:
-        ts(cf(23), cf(0), -32.0, OP.mult, [rc(0)], [rc(23)], (), 32.0, OP.add)
-    else:
-        ts(cf(23), cf(0), -1.0, OP.mult, [rc(0)], [rc(23)])
-        ts(cf(22), cf(6), 16.0, OP.add, [rc(6)], [rc(22)])
-        ts(T.wu[:], T.m1[:], cf(22), OP.is_equal, [A("m1"), rc(22), rc(21)], [A("wu")], (), cf(21), OP.mult, n=144)
+    ts(cf(23), cf(0), -32.0, OP.mult, [rc(0)], [rc(23)], (), 32.0, OP.add)
     ts(cf(25), cf(6), 0.0625, OP.mult, [rc(6)], [rc(25)], (), 1.0, OP.add)
     ts(cf(27), cf(0), 16.0, OP.mult, [rc(0)], [rc(27)], (), float(QC), OP.add)
     ts(T.rcp[:], T.m1[:, 0:8], cf(25), OP.is_equal, [A("m1"), rc(25)], [A("rcp")], (), -1.0, OP.mult)
-    for name, f in (("nid", -1.0), ("big", BIG), ("nbig", -BIG), ("i32", 32.0)):
+    for name, f in (("nid", -1.0), ("i2040", 2040.0), ("i75", 7.5), ("i4k", 4096.0), ("n4k", -4096.0), ("i155", 15.5), ("i32", 32.0), ("n32", -32.0),
+                    ("big", BIG), ("nbig", -BIG), ("i19", 2.0 ** 19), ("n19", -2.0 ** 19), ("i128", 128.0)):
         times(T[name][:], T.idn[:], [A(name)], [A("idn")], scale=f)
     times(T.nk[:], T.idn[:], [A("nk")], [A("idn"), rc(23)], scale=cf(23))
-    ts(T.g8[:], T.m1[:, 0:8], cf(25), OP.is_equal, [A("m1"), rc(25)], [A("g8")], (), 512.0 if UK else 16.0, OP.mult)
+    ts(T.g8[:], T.m1[:, 0:8], cf(25), OP.is_equal, [A("m1"), rc(25)], [A("g8")], (), 512.0, OP.mult)
     ts(T.gw[:, 0:8], T.m1[:, 0:8], cf(25), OP.is_equal, [A("m1"), rc(25), rc(21)], [A("gw", 0, 1)], (), cf(21), OP.mult)
-    ts(T.gw[:, 8:16], T.m1[:, 0:8], cf(25), OP.is_equal, [A("m1"), rc(25)], [A("gw", 1, 2)])
-    ts(T.gw[:, 16:24], T.m1[:, 0:8], cf(25), OP.is_equal, [A("m1"), rc(25)], [A("gw", 2, 3)], (), -1.0, OP.mult)
-    ts(T.dup[:], T.m64[:], cf(3), OP.is_equal, [A("m64"), rc(3)], [A("dup")], n=128)
-    ts(T.nbl[:], T.mg[:], cf(4), OP.is_equal, [A("mg"), rc(4)], [A("nbl")], (), -32.0, OP.mult, n=128)
-    ts(T.low[:], T.m64[:], cf(3), OP.is_gt, [A("m64"), rc(3)], [A("low")], n=128)
+    ts(T.gw[:, 8:16], T.m1[:, 0:8], cf(25), OP.is_equal, [A("m1"), rc(25)], [A("gw", 1, 2)], (), 2.0 ** 19, OP.mult)
+    ts(T.gw[:, 16:24], T.m1[:, 0:8], cf(25), OP.is_equal, [A("m1"), rc(25)], [A("gw", 2, 3)], (), -2.0 ** 19, OP.mult)
+    ts(T.gw[:, 24:32], T.gw[:, 0:8], -1.0, OP.mult, [A("gw", 0, 1)], [A("gw", 3, 4)])
+    ts(T.nbl[:], T.mg[:], cf(3), OP.is_equal, [A("mg"), rc(3)], [A("nbl")], (), -32.0, OP.mult, n=128)
+    ts(T.dup[:], T.m64[:], cf(4), OP.is_equal, [A("m64"), rc(4)], [A("dup")], n=128)
+    ts(T.low[:], T.m64[:], cf(4), OP.is_gt, [A("m64"), rc(4)], [A("low")], n=128)
     tt(T.t1[:], T.nbl[:], T.low[:], OP.mult, [A("nbl"), A("low")], [A("t1")], n=256)
     times(T.t2[:], T.dup[:], [A("t2")], [A("dup")], scale=2.0 * BIG)
     tt(T.am[:], T.t2[:], T.t1[:], OP.add, [A("t2"), A("t1")], [A("am")], n=256)
@@ -488,8 +485,9 @@ def rank_program(g, core, T, topo):
     def turned(s):
         ph, c = s % 2, (s // 2) % 4
         E, pe = MM(ph, c, "ef"), banks(ph)[0]
-        mms([(pe[:, 0:128], T.idn[:], T.c2k[:]), (pe[:, 0:128], T.ef[:, cls(ph, c)], T.idh[:]), (pe[:, 256:384], T.sm[:, cls(ph, c)], T.idn[:])],
+        mms([(pe[:, 0:128], T.idn[:], T.c2k[:]), (pe[:, 0:128], T.ef[:, cls(ph, c)], T.idh[:]), (pe[:, 128:256], T.sm[:, cls(ph, c)], T.idn[:])],
             384, E + MM(ph, c, "sm") + [A("idn"), A("idh"), A("c2k")], [ph])
+        act(T.es[:, 256 * ph:256 * ph + 256], pe[:, 0:256], AF.Copy, [], [A("es", ph, ph + 1)], [ph], n=256)
 
     def head(s):
         ph = s % 2
@@ -516,6 +514,13 @@ def rank_program(g, core, T, topo):
             tt(qq[:, QC + lo + 1:QC + hi:2], all_x.indirect(T.el16[:, 256 * s + 192 + lo // 32:256 * s + 192 + hi // 32]),
                T.bb[:, o.start:o.stop:2], OP.min, [RX, EL, ("bb", o.start, o.stop)], [("qo", o.start // 2, o.stop // 2)], cost=("gather", n // 2))
 
+    MOD = [A(name) for name in ("gw", "one", "cm", "idn", "nid", "i2040", "i75", "i155", "i4k", "n4k", "i32", "n32", "i19", "n19", "i128", "big", "nbig")]
+
+    def modulo(out, n, lines, half, up, down):
+        return [(o, q, T.gw[:, 24:32]) for o, q in lines] + [(out, c[:], T.one[:, 0:n]) for c in half] \
+            + [(out, up[:], T.cm[:, 0:n]), (out, down[:], T.cm[:, 0:n])] + [(o, q, T.gw[:, 0:8]) for o, q in lines] \
+            + [(out, T.idn[:], T.cm[:, 0:n]), (out, T.nid[:], T.cm[:, 0:n])]
+
     def hop(s, par):
         ph = s % 2
         pe = banks(ph)[0]
@@ -523,17 +528,18 @@ def rank_program(g, core, T, topo):
         qq = T["qq%d" % ph]
         z = 2 * ph + par
         stage(s, "hop%d" % par)
-        mms([(pu[:, k:64:8], qq[:, QC + 2 * k + par::16], T.gw[:, 0:8]) for k in range(8)], 512, [("qo" if par else "qe", 1024 * ph, 1024 * ph + 1024), A("gw")], [B])
-        o, o2 = slice(64 * z, 64 * z + 64), slice(128 * ph + par, 128 * ph + 128, 2)
+        mms(modulo(pu[:, 0:64], 64, [(pu[:, k:64:8], qq[:, QC + 2 * k + par::16]) for k in range(8)], (T.i2040, T.i75), T.i4k, T.n4k), 1408,
+            [("qo" if par else "qe", 1024 * ph, 1024 * ph + 1024)] + MOD, [B])
+        o = slice(64 * z, 64 * z + 64)
 
         def rg(b):
             return A(b, z, z + 1)
-        cp(T.ui[:, o2], pu[:, 0:64], [], [rg("ui")], [B])
-        ts(T.ua[:, o], T.ui[:, o2], 4095, OP.bitwise_and, [rg("ui")], [rg("ua")])
-        tt(T.ta[:, o], pe[:, par:128:2], T.ua[:, o], OP.mult, [rg("ua")], [rg("ta")], [ph])
+        tt(T.ta[:, o], pu[:, 0:64], T.es[:, 256 * ph + par:256 * ph + 128:2], OP.mult, [A("es", ph, ph + 1)], [rg("ta")], [B])
         ts(T.tb[:, o], T.ta[:, o], 5, OP.logical_shift_right, [rg("ta")], [rg("tb")])
-        k0 = 0 if s < 2 else 128
-        tt(T.tc[:, o], pe[:, k0 + par:k0 + 128:2], T.tb[:, o], OP.add, [rg("tb"), A("ek", ph, ph + 1)], [rg("tc")], [ph])
+        c, ek = (s // 2) % 4, pu[:, 64:128]
+        lst = [(ek, T.idn[:], T.c2k[:, 0:64]), (ek, T.ef[:, cls(ph, c)], T.idh[:, par::2]), (ek, T.idn[:], T.kb[:])][:2 if s < 2 else 3]
+        mms(lst, 64 * len(lst), MM(ph, c, "ef") + [A("idn"), A("idh"), A("c2k"), A("kb")], [B])
+        tt(T.tc[:, o], ek, T.tb[:, o], OP.add, [rg("tb")], [rg("tc")], [B])
         hh, HH = T.hh[:, 128 * s + par:128 * s + 128:2], A("hh", 2 * s + par, 2 * s + par + 1)
         ts(hh, T.tc[:, o], 4095, OP.bitwise_and, [rg("tc")], [HH])
         z0 = 17 * z
@@ -579,29 +585,30 @@ def rank_program(g, core, T, topo):
         hop(s, 0)
         hop(s, 1)
         stage(s, "gate0")
-        if UK:
-            ts(T.ub[:, o], T.ui[:, o], 31, OP.bitwise_and, [A("ui", 2 * ph, 2 * ph + 2)], [rg("ub")], n=128)
-            tt(T.us[:, o], pe[:, 256:384], T.ub[:, o], OP.mult, [rg("ub")], [rg("us")], [ph], n=128)
-        stage(s, "gate1")
         qq, Q = T["qq%d" % ph], [("qe", 1024 * ph, 1024 * ph + 1024), ("qo", 1024 * ph, 1024 * ph + 1024), A("gw")]
-        mmx([(pe[:, 384 + k:512:16], qq[:, QC + k::16], T.gw[:, 8:16], k == 0, False) for k in range(16)], 1024, Q, [ph])
-        mmx([(pe[:, 384:512], T.idn[:], T.cm[:], False, False), (pe[:, 384:512], T.nid[:], T.cm[:], False, False)], 256, [A("idn"), A("nid"), A("cm")], [ph])
-        mmx([(pe[:, 384 + k:512:16], qq[:, QC + k::16], T.gw[:, 16:24], False, k == 15) for k in range(16)], 1024, Q, [ph])
-        ts(T.ge[:, o], pe[:, 384:512], 7.5 * DEL, OP.is_lt, [], [rg("ge")], [ph], n=128)
-        stage(s, "gsg")
-        tt(T.gsg[:, o], pe[:, 256:384], T.ge[:, o], OP.mult, [rg("ge")], [rg("gsg")], [ph], n=128)
+        for par in range(2):
+            out, lines, cm = pe[:, par:128:2], [(pe[:, k:128:16], qq[:, QC + k::16]) for k in range(par, 16, 2)], T.cm[:, 0:64]
+            lst = [(a, q, T.gw[:, 8:16]) for a, q in lines] + [(out, T.i19[:], cm), (out, T.n19[:], cm)] \
+                + [(a, q, T.gw[:, 16:24]) for a, q in lines] + [(out, T.i128[:], T.one[:, 0:64]), (out, T.big[:], cm), (out, T.nbig[:], cm)] \
+                + modulo(out, 64, lines, (T.i155,), T.i32, T.n32)
+            for lo in range(0, 42, 14):
+                mmx([a + (j == 0, j == 41) for j, a in enumerate(lst)][lo:lo + 14], 896, [Q[par]] + MOD, [ph])
+        sig, ES = T.es[:, 256 * ph + 128:256 * ph + 256], A("es", ph, ph + 1)
+        stage(s, "gate1")
+        tt(T.us[:, o], pe[:, 0:128], sig, OP.mult, [ES], [rg("us")], [ph], n=128)
         look(s, 0)
         look(s, 1)
         stage(s, "score")
-        mmx([(pu[:, 384:512], T.sm[:, cls(ph, c)], T.nk[:], True, False), (pu[:, 384:512], T.nid[:], T.us[:, o], False, False)][:1 + UK], 128 + 128 * UK,
-            MM(ph, c, "sm") + [A("nk"), A("nid"), rg("us")], [2 + ph])
+        mmx([(pu[:, 384:512], T.sm[:, cls(ph, c)], T.nk[:], True, False)], 128, MM(ph, c, "sm") + [A("nk")], [2 + ph])
         for par in range(2):
+            if par:
+                mmx([(pu[:, 384:512], T.nid[:], T.us[:, o], False, False)], 128, [A("nid"), rg("us")], [2 + ph])
             mmx([(pu[:, 384 + k:512:16], T.sg[:, 2048 * ph + k:2048 * ph + 2048:16], T.g8[:], False, k == 15) for k in range(par, 16, 2)],
                 512, [("sg", 2048 * ph + 1024 * par, 2048 * ph + 1024 * par + 1024), A("g8")], [2 + ph])
         stage(s, "keys")
         kt, KT = T.kt[:, 128 * s:128 * s + 128], A("kt", s, s + 1)
-        tt(kt, pu[:, 384:512], T.gsg[:, o], OP.mult, [rg("gsg")], [KT], [2 + ph], n=128)
-        scn(T.sc[:, 128 * s:128 * s + 128], T.ke[:], kt, LOW, OP.min, OP.max, [A("ke"), KT], [A("sc", s, s + 1)], 128 if UK else 64)
+        tt(kt, pu[:, 384:512], sig, OP.mult, [ES], [KT], [2 + ph], n=128)
+        scn(T.sc[:, 128 * s:128 * s + 128], T.ke[:], kt, LOW, OP.min, OP.max, [A("ke"), KT], [A("sc", s, s + 1)], 128)
 
     def send(s, a, b, sm, w):
         t = s // 2
@@ -624,10 +631,10 @@ def rank_program(g, core, T, topo):
         tt(T.lm[:], T.sc[:, 128 * s:128 * s + 128].indirect(T.cl[:]), T.mr[:], OP.mult, [A("sc", s, s + 1), A("cl"), A("mr")], [A("lm")],
            cost=("gather", 128))
         kl = pu[:, 0:8]
-        mms([(kl, T.idn[:], T.zc[:]), (kl, T.lm[:], T.rcp[:])], 320 if UK else 128, [A("idn"), A("zc"), A("lm"), A("rcp")], [2 + ph])
-        ts(T.kn[:], kl, 32.0 * UK, OP.add, [], [A("kn")], [2 + ph])
+        mms([(kl, T.idn[:], T.zc[:]), (kl, T.lm[:], T.rcp[:])], 320, [A("idn"), A("zc"), A("lm"), A("rcp")], [2 + ph])
+        ts(T.kn[:], kl, 32.0, OP.add, [], [A("kn")], [2 + ph])
         tt(T.nf[:, 0:8], kl, T.thr[:], OP.is_gt, [A("thr")], [A("nf")], [2 + ph])
-        ts(T.li[:], T.kn[:], 5 * UK, OP.logical_shift_right, [A("kn")], [A("li")], (), 0x0F0F, OP.bitwise_and)
+        ts(T.li[:], T.kn[:], 5, OP.logical_shift_right, [A("kn")], [A("li")], (), 0x0F0F, OP.bitwise_and)
         ts(T.l16[:], T.li[:], cf(27), OP.add, [A("li"), rc(27)], [A("l16")])
         cp(T.qd[:, 128 * s:128 * s + 128], qq[:].indirect(T.l16[:]), [("qe", 1024 * ph, 1024 * ph + 1024), ("qo", 1024 * ph, 1024 * ph + 1024), A("l16")],
            [A("qd", s, s + 1)], cost=("gather", 128))
@@ -640,12 +647,7 @@ def rank_program(g, core, T, topo):
             lst += [(yb[:, 16 + 8 * b:24 + 8 * b], T.am2[:, r], T.nf[:, 0:8]), (yb[:, 16 + 8 * b:24 + 8 * b], T.nbl2[:, r], T.nfs[:, n0:n0 + 8])]
         mmx([a + (j == 0, False) for j, a in enumerate(lst)], 384, [A("am2"), A("nf"), A("nbl2"), NS, A("i32"), A("icn")], [5 + 2 * ph])
         stage(s, "tail2")
-        if UK:
-            ts(T.uwa[:], T.kn[:], 31, OP.bitwise_and, [A("kn")], [A("uwa")])
-        else:
-            mms([(pu[:, 32:40], T.wu[:, 15 - r:143 - r], T.qd[:, 128 * s + r:128 * s + 128:16]) for r in range(16)], 1024, [A("wu"), A("qd", s, s + 1)], [2 + ph])
-            cp(T.uwi[:], pu[:, 32:40], [], [A("uwi")], [2 + ph])
-            ts(T.uwa[:], T.uwi[:], 31, OP.bitwise_and, [A("uwi")], [A("uwa")])
+        ts(T.uwa[:], T.kn[:], 31, OP.bitwise_and, [A("kn")], [A("uwa")])
         cp(T.uwb[:], T.uwa[:], [A("uwa")], [A("uwb")])
         mmx([(yb[:, 16 + 8 * b:24 + 8 * b], T.dup2[:, 128 * b:128 * b + 128], T.uwb[:], False, b == 1) for b in range(2)], 128,
             [A("dup2"), A("uwb")], [5 + 2 * ph])
@@ -658,19 +660,7 @@ def rank_program(g, core, T, topo):
         mms([(pu[:, 48:49], T.one[:], T.nfs[:, 32 * ph + 8:32 * ph + 9]) for ph in range(2)], 128, [A("one"), A("nfs")], [3])
         ts(T.kcj[:], pu[:, 48:49], -1.0, OP.mult, [], [A("kcj")], [3], 8176.5, OP.add)
         ts(T.kap[:], pu[:, 48:49], -1.0, OP.mult, [A("kcj")], [A("kap")], [3], T.kcj[:], OP.subtract)
-        if "p" in ONV:
-            ts(T.kb[:], T.one[:], T.kap[:], OP.mult, [A("one"), A("kap")], [A("kb")], (), 8192.0, OP.add)
-
-    def plus_kappa(s):
-        ph, c = s % 2, (s // 2) % 4
-        pe = T["p%d" % ph]
-        if "p" in ONV:
-            mms([(pe[:, 128:256], T.idn[:], T.c2k[:]), (pe[:, 128:256], T.ef[:, cls(ph, c)], T.idh[:]), (pe[:, 128:256], T.idn[:], T.kb[:])], 384,
-                MM(ph, c, "ef") + [A("idn"), A("idh"), A("c2k"), A("kb")], [ph])
-        elif "k" in ONV:
-            ts(pe[:, 128:256], pe[:, 0:128], T.kap[:], OP.add, [A("kap")], [A("ek", ph, ph + 1)], [ph], n=128)
-        else:
-            act(pe[:, 128:256], pe[:, 0:128], AF.Identity, [A("kap")], [], [ph], n=128, bias=T.kap[:])
+        ts(T.kb[:], T.one[:, 0:64], T.kap[:], OP.mult, [A("one"), A("kap")], [A("kb")], (), 8192.0, OP.add)
 
     def update(s, bk, at=None):
         ph, t = s % 2, s // 2
@@ -719,13 +709,9 @@ def rank_program(g, core, T, topo):
         ya = banks(ph)[2]
         mms([(ya[:, 128 * b:128 * b + 128], T.dup2[:, 128 * b:128 * b + 128], T.lq[:, 128 * s:128 * s + 128]) for b in range(2)], 256,
             [A("dup2"), A("lq", s, s + 1)], [4 + 2 * ph])
-        if "q" in ONV:
-            cp(T.qw[:], ya[:, 0:256], [], [A("qw")], [4 + 2 * ph], n=256)
-        else:
-            act(T.qw[:], ya[:, 0:256], AF.Copy, [], [A("qw")], [4 + 2 * ph], n=256)
+        act(T.qw[:], ya[:, 0:256], AF.Copy, [], [A("qw")], [4 + 2 * ph], n=256, bias=2049.5)
         tt(T.av[:], win.indirect(lt), T.qw[:], OP.add, [WX, L, A("qw")], [A("av")], cost=("gather", 256))
-        ts(T.aw[:], T.av[:], 0.5, OP.mult, [A("av")], [A("aw")], (), 1279.75, OP.add, n=128)
-        ts(T.ax[:], T.aw[:], -1280.0 - (0.0 if last else DEL), OP.add, [A("aw")], [A("ax")], n=128)
+        ts(T.ax[:], T.av[:], 0.5, OP.mult, [A("av")], [A("ax")], (), -1025.0 - (0.0 if last else DEL), OP.add, n=128)
         cp(win.indirect(lt), T.ax[:], [A("ax"), L], [WX], cost=("scatter", 256))
         if last:
             back(ph, "sv")
@@ -754,7 +740,6 @@ def rank_program(g, core, T, topo):
         if s % 2 and s + 2 < ST:
             stage(s, "kappa")
             kappa()
-            plus_kappa(s + 1)
         if s not in LATE:
             update(s, s % 2)
         if s + 2 < ST:
@@ -762,8 +747,6 @@ def rank_program(g, core, T, topo):
             if s + 2 not in EARLY:
                 lists(s + 2, 2 + s % 2)
             turned(s + 2)
-            if s % 2:
-                plus_kappa(s + 2)
         else:
             for z in LATE:
                 if s == ST - 2:

@@ -15,65 +15,91 @@ DEL = 2.0 ** -10
 BIG = 8192.0
 KD = "float32"
 LOW = 32.625
-YS = (1024, 384)
+WIPE = 1.5 * 2.0 ** 38
+ESW = 264
+QW = 184
+KB = 1
+HASH = True
+EW = 256
+EV0 = 0
+UPD = "s"
+
+
+def RND(p):
+    return 1.5 * 2.0 ** (23 + p)
+
+
+YS = (768, 512)
 DCUT = (0, 1024, 2048)
-EV = 256
-EARLY = (2, 3)
+EV = 768
+EARLY = ()
 LATE = ()
-PARTS = ((("v", 1024),) * 4, ())
+ADD = False
+PARTS = ((("v", 1024),) * 4, (("s", 512),) * 1 + (("v", 512),) * 7)
 LOADS = ((("y", "e", 0), ("s", "e", 1), ("y", "m", 0), ("s", "m", 1), ("y", "x", 0), ("s", "x", 1)),
-         (("y", "e", 0), ("y", "e", 1), ("y", "m", 0), ("y", "m", 1), ("g", "a", 0), ("g", "a", 1)))
+         (("y", "e", 0), ("y", "e", 1), ("y", "m", 0), ("y", "m", 1), ("y", "x", 0), ("y", "x", 1)))
 GATE = 1
 STORES = ("yyyyy", "yyyyy")
 DIS = {"y": 0.5, "s": 0.5, "g": 1.8}
 DROW = 0.2
-RELU = ("VVSS", "SSSS")
+RELU = ("vvvv", "SSSS")
 
 SCRATCH = {"xw0": ("sbuf", [128, XW], "bfloat16"), "xw1": ("sbuf", [128, XW], "bfloat16"), "alt": ("sbuf", [128, 1024], "bfloat16")}
 for _n, _w, _d in (
         ("ei0", 1024, "int32"), ("ef", 1024, "float16"), ("mm", 1024, "bfloat16"), ("sm", 1024, "bfloat16"), ("ylb", 1024, "float32"),
         ("d0", 4096, "bfloat16"), ("bb", 4096, "bfloat16"), ("qq0", QC + 2048, "bfloat16"), ("qq1", QC + 2048, "bfloat16"), ("dq", 4096, "bfloat16"),
         ("sg", 4096, "bfloat16"), ("yb", 4096, "bfloat16"),
-        ("el16", 256 * ST, "uint16"), ("h16", 256, "uint16"),
-        ("es", 512, "float32"), ("ta", 256, "int32"), ("tb", 256, "int32"), ("tc", 256, "int32"), ("hh", 128 * ST, "int32"),
-        ("hf", 128 * ST, "float16"), ("eb", 256, "float32"), ("av", 256, "float16"), ("ax", 256, "bfloat16"),
-        ("qw", 256, "float32"), ("qd", 128 * ST, "bfloat16"), ("lq", 128 * ST, "bfloat16"), ("tg", 16 * ST, "uint16"), ("lt", 16 * ST, "uint16"),
-        ("pi", 1, "int32"), ("ci", 8, "int32"), ("cf", 32, "float32"), ("m1", 128, "float32"), ("m64", 128, "float32"), ("low", 128, "bfloat16"), ("t2", 128, "bfloat16"), ("si", 128, "float32"),
-        ("clf", 8, "float32"), ("cl", 8, "uint16"), ("icf", 16, "float32"), ("icn", 16, "bfloat16"), ("dum", 16, "int32"), ("mg", 128, "float32"),
-        ("zc", 8, "bfloat16"), ("thr", 8, "float32"), ("i32", 128, "bfloat16"),
-        ("dup2", 256, "bfloat16"), ("nbl2", 256, "bfloat16"), ("am2", 256, "bfloat16"), ("rcp", 8, KD), ("kb", 64, "bfloat16"), ("nbl", 128, "bfloat16"),
-        ("am", 128, "bfloat16"), ("mr", 128, "bfloat16"), ("z16", 16, "bfloat16"),
-        ("idn", 128, "bfloat16"), ("nid", 128, "bfloat16"), ("nk", 128, "bfloat16"),
-        ("idh", 128, "float16"), ("big", 128, "bfloat16"), ("nbig", 128, "bfloat16"), ("dup", 128, "bfloat16"),
-        ("g8", 8, "bfloat16"), ("gw", 32, "bfloat16"), ("i2040", 128, "bfloat16"), ("i75", 128, "bfloat16"), ("i155", 128, "bfloat16"),
-        ("i4k", 128, "bfloat16"), ("n4k", 128, "bfloat16"), ("n32", 128, "bfloat16"), ("cm", 128, "bfloat16"), ("cd", 128, "bfloat16"), ("id15", 128, "float16"), ("big15", 128, "bfloat16"), ("pm", 512, "float16"),
-        ("t1", 128, "bfloat16"), ("one", 128, "bfloat16"),
-        ("ke", 128, KD), ("c2k", 128, "bfloat16"),
-        ("i19", 128, "bfloat16"), ("n19", 128, "bfloat16"), ("i128", 128, "bfloat16"), ("kt", 128 * ST, KD), ("sc", 128 * ST, KD),
-        ("nw", 128 * ST, "bfloat16"), ("nf", 16, "bfloat16"), ("kn", 8, "int32"), ("li", 8, "int32"), ("lm", 128, KD), ("nfs", 64, "bfloat16"),
-        ("us", 256, "bfloat16"), ("l16", 8, "uint16"), ("uwa", 8, "int32"), ("uwb", 8, "bfloat16"), ("tgm", 16, "int32"),
-        ("kcj", 1, "bfloat16"), ("kap", 1, "float32")):
+        ("el16", 256 * ST, "uint16"), ("h16", 128 * ST, "uint16"),
+        ("es", 2 * ESW, "float32"), ("hf", 128 * ST, "float16"), ("av", 256, "float16"), ("ax", 256, "bfloat16"),
+        ("qw", 256, "float32"), ("qd", QW * ST, "bfloat16"), ("lq", QW * ST, "bfloat16"), ("lt", 16 * ST, "uint16"),
+        ("pi", 1, "int32"), ("ci", 8, "int32"), ("cf", 32, "float32"), ("m1", 128, "float32"), ("m64", 128, "float32"), ("low", 128, "bfloat16"), ("si", 128, "float32"),
+        ("clf", 16, "float32"), ("cl", 16, "uint16"), ("icf", 16, "float32"), ("icn", 16, "bfloat16"), ("mg", 128, "float32"),
+        ("zz", 128, "bfloat16"), ("mk32", 32, "bfloat16"), ("i31", 128, "bfloat16"),
+        ("dup2", 256, "bfloat16"), ("rcp", 80, KD), ("kb", 64, "float16"), ("nbl", 128, "bfloat16"),
+        ("mr", 128, "bfloat16"), ("z16", 16, "bfloat16"),
+        ("idn", 128, "bfloat16"), ("nid", 128, "bfloat16"), ("nk", 128, "bfloat16"), ("idf", 128, "float32"), ("nidf", 128, "float32"),
+        ("idh", 128, "float16"), ("nidh", 128, "float16"), ("ih32", 128, "float16"), ("big", 128, "bfloat16"), ("nbig", 128, "bfloat16"), ("dup", 128, "bfloat16"),
+        ("hdup", 128, "bfloat16"), ("ndup", 128, "bfloat16"), ("g8", 8, "bfloat16"), ("gw", 48, "bfloat16"),
+        ("cs", 576, "bfloat16"), ("ch", 320, "bfloat16"), ("ct", 112, "bfloat16"),
+        ("cd", 128, "bfloat16"), ("id15", 128, "float16"), ("big15", 128, "bfloat16"), ("pm", 512, "float16"),
+        ("p65", 512, "float16"), ("n65", 512, "float16"), ("pmt", 512, "float16"),
+        ("t1", 128, "bfloat16"), ("one", 128, "bfloat16"), ("non", 128, "bfloat16"), ("ke", 128, KD),
+        ("kt", 128 * ST, KD), ("sc", 128 * ST, KD),
+        ("nw", 128 * ST, "bfloat16"), ("lm", 128, KD),
+        ("kj", 16, "bfloat16"), ("kc", 1, "float32"), ("kl", 1, "float32"), ("kd", 1, "bfloat16"),
+        ("us", 512, "bfloat16"), ("l16", 8, "uint16")):
     SCRATCH[_n] = ("sbuf", [128, _w], _d)
-SCRATCH["hz"] = ("sbuf", [128, 68, 8], "float16")
+SCRATCH["hz"] = ("sbuf", [128, 68, 8], "float16" if HASH else "float32")
+SCRATCH["ta"] = SCRATCH["tb"] = ("sbuf", [128, 256], "int32")
 for _t in range(8):
-    SCRATCH["p%d" % _t] = ("psum", [128, 512], "float32")
-SEMAPHORES = ["cv", "cs", "cp", "cg", "ls"] + ["aq%d" % _t for _t in range(ST)] + ["at%d" % _t for _t in range(ST)] \
+    SCRATCH["p%d" % _t] = ("psum", [128, 128, 4], "float32")
+SEMAPHORES = ["cv", "cs", "cp", "cg", "ls"] + ["aq%d" % _t for _t in range(ST)] \
     + ["dm%d" % _t for _t in range(48)]
 
 ORDER = {}
 SEED = 4
 TRIES = 1700
-SWAPS = 9000
-HEAT2 = 0.08
+SWAPS = (36000, 36000, 1)
+HEAT2 = 0.04
 SHIFT = 2.5
 HEAT = 0.15
-PER = 10.5
-START = {"pre": -30.0, "fill": -29.0, "soon": -1.0, "next": 3.0, "e0": 0.0, "e1": 0.9, "d0": 0.1, "d1": 1.5, "d2": 2.5, "d3": 3.0, "g0": 1.8, "g1": 3.0, "g2": 3.7,
-         "g3": 4.2, "hop0": 2.5, "hop1": 5.5, "hf": 9.0, "gate0": 4.0, "gate1": 7.5, "gsg": 8.0, "y00": 5.3, "y01": 6.2, "s00": 7.1, "s01": 7.6, "y10": 8.2, "y11": 8.9, "s10": 9.3, "s11": 9.8, "v0": 5.0, "v1": 9.0, "score": 8.0,
-         "keys": 11.0, "nw": 15.0, "tail1": 11.5, "tail2": 14.0, "kappa": 12.5, "update": 16.0, "late": 17.0, "prep": 16.5, "arrive": 18.0}
-FIRST = ()
-MACHINES = ((0.89, 0.74, 0.75, 0.9, 1.0, 0.0, 0.9), (1.2, 1.45, 1.9, 1.2, 1.0, 0.0, 1.25))
-LAND = (1.9, 1.4)
+PER = 9.8
+SOON = (0.5, 4.0)
+FIRST = {"e1.s1": 2.0, "d1.s1": 1.0, "g0.v2": 2.0, "g1.v1": 2.7, "g1.v2": 3.3, "hop0.p2": 4.0, "hop0.p3": 4.1, "hop0.v1": 4.9, "hx0.v1": 5.2, "hx0.v2": 5.5,
+         "hop0.p5": 5.6, "hop0.p6": 5.7, "hop0.v2": 6.0, "gate0.v1": 5.3, "y00.s1": 6.1, "y01.s1": 6.2, "hop1.p2": 4.5, "hop1.p3": 4.6, "y00.p2": 6.5, "s00.s1": 6.9,
+         "y10.s1": 6.85, "v0.v1": 6.3, "v0.v2": 7.2}
+EM = (0, 1, 2, 3)
+GAP = 0.8
+ENDS = 0.6
+START = {"fill": (-9.0, 0.1), "next": (1.0, 0.3), "back0": (11.0, 0.1), "back1": (17.0, 0.1), "store": (14.0, 0.1), "keep": (12.0, 0.5), "load": (-12.0, 0.1), "add": (-4.0, 0.1),
+         "late1": (12.5, 0.2), "late2": (15.0, 0.2), "late3": (17.5, 0.2), "update": (12.3, 0.1)}
+PLAN7 = """9.10 e0.v1 -0.13 -0.58 e0.v2 -0.63 -0.08 e1.s1 -0.43 -0.38 d0.s1 0.00 0.05 g0.v1 1.44 1.49 g0.v2 2.52 2.68 d1.s1 1.84 1.39 g1.v1 3.38 3.33 g1.v2 4.02 3.97 hop0.p1 -4.89 -4.84 hop0.p2 0.41 0.46 hop0.p3 0.80 0.86 hop0.v1 1.32 1.37 hx0.v1 2.14 2.19 hx0.v2 3.17 2.58 hop0.p4 -2.56 -2.50 hop0.p5 3.32 2.83 hop0.p6 3.42 2.89 hop0.v2 3.87 3.82 gate0.v1 4.95 4.89 hop1.p1 -1.27 -1.22 hop1.p2 4.72 4.66 hop1.p3 5.11 5.06 hop1.v1 5.63 5.58 hx1.v1 5.89 5.84 hx1.v2 6.15 6.09 hop1.p4 5.86 5.81 hop1.p5 6.29 6.24 hop1.p6 6.35 6.30 hop1.v2 6.72 6.67 gate1.v1 5.73 5.68 y00.s1 4.02 3.97 y00.p1 2.53 2.58 y00.p2 5.99 5.93 s00.s1 6.29 6.24 y01.s1 4.75 4.70 y01.p1 4.02 3.97 y01.p2 6.72 6.67 s01.s1 7.60 7.55 y10.s1 6.86 6.81 y10.p1 7.06 7.00 y10.p2 7.70 7.65 s10.s1 8.16 8.11 v1.v1 6.98 6.93 v1.v2 8.26 8.20 score.p1 6.91 6.86 score.p2 7.02 6.97 score.p3 8.26 8.21 score.p4 8.57 8.52 score.p5 8.82 8.77 keys.v1 9.52 9.47 keys.v2 9.83 9.78 tail1.v1 10.14 10.09 tail1.p1 10.36 10.30 tail1.p2 10.45 10.40 tail1.v2 11.09 11.04 tail1.v3 11.19 11.14 tail1.v4 11.40 11.35 tail2.v1 11.60 11.55 tail2.g1 11.72 11.67 tail2.a1 12.51 12.46 lists.p1 11.34 11.29 lists.v1 13.73 13.78 turn.p1 10.86 10.81 turn.s1 11.84 12.29 kappa.s1 10.45 10.45 kappa.s2 10.77 10.77 kappa.p1 11.05 11.05 kappa.v1 12.38 12.38 arrive.p1 14.56 14.61 arrive.p2 10.74 10.68 arrive.p3 14.73 14.78 arrive.v1 15.05 15.10 arrive.s1 14.85 14.90 arrive.v2 15.30 15.35 arrive.v3 15.88 15.93 arrive.v4 16.69 16.74"""
+PLAN = """9.06 e0.v1 0.12 0.15 e0.v2 -0.23 -0.20 e0.v3 1.00 1.03 e1.s1 1.52 1.37 d0.s1 0.00 0.03 g0.v1 1.54 1.57 g0.v2 2.57 2.59 d1.s1 1.95 1.80 g1.v1 3.58 3.61 g1.v2 4.28 4.26 hop0.p1 0.99 1.02 hop0.p2 2.05 1.90 hop0.p3 2.45 2.30 hop0.v1 3.22 3.25 hx0.v1 3.48 3.51 hx0.v2 4.18 4.11 hop0.p4 2.84 3.04 hop0.p5 4.32 4.25 hop0.p6 4.39 4.31 hop0.v2 4.94 4.91 gate0.v1 3.32 3.35 hop1.p1 0.85 0.88 hop1.p2 4.98 4.95 hop1.p3 5.37 5.34 hop1.v1 5.89 5.86 hx1.v1 6.15 6.12 hx1.v2 6.41 6.38 hop1.p4 4.63 4.56 hop1.p5 6.55 6.52 hop1.p6 6.61 6.58 hop1.v2 7.02 6.99 gate1.v1 5.99 5.96 y00.s1 5.08 5.05 y00.p1 2.97 3.17 y00.p2 6.12 6.09 s00.s1 6.83 6.80 y01.s1 6.40 6.37 y01.p1 6.98 6.95 y01.p2 7.14 7.11 s01.s1 8.13 8.10 v0.v1 5.31 5.28 v0.v2 6.51 6.48 y10.s1 7.39 7.36 y10.p1 7.49 7.46 y10.p2 8.23 8.20 s10.s1 8.53 8.50 v1.v1 7.33 7.30 v1.v2 8.60 8.57 score.p1 6.86 6.83 score.p2 8.41 8.38 score.p3 8.57 8.54 score.p4 8.88 8.85 score.p5 9.19 9.16 keys.v1 9.62 9.59 keys.v2 9.93 9.90 tail1.v1 10.44 10.41 tail1.p1 9.85 9.82 tail1.p2 10.68 10.65 tail1.v2 11.13 11.10 tail1.v3 11.23 11.20 tail1.v4 11.38 11.35 tail2.v1 11.58 11.55 tail2.g1 11.70 11.67 tail2.a1 12.49 12.46 lists.p1 11.76 12.85 lists.v1 14.07 14.10 turn.p1 9.50 9.47 turn.s1 12.21 12.53 kappa.s1 10.41 10.41 kappa.s2 12.36 12.36 kappa.p1 12.63 12.63 kappa.v1 13.14 13.14 arrive.p1 14.80 14.83 arrive.p2 9.72 9.69 arrive.p3 14.97 15.00 arrive.v1 15.29 15.32 arrive.s1 15.09 15.12 arrive.v2 15.71 15.74 arrive.v3 16.20 16.23 arrive.v4 17.01 17.04"""
+PLAN5 = """9.15 e0.v1 -0.04 -0.04 e0.v2 0.31 0.31 e0.v3 0.81 0.81 e1.s1 1.34 1.34 d0.s1 0.00 0.00 g0.v1 1.67 1.67 g0.v2 2.69 2.69 d1.s1 1.95 1.77 g1.v1 3.96 3.96 g1.v2 4.61 4.61 hop0.p1 0.95 0.95 hop0.p2 1.99 1.99 hop0.p3 2.39 2.39 hop0.v1 3.34 3.34 hx0.v1 3.61 3.60 hx0.v2 3.86 3.86 hop0.p4 1.09 1.09 hop0.p5 4.00 4.00 hop0.p6 4.07 4.07 hop0.v2 4.46 4.46 gate0.v1 3.45 3.70 hop1.p1 -1.71 -1.71 hop1.p2 5.30 5.30 hop1.p3 5.69 5.69 hop1.v1 6.21 6.21 hx1.v1 6.47 6.47 hx1.v2 6.73 6.73 hop1.p4 4.31 4.31 hop1.p5 6.87 6.87 hop1.p6 6.93 6.93 hop1.v2 7.30 7.30 gate1.v1 6.31 6.31 y00.s1 4.60 4.60 y00.p1 4.78 4.56 y00.p2 6.44 6.44 s00.s1 6.75 6.75 y01.s1 5.68 5.68 y01.p1 7.18 7.18 y01.p2 7.34 7.34 s01.s1 8.18 8.18 v0.v1 5.26 5.26 v0.v2 5.87 5.87 y10.s1 7.45 7.45 y10.p1 7.57 7.57 y10.p2 8.28 8.28 s10.s1 8.58 8.58 v1.v1 7.57 7.57 v1.v2 8.84 8.84 score.p1 8.46 8.46 score.p2 8.58 8.58 score.p3 8.62 8.62 score.p4 8.93 8.93 score.p5 9.25 9.25 keys.v1 9.80 9.80 keys.v2 10.31 10.31 tail1.v1 10.62 10.62 tail1.p1 10.00 10.00 tail1.p2 10.85 10.85 tail1.v2 11.31 11.31 tail1.v3 11.41 11.41 tail1.v4 11.56 11.56 tail2.v1 11.76 11.76 tail2.g1 11.88 11.88 tail2.a1 12.67 12.67 lists.p1 12.15 12.28 lists.v1 14.75 14.75 turn.p1 11.93 13.71 turn.s1 14.48 14.48 kappa.s1 10.92 10.92 kappa.s2 10.93 10.93 kappa.p1 11.93 11.93 kappa.v1 12.86 12.86 arrive.p1 15.24 15.24 arrive.p2 13.59 13.59 arrive.p3 15.40 15.40 arrive.v1 15.72 15.72 arrive.s1 15.52 15.52 arrive.v2 15.98 15.98 arrive.v3 16.55 16.55 arrive.v4 17.36 17.36"""
+PLAN4 = """9.80 e1.s1 -1.34 -1.34 d0.s1 0.00 0.00 g0.v1 2.35 2.35 g0.v2 3.21 3.11 d1.s1 1.52 1.34 g1.v1 3.86 3.76 g1.v2 4.50 4.40 hop0.p1 -2.35 -2.35 hop0.p2 0.44 0.44 hop0.p3 0.83 0.83 hop0.v1 1.37 1.37 hx0.v1 1.67 1.67 hx0.v2 2.95 2.84 hop0.p4 2.55 2.20 hop0.p5 3.27 2.99 hop0.p6 3.33 3.05 hop0.v2 4.35 4.25 gate0.v1 5.80 5.80 hop1.p1 -3.44 -3.19 hop1.p2 5.57 5.57 hop1.p3 5.97 5.97 hop1.v1 6.49 6.49 hx1.v1 6.75 6.75 hx1.v2 7.01 7.01 hop1.p4 6.75 6.75 hop1.p5 7.15 7.15 hop1.p6 7.21 7.21 hop1.v2 7.73 7.73 gate1.v1 7.84 7.84 y00.s1 4.50 4.39 y00.p1 3.02 2.67 y00.p2 6.88 6.88 s00.s1 7.18 7.18 y01.s1 5.85 5.85 y01.p1 6.37 6.50 y01.p2 7.60 7.60 s01.s1 7.90 7.90 v1.v1 7.99 7.99 v1.v2 9.40 9.40 score.p1 8.69 8.69 score.p2 8.80 8.80 score.p3 8.83 8.83 score.p4 9.14 9.14 score.p5 9.93 9.93 keys.v1 10.36 10.36 keys.v2 10.67 10.67 tail1.v1 10.98 10.98 tail1.p1 11.03 11.03 tail1.p2 11.22 11.22 tail1.v2 11.62 11.62 tail1.v3 11.73 11.73 tail1.v4 11.88 11.88 tail2.v1 12.07 12.07 tail2.g1 12.20 12.20 tail2.a1 12.99 12.99 hf.v1 9.89 9.89 nw.v1 11.28 11.28 update.p1 11.50 11.85 update.p2 11.79 12.14 update.v1 12.75 12.86 update.s1 12.95 13.05 lists.p1 12.13 12.48 lists.v1 14.85 14.96 turn.p1 13.28 13.39 turn.s1 16.39 16.39 kappa.s1 11.15 11.15 kappa.p1 11.50 11.50 kappa.v1 12.65 12.65 arrive.p1 15.03 15.03 arrive.p2 8.56 8.56 arrive.p3 15.19 15.19 arrive.v1 15.50 15.50 arrive.s1 15.31 15.31 arrive.v2 15.76 15.76 arrive.v3 16.40 16.40 arrive.v4 16.91 16.91"""
+PLAN3 = """9.24 e1.s1 -1.34 -1.30 d0.s1 0.00 0.04 g0.v1 1.56 1.48 g0.v2 2.42 2.35 d1.s1 1.52 1.38 g1.v1 3.18 3.10 g1.v2 3.83 3.75 hop0.p1 -0.64 -0.60 hop0.p2 0.33 0.58 hop0.p3 0.94 0.97 hop0.v1 1.45 1.97 hop0.p4 -3.00 -2.96 hop0.p5 2.03 2.12 hop0.p6 2.46 2.43 hop0.v2 3.07 3.00 gate0.v1 3.67 3.59 hop1.p1 -1.60 -1.44 hop1.p2 4.52 4.44 hop1.p3 4.92 4.84 hop1.v1 5.43 5.35 hop1.p4 4.39 5.23 hop1.p5 5.58 5.54 hop1.p6 5.89 5.85 hop1.v2 6.39 6.35 gate1.v1 6.50 6.46 y00.s1 3.22 3.14 y00.p1 2.84 2.81 y00.p2 4.20 4.24 s00.s1 5.22 5.25 y01.s1 4.48 4.52 y01.p1 3.22 3.14 y01.p2 5.32 5.35 s01.s1 5.78 5.82 y10.s1 6.54 6.50 y10.p1 6.84 6.80 y10.p2 7.22 7.18 s10.s1 7.48 7.44 v1.v1 6.66 6.62 v1.v2 7.61 7.57 score.p1 6.70 6.66 score.p2 6.81 6.77 score.p3 7.48 7.32 score.p4 7.93 7.77 score.p5 8.03 7.99 keys.v1 8.46 8.42 keys.v2 8.77 8.73 tail1.v1 9.08 9.04 tail1.p1 8.77 8.73 tail1.p2 9.32 9.28 tail1.v2 9.72 9.68 tail1.v3 9.83 9.79 tail1.v4 9.98 9.94 tail2.v1 10.17 10.13 tail2.g1 10.29 10.26 tail2.a1 11.08 11.05 hf.v1 7.93 7.90 nw.v1 9.28 9.24 update.p1 8.34 8.30 update.p2 9.60 9.96 update.v1 10.25 10.29 update.s1 11.96 12.09 lists.p1 10.61 10.57 lists.v1 11.31 11.28 turn.p1 12.62 12.70 turn.s1 16.32 16.35 kappa.s1 10.58 10.58 kappa.p1 10.91 10.91 kappa.v1 11.55 11.55 arrive.p1 13.12 13.09 arrive.p2 7.36 6.48 arrive.p3 13.29 13.25 arrive.v1 13.64 13.71 arrive.s1 13.41 13.37 arrive.v2 13.89 13.97 arrive.v3 14.39 14.47 arrive.v4 14.70 14.78"""
+MACHINES = ((0.89, 0.74, 0.75, 0.9, 1.0, 0.0, 0.9), (1.2, 1.45, 1.9, 1.2, 1.0, 0.5, 1.4), (0.87, 1.08, 0.6, 0.87, 1.3, 1.5, 1.12), (1.1, 0.85, 1.4, 1.5, 1.3, 0.5, 1.15))
+LAND = 2.0
 WAKE = (0.15, 0.04)
 MORE = {"p": 0.08, "s": 0.06}
 CALL = 0.75
@@ -84,7 +110,7 @@ PCY = 0.00038
 PFX = 0.01
 PGR = 0.07
 SX = 0.08
-OUTL = (10, 5, 6)
+OUTL = (4.5, 4.5, 1.0)
 GAT = 0.0016
 SCA = 0.003
 DLAT = 1.5
@@ -92,6 +118,170 @@ DBW = 0.33e6
 
 
 def arrange(nodes, before):
+    n = len(nodes)
+    rn = range(n)
+    qs = ["vspgy".find(d["q"] or "-") for d in nodes]
+    late = [d["late"] for d in nodes]
+    pre, anc, last = [], [0] * n, {}
+    for i, d in enumerate(nodes):
+        lag = {}
+        for j, x in before[i]:
+            lag[j] = max(x, lag.get(j, 0.0))
+        if d["kind"] == "d" and d["tag"][0] < 0:
+            if d["q"] in last:
+                lag.setdefault(last[d["q"]], 0.0)
+            last[d["q"]] = i
+        keep = []
+        for j in sorted(lag, reverse=True):
+            if not anc[i] >> j & 1 or late[j]:
+                keep.append((j, lag[j]))
+            anc[i] |= anc[j] | 1 << j
+        pre.append(keep)
+    pj = [[j for j, _ in b] for b in pre]
+    waits = [set(p) for p in pj]
+    w = PLAN.split()
+    plan = {a: (float(x), float(y)) for a, x, y in zip(w[1::3], w[2::3], w[3::3])}
+    cnt, alike, kind, key = {}, {}, [], [None] * n
+    for i, d in enumerate(nodes):
+        s, name = d["tag"]
+        cnt[(s, name, d["q"])] = c = cnt.get((s, name, d["q"]), 0) + 1
+        k = "%s.%s%d" % (name, d["q"] or "a", c)
+        if k in plan:
+            key[i] = s * float(w[0]) + (FIRST.get(k, plan[k][0]) if s == 0 else plan[k][s % 2])
+        elif name in START:
+            key[i] = max(s, 0) * float(w[0]) + START[name][0] + START[name][1] * c
+        kind.append((k, s % 2) if k in plan else i)
+        alike.setdefault(kind[i], []).append(i)
+    need = [1e9] * n
+    for i in reversed(rn):
+        if key[i] is None:
+            key[i] = need[i] - nodes[i]["cost"]
+        for j, x in pre[i]:
+            need[j] = min(need[j], key[i] - x)
+    for i in rn:
+        if nodes[i]["tag"][1] in ("pre", "soon"):
+            key[i] = SOON[0] * key[i] - SOON[1]
+    extra = [kind[i] == i and nodes[i]["kind"] == "c" for i in rn]
+    bare = [dict(d, q=None, cost=0.0, fix=0.0) if x else d for d, x in zip(nodes, extra)]
+    end = list(polish(bare, pre, key, (), 0)[2])
+    cost = lengths(nodes, MACHINES[EM[0]])
+    for i in rn:
+        key[i] = end[i] - (0.0 if extra[i] else cost[i])
+    need, busy = [1e9] * n, {q: sorted((key[i], end[i]) for i in rn if nodes[i]["q"] == q and not extra[i]) for q in "vspg"}
+    for i in reversed(rn):
+        if extra[i]:
+            need[i] = min(need[i], end[-1] - 4.0) - cost[i]
+        for j, x in pre[i]:
+            need[j] = min(need[j], (need[i] if extra[i] else key[i]) - x)
+    for i in sorted((i for i in rn if extra[i]), key=lambda i: need[i]):
+        at = ready = max([end[j] + x for j, x in pre[i]] + [0.0])
+        gaps = busy[nodes[i]["q"]]
+        for a, b in gaps:
+            if at + cost[i] <= a + 0.02:
+                break
+            at = max(at, b)
+        if at > need[i]:
+            at = max(ready, min([need[i]] + [a - 1e-3 for a, b in gaps if a <= need[i] < b]))
+        key[i], end[i] = at, at + cost[i]
+        gaps.append((at, end[i]))
+        gaps.sort()
+    for lo, hi, free, swaps in ((-1, 5, range(-1, 3), SWAPS[0]), (ST - 5, ST, range(ST - 3, ST), SWAPS[1]), (-1, ST, range(-1, ST), SWAPS[2])):
+        ids = [i for i in rn if lo <= nodes[i]["tag"][0] <= hi]
+        at = {j: i for i, j in enumerate(ids)}
+        best = polish([nodes[i] for i in ids], [[(at[j], x) for j, x in pre[i] if j in at] for i in ids], [key[i] for i in ids], free, swaps)
+        for i, x in zip(ids, best[4]):
+            if nodes[i]["tag"][0] in free:
+                key[i] = x
+    return best
+
+
+def lengths(nodes, m):
+    f = {"p": m[3], "v": m[0], "s": m[0], "gather": m[1], "scatter": m[2]}
+    return [d["fix"] * m[0] + (d["cost"] - d["fix"]) * (f.get(d["by"], 1.0) if d["kind"] == "c" else 1.0) for d in nodes]
+
+
+def polish(nodes, pre, key, free, swaps):
+    n = len(nodes)
+    rn = range(n)
+    qs = ["vspgy".find(d["q"] or "-") for d in nodes]
+    late = [d["late"] for d in nodes]
+    pj = [[j for j, _ in b] for b in pre]
+    waits = [set(p) for p in pj]
+    sets = []
+    for fc, fg, fs, fp, fw, more, whole in [MACHINES[m] for m in EM]:
+        f = {"p": fp, "v": fc, "s": fc, "gather": fg, "scatter": fs}
+        sets.append(([d["fix"] * fc + (d["cost"] - d["fix"]) * (f.get(d["by"], 1.0) if d["kind"] == "c" else 1.0) for d in nodes],
+                     [[(j, late[j] + (more if nodes[j]["kind"] == "a" else 0.0) + fw * (x - late[j]) if x else 0.0) for j, x in b] for b in pre], whole))
+    ends = [i for i in rn if nodes[i]["tag"][0] >= nodes[-1]["tag"][0] - 1]
+
+    def judge(at):
+        for i in rn:
+            x = at[i]
+            for j in pj[i]:
+                if at[j] >= x:
+                    x = at[j] + 1e-6
+            at[i] = x
+        order, res = sorted(rn, key=lambda i: at[i]), []
+        for cost, pr, whole in sets:
+            end, why, last = [0.0] * n, [-1] * n, [-1] * 5
+            for i in order:
+                r, w = 0.0, -1
+                for j, x in pr[i]:
+                    e = end[j] + x
+                    if e > r:
+                        r = e
+                        w = j
+                q = qs[i]
+                if q >= 0:
+                    j = last[q]
+                    if j >= 0 and end[j] >= r:
+                        r = end[j]
+                        w = j
+                    last[q] = i
+                end[i] = r + cost[i]
+                why[i] = w
+            top = max(ends, key=lambda i: end[i] + late[i])
+            res.append((end[top] + late[top], end, why, top))
+        return sum(x[0] / s[2] for x, s in zip(res, sets)) / len(sets), order, res[0][1], res, at
+    seed = [SEED]
+
+    def rnd():
+        seed[0] = (seed[0] * 1103515245 + 12345) % 2147483648
+        return seed[0] / 2147483648
+    best = cur = judge(key)
+    for it in range(swaps):
+        _, _, why, i = cur[3][int(rnd() * len(sets))]
+        at, pairs = cur[4], []
+        while i >= 0:
+            j = why[i]
+            if j >= 0 and j not in waits[i] and (nodes[i]["tag"][0] in free or nodes[j]["tag"][0] in free):
+                pairs.append((j, i))
+            i = j
+        if not pairs:
+            continue
+        j, i = pairs[int(rnd() * len(pairs))]
+        x = at[i] - at[j] + (1e-3, 1e-3, 0.3, 1.0, 3.0)[int(rnd() * 5)] * rnd()
+        if nodes[j]["tag"][0] not in free or nodes[i]["tag"][0] in free and rnd() < 0.5:
+            move, todo = {i: -x}, [i]
+            while todo:
+                for b in pj[todo.pop()]:
+                    if b not in move and at[b] > at[i] - x:
+                        move[b] = at[i] - x - 1e-4 - at[b]
+                        todo.append(b)
+        else:
+            move = {j: x}
+        new = list(at)
+        for a, x in move.items():
+            new[a] += x
+        r = judge(new)
+        if r[0] - cur[0] < -math.log(1e-9 + rnd()) * (HEAT2 * (1.0 - it / swaps) + 0.003):
+            cur = r
+            if r[0] < best[0]:
+                best = r
+    return best
+
+
+def old_arrange(nodes, before):
     n = len(nodes)
     qs = [d["q"] for d in nodes]
     cost = [d["cost"] for d in nodes]
@@ -229,7 +419,7 @@ def arrange(nodes, before):
             cur, key = r, new
             if r[0] < best[0]:
                 best = r
-    return best[:3]
+    return best
 
 
 def rank_program(g, core, T, topo):
@@ -262,10 +452,11 @@ def rank_program(g, core, T, topo):
                 if l < hi and lo < h:
                     d.add(i)
         me = len(nodes)
-        by = q
+        by, fix = q, 0.0
         if isinstance(cost, tuple):
             by, n = cost
-            cost = (0.05 if q == "v" else 0.065 + SX) + n * (GAT if by == "gather" else SCA)
+            fix = 0.05 if q == "v" else 0.065 + SX
+            cost = fix + n * (GAT if by == "gather" else SCA)
         order = set()
         for b in B:
             prev, cur = bank.get(b, ([], []))
@@ -275,7 +466,7 @@ def rank_program(g, core, T, topo):
             if cur and q == "p":
                 order.add(cur[-1])
             bank[b] = (prev, cur + [me])
-        nodes.append({"q": q, "calls": calls, "cost": cost, "deps": d, "order": order - d, "kind": kind, "key": key, "late": late, "tag": tag[0], "by": by})
+        nodes.append({"q": q, "calls": calls, "cost": cost, "deps": d, "order": order - d, "kind": kind, "key": key, "late": late, "tag": tag[0], "by": by, "fix": fix})
         for (b, lo, hi) in W:
             wr[b] = [e for e in wr.get(b, ()) if not (lo <= e[0] and e[1] <= hi)] + [(lo, hi, me)]
             rd[b] = [e for e in rd.get(b, ()) if not (lo <= e[0] and e[1] <= hi)]
@@ -339,15 +530,16 @@ def rank_program(g, core, T, topo):
     fill(T.alt[:, 0::2], 4096.0, [A("alt", 0, 1)], 256)
     fill(T.alt[:, 1::2], DEL, [A("alt", 1, 2)], 256)
     stage(-1, "fill")
-    for lo in range(XC, XR, 1024):
+    for lo in range(XC, XR, 1024) if ADD else ():
         act(T.xw1[:, lo:lo + 1024], T.alt[:], AF.Copy, [A("alt")], [A("in1", lo, lo + 1024)], n=1024, scale=0.0, bias=-DEL)
-    stage(-1, "pre")
+    stage(-1, "load")
     gate, issued, landed = (), {"y": 0.0, "s": 0.0, "g": 0.0}, 0.0
     for ph in range(2):
         done, when = [], []
         for q, what, b in LOADS[ph]:
             rows, o, i = slice(64 * b, 64 * b + 64), slice(512 * ph, 512 * ph + 512), (slice(64 * ph, 64 * ph + 64), slice(512 * b, 512 * b + 512))
             if what == "a":
+                stage(-1, "add")
                 issued[q] += DIS[q]
                 landed = max(landed, issued[q] + DLAT) + 1048576 / DBW + DROW
                 added = dma(q, T.xw1[rows, XC:XR], T.xt[i[0], :], [A("in1")], [A("xw1", XC + 2048 * b, XC + 2048 * b + 2048)], landed - issued[q], gate,
@@ -363,14 +555,16 @@ def rank_program(g, core, T, topo):
             when.append(landed)
         gate = done[GATE:GATE + 1]
         issued["y"] = issued["g"] = max(issued["y"], when[GATE])
-    dma("y", T.xw1[:, XR + XC:2 * XR], T.xt[:], [], [A("xw1", XR + XC, 2 * XR)], DLAT + 1048576 / DBW + DROW, (added,))
+    if ADD:
+        dma("y", T.xw1[:, XR + XC:2 * XR], T.xt[:], [], [A("xw1", XR + XC, 2 * XR)], DLAT + 1048576 / DBW + DROW, (added,))
+    stage(-1, "pre")
 
     def convert(ph, first):
         o = slice(512 * ph + first, 512 * ph + 512, 4)
         ts(T.ef[:, o], T.ei0[:, o], -2048.0, OP.add, [A("ei0%d" % ph)], MM(ph, first, "ef"), n=128)
         if first == 0:
             o = slice(512 * ph, 512 * ph + 512)
-            ts(T.sm[:, o], T.mm[:, o], -2.0, OP.mult, MM(ph), MM(ph, None, "sm"), (), 1.0, OP.add, n=256)
+            act(T.sm[:, o], T.mm[:, o], AF.Copy, MM(ph), MM(ph, None, "sm"), n=512, scale=-2.0, bias=1.0)
             lo = XC
             for q, w in PARTS[ph]:
                 rg, R = A("xw%d" % ph, lo, lo + w), A("xw%d" % ph, XR + XC, XR + XC + 4096)
@@ -386,11 +580,52 @@ def rank_program(g, core, T, topo):
     iota(T.one[:], [[0, 128]], 1, 0, [A("one")], 128)
     node("g", [lambda e: e.affine_select(T.idn[:], T.one[:], [[1, 128]], OP.is_equal, 0.0, 0, -1)], 0.17 + 256 * CYC, [A("one")], [A("idn")])
     iota(T.m64[:], [[0, 2], [1, 64]], 0, 0, [A("m64")], 128)
-    iota(T.clf[:], [[16, 8]], 15, 0, [A("clf")], 8)
+    iota(T.clf[:], [[16, 16]], 15, 0, [A("clf")], 16)
     iota(T.mg[:], [[0, 2], [16, 4], [0, 16]], 0, 0, [A("mg")], 128)
     iota(T.si[:], [[0, 8], [1, 16]], 0, 0, [A("si")], 128)
     iota(T.icf[:], [[16, 16]], 0, 1, [A("icf")], 16)
-    iota(T.zc[:], [[8192, 8]], 8192, 0, [A("zc")], 8)
+    iota(T.non[:], [[0, 128]], -1, 0, [A("non")], 128)
+
+    def C(p, a, b, step=1):
+        if step == 1:
+            return p[:, a // 4:b // 4, :] if b - a > 1 else p[:, a // 4, a % 4:a % 4 + 1]
+        return p[:, a // 4:b // 4, a % 4::2] if step == 2 else p[:, a // 4:b // 4:step // 4, a % 4]
+
+    def rows(name, n, vals, on_g=False):
+        if n and on_g:
+            iota(T[name][0:65, :], [[0, n]], 0, 0, [A(name)], n)
+        elif n:
+            fill(T[name][0:65, :], 0.0, [A(name)], n // 2)
+        for j, (r, cols, v) in enumerate(vals):
+            w = len(range(cols.start, cols.stop, cols.step or 1))
+            if isinstance(v, tuple):
+                iota(T[name][r:r + 1, cols], v[0], v[1], 0, [A(name, j, j + 1)], w)
+            elif on_g:
+                where(T[name][0:r + 1, cols], [[0, w]], OP.not_equal, v, -r, 1, A(name, cols.start, cols.stop))
+            else:
+                act(T[name][r:r + 1, cols], T.m1[r:r + 1, 0:w] if w <= 128 else T.alt[r:r + 1, 0:w], AF.Copy, [A("m1"), A("alt")], [A(name, j, j + 1)], n=w,
+                    scale=0.0, bias=v)
+
+    def where(ap, pat, op, v, base, cm, W, src=None):
+        a, R = src or (ap, W)
+        node("g", [lambda e: e.affine_select(ap, a, pat, op, v, base, cm)], 0.17 + 2 * math.prod(c for _, c in pat) * CYC, [R], [W])
+
+    def diagonal(name, v, lo=0, both=False):
+        ap, W, pat = T[name][:, lo:lo + 128], A(name, lo, lo + 128), [[0, 2], [1, 64]] if both else [[1, 128]]
+        where(ap, pat, OP.not_equal, v, 64 * (lo > 0), -1, W, (T.zz[:], A("zz")))
+        if both is True:
+            where(ap, pat, OP.not_equal, v, 64, -1, W)
+
+    def blocks(name, parts):
+        n = parts[-1][1]
+        iota(T[name][:], [[0, n]], 0, 0, [A(name)], n)
+        for lo, hi, v in parts:
+            if v:
+                where(T[name][:, lo:hi], [[0, (hi - lo) // 8], [16, 8]], OP.is_gt, v, 0, -1, A(name, lo, hi))
+        where(T[name][:], [[0, n // 8], [16, 8]], OP.is_gt, 0.0, 16, -1, A(name))
+
+    def times(out, in_, W, R, **kw):
+        act(out, in_, AF.Identity, R, W, n=128, **kw)
 
     def ci(j):
         return T.ci[:, j:j + 1]
@@ -417,51 +652,62 @@ def rank_program(g, core, T, topo):
     ts(cf(19), cf(0), 14.5, OP.is_lt, [rc(0)], [rc(19)])
     ts(cf(20), cf(19), 2048.0 + XC - 16.0 - BIG, OP.mult, [rc(19)], [rc(20)], (), 16.0 - 2048.0 - XC, OP.add)
     cp(T.idh[:], T.idn[:], [A("idn")], [A("idh")])
+    ts(T.ih32[:], T.idn[:], 1.0 if HASH else 1 / 32, OP.mult, [A("idn")], [A("ih32")])
     ts(T.id15[:], T.idn[:], cf(19), OP.mult, [A("idn"), rc(19)], [A("id15")])
     ts(T.big15[:], T.idn[:], cf(19), OP.mult, [A("idn"), rc(19)], [A("big15")], (), BIG, OP.mult)
-    ts(T.cd[:], T.idn[:], 0.0, OP.mult, [A("idn"), rc(20)], [A("cd")], (), cf(20), OP.add)
+    times(T.cd[:], T.idn[:], [A("cd")], [A("idn"), rc(20)], scale=0.0, bias=cf(20))
     convert(0, 0)
     stage(-1, "soon")
-    for name, v, n in (("c2k", 2048, 128), ("cm", 3 << 22, 128), ("ke", 16384, 128), ("z16", 0, 16), ("nf", 0, 16), ("nfs", 0, 64)):
+    for name, v, n in (("ke", 16384, 128), ("z16", 0, 16)):
         iota(T[name][:], [[0, n]], v, 0, [A(name)], n)
+    iota(T.qd[:, 160::QW], [[0, ST]], 0, 0, [A("qd0")], ST)
+    for ph in range(2):
+        iota(T.es[:, ESW * ph + 256:ESW * ph + ESW], [[0, ESW - 256]], 1, 0, [A("esp", ph, ph + 1)], 8)
+    iota(T.zz[:], [[0, 128]], 0, 0, [A("zz")], 128)
+    rows("cs", 576, [(0, slice(0, 192), ([[0, 64], [1016, 3]], 16)), (32, slice(0, 192), -0.5),
+                     (0, slice(192, 384, 3), RND(5)), (0, slice(193, 384, 3), RND(6)), (0, slice(194, 384, 3), RND(12)),
+                     (0, slice(384, 576), ([[0, 192]], int(RND(0)))), (32, slice(385, 576, 3), 1.0),
+                     (64, slice(385, 576, 3), 1024.0), (64, slice(386, 576, 3), 32.0 if HASH else 2048.0)])
+    rows("ch", 0, [(0, slice(0, 64), 31 / 64), (0, slice(64, 128), ([[0, 64]], int(RND(0)))), (0, slice(128, 192), RND(12)), (0, slice(192, 320), ([[0, 128]], 2048 if HASH else 64))])
+    rows("ct", 112, [(0, slice(0, 8), 7.0), (32, slice(0, 8), -1 / 64), (0, slice(8, 24), 15.5), (0, slice(24, 40), 0.5),
+                     (32, slice(24, 40), 131 * 2.0 ** -16), (0, slice(40, 48), RND(4)), (0, slice(48, 64), RND(5)), (0, slice(64, 80), RND(0)),
+                     (32, slice(80, 88), 33 / 64), (0, slice(88, 104), -BIG), (32, slice(88, 104), BIG - XD)], True)
+    iota(T.ct[0:1, 80:88], [[256, 8]], 0, 0, [A("ct", 80, 88)], 8)
+    fill(T.kb[:], 33 / 64, [A("kb")])
+    where(T.kl[:], [[0, 1]], OP.is_gt, -LOW - 0.175, 0, 0, A("kl"), (T.m1[:, 0:1], A("m1")))
     for ph in range(2):
         iota(xw[ph][:, XC + XD:XW], [[0, 256]], 0, 0, [A("xw%d" % ph, XC + XD, XW)], 256)
-
-    def times(out, in_, W, R, **kw):
-        act(out, in_, AF.Identity, R, W, n=128, **kw)
-    fill(T.hz[:], 0.0, [A("hz")], 272)
-    ts(cf(21), cf(0), 2.0, OP.mult, [rc(0)], [rc(21)], (), 1.0, OP.add)
-    ts(cf(23), cf(0), -32.0, OP.mult, [rc(0)], [rc(23)], (), 32.0, OP.add)
-    ts(cf(25), cf(6), 0.0625, OP.mult, [rc(6)], [rc(25)], (), 1.0, OP.add)
-    ts(cf(27), cf(0), 16.0, OP.mult, [rc(0)], [rc(27)], (), float(QC), OP.add)
-    ts(T.rcp[:], T.m1[:, 0:8], cf(25), OP.is_equal, [A("m1"), rc(25)], [A("rcp")], (), -1.0, OP.mult)
-    for name, f in (("nid", -1.0), ("i2040", 2040.0), ("i75", 7.5), ("i4k", 4096.0), ("n4k", -4096.0), ("i155", 15.5), ("i32", 32.0), ("n32", -32.0),
-                    ("big", BIG), ("nbig", -BIG), ("i19", 2.0 ** 19), ("n19", -2.0 ** 19), ("i128", 128.0)):
+    fill(T.hz[:], 0.0, [A("hz")], 272 if HASH else 544)
+    for j, i, a, b in ((21, 0, -2.0, -1.0), (23, 0, -32.0, 32.0), (25, 6, 0.0625, 1.0), (27, 0, -16.0, RND(0) - QC)):
+        act(cf(j), cf(i), AF.Copy, [rc(i)], [rc(j)], scale=a, bias=b)
+    blocks("rcp", ((0, 8, 1 / 32), (8, 24, 1.0), (24, 40, -2.0 ** -14), (40, 48, -1 / 32), (48, 64, -1.0), (64, 80, 0.0)))
+    blocks("g8", ((0, 8, 512.0),))
+    for name, f in (("nid", -1.0), ("i31", 31.0), ("big", WIPE), ("nbig", -WIPE)) + (() if HASH else (("idf", 1.0), ("nidf", -1.0))):
         times(T[name][:], T.idn[:], [A(name)], [A("idn")], scale=f)
+    ts(T.nidh[:], T.idn[:], -1.0, OP.mult, [A("idn")], [A("nidh")])
+    ts(T.p65[:], T.pm[:], 2.0 if HASH else 65.0, OP.mult, [A("pm")], [A("p65")], n=256)
+    ts(T.n65[:], T.pm[:], -2.0 if HASH else -65.0, OP.mult, [A("pm")], [A("n65")], n=256)
     times(T.nk[:], T.idn[:], [A("nk")], [A("idn"), rc(23)], scale=cf(23))
-    ts(T.g8[:], T.m1[:, 0:8], cf(25), OP.is_equal, [A("m1"), rc(25)], [A("g8")], (), 512.0, OP.mult)
-    ts(T.gw[:, 0:8], T.m1[:, 0:8], cf(25), OP.is_equal, [A("m1"), rc(25), rc(21)], [A("gw", 0, 1)], (), cf(21), OP.mult)
-    ts(T.gw[:, 8:16], T.m1[:, 0:8], cf(25), OP.is_equal, [A("m1"), rc(25)], [A("gw", 1, 2)], (), 2.0 ** 19, OP.mult)
-    ts(T.gw[:, 16:24], T.m1[:, 0:8], cf(25), OP.is_equal, [A("m1"), rc(25)], [A("gw", 2, 3)], (), -2.0 ** 19, OP.mult)
-    ts(T.gw[:, 24:32], T.gw[:, 0:8], -1.0, OP.mult, [A("gw", 0, 1)], [A("gw", 3, 4)])
+    for t in range(3):
+        ts(T.gw[:, t:24:3], T.m1[:, 0:8], cf(25), OP.is_equal, [A("m1"), rc(25), rc(21)], [A("gw", t, t + 1)], (), 64.0 if t == 1 else cf(21), OP.mult)
+    act(T.gw[:, 24:48], T.gw[:, 0:24], AF.Copy, [A("gw", 0, 3)], [A("gw", 3, 4)], scale=-1.0)
     ts(T.nbl[:], T.mg[:], cf(3), OP.is_equal, [A("mg"), rc(3)], [A("nbl")], (), -32.0, OP.mult, n=128)
-    ts(T.dup[:], T.m64[:], cf(4), OP.is_equal, [A("m64"), rc(4)], [A("dup")], n=128)
     ts(T.low[:], T.m64[:], cf(4), OP.is_gt, [A("m64"), rc(4)], [A("low")], n=128)
     tt(T.t1[:], T.nbl[:], T.low[:], OP.mult, [A("nbl"), A("low")], [A("t1")], n=256)
-    times(T.t2[:], T.dup[:], [A("t2")], [A("dup")], scale=2.0 * BIG)
-    tt(T.am[:], T.t2[:], T.t1[:], OP.add, [A("t2"), A("t1")], [A("am")], n=256)
-    ts(cf(28), cf(5), 63.5, OP.is_lt, [rc(5)], [rc(28)])
-    ts(cf(29), cf(5), 63.5, OP.is_gt, [rc(5)], [rc(29)])
-    for name in ("dup", "nbl", "am"):
-        for b in range(2):
-            times(T[name + "2"][:, 128 * b:128 * b + 128], T[name][:], [A(name + "2", b, b + 1)], [A(name), rc(28 + b)], scale=cf(28 + b))
+    for name, f in (("dup", 1.0), ("hdup", WIPE), ("ndup", -WIPE)):
+        diagonal(name, f, 0, True)
+    for b in range(2):
+        diagonal("dup2", 1.0, 128 * b, "half")
+    iota(T.mk32[:], [[0, 32]], 1, 0, [A("mk32")], 32)
+    where(T.mk32[:], [[0, 2], [-64, 2], [0, 8]], OP.is_ge, 0.0, 0, 1, A("mk32"))
+    where(T.mk32[:], [[0, 2], [64, 2], [0, 8]], OP.is_gt, 0.0, 64, -1, A("mk32"))
     ts(T.icn[:], T.icf[:], cf(6), OP.subtract, [A("icf"), rc(6)], [A("icn")])
-    ts(T.dum[:], T.icf[:], cf(6), OP.subtract, [A("icf"), rc(6)], [A("dum")], (), float(XD), OP.add)
-    act(T.thr[:], T.zc[:], AF.Copy, [A("zc")], [A("thr")], bias=-LOW - 0.175)
     ts(T.mr[:], T.si[:], cf(0), OP.is_equal, [A("si"), rc(0)], [A("mr")], n=128)
     cp(T.cl[:], T.clf[:], [A("clf")], [A("cl")])
-    fill(T.ke[:, 0::16], LOW, [A("ke")])
+    where(T.ke[:, 0::16], [[0, 8]], OP.is_gt, LOW, 0, 0, A("ke"))
     stage(-1, "next")
+    mms([(C(T.p7, 128 * j, 128 * j + 128), T.pm[:, 128 * j:128 * j + 128], T.idh[:]) for j in range(4)], 512, [A("pm"), A("idh")], [7])
+    cp(T.pmt[:], T.p7[:], [], [A("pmt")], [7], n=512)
     convert(1, 0)
     for c in range(1, 4):
         convert(0, c)
@@ -477,29 +723,31 @@ def rank_program(g, core, T, topo):
         ph, c = s % 2, (s // 2) % 4
         E, M = MM(ph, c, "ef"), MM(ph, c)
         pu = T["p%d" % B]
-        mms([(pu[:, 0:128], T.idn[:], T.cd[:]), (pu[:, 0:128], T.id15[:], T.ef[:, cls(ph, c)]), (pu[:, 0:128], T.big15[:], T.mm[:, cls(ph, c)])]
-            + [(pu[:, 128 + 64 * par:192 + 64 * par], T.pm[:, 256 * par + 128 * b:256 * par + 128 * b + 128], T.ef[:, cls(ph, c, 4 * b, 8)])
+        d = C(pu, 0, 128)
+        mms([(d, T.idn[:], T.cd[:]), (d, T.id15[:], T.ef[:, cls(ph, c)]), (d, T.big15[:], T.mm[:, cls(ph, c)])]
+            + [(C(pu, 128 + 64 * par, 192 + 64 * par), T.pm[:, 256 * par + 128 * b:256 * par + 128 * b + 128], T.ef[:, cls(ph, c, 4 * b, 8)])
                for par in range(2) for b in range(2)], 640, E + M + [A("idn"), A("cd"), A("id15"), A("big15"), A("pm")], [B])
-        ts(T.el16[:, 256 * s:256 * s + 256], pu[:, 0:256], 2048.0 + XC, OP.add, [], [A("el16", s, s + 1)], [B], n=256)
+        ts(T.el16[:, 256 * s:256 * s + 256], C(pu, 0, 256), 2048.0 + XC, OP.add, [], [A("el16", s, s + 1)], [B], n=256)
 
     def turned(s):
         ph, c = s % 2, (s // 2) % 4
         E, pe = MM(ph, c, "ef"), banks(ph)[0]
-        mms([(pe[:, 0:128], T.idn[:], T.c2k[:]), (pe[:, 0:128], T.ef[:, cls(ph, c)], T.idh[:]), (pe[:, 128:256], T.sm[:, cls(ph, c)], T.idn[:])],
-            384, E + MM(ph, c, "sm") + [A("idn"), A("idh"), A("c2k")], [ph])
-        act(T.es[:, 256 * ph:256 * ph + 256], pe[:, 0:256], AF.Copy, [], [A("es", ph, ph + 1)], [ph], n=256)
+        mms([(C(pe, 0, 128), T.one[0:1, :], T.ch[0:1, 192:320]), (C(pe, 0, 128), T.ef[:, cls(ph, c)], T.ih32[:]),
+             (C(pe, 128, 256), T.sm[:, cls(ph, c)], T.idn[:])], 384, E + MM(ph, c, "sm") + [A("idn"), A("ih32"), A("ch"), A("one")], [ph])
+        act(T.es[:, ESW * ph:ESW * ph + 256], C(pe, 0, 256), AF.Copy, [], [A("es", ph, ph + 1)], [ph], n=256)
 
     def head(s):
         ph = s % 2
         all_x, RX = xw[ph][:, 0:XC + 4096], A("xw%d" % ph, 0, XC + 4096)
-        raw, RR = (xw[ph][:, XR:2 * XR], A("xw%d" % ph, XR, 2 * XR)) if s == 0 else (all_x, RX)
+        raw, RR = (xw[ph][:, XR:2 * XR], A("xw%d" % ph, XR, 2 * XR)) if s < 2 - ADD else (all_x, RX)
         qq, EL = T["qq%d" % ph], A("el16", s, s + 1)
-        for h, (lo, hi) in enumerate(((0, EV), (EV, 1024))):
+        ev = EV if s else EV0
+        for h, lo, hi in [(0, lo, min(lo + EW, ev)) for lo in range(0, ev, EW)] + [(1, ev, 1024)]:
             stage(s, "e%d" % h)
             if lo < hi:
                 out = qq[:, QC + 2 * lo:QC + 2 * hi:2]
                 src = raw.indirect(T.el16[:, 256 * s + 128 + lo // 16:256 * s + 128 + hi // 16])
-                W, less = [("qe", 1024 * ph + lo, 1024 * ph + hi)], -DEL if s == 0 else 0.0
+                W, less = [("qe", 1024 * ph + lo, 1024 * ph + hi)], -DEL if s < 2 - ADD else 0.0
                 if h == 0:
                     ts(out, src, less, OP.add, [RR, EL], W, cost=("gather", hi - lo))
                 else:
@@ -514,55 +762,74 @@ def rank_program(g, core, T, topo):
             tt(qq[:, QC + lo + 1:QC + hi:2], all_x.indirect(T.el16[:, 256 * s + 192 + lo // 32:256 * s + 192 + hi // 32]),
                T.bb[:, o.start:o.stop:2], OP.min, [RX, EL, ("bb", o.start, o.stop)], [("qo", o.start // 2, o.stop // 2)], cost=("gather", n // 2))
 
-    MOD = [A(name) for name in ("gw", "one", "cm", "idn", "nid", "i2040", "i75", "i155", "i4k", "n4k", "i32", "n32", "i19", "n19", "i128", "big", "nbig")]
+    def plus(out, name, k, lo, n, sign=1):
+        return (out, (T.one if sign > 0 else T.non)[0:k, :], T[name][0:k, lo:lo + n])
 
-    def modulo(out, n, lines, half, up, down):
-        return [(o, q, T.gw[:, 24:32]) for o, q in lines] + [(out, c[:], T.one[:, 0:n]) for c in half] \
-            + [(out, up[:], T.cm[:, 0:n]), (out, down[:], T.cm[:, 0:n])] + [(o, q, T.gw[:, 0:8]) for o, q in lines] \
-            + [(out, T.idn[:], T.cm[:, 0:n]), (out, T.nid[:], T.cm[:, 0:n])]
+    def passing(out, name, lo, n, k=1, k2=None):
+        return [plus(out, name, k, lo, n), plus(out, name, k2 or k, lo, n, -1)]
+    ONES = [A("one"), A("non")]
 
     def hop(s, par):
-        ph = s % 2
-        pe = banks(ph)[0]
-        pu, B = (banks(ph)[1], 2 + ph) if par else (banks(ph)[3], 5 + 2 * ph)
+        ph, c = s % 2, (s // 2) % 4
+        pe, pu, ya, yb = banks(ph)
+        (p, B, r), (pl, BL) = ((pu, 2 + ph, 0), (C(pe, 0, 64), ph)) if par else ((pe, ph, 64), (C(yb, 256, 320), 5 + 2 * ph))
         qq = T["qq%d" % ph]
         z = 2 * ph + par
         stage(s, "hop%d" % par)
-        mms(modulo(pu[:, 0:64], 64, [(pu[:, k:64:8], qq[:, QC + 2 * k + par::16]) for k in range(8)], (T.i2040, T.i75), T.i4k, T.n4k), 1408,
-            [("qo" if par else "qe", 1024 * ph, 1024 * ph + 1024)] + MOD, [B])
-        o = slice(64 * z, 64 * z + 64)
+        out = p[:, r:r + 64, 0:3]
+        sums = [[(p[:, r + k:r + 64:8, 0:3], qq[:, QC + 2 * k + par::16], T.gw[:, 24 * j:24 * j + 24]) for k in range(8)] for j in range(2)]
+        mmx([plus(out, "cs", 33, 0, 192) + (True, False)], 192, ONES + [A("cs")], [B])
+        lst = sums[0] + passing(out, "cs", 192, 192) + sums[1] + passing(out, "cs", 384, 192, 33, 65)
+        for lo in (0, 10):
+            mmx([a + (False, j == 19) for j, a in enumerate(lst)][lo:lo + 10], 896, [("qo" if par else "qe", 1024 * ph, 1024 * ph + 1024), A("gw"), A("cs")] + ONES, [B])
+        o, ES = slice(64 * z, 64 * z + 64), A("es", ph, ph + 1)
 
         def rg(b):
             return A(b, z, z + 1)
-        tt(T.ta[:, o], pu[:, 0:64], T.es[:, 256 * ph + par:256 * ph + 128:2], OP.mult, [A("es", ph, ph + 1)], [rg("ta")], [B])
-        ts(T.tb[:, o], T.ta[:, o], 5, OP.logical_shift_right, [rg("ta")], [rg("tb")])
-        c, ek = (s // 2) % 4, pu[:, 64:128]
-        lst = [(ek, T.idn[:], T.c2k[:, 0:64]), (ek, T.ef[:, cls(ph, c)], T.idh[:, par::2]), (ek, T.idn[:], T.kb[:])][:2 if s < 2 else 3]
-        mms(lst, 64 * len(lst), MM(ph, c, "ef") + [A("idn"), A("idh"), A("c2k"), A("kb")], [B])
-        tt(T.tc[:, o], ek, T.tb[:, o], OP.add, [rg("tb")], [rg("tc")], [B])
-        hh, HH = T.hh[:, 128 * s + par:128 * s + 128:2], A("hh", 2 * s + par, 2 * s + par + 1)
-        ts(hh, T.tc[:, o], 4095, OP.bitwise_and, [rg("tc")], [HH])
         z0 = 17 * z
-        ts(T.hz[:, z0 + 1:z0 + 17:2, :], hh, -2048.0, OP.add, [HH], [rg("hz")])
-        pl = pu[:, 256:320]
-        mms([(pl, T.hz[:, z0 + 1 - b:z0 + 17 - b, :], T.idh[:, b::2]) for b in range(2)], 128, [rg("hz"), A("idh")], [B])
-        ts(T.h16[:, o], pl, 2048.0, OP.add, [], [rg("h16")], [B])
+        def prod(i):
+            return [(pl, T.hz[:, z0 + 1 - b:z0 + 17 - b, :], i[:, b::2]) for b in range(2)]
+
+        def e65(m):
+            return [(pl, m[:, 256 * par + 128 * b:256 * par + 128 * b + 128], T.ef[:, cls(ph, c, 4 * b, 8)]) for b in range(2)]
+        RH = [A("idf"), A("nidf"), A("ch"), A("n65"), A("p65"), A("idh"), A("nidh")] + ONES + MM(ph, c, "ef")
+        if HASH:
+            tt(T.ta[:, o], p[:, r:r + 64, 2], T.es[:, ESW * ph + par:ESW * ph + 128:2], OP.mult, [ES], [rg("ta")], [B])
+            stage(s, "hx%d" % par)
+            ts(T.tb[:, o], T.ta[:, o], 5, OP.arith_shift_right, [rg("ta")], [rg("tb")], (), 4095, OP.bitwise_and)
+            ts(T.hz[:, z0 + 1:z0 + 17:2, :], T.tb[:, o], -2048.0, OP.add, [rg("tb")], [rg("hz")])
+            stage(s, "hop%d" % par)
+            mmx([a + (j == 0, False) for j, a in enumerate(e65(T.n65))], 128, RH, [BL])
+            mmx([a + (False, False) for a in prod(T.nidh)], 128, RH + [rg("hz")], [BL])
+            lst = [(pl, T.nidh[:], T.kb[:])] + passing(pl, "ch", 128, 64) + e65(T.p65) + prod(T.idh) + [(pl, T.idh[:], T.kb[:])]
+            mmx([a + (False, j == 7) for j, a in enumerate(lst)], 512, RH + [rg("hz"), A("kb")], [BL])
+        else:
+            tt(T.hz[:, z0 + 1:z0 + 17:2, :], p[:, r:r + 64, 2], T.es[:, ESW * ph + par:ESW * ph + 128:2], OP.mult, [ES], [rg("hz")], [B])
+            mmx([plus(pl, "ch", 1, 0, 64) + (True, False)], 64, ONES + [A("ch")], [BL])
+            lst = prod(T.nidf) + passing(pl, "ch", 64, 64) + e65(T.n65) + [(pl, T.nidh[:], T.kb[:])] + passing(pl, "ch", 128, 64) \
+                + e65(T.p65) + prod(T.idf) + [(pl, T.idh[:], T.kb[:])]
+            for lo, hi, n, R in ((0, 6, 768, []), (6, 14, 896, [A("kb")])):
+                mmx([a + (False, j == 13) for j, a in enumerate(lst)][lo:hi], n, [rg("hz")] + R + RH, [BL])
+        ts(T.h16[:, 128 * s + 64 * par:128 * s + 64 * par + 64], pl, RND(0), OP.add, [], [A("h16", 2 * s + par, 2 * s + par + 1)], [BL], RND(0) - 2047.0, OP.subtract)
+        stage(s, "gate%d" % par)
+        e0 = ESW * ph + 128 + par
+        tt(T.us[:, 128 * z:128 * z + 128], p[:, r:r + 64, 0:2], T.es[:, e0:e0 + 128], OP.mult, [ES, A("esp")], [rg("us")], [B], n=128)
 
     def look(s, par):
         ph = s % 2
         qq, Q = T["qq%d" % ph], ("qo" if par else "qe", 1024 * ph, 1024 * ph + 1024)
         items, RX = xw[ph][:, XC:XC + 4096], A("xw%d" % ph, 0, XC + 4096)
         z = 2 * ph + par
-        H16 = A("h16", z, z + 1)
+        H16, h0 = A("h16", 2 * s + par, 2 * s + par + 1), 128 * s + 64 * par
         ns = YS[par]
         for x, (lo, hi) in enumerate(((0, min(ns, 512)), (512, ns))):
             if lo >= hi:
                 continue
             n, cols = hi - lo, slice(1024 * z + lo, 1024 * z + hi)
             stage(s, "y%d%d" % (par, x))
-            act(T.yb[:, cols], items.indirect(T.h16[:, 64 * z + lo // 16:64 * z + hi // 16]), AF.Copy, [RX, H16], [("yb", cols.start, cols.stop)],
+            act(T.yb[:, cols], items.indirect(T.h16[:, h0 + lo // 16:h0 + hi // 16]), AF.Copy, [RX, H16], [("yb", cols.start, cols.stop)],
                 cost=("gather", n))
-            ps, B = banks(ph)[2 + x][:, 0:n], 4 + 2 * ph + x
+            ps, B = C(banks(ph)[2 + x], 0, n), 4 + 2 * ph + x
             mmx([(ps, T.nid[:], qq[:, QC + 2 * lo + par:QC + 2 * hi:2], True, False)], n, [A("nid"), Q], [B])
             mmx([(ps, T.idn[:], T.yb[:, cols], False, True)], n, [A("idn"), ("yb", cols.start, cols.stop)], [B])
             stage(s, "s%d%d" % (par, x))
@@ -571,46 +838,33 @@ def rank_program(g, core, T, topo):
             lo, hi = 1024 * z + ns, 1024 * z + 1024
             cols = slice(2048 * ph + 2 * ns + par, 2048 * ph + 2048, 2)
             stage(s, "v%d" % par)
-            tt(T.dq[:, cols], items.indirect(T.h16[:, lo // 16:hi // 16]), qq[:, QC + 2 * ns + par:QC + 2048:2], OP.subtract,
+            tt(T.dq[:, cols], items.indirect(T.h16[:, h0 + ns // 16:h0 + 64]), qq[:, QC + 2 * ns + par:QC + 2048:2], OP.subtract,
                [RX, H16, Q], [("dq", lo, hi)], cost=("gather", hi - lo))
             ts(T.sg[:, cols], T.dq[:, cols], 1.0, OP.min, [("dq", lo, hi)], [("sg", lo, hi)], (), -1.0, OP.max, n=(hi - lo) // 2)
 
     def mid(s):
         ph, c = s % 2, (s // 2) % 4
         pe, pu = banks(ph)[:2]
-        o = slice(128 * ph, 128 * ph + 128)
-
-        def rg(b):
-            return A(b, ph, ph + 1)
         hop(s, 0)
         hop(s, 1)
-        stage(s, "gate0")
-        qq, Q = T["qq%d" % ph], [("qe", 1024 * ph, 1024 * ph + 1024), ("qo", 1024 * ph, 1024 * ph + 1024), A("gw")]
-        for par in range(2):
-            out, lines, cm = pe[:, par:128:2], [(pe[:, k:128:16], qq[:, QC + k::16]) for k in range(par, 16, 2)], T.cm[:, 0:64]
-            lst = [(a, q, T.gw[:, 8:16]) for a, q in lines] + [(out, T.i19[:], cm), (out, T.n19[:], cm)] \
-                + [(a, q, T.gw[:, 16:24]) for a, q in lines] + [(out, T.i128[:], T.one[:, 0:64]), (out, T.big[:], cm), (out, T.nbig[:], cm)] \
-                + modulo(out, 64, lines, (T.i155,), T.i32, T.n32)
-            for lo in range(0, 42, 14):
-                mmx([a + (j == 0, j == 41) for j, a in enumerate(lst)][lo:lo + 14], 896, [Q[par]] + MOD, [ph])
-        sig, ES = T.es[:, 256 * ph + 128:256 * ph + 256], A("es", ph, ph + 1)
-        stage(s, "gate1")
-        tt(T.us[:, o], pe[:, 0:128], sig, OP.mult, [ES], [rg("us")], [ph], n=128)
+        sig, ES = T.es[:, ESW * ph + 128:ESW * ph + 256], A("es", ph, ph + 1)
         look(s, 0)
         look(s, 1)
         stage(s, "score")
-        mmx([(pu[:, 384:512], T.sm[:, cls(ph, c)], T.nk[:], True, False)], 128, MM(ph, c, "sm") + [A("nk")], [2 + ph])
+        mmx([(C(pu, 384, 512), T.sm[:, cls(ph, c)], T.nk[:], True, False)], 128, MM(ph, c, "sm") + [A("nk")], [2 + ph])
         for par in range(2):
-            if par:
-                mmx([(pu[:, 384:512], T.nid[:], T.us[:, o], False, False)], 128, [A("nid"), rg("us")], [2 + ph])
-            mmx([(pu[:, 384 + k:512:16], T.sg[:, 2048 * ph + k:2048 * ph + 2048:16], T.g8[:], False, k == 15) for k in range(par, 16, 2)],
-                512, [("sg", 2048 * ph + 1024 * par, 2048 * ph + 1024 * par + 1024), A("g8")], [2 + ph])
+            z, out = 2 * ph + par, C(pu, 384 + par, 512, 2)
+            US, many = A("us", z, z + 1), T.us[:, 128 * z + 1:128 * z + 128:2]
+            mmx([(out, T.nid[:], T.us[:, 128 * z:128 * z + 128:2], False, False)], 64, [A("nid"), US], [2 + ph])
+            mmx([(C(pu, 384 + k, 512, 16), T.sg[:, 2048 * ph + k:2048 * ph + 2048:16], T.g8[:], False, False) for k in range(par, 16, 2)]
+                + [(out, T.big[:], many, False, False), (out, T.nbig[:], many, False, par == 1)],
+                640, [("sg", 2048 * ph + 1024 * par, 2048 * ph + 1024 * par + 1024), A("g8"), A("big"), A("nbig"), US], [2 + ph])
         stage(s, "keys")
         kt, KT = T.kt[:, 128 * s:128 * s + 128], A("kt", s, s + 1)
-        tt(kt, pu[:, 384:512], sig, OP.mult, [ES], [KT], [2 + ph], n=128)
+        tt(kt, C(pu, 384, 512), sig, OP.mult, [ES], [KT], [2 + ph], n=128)
         scn(T.sc[:, 128 * s:128 * s + 128], T.ke[:], kt, LOW, OP.min, OP.max, [A("ke"), KT], [A("sc", s, s + 1)], 128)
 
-    def send(s, a, b, sm, w):
+    def send(s):
         t = s // 2
         dst = T.cores[(rank + 1 + t % (n_ranks - 1)) % n_ranks]
         es = topo.engines(core, dst)[:8]
@@ -618,76 +872,68 @@ def rank_program(g, core, T, topo):
         rid, pid, _ = topo.addr(dst)
         src = T.cores[(rank - 1 - t % (n_ranks - 1)) % n_ranks]
         n_in = len(topo.engines(src, core)[:8])
-        name, o = "%s%d" % (sm, s), slice(w * s, w * s + w)
-        i = node("g", [lambda e: e.remote_dma(T[b][:, o], T[a][:, o], T.sem[name], T.sem.ls, pid, rid, mask)],
-                 CALL, [A(a, s, s + 1)], [], (), "r", len(es))
-        node(None, [], 0.0, [], [A(b, s, s + 1)], (), "a", (name, n_in), LAND[a != "qd"], (i,))
+        name, o = "aq%d" % s, slice(QW * s, QW * s + 176)
+        i = node("g", [lambda e: e.remote_dma(T.lq[:, o], T.qd[:, o], T.sem[name], T.sem.ls, pid, rid, mask)],
+                 CALL, [A("qd", 3 * s, 3 * s + 3), A("qd0")], [], (), "r", len(es))
+        node(None, [], 0.0, [], [A("lq", s, s + 1)], (), "a", (name, n_in), LAND, (i,))
 
     def tail(s):
         ph = s % 2
         qq = T["qq%d" % ph]
         pe, pu, ya, yb = banks(ph)
         stage(s, "tail1")
-        tt(T.lm[:], T.sc[:, 128 * s:128 * s + 128].indirect(T.cl[:]), T.mr[:], OP.mult, [A("sc", s, s + 1), A("cl"), A("mr")], [A("lm")],
+        tt(T.lm[:], T.sc[:, 128 * s:128 * s + 128].indirect(T.cl[:, 0:8]), T.mr[:], OP.mult, [A("sc", s, s + 1), A("cl"), A("mr")], [A("lm")],
            cost=("gather", 128))
-        kl = pu[:, 0:8]
-        mms([(kl, T.idn[:], T.zc[:]), (kl, T.lm[:], T.rcp[:])], 320, [A("idn"), A("zc"), A("lm"), A("rcp")], [2 + ph])
-        ts(T.kn[:], kl, 32.0, OP.add, [], [A("kn")], [2 + ph])
-        tt(T.nf[:, 0:8], kl, T.thr[:], OP.is_gt, [A("thr")], [A("nf")], [2 + ph])
-        ts(T.li[:], T.kn[:], 5, OP.logical_shift_right, [A("kn")], [A("li")], (), 0x0F0F, OP.bitwise_and)
-        ts(T.l16[:], T.li[:], cf(27), OP.add, [A("li"), rc(27)], [A("l16")])
-        cp(T.qd[:, 128 * s:128 * s + 128], qq[:].indirect(T.l16[:]), [("qe", 1024 * ph, 1024 * ph + 1024), ("qo", 1024 * ph, 1024 * ph + 1024), A("l16")],
-           [A("qd", s, s + 1)], cost=("gather", 128))
-        send(s, "qd", "lq", "aq", 128)
-        n0, NS = 32 * ph, A("nfs", ph, ph + 1)
-        scn(T.nfs[:, n0 + 1:n0 + 17], T.nf[:], T.z16[:], 0.0, OP.add, OP.max, [A("nf"), A("z16")], [NS], 16)
-        lst = [(yb[:, 16:32], T.i32[:], T.icn[:]), (yb[:, 24:32], T.nbl2[:, 0:128], T.nfs[:, n0 + 8:n0 + 16])]
-        for b in range(2):
-            r = slice(128 * b, 128 * b + 128)
-            lst += [(yb[:, 16 + 8 * b:24 + 8 * b], T.am2[:, r], T.nf[:, 0:8]), (yb[:, 16 + 8 * b:24 + 8 * b], T.nbl2[:, r], T.nfs[:, n0:n0 + 8])]
-        mmx([a + (j == 0, False) for j, a in enumerate(lst)], 384, [A("am2"), A("nf"), A("nbl2"), NS, A("i32"), A("icn")], [5 + 2 * ph])
+        kl, CT = C(pu, 0, 40), ONES + [A("ct")]
+        mmx([plus(kl, "ct", 33, 0, 40) + (True, False)], 64, CT, [2 + ph])
+        lst = [(kl, T.lm[:], T.rcp[:, 0:40])] + passing(kl, "ct", 40, 40) + [(kl, T.lm[:], T.rcp[:, 40:80]), plus(C(pu, 0, 8), "ct", 33, 80, 8)]
+        mmx([a + (False, j == 4) for j, a in enumerate(lst)], 704, CT + [A("lm"), A("rcp")], [2 + ph])
+        ts(T.l16[:], C(pu, 0, 8), RND(0), OP.add, [rc(27)], [A("l16")], [2 + ph], cf(27), OP.subtract)
+        n0, UN = QW * s, A("qd", 3 * s + 1, 3 * s + 2)
+        tt(T.qd[:, n0 + 128:n0 + 160], C(pu, 8, 40), T.mk32[:], OP.mult, [A("mk32")], [UN], [2 + ph])
+        cp(T.qd[:, n0:n0 + 128], qq[:].indirect(T.l16[:]), [("qe", 1024 * ph, 1024 * ph + 1024), ("qo", 1024 * ph, 1024 * ph + 1024), A("l16")],
+           [A("qd", 3 * s, 3 * s + 1)], cost=("gather", 128))
         stage(s, "tail2")
-        ts(T.uwa[:], T.kn[:], 31, OP.bitwise_and, [A("kn")], [A("uwa")])
-        cp(T.uwb[:], T.uwa[:], [A("uwa")], [A("uwb")])
-        mmx([(yb[:, 16 + 8 * b:24 + 8 * b], T.dup2[:, 128 * b:128 * b + 128], T.uwb[:], False, b == 1) for b in range(2)], 128,
-            [A("dup2"), A("uwb")], [5 + 2 * ph])
-        tt(T.tgm[:], yb[:, 16:32], T.dum[:], OP.min, [A("dum")], [A("tgm")], [5 + 2 * ph])
-        cp(T.tg[:, 16 * s:16 * s + 16], T.tgm[:], [A("tgm")], [A("tg", s, s + 1)])
-        send(s, "tg", "lt", "at", 16)
+        scn(T.qd[:, n0 + 161:n0 + 177], T.qd[:, n0 + 144:n0 + 160], T.z16[:], 0.0, OP.add, OP.max, [UN, A("z16")], [A("qd", 3 * s + 2, 3 * s + 3)], 16)
+        send(s)
 
-    def kappa():
-        pu = banks(1)[1]
-        mms([(pu[:, 48:49], T.one[:], T.nfs[:, 32 * ph + 8:32 * ph + 9]) for ph in range(2)], 128, [A("one"), A("nfs")], [3])
-        ts(T.kcj[:], pu[:, 48:49], -1.0, OP.mult, [], [A("kcj")], [3], 8176.5, OP.add)
-        ts(T.kap[:], pu[:, 48:49], -1.0, OP.mult, [A("kcj")], [A("kap")], [3], T.kcj[:], OP.subtract)
-        ts(T.kb[:], T.one[:, 0:64], T.kap[:], OP.mult, [A("one"), A("kap")], [A("kb")], (), 8192.0, OP.add)
+    def kappa(s):
+        act(T.kj[:], T.sc[:, 128 * s - 113:128 * s + 128:16], AF.Sign, [A("sc", s - 1, s + 1), A("kl")], [A("kc")], bias=T.kl[:], accum_out=T.kc[:])
+        act(T.kd[:], T.kc[:], AF.Copy, [A("kc")], [A("kd")], scale=0.5)
+        kp = C(banks(KB)[2], 508, 509)
+        mms([plus(kp, "ct", 1, 8, 1), (kp, T.non[:], T.kd[:])] + passing(kp, "ct", 48, 1) + [(kp, T.one[:], T.kd[:])], 320,
+            ONES + [A("ct"), A("kd")], [4 + 2 * KB])
+        ts(T.kb[:], T.one[:, 0:64], kp, OP.mult, [A("one")], [A("kb")], [4 + 2 * KB], 33 / 64, OP.add)
 
-    def update(s, bk, at=None):
-        ph, t = s % 2, s // 2
-        c = t % 4
-        o = slice(128 * s, 128 * s + 128)
-        E, M, NW = MM(ph, c, "ef"), MM(ph, c), A("nw", s, s + 1)
-        pe, pu, ya, yb = banks(bk)
-        nw, eb, EB = T.nw[:, o], T.eb[:, 128 * ph:128 * ph + 128], A("eb", ph, ph + 1)
-        stage(at or s, "late" if at else "hf")
-        ts(T.hf[:, o], T.hh[:, o], -2048.0, OP.add, [A("hh", 2 * s, 2 * s + 2)], [A("hf", s, s + 1)], n=128)
-        stage(at or s, "late" if at else "nw")
-        tt(nw, T.sc[:, o].indirect(T.cl[:]), T.kt[:, o], OP.not_equal, [A("kt", s, s + 1), A("cl"), A("sc", s, s + 1)], [NW], cost=("gather", 128))
-        stage(at or s, "late" if at else "update")
+    def update(s, k, bk, at, name):
+        t, n = s // 2, 128 * k
+        c, phs = t % 4, [z % 2 for z in range(s, s + k)]
+        o, cols = slice(128 * s, 128 * s + n), slice(512 * phs[0] + c, 512 * phs[-1] + 512, 4)
+        E, M, NW, HF = [MM(ph, c, "ef")[0] for ph in phs], [MM(ph, c)[0] for ph in phs], A("nw", s, s + k), A("hf", s, s + k)
+        pe = T["p%d" % bk]
+        ef, en, mn = T.ef[:, cols], C(pe, 0, n), C(pe, n, 2 * n)
+        stage(at, name)
+        ts(T.hf[:, o], T.h16[:, o], -2048.0, OP.add, [A("h16", 2 * s, 2 * s + 2 * k)], [HF], n=n // 2)
+        tt(T.nw[:, o], T.sc[:, o].indirect(T.cl[:, 0:8 * k]), T.kt[:, o], OP.not_equal, [A("kt", s, s + k), A("cl"), A("sc", s, s + k)], [NW], cost=("gather", n))
         keep = t + 4 < RO
-        mms([(pe[:, 0:128], T.idh[:], T.ef[:, cls(ph, c)]), (pe[:, 0:128], nw, T.nbig[:]),
-             (pe[:, 128:256], T.idn[:], T.mm[:, cls(ph, c)]), (pe[:, 128:256], nw, T.idn[:])], 512, E + M + [NW, A("idh"), A("nbig"), A("idn")], [bk])
-        act(eb, pe[:, 0:128], AF.Copy, [], [EB], [bk], n=128, bias=BIG + (0.0 if keep else 2048.0))
-        act(T.mm[:, cls(ph, c)], pe[:, 128:256], AF.Abs, [], M, [bk], n=128, bias=-1.0)
-        lst = [(yb[:, 128:256], T.hf[:, o], T.idh[:]), (yb[:, 128:256], nw, T.big[:])]
-        if not keep:
-            lst.append((yb[:, 128:256], T.idn[:], T.c2k[:]))
-        mms(lst, 128 * len(lst), [NW, A("hf", s, s + 1), A("c2k"), A("idn"), A("idh"), A("big")], [5 + 2 * bk])
+        for z in range(k):
+            mmx([(C(pe, 128 * z + j % 2, 128 * z + 128, 2), T.pmt[:, 128 * j:128 * j + 128], T.hf[:, 128 * (s + z) + 64 * (j // 2):128 * (s + z) + 64 * (j // 2) + 64],
+                  z + j == 0, False) for j in range(4)], 256, [HF, A("pmt")], [bk])
+        mmx([(en, T.nidh[:], ef, False, False), (mn, T.idn[:], T.mm[:, cols], False, False)], 2 * n, E + M + [A("nidh"), A("idn")], [bk])
+        for z in range(k):
+            nw, a, b = T.nw[:, 128 * (s + z):128 * (s + z) + 128], C(pe, 128 * z, 128 * z + 128), C(pe, n + 128 * z, n + 128 * z + 128)
+            mmx([(a, nw, T.big[:], False, False), (a, nw, T.nbig[:], False, False), (b, nw, T.idn[:], False, False)], 384, [NW, A("big"), A("nbig"), A("idn")], [bk])
+        mmx([(en, T.idh[:], ef, False, True)], n, E + [A("idh")], [bk])
+        YL = [A("yl%d%d" % (ph, c)) for ph in phs]
         if keep:
-            ts(T.sm[:, cls(ph, c)], T.mm[:, cls(ph, c)], -2.0, OP.mult, M, MM(ph, c, "sm"), (), 1.0, OP.add)
-            tt(T.ef[:, cls(ph, c)], yb[:, 128:256], eb, OP.min, [EB], E, [5 + 2 * bk], n=128)
+            cp(ef, en, [], E, [bk], n=n)
+        elif UPD == "v":
+            ts(T.ylb[:, cols], en, 2048.0, OP.add, [], YL, [bk], n=n)
         else:
-            tt(T.ylb[:, cls(ph, c)], yb[:, 128:256], eb, OP.min, [EB], [A("yl%d%d" % (ph, c))], [5 + 2 * bk], n=128)
+            act(T.ylb[:, cols], en, AF.Copy, [], YL, [bk], n=n, bias=2048.0)
+        act(T.mm[:, cols], mn, AF.Abs, [], M, [bk], n=n, bias=-1.0)
+        if keep:
+            act(T.sm[:, cols], T.mm[:, cols], AF.Copy, M, [MM(ph, c, "sm")[0] for ph in phs], n=n, scale=-2.0, bias=1.0)
 
     def back(ph, which):
         for z, q in enumerate(RELU[ph]):
@@ -704,16 +950,26 @@ def rank_program(g, core, T, topo):
         win, WX = xw[ph][:, XC:XW], A("xw%d" % ph, XC, XW)
         last = s >= ST - 2
         if last:
+            stage(s, "back0")
             back(ph, "SV")
+            stage(s, "arrive")
         lt, L = T.lt[:, 16 * s:16 * s + 16], A("lt", s, s + 1)
-        ya = banks(ph)[2]
-        mms([(ya[:, 128 * b:128 * b + 128], T.dup2[:, 128 * b:128 * b + 128], T.lq[:, 128 * s:128 * s + 128]) for b in range(2)], 256,
-            [A("dup2"), A("lq", s, s + 1)], [4 + 2 * ph])
-        act(T.qw[:], ya[:, 0:256], AF.Copy, [], [A("qw")], [4 + 2 * ph], n=256, bias=2049.5)
+        ya, yb = banks(ph)[2:]
+        n0, LQ, tg = QW * s, A("lq", s, s + 1), C(yb, 16, 32)
+        nf = T.lq[:, n0 + 144:n0 + 160]
+        mms([(C(ya, 128 * b, 128 * b + 128), T.dup2[:, 128 * b:128 * b + 128], T.lq[:, n0:n0 + 128]) for b in range(2)], 256,
+            [A("dup2"), LQ], [4 + 2 * ph])
+        mmx([(tg, T.i31[:], T.icn[:], True, False), plus(tg, "ct", 33, 88, 16) + (False, False)], 128, ONES + [A("ct"), A("i31"), A("icn")], [5 + 2 * ph])
+        mmx([(tg, T.t1[:], nf, False, False), (tg, T.dup[:], T.lq[:, n0 + 128:n0 + 144], False, False), (tg, T.nbl[:], T.lq[:, n0 + 160:n0 + 176], False, False),
+             (tg, T.hdup[:], nf, False, False), (tg, T.ndup[:], nf, False, False), (tg, T.idn[:], T.icn[:], False, True)], 384,
+            [A("t1"), A("dup"), A("nbl"), A("hdup"), A("ndup"), A("idn"), A("icn"), LQ], [5 + 2 * ph])
+        ts(lt, tg, float(XD), OP.add, [], [L], [5 + 2 * ph])
+        act(T.qw[:], C(ya, 0, 256), AF.Copy, [], [A("qw")], [4 + 2 * ph], n=256, bias=2049.5)
         tt(T.av[:], win.indirect(lt), T.qw[:], OP.add, [WX, L, A("qw")], [A("av")], cost=("gather", 256))
         ts(T.ax[:], T.av[:], 0.5, OP.mult, [A("av")], [A("ax")], (), -1025.0 - (0.0 if last else DEL), OP.add, n=128)
         cp(win.indirect(lt), T.ax[:], [A("ax"), L], [WX], cost=("scatter", 256))
         if last:
+            stage(s, "back1")
             back(ph, "sv")
             dma(STORES[ph][4], T.yx[64 * ph:64 * ph + 64, :], xw[ph][0:64, XC:XR], [A("xw%d" % ph, XC, XR)], [],
                 DLAT + 524288 / DBW + DROW + (0.0 if ph else OUTL[2]))
@@ -725,7 +981,7 @@ def rank_program(g, core, T, topo):
                 [A("yl%d%d" % (ph, c)) for c in range(4)], [], OUTL[ph])
 
     for ph in range(2):
-        stage(ph - 2, "prep")
+        stage(-1, "soon")
         lists(ph, 2 + ph)
         turned(ph)
     stage(-1, "next")
@@ -739,19 +995,22 @@ def rank_program(g, core, T, topo):
         tail(s)
         if s % 2 and s + 2 < ST:
             stage(s, "kappa")
-            kappa()
-        if s not in LATE:
-            update(s, s % 2)
+            kappa(s)
+        if s == 1:
+            update(0, 2, 1, s, "keep")
+        if s == ST - 2:
+            for z in range(2, ST - 2, 2):
+                update(z, 2, z % 4, s, "late%d" % (z // 2))
+        if s >= ST - 2:
+            update(s, 1, s % 2, s, "update")
         if s + 2 < ST:
-            stage(s, "prep")
+            stage(s, "lists")
             if s + 2 not in EARLY:
                 lists(s + 2, 2 + s % 2)
+            stage(s, "turn")
             turned(s + 2)
         else:
-            for z in LATE:
-                if s == ST - 2:
-                    update(z, 0, s)
-            stage(s, "prep")
+            stage(s, "store")
             lists_out(s % 2)
     arrive(ST - 2)
     arrive(ST - 1)
@@ -764,9 +1023,9 @@ def rank_program(g, core, T, topo):
             lag = f["late"] + ((WAKE[0] if f["q"] == d["q"] else WAKE[1] + MORE.get(f["q"], 0.0)) if j in d["deps"] else 0.0)
             before[i].append((j, lag))
 
+    ORDER["x"] = (nodes, before)
     if "order" not in ORDER:
         ORDER["order"] = arrange(nodes, before)
-        ORDER["x"] = (nodes, before)
     orders, fin = ORDER["order"][1], ORDER["order"][2]
 
     cnt = {q: 0 for q in eng}

import math
from concourse.bass import DstId, RemoteDMATransfer
from concourse.mybir import dt, AluOpType, AxisListType, ActivationFunctionType

OP = AluOpType
AF = ActivationFunctionType
RO = 5
ST = 2 * RO
XC = 32
XR = XC + 4096
XD = 2 * XR - XC
XW = XC + XD + 256
QC = 0
DEL = 2.0 ** -10
BIG = 8192.0
KD = "float32"
LOW = 32.625
WIPE = 1.5 * 2.0 ** 38
ESW = 264
QW = 184
KB = 1
HASH = True
EW = 256
EV0 = 0
UPD = "s"


def RND(p):
    return 1.5 * 2.0 ** (23 + p)


YS = (768, 512)
DCUT = (0, 1024, 2048)
EV = 768
EARLY = ()
LATE = ()
ADD = False
PARTS = ((("v", 1024),) * 4, (("s", 512),) * 1 + (("v", 512),) * 7)
LOADS = ((("y", "e", 0), ("s", "e", 1), ("y", "m", 0), ("s", "m", 1), ("y", "x", 0), ("s", "x", 1)),
         (("y", "e", 0), ("y", "e", 1), ("y", "m", 0), ("y", "m", 1), ("y", "x", 0), ("y", "x", 1)))
GATE = 1
STORES = ("yyyyy", "yyyyy")
DIS = {"y": 0.5, "s": 0.5, "g": 1.8}
DROW = 0.2
RELU = ("vvvv", "SSSS")

SCRATCH = {"xw0": ("sbuf", [128, XW], "bfloat16"), "xw1": ("sbuf", [128, XW], "bfloat16"), "alt": ("sbuf", [128, 1024], "bfloat16")}
for _n, _w, _d in (
        ("ei0", 1024, "int32"), ("ef", 1024, "float16"), ("mm", 1024, "bfloat16"), ("sm", 1024, "bfloat16"), ("ylb", 1024, "float32"),
        ("d0", 4096, "bfloat16"), ("bb", 4096, "bfloat16"), ("qq0", QC + 2048, "bfloat16"), ("qq1", QC + 2048, "bfloat16"), ("dq", 4096, "bfloat16"),
        ("sg", 4096, "bfloat16"), ("yb", 4096, "bfloat16"),
        ("el16", 256 * ST, "uint16"), ("h16", 128 * ST, "uint16"),
        ("es", 2 * ESW, "float32"), ("hf", 128 * ST, "float16"), ("av", 256, "float16"), ("ax", 256, "bfloat16"),
        ("qw", 256, "float32"), ("qd", QW * ST, "bfloat16"), ("lq", QW * ST, "bfloat16"), ("lt", 16 * ST, "uint16"),
        ("pi", 1, "int32"), ("ci", 8, "int32"), ("cf", 32, "float32"), ("m1", 128, "float32"), ("m64", 128, "float32"), ("low", 128, "bfloat16"), ("si", 128, "float32"),
        ("clf", 16, "float32"), ("cl", 16, "uint16"), ("icf", 16, "float32"), ("icn", 16, "bfloat16"), ("mg", 128, "float32"),
        ("zz", 128, "bfloat16"), ("mk32", 32, "bfloat16"), ("i31", 128, "bfloat16"),
        ("dup2", 256, "bfloat16"), ("rcp", 80, KD), ("kb", 64, "float16"), ("nbl", 128, "bfloat16"),
        ("mr", 128, "bfloat16"), ("z16", 16, "bfloat16"),
        ("idn", 128, "bfloat16"), ("nid", 128, "bfloat16"), ("nk", 128, "bfloat16"), ("idf", 128, "float32"), ("nidf", 128, "float32"),
        ("idh", 128, "float16"), ("nidh", 128, "float16"), ("ih32", 128, "float16"), ("big", 128, "bfloat16"), ("nbig", 128, "bfloat16"), ("dup", 128, "bfloat16"),
        ("hdup", 128, "bfloat16"), ("ndup", 128, "bfloat16"), ("g8", 8, "bfloat16"), ("gw", 48, "bfloat16"),
        ("cs", 576, "bfloat16"), ("ch", 320, "bfloat16"), ("ct", 112, "bfloat16"),
        ("cd", 128, "bfloat16"), ("id15", 128, "float16"), ("big15", 128, "bfloat16"), ("pm", 512, "float16"),
        ("p65", 512, "float16"), ("n65", 512, "float16"), ("pmt", 512, "float16"),
        ("t1", 128, "bfloat16"), ("one", 128, "bfloat16"), ("non", 128, "bfloat16"), ("ke", 128, KD),
        ("kt", 128 * ST, KD), ("sc", 128 * ST, KD),
        ("nw", 128 * ST, "bfloat16"), ("lm", 128, KD),
        ("kj", 16, "bfloat16"), ("kc", 1, "float32"), ("kl", 1, "float32"), ("kd", 1, "bfloat16"),
        ("us", 512, "bfloat16"), ("l16", 8, "uint16")):
    SCRATCH[_n] = ("sbuf", [128, _w], _d)
SCRATCH["hz"] = ("sbuf", [128, 68, 8], "float16" if HASH else "float32")
SCRATCH["ta"] = SCRATCH["tb"] = ("sbuf", [128, 256], "int32")
for _t in range(8):
    SCRATCH["p%d" % _t] = ("psum", [128, 128, 4], "float32")
SEMAPHORES = ["cv", "cs", "cp", "cg", "ls"] + ["aq%d" % _t for _t in range(ST)] \
    + ["dm%d" % _t for _t in range(48)]

ORDER = {}
SEED = 4
TRIES = 1700
SWAPS = (36000, 36000, 1)
HEAT2 = 0.04
SHIFT = 2.5
HEAT = 0.15
PER = 9.8
SOON = (0.5, 4.0)
FIRST = {"e1.s1": 2.0, "d1.s1": 1.0, "g0.v2": 2.0, "g1.v1": 2.7, "g1.v2": 3.3, "hop0.p2": 4.0, "hop0.p3": 4.1, "hop0.v1": 4.9, "hx0.v1": 5.2, "hx0.v2": 5.5,
         "hop0.p5": 5.6, "hop0.p6": 5.7, "hop0.v2": 6.0, "gate0.v1": 5.3, "y00.s1": 6.1, "y01.s1": 6.2, "hop1.p2": 4.5, "hop1.p3": 4.6, "y00.p2": 6.5, "s00.s1": 6.9,
         "y10.s1": 6.85, "v0.v1": 6.3, "v0.v2": 7.2}
EM = (0, 1, 2, 3)
GAP = 0.8
ENDS = 0.6
START = {"fill": (-9.0, 0.1), "next": (1.0, 0.3), "back0": (11.0, 0.1), "back1": (17.0, 0.1), "store": (14.0, 0.1), "keep": (12.0, 0.5), "load": (-12.0, 0.1), "add": (-4.0, 0.1),
         "late1": (12.5, 0.2), "late2": (15.0, 0.2), "late3": (17.5, 0.2), "update": (12.3, 0.1)}
PLAN7 = """9.10 e0.v1 -0.13 -0.58 e0.v2 -0.63 -0.08 e1.s1 -0.43 -0.38 d0.s1 0.00 0.05 g0.v1 1.44 1.49 g0.v2 2.52 2.68 d1.s1 1.84 1.39 g1.v1 3.38 3.33 g1.v2 4.02 3.97 hop0.p1 -4.89 -4.84 hop0.p2 0.41 0.46 hop0.p3 0.80 0.86 hop0.v1 1.32 1.37 hx0.v1 2.14 2.19 hx0.v2 3.17 2.58 hop0.p4 -2.56 -2.50 hop0.p5 3.32 2.83 hop0.p6 3.42 2.89 hop0.v2 3.87 3.82 gate0.v1 4.95 4.89 hop1.p1 -1.27 -1.22 hop1.p2 4.72 4.66 hop1.p3 5.11 5.06 hop1.v1 5.63 5.58 hx1.v1 5.89 5.84 hx1.v2 6.15 6.09 hop1.p4 5.86 5.81 hop1.p5 6.29 6.24 hop1.p6 6.35 6.30 hop1.v2 6.72 6.67 gate1.v1 5.73 5.68 y00.s1 4.02 3.97 y00.p1 2.53 2.58 y00.p2 5.99 5.93 s00.s1 6.29 6.24 y01.s1 4.75 4.70 y01.p1 4.02 3.97 y01.p2 6.72 6.67 s01.s1 7.60 7.55 y10.s1 6.86 6.81 y10.p1 7.06 7.00 y10.p2 7.70 7.65 s10.s1 8.16 8.11 v1.v1 6.98 6.93 v1.v2 8.26 8.20 score.p1 6.91 6.86 score.p2 7.02 6.97 score.p3 8.26 8.21 score.p4 8.57 8.52 score.p5 8.82 8.77 keys.v1 9.52 9.47 keys.v2 9.83 9.78 tail1.v1 10.14 10.09 tail1.p1 10.36 10.30 tail1.p2 10.45 10.40 tail1.v2 11.09 11.04 tail1.v3 11.19 11.14 tail1.v4 11.40 11.35 tail2.v1 11.60 11.55 tail2.g1 11.72 11.67 tail2.a1 12.51 12.46 lists.p1 11.34 11.29 lists.v1 13.73 13.78 turn.p1 10.86 10.81 turn.s1 11.84 12.29 kappa.s1 10.45 10.45 kappa.s2 10.77 10.77 kappa.p1 11.05 11.05 kappa.v1 12.38 12.38 arrive.p1 14.56 14.61 arrive.p2 10.74 10.68 arrive.p3 14.73 14.78 arrive.v1 15.05 15.10 arrive.s1 14.85 14.90 arrive.v2 15.30 15.35 arrive.v3 15.88 15.93 arrive.v4 16.69 16.74"""
PLAN = """9.06 e0.v1 0.12 0.15 e0.v2 -0.23 -0.20 e0.v3 1.00 1.03 e1.s1 1.52 1.37 d0.s1 0.00 0.03 g0.v1 1.54 1.57 g0.v2 2.57 2.59 d1.s1 1.95 1.80 g1.v1 3.58 3.61 g1.v2 4.28 4.26 hop0.p1 0.99 1.02 hop0.p2 2.05 1.90 hop0.p3 2.45 2.30 hop0.v1 3.22 3.25 hx0.v1 3.48 3.51 hx0.v2 4.18 4.11 hop0.p4 2.84 3.04 hop0.p5 4.32 4.25 hop0.p6 4.39 4.31 hop0.v2 4.94 4.91 gate0.v1 3.32 3.35 hop1.p1 0.85 0.88 hop1.p2 4.98 4.95 hop1.p3 5.37 5.34 hop1.v1 5.89 5.86 hx1.v1 6.15 6.12 hx1.v2 6.41 6.38 hop1.p4 4.63 4.56 hop1.p5 6.55 6.52 hop1.p6 6.61 6.58 hop1.v2 7.02 6.99 gate1.v1 5.99 5.96 y00.s1 5.08 5.05 y00.p1 2.97 3.17 y00.p2 6.12 6.09 s00.s1 6.83 6.80 y01.s1 6.40 6.37 y01.p1 6.98 6.95 y01.p2 7.14 7.11 s01.s1 8.13 8.10 v0.v1 5.31 5.28 v0.v2 6.51 6.48 y10.s1 7.39 7.36 y10.p1 7.49 7.46 y10.p2 8.23 8.20 s10.s1 8.53 8.50 v1.v1 7.33 7.30 v1.v2 8.60 8.57 score.p1 6.86 6.83 score.p2 8.41 8.38 score.p3 8.57 8.54 score.p4 8.88 8.85 score.p5 9.19 9.16 keys.v1 9.62 9.59 keys.v2 9.93 9.90 tail1.v1 10.44 10.41 tail1.p1 9.85 9.82 tail1.p2 10.68 10.65 tail1.v2 11.13 11.10 tail1.v3 11.23 11.20 tail1.v4 11.38 11.35 tail2.v1 11.58 11.55 tail2.g1 11.70 11.67 tail2.a1 12.49 12.46 lists.p1 11.76 12.85 lists.v1 14.07 14.10 turn.p1 9.50 9.47 turn.s1 12.21 12.53 kappa.s1 10.41 10.41 kappa.s2 12.36 12.36 kappa.p1 12.63 12.63 kappa.v1 13.14 13.14 arrive.p1 14.80 14.83 arrive.p2 9.72 9.69 arrive.p3 14.97 15.00 arrive.v1 15.29 15.32 arrive.s1 15.09 15.12 arrive.v2 15.71 15.74 arrive.v3 16.20 16.23 arrive.v4 17.01 17.04"""
PLAN5 = """9.15 e0.v1 -0.04 -0.04 e0.v2 0.31 0.31 e0.v3 0.81 0.81 e1.s1 1.34 1.34 d0.s1 0.00 0.00 g0.v1 1.67 1.67 g0.v2 2.69 2.69 d1.s1 1.95 1.77 g1.v1 3.96 3.96 g1.v2 4.61 4.61 hop0.p1 0.95 0.95 hop0.p2 1.99 1.99 hop0.p3 2.39 2.39 hop0.v1 3.34 3.34 hx0.v1 3.61 3.60 hx0.v2 3.86 3.86 hop0.p4 1.09 1.09 hop0.p5 4.00 4.00 hop0.p6 4.07 4.07 hop0.v2 4.46 4.46 gate0.v1 3.45 3.70 hop1.p1 -1.71 -1.71 hop1.p2 5.30 5.30 hop1.p3 5.69 5.69 hop1.v1 6.21 6.21 hx1.v1 6.47 6.47 hx1.v2 6.73 6.73 hop1.p4 4.31 4.31 hop1.p5 6.87 6.87 hop1.p6 6.93 6.93 hop1.v2 7.30 7.30 gate1.v1 6.31 6.31 y00.s1 4.60 4.60 y00.p1 4.78 4.56 y00.p2 6.44 6.44 s00.s1 6.75 6.75 y01.s1 5.68 5.68 y01.p1 7.18 7.18 y01.p2 7.34 7.34 s01.s1 8.18 8.18 v0.v1 5.26 5.26 v0.v2 5.87 5.87 y10.s1 7.45 7.45 y10.p1 7.57 7.57 y10.p2 8.28 8.28 s10.s1 8.58 8.58 v1.v1 7.57 7.57 v1.v2 8.84 8.84 score.p1 8.46 8.46 score.p2 8.58 8.58 score.p3 8.62 8.62 score.p4 8.93 8.93 score.p5 9.25 9.25 keys.v1 9.80 9.80 keys.v2 10.31 10.31 tail1.v1 10.62 10.62 tail1.p1 10.00 10.00 tail1.p2 10.85 10.85 tail1.v2 11.31 11.31 tail1.v3 11.41 11.41 tail1.v4 11.56 11.56 tail2.v1 11.76 11.76 tail2.g1 11.88 11.88 tail2.a1 12.67 12.67 lists.p1 12.15 12.28 lists.v1 14.75 14.75 turn.p1 11.93 13.71 turn.s1 14.48 14.48 kappa.s1 10.92 10.92 kappa.s2 10.93 10.93 kappa.p1 11.93 11.93 kappa.v1 12.86 12.86 arrive.p1 15.24 15.24 arrive.p2 13.59 13.59 arrive.p3 15.40 15.40 arrive.v1 15.72 15.72 arrive.s1 15.52 15.52 arrive.v2 15.98 15.98 arrive.v3 16.55 16.55 arrive.v4 17.36 17.36"""
PLAN4 = """9.80 e1.s1 -1.34 -1.34 d0.s1 0.00 0.00 g0.v1 2.35 2.35 g0.v2 3.21 3.11 d1.s1 1.52 1.34 g1.v1 3.86 3.76 g1.v2 4.50 4.40 hop0.p1 -2.35 -2.35 hop0.p2 0.44 0.44 hop0.p3 0.83 0.83 hop0.v1 1.37 1.37 hx0.v1 1.67 1.67 hx0.v2 2.95 2.84 hop0.p4 2.55 2.20 hop0.p5 3.27 2.99 hop0.p6 3.33 3.05 hop0.v2 4.35 4.25 gate0.v1 5.80 5.80 hop1.p1 -3.44 -3.19 hop1.p2 5.57 5.57 hop1.p3 5.97 5.97 hop1.v1 6.49 6.49 hx1.v1 6.75 6.75 hx1.v2 7.01 7.01 hop1.p4 6.75 6.75 hop1.p5 7.15 7.15 hop1.p6 7.21 7.21 hop1.v2 7.73 7.73 gate1.v1 7.84 7.84 y00.s1 4.50 4.39 y00.p1 3.02 2.67 y00.p2 6.88 6.88 s00.s1 7.18 7.18 y01.s1 5.85 5.85 y01.p1 6.37 6.50 y01.p2 7.60 7.60 s01.s1 7.90 7.90 v1.v1 7.99 7.99 v1.v2 9.40 9.40 score.p1 8.69 8.69 score.p2 8.80 8.80 score.p3 8.83 8.83 score.p4 9.14 9.14 score.p5 9.93 9.93 keys.v1 10.36 10.36 keys.v2 10.67 10.67 tail1.v1 10.98 10.98 tail1.p1 11.03 11.03 tail1.p2 11.22 11.22 tail1.v2 11.62 11.62 tail1.v3 11.73 11.73 tail1.v4 11.88 11.88 tail2.v1 12.07 12.07 tail2.g1 12.20 12.20 tail2.a1 12.99 12.99 hf.v1 9.89 9.89 nw.v1 11.28 11.28 update.p1 11.50 11.85 update.p2 11.79 12.14 update.v1 12.75 12.86 update.s1 12.95 13.05 lists.p1 12.13 12.48 lists.v1 14.85 14.96 turn.p1 13.28 13.39 turn.s1 16.39 16.39 kappa.s1 11.15 11.15 kappa.p1 11.50 11.50 kappa.v1 12.65 12.65 arrive.p1 15.03 15.03 arrive.p2 8.56 8.56 arrive.p3 15.19 15.19 arrive.v1 15.50 15.50 arrive.s1 15.31 15.31 arrive.v2 15.76 15.76 arrive.v3 16.40 16.40 arrive.v4 16.91 16.91"""
PLAN3 = """9.24 e1.s1 -1.34 -1.30 d0.s1 0.00 0.04 g0.v1 1.56 1.48 g0.v2 2.42 2.35 d1.s1 1.52 1.38 g1.v1 3.18 3.10 g1.v2 3.83 3.75 hop0.p1 -0.64 -0.60 hop0.p2 0.33 0.58 hop0.p3 0.94 0.97 hop0.v1 1.45 1.97 hop0.p4 -3.00 -2.96 hop0.p5 2.03 2.12 hop0.p6 2.46 2.43 hop0.v2 3.07 3.00 gate0.v1 3.67 3.59 hop1.p1 -1.60 -1.44 hop1.p2 4.52 4.44 hop1.p3 4.92 4.84 hop1.v1 5.43 5.35 hop1.p4 4.39 5.23 hop1.p5 5.58 5.54 hop1.p6 5.89 5.85 hop1.v2 6.39 6.35 gate1.v1 6.50 6.46 y00.s1 3.22 3.14 y00.p1 2.84 2.81 y00.p2 4.20 4.24 s00.s1 5.22 5.25 y01.s1 4.48 4.52 y01.p1 3.22 3.14 y01.p2 5.32 5.35 s01.s1 5.78 5.82 y10.s1 6.54 6.50 y10.p1 6.84 6.80 y10.p2 7.22 7.18 s10.s1 7.48 7.44 v1.v1 6.66 6.62 v1.v2 7.61 7.57 score.p1 6.70 6.66 score.p2 6.81 6.77 score.p3 7.48 7.32 score.p4 7.93 7.77 score.p5 8.03 7.99 keys.v1 8.46 8.42 keys.v2 8.77 8.73 tail1.v1 9.08 9.04 tail1.p1 8.77 8.73 tail1.p2 9.32 9.28 tail1.v2 9.72 9.68 tail1.v3 9.83 9.79 tail1.v4 9.98 9.94 tail2.v1 10.17 10.13 tail2.g1 10.29 10.26 tail2.a1 11.08 11.05 hf.v1 7.93 7.90 nw.v1 9.28 9.24 update.p1 8.34 8.30 update.p2 9.60 9.96 update.v1 10.25 10.29 update.s1 11.96 12.09 lists.p1 10.61 10.57 lists.v1 11.31 11.28 turn.p1 12.62 12.70 turn.s1 16.32 16.35 kappa.s1 10.58 10.58 kappa.p1 10.91 10.91 kappa.v1 11.55 11.55 arrive.p1 13.12 13.09 arrive.p2 7.36 6.48 arrive.p3 13.29 13.25 arrive.v1 13.64 13.71 arrive.s1 13.41 13.37 arrive.v2 13.89 13.97 arrive.v3 14.39 14.47 arrive.v4 14.70 14.78"""
MACHINES = ((0.89, 0.74, 0.75, 0.9, 1.0, 0.0, 0.9), (1.2, 1.45, 1.9, 1.2, 1.0, 0.5, 1.4), (0.87, 1.08, 0.6, 0.87, 1.3, 1.5, 1.12), (1.1, 0.85, 1.4, 1.5, 1.3, 0.5, 1.15))
LAND = 2.0
WAKE = (0.15, 0.04)
MORE = {"p": 0.08, "s": 0.06}
CALL = 0.75
FIX = 0.03
C0 = 26
CYC = 0.00097
PCY = 0.00038
PFX = 0.01
PGR = 0.07
SX = 0.08
OUTL = (4.5, 4.5, 1.0)
GAT = 0.0016
SCA = 0.003
DLAT = 1.5
DBW = 0.33e6


def arrange(nodes, before):
    n = len(nodes)
    rn = range(n)
    qs = ["vspgy".find(d["q"] or "-") for d in nodes]
    late = [d["late"] for d in nodes]
    pre, anc, last = [], [0] * n, {}
    for i, d in enumerate(nodes):
        lag = {}
        for j, x in before[i]:
            lag[j] = max(x, lag.get(j, 0.0))
        if d["kind"] == "d" and d["tag"][0] < 0:
            if d["q"] in last:
                lag.setdefault(last[d["q"]], 0.0)
            last[d["q"]] = i
        keep = []
        for j in sorted(lag, reverse=True):
            if not anc[i] >> j & 1 or late[j]:
                keep.append((j, lag[j]))
            anc[i] |= anc[j] | 1 << j
        pre.append(keep)
    pj = [[j for j, _ in b] for b in pre]
    waits = [set(p) for p in pj]
    w = PLAN.split()
    plan = {a: (float(x), float(y)) for a, x, y in zip(w[1::3], w[2::3], w[3::3])}
    cnt, alike, kind, key = {}, {}, [], [None] * n
    for i, d in enumerate(nodes):
        s, name = d["tag"]
        cnt[(s, name, d["q"])] = c = cnt.get((s, name, d["q"]), 0) + 1
        k = "%s.%s%d" % (name, d["q"] or "a", c)
        if k in plan:
            key[i] = s * float(w[0]) + (FIRST.get(k, plan[k][0]) if s == 0 else plan[k][s % 2])
        elif name in START:
            key[i] = max(s, 0) * float(w[0]) + START[name][0] + START[name][1] * c
        kind.append((k, s % 2) if k in plan else i)
        alike.setdefault(kind[i], []).append(i)
    need = [1e9] * n
    for i in reversed(rn):
        if key[i] is None:
            key[i] = need[i] - nodes[i]["cost"]
        for j, x in pre[i]:
            need[j] = min(need[j], key[i] - x)
    for i in rn:
        if nodes[i]["tag"][1] in ("pre", "soon"):
            key[i] = SOON[0] * key[i] - SOON[1]
    extra = [kind[i] == i and nodes[i]["kind"] == "c" for i in rn]
    bare = [dict(d, q=None, cost=0.0, fix=0.0) if x else d for d, x in zip(nodes, extra)]
    end = list(polish(bare, pre, key, (), 0)[2])
    cost = lengths(nodes, MACHINES[EM[0]])
    for i in rn:
        key[i] = end[i] - (0.0 if extra[i] else cost[i])
    need, busy = [1e9] * n, {q: sorted((key[i], end[i]) for i in rn if nodes[i]["q"] == q and not extra[i]) for q in "vspg"}
    for i in reversed(rn):
        if extra[i]:
            need[i] = min(need[i], end[-1] - 4.0) - cost[i]
        for j, x in pre[i]:
            need[j] = min(need[j], (need[i] if extra[i] else key[i]) - x)
    for i in sorted((i for i in rn if extra[i]), key=lambda i: need[i]):
        at = ready = max([end[j] + x for j, x in pre[i]] + [0.0])
        gaps = busy[nodes[i]["q"]]
        for a, b in gaps:
            if at + cost[i] <= a + 0.02:
                break
            at = max(at, b)
        if at > need[i]:
            at = max(ready, min([need[i]] + [a - 1e-3 for a, b in gaps if a <= need[i] < b]))
        key[i], end[i] = at, at + cost[i]
        gaps.append((at, end[i]))
        gaps.sort()
    for lo, hi, free, swaps in ((-1, 5, range(-1, 3), SWAPS[0]), (ST - 5, ST, range(ST - 3, ST), SWAPS[1]), (-1, ST, range(-1, ST), SWAPS[2])):
        ids = [i for i in rn if lo <= nodes[i]["tag"][0] <= hi]
        at = {j: i for i, j in enumerate(ids)}
        best = polish([nodes[i] for i in ids], [[(at[j], x) for j, x in pre[i] if j in at] for i in ids], [key[i] for i in ids], free, swaps)
        for i, x in zip(ids, best[4]):
            if nodes[i]["tag"][0] in free:
                key[i] = x
    return best


def lengths(nodes, m):
    f = {"p": m[3], "v": m[0], "s": m[0], "gather": m[1], "scatter": m[2]}
    return [d["fix"] * m[0] + (d["cost"] - d["fix"]) * (f.get(d["by"], 1.0) if d["kind"] == "c" else 1.0) for d in nodes]


def polish(nodes, pre, key, free, swaps):
    n = len(nodes)
    rn = range(n)
    qs = ["vspgy".find(d["q"] or "-") for d in nodes]
    late = [d["late"] for d in nodes]
    pj = [[j for j, _ in b] for b in pre]
    waits = [set(p) for p in pj]
    sets = []
    for fc, fg, fs, fp, fw, more, whole in [MACHINES[m] for m in EM]:
        f = {"p": fp, "v": fc, "s": fc, "gather": fg, "scatter": fs}
        sets.append(([d["fix"] * fc + (d["cost"] - d["fix"]) * (f.get(d["by"], 1.0) if d["kind"] == "c" else 1.0) for d in nodes],
                     [[(j, late[j] + (more if nodes[j]["kind"] == "a" else 0.0) + fw * (x - late[j]) if x else 0.0) for j, x in b] for b in pre], whole))
    ends = [i for i in rn if nodes[i]["tag"][0] >= nodes[-1]["tag"][0] - 1]

    def judge(at):
        for i in rn:
            x = at[i]
            for j in pj[i]:
                if at[j] >= x:
                    x = at[j] + 1e-6
            at[i] = x
        order, res = sorted(rn, key=lambda i: at[i]), []
        for cost, pr, whole in sets:
            end, why, last = [0.0] * n, [-1] * n, [-1] * 5
            for i in order:
                r, w = 0.0, -1
                for j, x in pr[i]:
                    e = end[j] + x
                    if e > r:
                        r = e
                        w = j
                q = qs[i]
                if q >= 0:
                    j = last[q]
                    if j >= 0 and end[j] >= r:
                        r = end[j]
                        w = j
                    last[q] = i
                end[i] = r + cost[i]
                why[i] = w
            top = max(ends, key=lambda i: end[i] + late[i])
            res.append((end[top] + late[top], end, why, top))
        return sum(x[0] / s[2] for x, s in zip(res, sets)) / len(sets), order, res[0][1], res, at
    seed = [SEED]

    def rnd():
        seed[0] = (seed[0] * 1103515245 + 12345) % 2147483648
        return seed[0] / 2147483648
    best = cur = judge(key)
    for it in range(swaps):
        _, _, why, i = cur[3][int(rnd() * len(sets))]
        at, pairs = cur[4], []
        while i >= 0:
            j = why[i]
            if j >= 0 and j not in waits[i] and (nodes[i]["tag"][0] in free or nodes[j]["tag"][0] in free):
                pairs.append((j, i))
            i = j
        if not pairs:
            continue
        j, i = pairs[int(rnd() * len(pairs))]
        x = at[i] - at[j] + (1e-3, 1e-3, 0.3, 1.0, 3.0)[int(rnd() * 5)] * rnd()
        if nodes[j]["tag"][0] not in free or nodes[i]["tag"][0] in free and rnd() < 0.5:
            move, todo = {i: -x}, [i]
            while todo:
                for b in pj[todo.pop()]:
                    if b not in move and at[b] > at[i] - x:
                        move[b] = at[i] - x - 1e-4 - at[b]
                        todo.append(b)
        else:
            move = {j: x}
        new = list(at)
        for a, x in move.items():
            new[a] += x
        r = judge(new)
        if r[0] - cur[0] < -math.log(1e-9 + rnd()) * (HEAT2 * (1.0 - it / swaps) + 0.003):
            cur = r
            if r[0] < best[0]:
                best = r
    return best


def old_arrange(nodes, before):
    n = len(nodes)
    qs = [d["q"] for d in nodes]
    cost = [d["cost"] for d in nodes]
    late = [d["late"] for d in nodes]
    pre = [list(b) for b in before]
    last, cnt, kinds, key = {}, {}, {}, []
    for i, d in enumerate(nodes):
        s, name = d["tag"]
        cnt[(s, name, d["q"])] = c = cnt.get((s, name, d["q"]), 0) + 1
        if d["kind"] == "d" and s < 0:
            if d["q"] in last:
                pre[i].append((last[d["q"]], 0.0))
            last[d["q"]] = i
        if name in ("pre", "fill", "soon", "next"):
            key.append(START[name] + 0.1 * c)
        else:
            key.append(s * PER + START[name] + 0.1 * c)
        if name not in ("pre", "soon"):
            kinds.setdefault((name, d["q"], c), []).append(i)
            kinds.setdefault(name, []).append(i)
    for a, b in FIRST:
        for i, j in zip(kinds[a], kinds[b]):
            pre[j].append((i, 0.0))
    alike = [(i,) for i in range(n)]
    for k, v in kinds.items():
        if k not in START and k[0] != "next":
            for i in v:
                alike[i] = [j for j in v if (nodes[j]["tag"][0] - nodes[i]["tag"][0]) % 2 == 0]
    kinds = list(kinds.values())
    suc = [[] for _ in range(n)]
    for i in range(n):
        for j, lag in pre[i]:
            suc[j].append((i, lag))

    def feasible(at, edges, run):
        for i in run:
            x = at[i]
            for j, _ in edges[i]:
                if at[j] >= x:
                    x = at[j] + 1e-7
            at[i] = x
        return sorted(range(n), key=lambda i: at[i])

    def place(order, edges, head):
        end = [0.0] * n
        busy = {q: ([], []) for q in qs}
        for i in order:
            r = head[i]
            for j, lag in edges[i]:
                e = end[j] + lag
                if e > r:
                    r = e
            c = cost[i]
            if qs[i] is not None:
                a, b = busy[qs[i]]
                k = m = len(a)
                while k and b[k - 1] > r:
                    k -= 1
                while k < m and r + c > a[k] + 1e-9:
                    r = b[k]
                    k += 1
                a.insert(k, r)
                b.insert(k, r + c)
            end[i] = r + c
        return end
    seed = [SEED]

    def rnd():
        seed[0] = (seed[0] * 1103515245 + 12345) % 2147483648
        return seed[0] / 2147483648
    up, down, zero = range(n), range(n - 1, -1, -1), [0.0] * n
    ends = [i for i in up if not suc[i]]
    sets = []
    for fc, fg, fs, fp, fw, more, whole in MACHINES:
        f = {"p": fp, "v": fc, "s": fc, "gather": fg, "scatter": fs}
        sets.append(([c * (f.get(d["by"], 1.0) if d["kind"] == "c" else 1.0) for c, d in zip(cost, nodes)],
                     [[(j, late[j] + (more if nodes[j]["kind"] == "a" else 0.0) + fw * (lag - late[j]) if lag else 0.0) for j, lag in b] for b in pre], whole))

    def replay(order, cost, pre):
        end, why, last = [0.0] * n, [-1] * n, {}
        for i in order:
            r, w = 0.0, -1
            for j, lag in pre[i]:
                e = end[j] + lag
                if e > r:
                    r = e
                    w = j
            q = qs[i]
            if q is not None:
                j = last.get(q, -1)
                if j >= 0 and end[j] >= r:
                    r = end[j]
                    w = j
                last[q] = i
            end[i] = r + cost[i]
            why[i] = w
        top = max(ends, key=lambda i: end[i] + late[i])
        return end[top] + late[top], end, why, top

    def judge(order):
        r = [replay(order, c, p) for c, p, _ in sets]
        return sum(x[0] / s[2] for x, s in zip(r, sets)) / len(sets), order, r[0][1], r
    best = cur = None
    for it in range(TRIES):
        end = place(feasible(key, pre, up), pre, zero)
        total = judge(feasible([e - c for e, c in zip(end, cost)], pre, up))[0]
        if cur is None or total - cur[0] < -math.log(1e-9 + rnd()) * HEAT * (1.0 - it / TRIES):
            cur = (total, end, place(feasible([-e for e in end], suc, down), suc, late))
            if best is None or total < best[0]:
                best = cur
        key = [-x for x in cur[2]] if rnd() < 0.8 else [e - c for e, c in zip(cur[1], cost)]
        for _ in range(1 + int(rnd() * 3)):
            x = SHIFT * (2.0 * rnd() - 1.0)
            for i in kinds[int(rnd() * len(kinds))]:
                key[i] += x
    waits = [set(j for j, _ in b) for b in pre]
    key = [e - c for e, c in zip(best[1], cost)]
    best = cur = judge(feasible(key, pre, up))
    for it in range(SWAPS):
        _, _, why, i = cur[3][int(rnd() * len(sets))]
        pairs = []
        while i >= 0:
            j = why[i]
            if j >= 0 and j not in waits[i]:
                pairs.append((j, i))
            i = j
        j, i = pairs[int(rnd() * len(pairs))]
        x = key[i] - key[j] + (1e-4, 1e-4, 0.3, 1.0)[int(rnd() * 4)] * rnd()
        k, x = (i, -x) if rnd() < 0.5 else (j, x)
        new = list(key)
        for z in alike[k] if rnd() < 0.8 else (k,):
            new[z] += x
        r = judge(feasible(new, pre, up))
        if r[0] - cur[0] < -math.log(1e-9 + rnd()) * (HEAT2 * (1.0 - it / SWAPS) + 0.003):
            cur, key = r, new
            if r[0] < best[0]:
                best = r
    return best


def rank_program(g, core, T, topo):
    rank = T.rank_of(core)
    if rank is None:
        return
    n_ranks = len(T.cores)
    eng = {"v": g.vector, "s": g.scalar, "p": g.tensor, "g": g, "y": g.sync}
    semname = {"v": "cv", "s": "cs", "p": "cp", "g": "cg"}

    nodes = []
    wr, rd, bank = {}, {}, {}
    ndma = [0]
    tag = [(-1, "pre")]

    def stage(s, name):
        tag[0] = (s, name)

    def node(q, calls, cost, R, W, B=(), kind="c", key=None, late=0.0, extra=()):
        d = set(extra)
        for (b, lo, hi) in R:
            for (l, h, i) in wr.get(b, ()):
                if l < hi and lo < h:
                    d.add(i)
        for (b, lo, hi) in W:
            for (l, h, i) in wr.get(b, ()):
                if l < hi and lo < h:
                    d.add(i)
            for (l, h, i) in rd.get(b, ()):
                if l < hi and lo < h:
                    d.add(i)
        me = len(nodes)
        by, fix = q, 0.0
        if isinstance(cost, tuple):
            by, n = cost
            fix = 0.05 if q == "v" else 0.065 + SX
            cost = fix + n * (GAT if by == "gather" else SCA)
        order = set()
        for b in B:
            prev, cur = bank.get(b, ([], []))
            if cur and nodes[cur[-1]]["q"] != q:
                prev, cur = cur, []
            d.update(prev)
            if cur and q == "p":
                order.add(cur[-1])
            bank[b] = (prev, cur + [me])
        nodes.append({"q": q, "calls": calls, "cost": cost, "deps": d, "order": order - d, "kind": kind, "key": key, "late": late, "tag": tag[0], "by": by, "fix": fix})
        for (b, lo, hi) in W:
            wr[b] = [e for e in wr.get(b, ()) if not (lo <= e[0] and e[1] <= hi)] + [(lo, hi, me)]
            rd[b] = [e for e in rd.get(b, ()) if not (lo <= e[0] and e[1] <= hi)]
        for (b, lo, hi) in R:
            rd.setdefault(b, []).append((lo, hi, me))
        return me

    def dma(q, out, in_, R, W, late, extra=(), **kw):
        name = "dm%d" % ndma[0]
        ndma[0] += 1
        return node(q, [lambda e: e.dma_start(out, in_, **kw)], DIS[q], R, W, (), "d", name, late, extra)

    def A(b, lo=0, hi=1 << 20):
        return (b, lo, hi)

    def cy(n):
        return max(64, n + C0) * CYC + FIX

    def mms(lst, n, R, B):
        last = len(lst) - 1
        node("p", [lambda e, a=a, j=j: e.matmul(a[0], a[1], a[2], j == 0, j == last) for j, a in enumerate(lst)], n * PCY + len(lst) * PFX + PGR, R, [], B)

    def mmx(lst, n, R, B):
        node("p", [lambda e, a=a: e.matmul(*a) for a in lst], n * PCY + len(lst) * PFX + PGR * lst[0][3], R, [], B)

    def ts(out, in0, s1, o1, R, W, B=(), s2=None, o2=None, n=64, cost=None):
        if o2 is None:
            node("v", [lambda e: e.tensor_scalar(out, in0, s1, None, o1)], cost or cy(n), R, W, B)
        else:
            node("v", [lambda e: e.tensor_scalar(out, in0, s1, s2, o1, o2)], cost or cy(n), R, W, B)

    def tt(out, a, b, o, R, W, B=(), n=64, cost=None):
        node("v", [lambda e: e.tensor_tensor(out, a, b, o)], cost or cy(n), R, W, B)

    def cp(out, in_, R, W, B=(), n=64, cost=None):
        node("v", [lambda e: e.tensor_copy(out, in_)], cost or cy(n), R, W, B)

    def scn(out, a, b, init, o1, o2, R, W, n):
        node("v", [lambda e: e.tensor_tensor_scan(out, a, b, init, o1, o2)], cy(n), R, W)

    def act(out, in_, f, R, W, B=(), n=64, cost=None, **kw):
        node("s", [lambda e: e.activation(out, in_, f, **kw)], cost or cy(n) + SX, R, W, B)

    def fill(ap, c, W, n=64):
        node("v", [lambda e: e.memset(ap, c)], cy(n), [], W)

    def iota(ap, pat, base, cm, W, n, fl=True):
        if fl:
            node("g", [lambda e: e.iota(ap, pat, base, cm, allow_small_or_imprecise_dtypes=True)], 0.13 + 2 * n * CYC, [], W)
        else:
            node("g", [lambda e: e.iota(ap, pat, base, cm)], 0.13 + 2 * n * CYC, [], W)

    xw = (T.xw0, T.xw1)

    def MM(ph, c=None, name="mm"):
        return [A("%s%d%d" % (name, ph, k)) for k in range(4) if c in (None, k)]

    iota(T.pi[:], [[0, 1]], 0, 1, [A("pi")], 1, False)
    iota(T.cf[:, 5:6], [[0, 1]], 0, 1, [("cf", 5, 6)], 1)
    iota(T.m1[:], [[1, 128]], 1, 0, [A("m1")], 128)
    fill(T.alt[:, 0::2], 4096.0, [A("alt", 0, 1)], 256)
    fill(T.alt[:, 1::2], DEL, [A("alt", 1, 2)], 256)
    stage(-1, "fill")
    for lo in range(XC, XR, 1024) if ADD else ():
        act(T.xw1[:, lo:lo + 1024], T.alt[:], AF.Copy, [A("alt")], [A("in1", lo, lo + 1024)], n=1024, scale=0.0, bias=-DEL)
    stage(-1, "load")
    gate, issued, landed = (), {"y": 0.0, "s": 0.0, "g": 0.0}, 0.0
    for ph in range(2):
        done, when = [], []
        for q, what, b in LOADS[ph]:
            rows, o, i = slice(64 * b, 64 * b + 64), slice(512 * ph, 512 * ph + 512), (slice(64 * ph, 64 * ph + 64), slice(512 * b, 512 * b + 512))
            if what == "a":
                stage(-1, "add")
                issued[q] += DIS[q]
                landed = max(landed, issued[q] + DLAT) + 1048576 / DBW + DROW
                added = dma(q, T.xw1[rows, XC:XR], T.xt[i[0], :], [A("in1")], [A("xw1", XC + 2048 * b, XC + 2048 * b + 2048)], landed - issued[q], gate,
                            accum_op=OP.add, max_dma_last_dim=4096)
                continue
            out, in_, W, size = {
                "x": (xw[ph][rows, XR + XC:XR + XC + 4096], T.xt[i[0], :], [A("xw%d" % ph, XR + XC + 2048 * b, XR + XC + 2048 * b + 2048)], 524288),
                "e": (T.ei0[rows, o], T.led[i], [A("ei0%d" % ph, b, b + 1)], 131072),
                "m": (T.mm[rows, o], T.mk[i], [A(n, b, b + 1) for n, _, _ in MM(ph)], 65536)}[what]
            issued[q] += DIS[q]
            landed = max(landed, issued[q] + DLAT) + size / DBW + DROW
            done.append(dma(q, out, in_, [], W, landed - issued[q], gate))
            when.append(landed)
        gate = done[GATE:GATE + 1]
        issued["y"] = issued["g"] = max(issued["y"], when[GATE])
    if ADD:
        dma("y", T.xw1[:, XR + XC:2 * XR], T.xt[:], [], [A("xw1", XR + XC, 2 * XR)], DLAT + 1048576 / DBW + DROW, (added,))
    stage(-1, "pre")

    def convert(ph, first):
        o = slice(512 * ph + first, 512 * ph + 512, 4)
        ts(T.ef[:, o], T.ei0[:, o], -2048.0, OP.add, [A("ei0%d" % ph)], MM(ph, first, "ef"), n=128)
        if first == 0:
            o = slice(512 * ph, 512 * ph + 512)
            act(T.sm[:, o], T.mm[:, o], AF.Copy, MM(ph), MM(ph, None, "sm"), n=512, scale=-2.0, bias=1.0)
            lo = XC
            for q, w in PARTS[ph]:
                rg, R = A("xw%d" % ph, lo, lo + w), A("xw%d" % ph, XR + XC, XR + XC + 4096)
                if q == "v":
                    ts(xw[ph][:, lo:lo + w], xw[ph][:, XR + lo:XR + lo + w], -DEL, OP.add, [R], [rg], n=w // 2)
                else:
                    act(xw[ph][:, lo:lo + w], xw[ph][:, XR + lo:XR + lo + w], AF.Copy, [R], [rg], n=w, bias=-DEL)
                lo += w
    for ph in range(2):
        for lo in (XR, 0):
            iota(xw[ph][:, lo:lo + XC], [[4096, 2], [0, 16]], 0, 0, [A("xw%d" % ph, lo, lo + XC)], XC)

    iota(T.one[:], [[0, 128]], 1, 0, [A("one")], 128)
    node("g", [lambda e: e.affine_select(T.idn[:], T.one[:], [[1, 128]], OP.is_equal, 0.0, 0, -1)], 0.17 + 256 * CYC, [A("one")], [A("idn")])
    iota(T.m64[:], [[0, 2], [1, 64]], 0, 0, [A("m64")], 128)
    iota(T.clf[:], [[16, 16]], 15, 0, [A("clf")], 16)
    iota(T.mg[:], [[0, 2], [16, 4], [0, 16]], 0, 0, [A("mg")], 128)
    iota(T.si[:], [[0, 8], [1, 16]], 0, 0, [A("si")], 128)
    iota(T.icf[:], [[16, 16]], 0, 1, [A("icf")], 16)
    iota(T.non[:], [[0, 128]], -1, 0, [A("non")], 128)

    def C(p, a, b, step=1):
        if step == 1:
            return p[:, a // 4:b // 4, :] if b - a > 1 else p[:, a // 4, a % 4:a % 4 + 1]
        return p[:, a // 4:b // 4, a % 4::2] if step == 2 else p[:, a // 4:b // 4:step // 4, a % 4]

    def rows(name, n, vals, on_g=False):
        if n and on_g:
            iota(T[name][0:65, :], [[0, n]], 0, 0, [A(name)], n)
        elif n:
            fill(T[name][0:65, :], 0.0, [A(name)], n // 2)
        for j, (r, cols, v) in enumerate(vals):
            w = len(range(cols.start, cols.stop, cols.step or 1))
            if isinstance(v, tuple):
                iota(T[name][r:r + 1, cols], v[0], v[1], 0, [A(name, j, j + 1)], w)
            elif on_g:
                where(T[name][0:r + 1, cols], [[0, w]], OP.not_equal, v, -r, 1, A(name, cols.start, cols.stop))
            else:
                act(T[name][r:r + 1, cols], T.m1[r:r + 1, 0:w] if w <= 128 else T.alt[r:r + 1, 0:w], AF.Copy, [A("m1"), A("alt")], [A(name, j, j + 1)], n=w,
                    scale=0.0, bias=v)

    def where(ap, pat, op, v, base, cm, W, src=None):
        a, R = src or (ap, W)
        node("g", [lambda e: e.affine_select(ap, a, pat, op, v, base, cm)], 0.17 + 2 * math.prod(c for _, c in pat) * CYC, [R], [W])

    def diagonal(name, v, lo=0, both=False):
        ap, W, pat = T[name][:, lo:lo + 128], A(name, lo, lo + 128), [[0, 2], [1, 64]] if both else [[1, 128]]
        where(ap, pat, OP.not_equal, v, 64 * (lo > 0), -1, W, (T.zz[:], A("zz")))
        if both is True:
            where(ap, pat, OP.not_equal, v, 64, -1, W)

    def blocks(name, parts):
        n = parts[-1][1]
        iota(T[name][:], [[0, n]], 0, 0, [A(name)], n)
        for lo, hi, v in parts:
            if v:
                where(T[name][:, lo:hi], [[0, (hi - lo) // 8], [16, 8]], OP.is_gt, v, 0, -1, A(name, lo, hi))
        where(T[name][:], [[0, n // 8], [16, 8]], OP.is_gt, 0.0, 16, -1, A(name))

    def times(out, in_, W, R, **kw):
        act(out, in_, AF.Identity, R, W, n=128, **kw)

    def ci(j):
        return T.ci[:, j:j + 1]

    def cf(j):
        return T.cf[:, j:j + 1]

    def rc(j):
        return ("cf", j, j + 1)
    ts(ci(0), T.pi[:], 15, OP.bitwise_and, [A("pi")], [("ci", 0, 1)])
    ts(ci(1), T.pi[:], 1, OP.bitwise_and, [A("pi")], [("ci", 1, 2)])
    ts(ci(2), T.pi[:], 1, OP.logical_shift_right, [A("pi")], [("ci", 2, 3)], (), 7, OP.bitwise_and)
    ts(ci(3), T.pi[:], 48, OP.bitwise_and, [A("pi")], [("ci", 3, 4)])
    ts(ci(4), T.pi[:], 63, OP.bitwise_and, [A("pi")], [("ci", 4, 5)])
    cp(T.cf[:, 0:5], T.ci[:, 0:5], [("ci", 0, 5)], [("cf", 0, 5)])
    tt(cf(6), cf(5), cf(0), OP.subtract, [rc(5), rc(0)], [rc(6)])
    ts(cf(7), cf(1), -1.0, OP.mult, [rc(1)], [rc(7)], (), 1.0, OP.add)
    tt(cf(9), cf(6), cf(2), OP.add, [rc(6), rc(2)], [rc(9)])
    for par in range(2):
        for b in range(2):
            j = 2 * par + b
            ts(cf(11 + j), cf(9), float(8 * b + 1), OP.add, [rc(9), rc(7), rc(1)], [rc(11 + j)], (), cf(1 if par else 7), OP.mult)
            ts(T.pm[:, 128 * j:128 * j + 128], T.m1[:, 0:128], cf(11 + j), OP.is_equal, [A("m1"), rc(11 + j)], [("pm", j, j + 1)], n=128)
    ts(cf(19), cf(0), 14.5, OP.is_lt, [rc(0)], [rc(19)])
    ts(cf(20), cf(19), 2048.0 + XC - 16.0 - BIG, OP.mult, [rc(19)], [rc(20)], (), 16.0 - 2048.0 - XC, OP.add)
    cp(T.idh[:], T.idn[:], [A("idn")], [A("idh")])
    ts(T.ih32[:], T.idn[:], 1.0 if HASH else 1 / 32, OP.mult, [A("idn")], [A("ih32")])
    ts(T.id15[:], T.idn[:], cf(19), OP.mult, [A("idn"), rc(19)], [A("id15")])
    ts(T.big15[:], T.idn[:], cf(19), OP.mult, [A("idn"), rc(19)], [A("big15")], (), BIG, OP.mult)
    times(T.cd[:], T.idn[:], [A("cd")], [A("idn"), rc(20)], scale=0.0, bias=cf(20))
    convert(0, 0)
    stage(-1, "soon")
    for name, v, n in (("ke", 16384, 128), ("z16", 0, 16)):
        iota(T[name][:], [[0, n]], v, 0, [A(name)], n)
    iota(T.qd[:, 160::QW], [[0, ST]], 0, 0, [A("qd0")], ST)
    for ph in range(2):
        iota(T.es[:, ESW * ph + 256:ESW * ph + ESW], [[0, ESW - 256]], 1, 0, [A("esp", ph, ph + 1)], 8)
    iota(T.zz[:], [[0, 128]], 0, 0, [A("zz")], 128)
    rows("cs", 576, [(0, slice(0, 192), ([[0, 64], [1016, 3]], 16)), (32, slice(0, 192), -0.5),
                     (0, slice(192, 384, 3), RND(5)), (0, slice(193, 384, 3), RND(6)), (0, slice(194, 384, 3), RND(12)),
                     (0, slice(384, 576), ([[0, 192]], int(RND(0)))), (32, slice(385, 576, 3), 1.0),
                     (64, slice(385, 576, 3), 1024.0), (64, slice(386, 576, 3), 32.0 if HASH else 2048.0)])
    rows("ch", 0, [(0, slice(0, 64), 31 / 64), (0, slice(64, 128), ([[0, 64]], int(RND(0)))), (0, slice(128, 192), RND(12)), (0, slice(192, 320), ([[0, 128]], 2048 if HASH else 64))])
    rows("ct", 112, [(0, slice(0, 8), 7.0), (32, slice(0, 8), -1 / 64), (0, slice(8, 24), 15.5), (0, slice(24, 40), 0.5),
                     (32, slice(24, 40), 131 * 2.0 ** -16), (0, slice(40, 48), RND(4)), (0, slice(48, 64), RND(5)), (0, slice(64, 80), RND(0)),
                     (32, slice(80, 88), 33 / 64), (0, slice(88, 104), -BIG), (32, slice(88, 104), BIG - XD)], True)
    iota(T.ct[0:1, 80:88], [[256, 8]], 0, 0, [A("ct", 80, 88)], 8)
    fill(T.kb[:], 33 / 64, [A("kb")])
    where(T.kl[:], [[0, 1]], OP.is_gt, -LOW - 0.175, 0, 0, A("kl"), (T.m1[:, 0:1], A("m1")))
    for ph in range(2):
        iota(xw[ph][:, XC + XD:XW], [[0, 256]], 0, 0, [A("xw%d" % ph, XC + XD, XW)], 256)
    fill(T.hz[:], 0.0, [A("hz")], 272 if HASH else 544)
    for j, i, a, b in ((21, 0, -2.0, -1.0), (23, 0, -32.0, 32.0), (25, 6, 0.0625, 1.0), (27, 0, -16.0, RND(0) - QC)):
        act(cf(j), cf(i), AF.Copy, [rc(i)], [rc(j)], scale=a, bias=b)
    blocks("rcp", ((0, 8, 1 / 32), (8, 24, 1.0), (24, 40, -2.0 ** -14), (40, 48, -1 / 32), (48, 64, -1.0), (64, 80, 0.0)))
    blocks("g8", ((0, 8, 512.0),))
    for name, f in (("nid", -1.0), ("i31", 31.0), ("big", WIPE), ("nbig", -WIPE)) + (() if HASH else (("idf", 1.0), ("nidf", -1.0))):
        times(T[name][:], T.idn[:], [A(name)], [A("idn")], scale=f)
    ts(T.nidh[:], T.idn[:], -1.0, OP.mult, [A("idn")], [A("nidh")])
    ts(T.p65[:], T.pm[:], 2.0 if HASH else 65.0, OP.mult, [A("pm")], [A("p65")], n=256)
    ts(T.n65[:], T.pm[:], -2.0 if HASH else -65.0, OP.mult, [A("pm")], [A("n65")], n=256)
    times(T.nk[:], T.idn[:], [A("nk")], [A("idn"), rc(23)], scale=cf(23))
    for t in range(3):
        ts(T.gw[:, t:24:3], T.m1[:, 0:8], cf(25), OP.is_equal, [A("m1"), rc(25), rc(21)], [A("gw", t, t + 1)], (), 64.0 if t == 1 else cf(21), OP.mult)
    act(T.gw[:, 24:48], T.gw[:, 0:24], AF.Copy, [A("gw", 0, 3)], [A("gw", 3, 4)], scale=-1.0)
    ts(T.nbl[:], T.mg[:], cf(3), OP.is_equal, [A("mg"), rc(3)], [A("nbl")], (), -32.0, OP.mult, n=128)
    ts(T.low[:], T.m64[:], cf(4), OP.is_gt, [A("m64"), rc(4)], [A("low")], n=128)
    tt(T.t1[:], T.nbl[:], T.low[:], OP.mult, [A("nbl"), A("low")], [A("t1")], n=256)
    for name, f in (("dup", 1.0), ("hdup", WIPE), ("ndup", -WIPE)):
        diagonal(name, f, 0, True)
    for b in range(2):
        diagonal("dup2", 1.0, 128 * b, "half")
    iota(T.mk32[:], [[0, 32]], 1, 0, [A("mk32")], 32)
    where(T.mk32[:], [[0, 2], [-64, 2], [0, 8]], OP.is_ge, 0.0, 0, 1, A("mk32"))
    where(T.mk32[:], [[0, 2], [64, 2], [0, 8]], OP.is_gt, 0.0, 64, -1, A("mk32"))
    ts(T.icn[:], T.icf[:], cf(6), OP.subtract, [A("icf"), rc(6)], [A("icn")])
    ts(T.mr[:], T.si[:], cf(0), OP.is_equal, [A("si"), rc(0)], [A("mr")], n=128)
    cp(T.cl[:], T.clf[:], [A("clf")], [A("cl")])
    where(T.ke[:, 0::16], [[0, 8]], OP.is_gt, LOW, 0, 0, A("ke"))
    stage(-1, "next")
    mms([(C(T.p7, 128 * j, 128 * j + 128), T.pm[:, 128 * j:128 * j + 128], T.idh[:]) for j in range(4)], 512, [A("pm"), A("idh")], [7])
    cp(T.pmt[:], T.p7[:], [], [A("pmt")], [7], n=512)
    convert(1, 0)
    for c in range(1, 4):
        convert(0, c)
        convert(1, c)

    def cls(ph, c, first=0, step=4):
        return slice(512 * ph + c + first, 512 * ph + 512, step)

    def banks(ph):
        return T["p%d" % ph], T["p%d" % (2 + ph)], T["p%d" % (4 + 2 * ph)], T["p%d" % (5 + 2 * ph)]

    def lists(s, B):
        ph, c = s % 2, (s // 2) % 4
        E, M = MM(ph, c, "ef"), MM(ph, c)
        pu = T["p%d" % B]
        d = C(pu, 0, 128)
        mms([(d, T.idn[:], T.cd[:]), (d, T.id15[:], T.ef[:, cls(ph, c)]), (d, T.big15[:], T.mm[:, cls(ph, c)])]
            + [(C(pu, 128 + 64 * par, 192 + 64 * par), T.pm[:, 256 * par + 128 * b:256 * par + 128 * b + 128], T.ef[:, cls(ph, c, 4 * b, 8)])
               for par in range(2) for b in range(2)], 640, E + M + [A("idn"), A("cd"), A("id15"), A("big15"), A("pm")], [B])
        ts(T.el16[:, 256 * s:256 * s + 256], C(pu, 0, 256), 2048.0 + XC, OP.add, [], [A("el16", s, s + 1)], [B], n=256)

    def turned(s):
        ph, c = s % 2, (s // 2) % 4
        E, pe = MM(ph, c, "ef"), banks(ph)[0]
        mms([(C(pe, 0, 128), T.one[0:1, :], T.ch[0:1, 192:320]), (C(pe, 0, 128), T.ef[:, cls(ph, c)], T.ih32[:]),
             (C(pe, 128, 256), T.sm[:, cls(ph, c)], T.idn[:])], 384, E + MM(ph, c, "sm") + [A("idn"), A("ih32"), A("ch"), A("one")], [ph])
        act(T.es[:, ESW * ph:ESW * ph + 256], C(pe, 0, 256), AF.Copy, [], [A("es", ph, ph + 1)], [ph], n=256)

    def head(s):
        ph = s % 2
        all_x, RX = xw[ph][:, 0:XC + 4096], A("xw%d" % ph, 0, XC + 4096)
        raw, RR = (xw[ph][:, XR:2 * XR], A("xw%d" % ph, XR, 2 * XR)) if s < 2 - ADD else (all_x, RX)
        qq, EL = T["qq%d" % ph], A("el16", s, s + 1)
        ev = EV if s else EV0
        for h, lo, hi in [(0, lo, min(lo + EW, ev)) for lo in range(0, ev, EW)] + [(1, ev, 1024)]:
            stage(s, "e%d" % h)
            if lo < hi:
                out = qq[:, QC + 2 * lo:QC + 2 * hi:2]
                src = raw.indirect(T.el16[:, 256 * s + 128 + lo // 16:256 * s + 128 + hi // 16])
                W, less = [("qe", 1024 * ph + lo, 1024 * ph + hi)], -DEL if s < 2 - ADD else 0.0
                if h == 0:
                    ts(out, src, less, OP.add, [RR, EL], W, cost=("gather", hi - lo))
                else:
                    act(out, src, AF.Copy, [RR, EL], W, cost=("gather", hi - lo), bias=less)
        for h, (lo, hi) in enumerate(zip(DCUT[:-1], DCUT[1:])):
            n, o = hi - lo, slice(2048 * ph + lo, 2048 * ph + hi)
            stage(s, "d%d" % h)
            act(T.d0[:, o], raw.indirect(T.el16[:, 256 * s + lo // 16:256 * s + hi // 16]), AF.Relu, [RR, EL], [("d0", o.start, o.stop)],
                cost=("gather", n))
            stage(s, "g%d" % h)
            scn(T.bb[:, o], T.d0[:, o], T.alt[:, 0:n], DEL, OP.subtract, OP.min, [("d0", o.start, o.stop), A("alt")], [("bb", o.start, o.stop)], n // 2)
            tt(qq[:, QC + lo + 1:QC + hi:2], all_x.indirect(T.el16[:, 256 * s + 192 + lo // 32:256 * s + 192 + hi // 32]),
               T.bb[:, o.start:o.stop:2], OP.min, [RX, EL, ("bb", o.start, o.stop)], [("qo", o.start // 2, o.stop // 2)], cost=("gather", n // 2))

    def plus(out, name, k, lo, n, sign=1):
        return (out, (T.one if sign > 0 else T.non)[0:k, :], T[name][0:k, lo:lo + n])

    def passing(out, name, lo, n, k=1, k2=None):
        return [plus(out, name, k, lo, n), plus(out, name, k2 or k, lo, n, -1)]
    ONES = [A("one"), A("non")]

    def hop(s, par):
        ph, c = s % 2, (s // 2) % 4
        pe, pu, ya, yb = banks(ph)
        (p, B, r), (pl, BL) = ((pu, 2 + ph, 0), (C(pe, 0, 64), ph)) if par else ((pe, ph, 64), (C(yb, 256, 320), 5 + 2 * ph))
        qq = T["qq%d" % ph]
        z = 2 * ph + par
        stage(s, "hop%d" % par)
        out = p[:, r:r + 64, 0:3]
        sums = [[(p[:, r + k:r + 64:8, 0:3], qq[:, QC + 2 * k + par::16], T.gw[:, 24 * j:24 * j + 24]) for k in range(8)] for j in range(2)]
        mmx([plus(out, "cs", 33, 0, 192) + (True, False)], 192, ONES + [A("cs")], [B])
        lst = sums[0] + passing(out, "cs", 192, 192) + sums[1] + passing(out, "cs", 384, 192, 33, 65)
        for lo in (0, 10):
            mmx([a + (False, j == 19) for j, a in enumerate(lst)][lo:lo + 10], 896, [("qo" if par else "qe", 1024 * ph, 1024 * ph + 1024), A("gw"), A("cs")] + ONES, [B])
        o, ES = slice(64 * z, 64 * z + 64), A("es", ph, ph + 1)

        def rg(b):
            return A(b, z, z + 1)
        z0 = 17 * z
        def prod(i):
            return [(pl, T.hz[:, z0 + 1 - b:z0 + 17 - b, :], i[:, b::2]) for b in range(2)]

        def e65(m):
            return [(pl, m[:, 256 * par + 128 * b:256 * par + 128 * b + 128], T.ef[:, cls(ph, c, 4 * b, 8)]) for b in range(2)]
        RH = [A("idf"), A("nidf"), A("ch"), A("n65"), A("p65"), A("idh"), A("nidh")] + ONES + MM(ph, c, "ef")
        if HASH:
            tt(T.ta[:, o], p[:, r:r + 64, 2], T.es[:, ESW * ph + par:ESW * ph + 128:2], OP.mult, [ES], [rg("ta")], [B])
            stage(s, "hx%d" % par)
            ts(T.tb[:, o], T.ta[:, o], 5, OP.arith_shift_right, [rg("ta")], [rg("tb")], (), 4095, OP.bitwise_and)
            ts(T.hz[:, z0 + 1:z0 + 17:2, :], T.tb[:, o], -2048.0, OP.add, [rg("tb")], [rg("hz")])
            stage(s, "hop%d" % par)
            mmx([a + (j == 0, False) for j, a in enumerate(e65(T.n65))], 128, RH, [BL])
            mmx([a + (False, False) for a in prod(T.nidh)], 128, RH + [rg("hz")], [BL])
            lst = [(pl, T.nidh[:], T.kb[:])] + passing(pl, "ch", 128, 64) + e65(T.p65) + prod(T.idh) + [(pl, T.idh[:], T.kb[:])]
            mmx([a + (False, j == 7) for j, a in enumerate(lst)], 512, RH + [rg("hz"), A("kb")], [BL])
        else:
            tt(T.hz[:, z0 + 1:z0 + 17:2, :], p[:, r:r + 64, 2], T.es[:, ESW * ph + par:ESW * ph + 128:2], OP.mult, [ES], [rg("hz")], [B])
            mmx([plus(pl, "ch", 1, 0, 64) + (True, False)], 64, ONES + [A("ch")], [BL])
            lst = prod(T.nidf) + passing(pl, "ch", 64, 64) + e65(T.n65) + [(pl, T.nidh[:], T.kb[:])] + passing(pl, "ch", 128, 64) \
                + e65(T.p65) + prod(T.idf) + [(pl, T.idh[:], T.kb[:])]
            for lo, hi, n, R in ((0, 6, 768, []), (6, 14, 896, [A("kb")])):
                mmx([a + (False, j == 13) for j, a in enumerate(lst)][lo:hi], n, [rg("hz")] + R + RH, [BL])
        ts(T.h16[:, 128 * s + 64 * par:128 * s + 64 * par + 64], pl, RND(0), OP.add, [], [A("h16", 2 * s + par, 2 * s + par + 1)], [BL], RND(0) - 2047.0, OP.subtract)
        stage(s, "gate%d" % par)
        e0 = ESW * ph + 128 + par
        tt(T.us[:, 128 * z:128 * z + 128], p[:, r:r + 64, 0:2], T.es[:, e0:e0 + 128], OP.mult, [ES, A("esp")], [rg("us")], [B], n=128)

    def look(s, par):
        ph = s % 2
        qq, Q = T["qq%d" % ph], ("qo" if par else "qe", 1024 * ph, 1024 * ph + 1024)
        items, RX = xw[ph][:, XC:XC + 4096], A("xw%d" % ph, 0, XC + 4096)
        z = 2 * ph + par
        H16, h0 = A("h16", 2 * s + par, 2 * s + par + 1), 128 * s + 64 * par
        ns = YS[par]
        for x, (lo, hi) in enumerate(((0, min(ns, 512)), (512, ns))):
            if lo >= hi:
                continue
            n, cols = hi - lo, slice(1024 * z + lo, 1024 * z + hi)
            stage(s, "y%d%d" % (par, x))
            act(T.yb[:, cols], items.indirect(T.h16[:, h0 + lo // 16:h0 + hi // 16]), AF.Copy, [RX, H16], [("yb", cols.start, cols.stop)],
                cost=("gather", n))
            ps, B = C(banks(ph)[2 + x], 0, n), 4 + 2 * ph + x
            mmx([(ps, T.nid[:], qq[:, QC + 2 * lo + par:QC + 2 * hi:2], True, False)], n, [A("nid"), Q], [B])
            mmx([(ps, T.idn[:], T.yb[:, cols], False, True)], n, [A("idn"), ("yb", cols.start, cols.stop)], [B])
            stage(s, "s%d%d" % (par, x))
            act(T.sg[:, 2048 * ph + 2 * lo + par:2048 * ph + 2 * hi:2], ps, AF.Sign, [], [("sg", cols.start, cols.stop)], [B], n=n)
        if ns < 1024:
            lo, hi = 1024 * z + ns, 1024 * z + 1024
            cols = slice(2048 * ph + 2 * ns + par, 2048 * ph + 2048, 2)
            stage(s, "v%d" % par)
            tt(T.dq[:, cols], items.indirect(T.h16[:, h0 + ns // 16:h0 + 64]), qq[:, QC + 2 * ns + par:QC + 2048:2], OP.subtract,
               [RX, H16, Q], [("dq", lo, hi)], cost=("gather", hi - lo))
            ts(T.sg[:, cols], T.dq[:, cols], 1.0, OP.min, [("dq", lo, hi)], [("sg", lo, hi)], (), -1.0, OP.max, n=(hi - lo) // 2)

    def mid(s):
        ph, c = s % 2, (s // 2) % 4
        pe, pu = banks(ph)[:2]
        hop(s, 0)
        hop(s, 1)
        sig, ES = T.es[:, ESW * ph + 128:ESW * ph + 256], A("es", ph, ph + 1)
        look(s, 0)
        look(s, 1)
        stage(s, "score")
        mmx([(C(pu, 384, 512), T.sm[:, cls(ph, c)], T.nk[:], True, False)], 128, MM(ph, c, "sm") + [A("nk")], [2 + ph])
        for par in range(2):
            z, out = 2 * ph + par, C(pu, 384 + par, 512, 2)
            US, many = A("us", z, z + 1), T.us[:, 128 * z + 1:128 * z + 128:2]
            mmx([(out, T.nid[:], T.us[:, 128 * z:128 * z + 128:2], False, False)], 64, [A("nid"), US], [2 + ph])
            mmx([(C(pu, 384 + k, 512, 16), T.sg[:, 2048 * ph + k:2048 * ph + 2048:16], T.g8[:], False, False) for k in range(par, 16, 2)]
                + [(out, T.big[:], many, False, False), (out, T.nbig[:], many, False, par == 1)],
                640, [("sg", 2048 * ph + 1024 * par, 2048 * ph + 1024 * par + 1024), A("g8"), A("big"), A("nbig"), US], [2 + ph])
        stage(s, "keys")
        kt, KT = T.kt[:, 128 * s:128 * s + 128], A("kt", s, s + 1)
        tt(kt, C(pu, 384, 512), sig, OP.mult, [ES], [KT], [2 + ph], n=128)
        scn(T.sc[:, 128 * s:128 * s + 128], T.ke[:], kt, LOW, OP.min, OP.max, [A("ke"), KT], [A("sc", s, s + 1)], 128)

    def send(s):
        t = s // 2
        dst = T.cores[(rank + 1 + t % (n_ranks - 1)) % n_ranks]
        es = topo.engines(core, dst)[:8]
        mask = sum(1 << e for e in es)
        rid, pid, _ = topo.addr(dst)
        src = T.cores[(rank - 1 - t % (n_ranks - 1)) % n_ranks]
        n_in = len(topo.engines(src, core)[:8])
        name, o = "aq%d" % s, slice(QW * s, QW * s + 176)
        i = node("g", [lambda e: e.remote_dma(T.lq[:, o], T.qd[:, o], T.sem[name], T.sem.ls, pid, rid, mask)],
                 CALL, [A("qd", 3 * s, 3 * s + 3), A("qd0")], [], (), "r", len(es))
        node(None, [], 0.0, [], [A("lq", s, s + 1)], (), "a", (name, n_in), LAND, (i,))

    def tail(s):
        ph = s % 2
        qq = T["qq%d" % ph]
        pe, pu, ya, yb = banks(ph)
        stage(s, "tail1")
        tt(T.lm[:], T.sc[:, 128 * s:128 * s + 128].indirect(T.cl[:, 0:8]), T.mr[:], OP.mult, [A("sc", s, s + 1), A("cl"), A("mr")], [A("lm")],
           cost=("gather", 128))
        kl, CT = C(pu, 0, 40), ONES + [A("ct")]
        mmx([plus(kl, "ct", 33, 0, 40) + (True, False)], 64, CT, [2 + ph])
        lst = [(kl, T.lm[:], T.rcp[:, 0:40])] + passing(kl, "ct", 40, 40) + [(kl, T.lm[:], T.rcp[:, 40:80]), plus(C(pu, 0, 8), "ct", 33, 80, 8)]
        mmx([a + (False, j == 4) for j, a in enumerate(lst)], 704, CT + [A("lm"), A("rcp")], [2 + ph])
        ts(T.l16[:], C(pu, 0, 8), RND(0), OP.add, [rc(27)], [A("l16")], [2 + ph], cf(27), OP.subtract)
        n0, UN = QW * s, A("qd", 3 * s + 1, 3 * s + 2)
        tt(T.qd[:, n0 + 128:n0 + 160], C(pu, 8, 40), T.mk32[:], OP.mult, [A("mk32")], [UN], [2 + ph])
        cp(T.qd[:, n0:n0 + 128], qq[:].indirect(T.l16[:]), [("qe", 1024 * ph, 1024 * ph + 1024), ("qo", 1024 * ph, 1024 * ph + 1024), A("l16")],
           [A("qd", 3 * s, 3 * s + 1)], cost=("gather", 128))
        stage(s, "tail2")
        scn(T.qd[:, n0 + 161:n0 + 177], T.qd[:, n0 + 144:n0 + 160], T.z16[:], 0.0, OP.add, OP.max, [UN, A("z16")], [A("qd", 3 * s + 2, 3 * s + 3)], 16)
        send(s)

    def kappa(s):
        act(T.kj[:], T.sc[:, 128 * s - 113:128 * s + 128:16], AF.Sign, [A("sc", s - 1, s + 1), A("kl")], [A("kc")], bias=T.kl[:], accum_out=T.kc[:])
        act(T.kd[:], T.kc[:], AF.Copy, [A("kc")], [A("kd")], scale=0.5)
        kp = C(banks(KB)[2], 508, 509)
        mms([plus(kp, "ct", 1, 8, 1), (kp, T.non[:], T.kd[:])] + passing(kp, "ct", 48, 1) + [(kp, T.one[:], T.kd[:])], 320,
            ONES + [A("ct"), A("kd")], [4 + 2 * KB])
        ts(T.kb[:], T.one[:, 0:64], kp, OP.mult, [A("one")], [A("kb")], [4 + 2 * KB], 33 / 64, OP.add)

    def update(s, k, bk, at, name):
        t, n = s // 2, 128 * k
        c, phs = t % 4, [z % 2 for z in range(s, s + k)]
        o, cols = slice(128 * s, 128 * s + n), slice(512 * phs[0] + c, 512 * phs[-1] + 512, 4)
        E, M, NW, HF = [MM(ph, c, "ef")[0] for ph in phs], [MM(ph, c)[0] for ph in phs], A("nw", s, s + k), A("hf", s, s + k)
        pe = T["p%d" % bk]
        ef, en, mn = T.ef[:, cols], C(pe, 0, n), C(pe, n, 2 * n)
        stage(at, name)
        ts(T.hf[:, o], T.h16[:, o], -2048.0, OP.add, [A("h16", 2 * s, 2 * s + 2 * k)], [HF], n=n // 2)
        tt(T.nw[:, o], T.sc[:, o].indirect(T.cl[:, 0:8 * k]), T.kt[:, o], OP.not_equal, [A("kt", s, s + k), A("cl"), A("sc", s, s + k)], [NW], cost=("gather", n))
        keep = t + 4 < RO
        for z in range(k):
            mmx([(C(pe, 128 * z + j % 2, 128 * z + 128, 2), T.pmt[:, 128 * j:128 * j + 128], T.hf[:, 128 * (s + z) + 64 * (j // 2):128 * (s + z) + 64 * (j // 2) + 64],
                  z + j == 0, False) for j in range(4)], 256, [HF, A("pmt")], [bk])
        mmx([(en, T.nidh[:], ef, False, False), (mn, T.idn[:], T.mm[:, cols], False, False)], 2 * n, E + M + [A("nidh"), A("idn")], [bk])
        for z in range(k):
            nw, a, b = T.nw[:, 128 * (s + z):128 * (s + z) + 128], C(pe, 128 * z, 128 * z + 128), C(pe, n + 128 * z, n + 128 * z + 128)
            mmx([(a, nw, T.big[:], False, False), (a, nw, T.nbig[:], False, False), (b, nw, T.idn[:], False, False)], 384, [NW, A("big"), A("nbig"), A("idn")], [bk])
        mmx([(en, T.idh[:], ef, False, True)], n, E + [A("idh")], [bk])
        YL = [A("yl%d%d" % (ph, c)) for ph in phs]
        if keep:
            cp(ef, en, [], E, [bk], n=n)
        elif UPD == "v":
            ts(T.ylb[:, cols], en, 2048.0, OP.add, [], YL, [bk], n=n)
        else:
            act(T.ylb[:, cols], en, AF.Copy, [], YL, [bk], n=n, bias=2048.0)
        act(T.mm[:, cols], mn, AF.Abs, [], M, [bk], n=n, bias=-1.0)
        if keep:
            act(T.sm[:, cols], T.mm[:, cols], AF.Copy, M, [MM(ph, c, "sm")[0] for ph in phs], n=n, scale=-2.0, bias=1.0)

    def back(ph, which):
        for z, q in enumerate(RELU[ph]):
            if q in which:
                ap, rg = xw[ph][:, XC + 1024 * z:XC + 1024 * z + 1024], A("xw%d" % ph, XC + 1024 * z, XC + 1024 * z + 1024)
                if q in "sS":
                    act(ap, ap, AF.Relu, [rg], [rg], n=1024)
                else:
                    ts(ap, ap, 0.0, OP.max, [rg], [rg], n=512)

    def arrive(s):
        ph = s % 2
        stage(s, "arrive")
        win, WX = xw[ph][:, XC:XW], A("xw%d" % ph, XC, XW)
        last = s >= ST - 2
        if last:
            stage(s, "back0")
            back(ph, "SV")
            stage(s, "arrive")
        lt, L = T.lt[:, 16 * s:16 * s + 16], A("lt", s, s + 1)
        ya, yb = banks(ph)[2:]
        n0, LQ, tg = QW * s, A("lq", s, s + 1), C(yb, 16, 32)
        nf = T.lq[:, n0 + 144:n0 + 160]
        mms([(C(ya, 128 * b, 128 * b + 128), T.dup2[:, 128 * b:128 * b + 128], T.lq[:, n0:n0 + 128]) for b in range(2)], 256,
            [A("dup2"), LQ], [4 + 2 * ph])
        mmx([(tg, T.i31[:], T.icn[:], True, False), plus(tg, "ct", 33, 88, 16) + (False, False)], 128, ONES + [A("ct"), A("i31"), A("icn")], [5 + 2 * ph])
        mmx([(tg, T.t1[:], nf, False, False), (tg, T.dup[:], T.lq[:, n0 + 128:n0 + 144], False, False), (tg, T.nbl[:], T.lq[:, n0 + 160:n0 + 176], False, False),
             (tg, T.hdup[:], nf, False, False), (tg, T.ndup[:], nf, False, False), (tg, T.idn[:], T.icn[:], False, True)], 384,
            [A("t1"), A("dup"), A("nbl"), A("hdup"), A("ndup"), A("idn"), A("icn"), LQ], [5 + 2 * ph])
        ts(lt, tg, float(XD), OP.add, [], [L], [5 + 2 * ph])
        act(T.qw[:], C(ya, 0, 256), AF.Copy, [], [A("qw")], [4 + 2 * ph], n=256, bias=2049.5)
        tt(T.av[:], win.indirect(lt), T.qw[:], OP.add, [WX, L, A("qw")], [A("av")], cost=("gather", 256))
        ts(T.ax[:], T.av[:], 0.5, OP.mult, [A("av")], [A("ax")], (), -1025.0 - (0.0 if last else DEL), OP.add, n=128)
        cp(win.indirect(lt), T.ax[:], [A("ax"), L], [WX], cost=("scatter", 256))
        if last:
            stage(s, "back1")
            back(ph, "sv")
            dma(STORES[ph][4], T.yx[64 * ph:64 * ph + 64, :], xw[ph][0:64, XC:XR], [A("xw%d" % ph, XC, XR)], [],
                DLAT + 524288 / DBW + DROW + (0.0 if ph else OUTL[2]))

    def lists_out(ph):
        for b in range(2):
            dma(STORES[ph][b], T.ym[64 * ph:64 * ph + 64, 512 * b:512 * b + 512], T.mm[64 * b:64 * b + 64, 512 * ph:512 * ph + 512], MM(ph), [], OUTL[ph])
            dma(STORES[ph][2 + b], T.yl[64 * ph:64 * ph + 64, 512 * b:512 * b + 512], T.ylb[64 * b:64 * b + 64, 512 * ph:512 * ph + 512],
                [A("yl%d%d" % (ph, c)) for c in range(4)], [], OUTL[ph])

    for ph in range(2):
        stage(-1, "soon")
        lists(ph, 2 + ph)
        turned(ph)
    stage(-1, "next")
    for s in EARLY:
        lists(s, 6)
    for s in range(ST):
        if s >= 2:
            arrive(s - 2)
        head(s)
        mid(s)
        tail(s)
        if s % 2 and s + 2 < ST:
            stage(s, "kappa")
            kappa(s)
        if s == 1:
            update(0, 2, 1, s, "keep")
        if s == ST - 2:
            for z in range(2, ST - 2, 2):
                update(z, 2, z % 4, s, "late%d" % (z // 2))
        if s >= ST - 2:
            update(s, 1, s % 2, s, "update")
        if s + 2 < ST:
            stage(s, "lists")
            if s + 2 not in EARLY:
                lists(s + 2, 2 + s % 2)
            stage(s, "turn")
            turned(s + 2)
        else:
            stage(s, "store")
            lists_out(s % 2)
    arrive(ST - 2)
    arrive(ST - 1)

    n = len(nodes)
    before = [[] for _ in range(n)]
    for i, d in enumerate(nodes):
        for j in d["deps"] | d["order"]:
            f = nodes[j]
            lag = f["late"] + ((WAKE[0] if f["q"] == d["q"] else WAKE[1] + MORE.get(f["q"], 0.0)) if j in d["deps"] else 0.0)
            before[i].append((j, lag))

    ORDER["x"] = (nodes, before)
    if "order" not in ORDER:
        ORDER["order"] = arrange(nodes, before)
    orders, fin = ORDER["order"][1], ORDER["order"][2]

    cnt = {q: 0 for q in eng}
    known = {q: {} for q in eng}
    stamp, snap = {}, {}
    nloc = 0
    for i in orders:
        d = nodes[i]
        q = d["q"]
        if q is None:
            stamp[i] = (d["key"][0], 1, d["key"][1])
            snap[i] = {}
            continue
        kq = known[q]
        latest = {}
        for j in d["deps"]:
            s, k, v = stamp[j]
            if s not in latest or latest[s][0] < k:
                latest[s] = (k, v, j)
        for s in sorted(latest, key=lambda s: -fin[latest[s][2]]):
            k, v, j = latest[s]
            if kq.get(s, 0) >= k:
                continue
            eng[q].wait_ge(T.sem[s], v)
            kq[s] = k
            for s2, k2 in snap[j].items():
                if k2 > kq.get(s2, 0):
                    kq[s2] = k2
        snap[i] = dict(kq)
        if d["kind"] == "d":
            d["calls"][0](eng[q]).then_inc(T.sem[d["key"]], 16)
            stamp[i] = (d["key"], 1, 16)
        elif d["kind"] == "r":
            d["calls"][0](eng[q])
            nloc += d["key"]
            stamp[i] = ("ls", nloc, nloc)
        else:
            for f in d["calls"]:
                f(eng[q]).then_inc(T.sem[semname[q]], 1)
                cnt[q] += 1
            stamp[i] = (semname[q], cnt[q], cnt[q])
    for q in ("v", "s", "p", "g"):
        g.wait_ge(T.sem[semname[q]], cnt[q])
    for j in range(ndma[0]):
        g.wait_ge(T.sem["dm%d" % j], 16)
    g.wait_ge(T.sem.ls, nloc)
